import numpy as np
import ml_dtypes


def mxq(x, axis, fmt="e4m3"):
    dtype, down = {"e4m3": (ml_dtypes.float8_e4m3fn, 7), "e5m2": (ml_dtypes.float8_e5m2, 14)}[fmt]
    v = np.moveaxis(np.asarray(x, np.float32).astype(ml_dtypes.bfloat16).astype(np.float64), axis, -1)
    blocks = v.reshape(v.shape[:-1] + (-1, 32))
    amax = np.abs(blocks).max(-1, keepdims=True)
    byte = np.maximum(np.where(amax > 0, np.frexp(amax)[1] - 1 + 127, 0) - down, 1)
    scale = np.exp2(byte - 127.0)
    codes = (blocks / scale).astype(np.float32).astype(dtype).astype(np.float64)
    return np.moveaxis((codes * scale).reshape(v.shape), -1, axis)


WIDE = False


def mx_kscale(k):
    if not WIDE:
        return np.ones(k)
    levels = np.array([10, -10, 5, -5, 0])
    if k % 512:
        return np.exp2(np.random.permutation(np.resize(levels, k // 32))).repeat(32)
    a = np.empty((k // 512, 16))
    for p in range(k // 512):
        a[p, :8] = np.random.permutation(np.resize(levels, 8))
        for g in range(8):
            far = levels[np.abs(levels - a[p, g]) >= 10]
            a[p, g + 8] = far[np.random.randint(len(far))]
    return np.exp2(a.ravel()).repeat(32)


def f64(x):
    return np.asarray(x).astype(np.float64)


def striped(idx):
    return np.tile(idx.reshape(-1, 16).T, (8, 1)).astype(np.uint16)


def unstriped(offs):
    return offs[:16].T.reshape(-1).astype(np.int64)


E2M1 = np.array([0.0, 0.5, 1.0, 1.5, 2.0, 3.0, 4.0, 6.0, -0.0, -0.5, -1.0, -1.5, -2.0, -3.0, -4.0, -6.0])


def pack_weight(w, fmt):
    k, n = w.shape
    w = f64(np.asarray(w, np.float32).astype(ml_dtypes.bfloat16)).reshape(k // 32, 32, n)
    amax = np.abs(w).max(1)
    if fmt == "e4m3":
        byte = np.frexp(amax)[1] - 1 + 127 - 7
    else:
        mant, ex = np.frexp(amax / 6.0)
        byte = np.where(mant > 0.5, ex, ex - 1) + 127
    byte = np.clip(np.where(amax > 0, byte, 1), 1, 254)
    scaled = (w * np.exp2(127.0 - byte)[:, None, :]).reshape(k, n).astype(np.float32)
    by_word = np.ascontiguousarray(scaled.reshape(k // 512, 128, 4, n).transpose(0, 1, 3, 2))
    if fmt == "e4m3":
        words = by_word.astype(ml_dtypes.float8_e4m3fn).view(np.uint8)
    else:
        c = by_word.astype(ml_dtypes.float4_e2m1fn).view(np.uint8) & 0xF
        words = (c[..., 0::2] | (c[..., 1::2] << 4)).reshape(k // 512, 128, 2 * n)
    return np.ascontiguousarray(words), np.ascontiguousarray(byte.astype(np.uint8).reshape(k // 512, 16, n))


def unpack_weight(words, scales, fmt):
    g, _, n = scales.shape
    words = np.ascontiguousarray(words).reshape(g, 128, n, -1)
    if fmt == "e4m3":
        vals = words.view(ml_dtypes.float8_e4m3fn).astype(np.float64)
    else:
        nib = np.empty((g, 128, n, 4), np.uint8)
        nib[..., 0::2] = words & 0xF
        nib[..., 1::2] = words >> 4
        vals = E2M1[nib]
    vals = vals * np.repeat(np.exp2(scales.astype(np.float64) - 127.0), 8, axis=1)[..., None]
    return vals.transpose(0, 1, 3, 2).reshape(g * 512, n)


def gelu(v):
    return 0.5 * v * (1.0 + np.tanh(np.sqrt(2.0 / np.pi) * (v + 0.044715 * v**3)))


def striped8(idx):
    return np.concatenate([v.reshape(-1, 16).T for v in idx]).astype(np.uint16)


def unstriped8(offs):
    return np.stack([offs[16 * g:16 * g + 16].T.reshape(-1) for g in range(8)]).astype(np.int64)


def put_heads(h, wgs, idx8, t2):
    r = np.arange(h.shape[0])
    page = np.zeros((h.shape[0], t2))
    page[r[:, None], idx8[r % 512 // 64]] = wgs[r // 4 % 128] * h
    return page


K, T, S, H, T2, N = 1536, 2048, 1024, 1024, 2048, 384

def setup_inputs():
    n = np.random.standard_normal
    s = mx_kscale(K)[:, None]
    u = mx_kscale(H)[:, None]
    tab_words, tab_scales = pack_weight(n((K, T)) * s, "e4m3")
    w4_words, w4_scales = pack_weight(n((K, H)) / np.sqrt(K) / s, "e2m1")
    return {
        "tab_words": tab_words, "tab_scales": tab_scales,
        "offs": striped(np.random.permutation(T)[:S]),
        "w4_words": w4_words, "w4_scales": w4_scales,
        "offs2": striped8(np.stack([np.random.permutation(T2)[:S] for _ in range(8)])),
        "wgs": np.repeat(np.random.uniform(0.5, 2.0, (8, S)), 16, axis=0).astype(np.float32),
        "rack": n((H, T2)).astype(np.float32),
        "sharp": np.random.uniform(0.15, 0.4, H).astype(np.float32),
        "gain": (np.exp(0.3 * n(H)) * u[:, 0]).astype(np.float32),
        "w2": (n((H, N)) / np.sqrt(H) / u).astype(np.float32),
    }

def reference(tab_words, tab_scales, offs, w4_words, w4_scales, offs2, wgs, rack, sharp, gain, w2):
    v = unpack_weight(tab_words, tab_scales, "e4m3")[:, unstriped(offs)]
    w4 = unpack_weight(w4_words, w4_scales, "e2m1")
    h = w4.T @ v
    page = put_heads(h, f64(wgs), unstriped8(offs2), T2)
    d2 = np.square(page - f64(rack))
    z = f64(gain)[:, None] * np.exp(-(f64(sharp)[:, None] * d2))
    out = mxq(f64(w2), 0, "e4m3").T @ mxq(z, 0, "e4m3")
    return out

@@ -1,0 +1,322 @@
+from contextlib import ExitStack
+
+import concourse.mybir as mybir
+from concourse.masks import make_identity
+
+K, T, S, H, T2, N = 1536, 2048, 1024, 1024, 2048, 384
+FLOPS = 2 * K * H * S + 2 * H * N * T2
+
+F32 = mybir.dt.float32
+BF16 = mybir.dt.bfloat16
+I32 = mybir.dt.int32
+U32 = mybir.dt.uint32
+U16 = mybir.dt.uint16
+U8 = mybir.dt.uint8
+FP8X4 = mybir.dt.float8_e4m3fn_x4
+FP4X4 = mybir.dt.float4_e2m1fn_x4
+ACT = mybir.ActivationFunctionType
+ALU = mybir.AluOpType
+
+P = 128
+PACK = 4
+KA = K // (P * PACK)
+RB = H // (P * PACK)
+SLOTS = RB * PACK
+BANK = 512
+CHUNKS = T2 // BANK
+HALVES = S // BANK
+NT = N // P
+SHIFT_ROWS = 112
+H_BUFS = 8
+PAGES = 3
+SQ_BUFS = 3
+VECTOR_CHUNKS = 1
+
+
+def tile_list_pallet_slot_fit_kernel(tc, tab_words, tab_scales, offs, w4_words, w4_scales, offs2, wgs, rack, sharp, gain, w2, out):
+    nc = tc.nc
+    with ExitStack() as ctx:
+        lists = ctx.enter_context(tc.tile_pool(name="lists", bufs=1))
+        keep = ctx.enter_context(tc.tile_pool(name="keep", bufs=1))
+        big = ctx.enter_context(tc.tile_pool(name="big", bufs=1))
+        stage = ctx.enter_context(tc.tile_pool(name="stage", bufs=6))
+        psum = ctx.enter_context(tc.psum_pool(name="psum", bufs=1))
+
+        offs_t = lists.tile([P, S // 16], U16, name="offs_t")
+        offs2_t = lists.tile([P, S // 16], U16, name="offs2_t")
+
+        banks = [psum.tile([P, BANK], F32, name="bank%d" % j) for j in range(8)]
+        turn = [0]
+
+        def next_bank():
+            bank = banks[turn[0] % 8]
+            turn[0] = turn[0] + 1
+            return bank
+
+        tabs_win = big.tile([P, T], U8, name="slot_e", align_bytes=64)
+        w4s_raw = keep.tile([P, H], U8, name="picked0", align_bytes=64)
+        tabs_shift = [keep.tile([P, S], U8, name="tabs_shift%d" % a, align_bytes=64) for a in range(1, KA)]
+        w4s_shift = [keep.tile([P, H], U8, name="w4s_shift%d" % a, align_bytes=64) for a in range(1, KA)]
+        pages = [keep.tile([P, T2], F32, name="page%d" % j, align_bytes=64) for j in range(PAGES - 1)]
+        nc.gpsimd.memset(tabs_win[:].bitcast(I32), 0)
+        nc.gpsimd.memset(w4s_raw[:].bitcast(I32), 0)
+
+        w4_first = big.tile([P, 1, 2 * H], U8, name="slot_d", align_bytes=64)
+        w4_rest = big.tile([P, KA - 1, 2 * H], U8, name="slot_c", align_bytes=64)
+        w4_raw = [w4_first[:, 0, :]] + [w4_rest[:, a, :] for a in range(KA - 1)]
+        nc.sync.dma_start(offs_t[:], offs)
+        nc.sync.dma_start(offs2_t[:], offs2)
+        sharp_t = keep.tile([P, RB, PACK], F32, name="sharp_t")
+        gain_t = keep.tile([P, RB, PACK], F32, name="gain_t")
+        nc.sync.dma_start(w4_first[:].bitcast(I32), w4_words[0:1].rearrange("a p c -> p a c").bitcast(I32))
+        nc.sync.dma_start(w4_rest[:].bitcast(I32), w4_words[1:KA].rearrange("a p c -> p a c").bitcast(I32))
+        for q in range(4):
+            nc.scalar.dma_start(tabs_win[32 * q : 32 * q + 4 * KA, :].bitcast(I32), tab_scales[:, 4 * q : 4 * q + 4, :].bitcast(I32))
+        for q in range(4):
+            nc.gpsimd.dma_start(w4s_raw[32 * q : 32 * q + 4 * KA, :].bitcast(I32), w4_scales[:, 4 * q : 4 * q + 4, :].bitcast(I32))
+        nc.gpsimd.dma_start(sharp_t[:], sharp.rearrange("(b p i) -> p b i", b=RB, i=PACK))
+        nc.gpsimd.dma_start(gain_t[:], gain.rearrange("(b p i) -> p b i", b=RB, i=PACK))
+        tab_win = {}
+
+        def load_table(a, slot):
+            tab_win[a] = big.tile([P, T], I32, name=slot, align_bytes=64)
+            nc.sync.dma_start(tab_win[a][:], tab_words[a].rearrange("p t i -> p (t i)").bitcast(I32))
+
+        load_table(1, "slot_a")
+        load_table(0, "slot_b")
+        for t in tabs_shift + w4s_shift:
+            nc.vector.memset(t[:].bitcast(I32), 0)
+        for page in pages:
+            nc.vector.memset(page[:], 0.0)
+        ident = keep.tile([P, P], F32, name="ident", align_bytes=64)
+        make_identity(nc, ident[:])
+
+        w4_ord = [keep.tile([P, 2 * H], U8, name="w4_ord%d" % a, align_bytes=64) for a in range(KA)]
+        for a in range(KA):
+            nc.vector.tensor_copy(
+                w4_ord[a][:].bitcast(U16).rearrange("p (b i m) -> p b i m", b=RB, i=PACK),
+                w4_raw[a].bitcast(U16).rearrange("p (b m i) -> p b i m", b=RB, i=PACK),
+            )
+        wgs_t = big.tile([P, S], F32, name="slot_d", align_bytes=64)
+        nc.sync.dma_start(wgs_t[:], wgs)
+        last_page = big.tile([P, T2], F32, name="slot_c", align_bytes=64)
+        nc.gpsimd.memset(last_page[:], 0.0)
+        pages.append(last_page)
+
+        picked = {}
+
+        def gather_words(a, pieces):
+            picked[a] = keep.tile([P, S], U32, name="picked%d" % a, align_bytes=64)
+            width = S // pieces
+            for u in range(pieces):
+                nc.vector.tensor_copy(
+                    picked[a][:, u * width : (u + 1) * width],
+                    tab_win[a][:].bitcast(U32).indirect(offs_t[:, u * width // 16 : (u + 1) * width // 16]),
+                )
+
+        gather_words(1, 1)
+        load_table(2, "slot_a")
+        tabs_g = keep.tile([P, S], U8, name="tabs_g", align_bytes=64)
+        nc.vector.tensor_copy(tabs_g[:], tabs_win[:].indirect(offs_t[:]))
+        for a in range(1, KA):
+            nc.gpsimd.dma_start(tabs_shift[a - 1][0:SHIFT_ROWS, :].bitcast(I32), tabs_g[4 * a : 4 * a + SHIFT_ROWS, :].bitcast(I32))
+        w4s_ord = keep.tile([P, H], U8, name="w4s_ord", align_bytes=64)
+        nc.vector.tensor_copy(
+            w4s_ord[:].rearrange("p (b i m) -> p b i m", b=RB, i=PACK),
+            w4s_raw[:].rearrange("p (b m i) -> p b i m", b=RB, i=PACK),
+        )
+        for a in range(1, KA):
+            nc.scalar.dma_start(w4s_shift[a - 1][0:SHIFT_ROWS, :].bitcast(I32), w4s_ord[4 * a : 4 * a + SHIFT_ROWS, :].bitcast(I32))
+        tab_planes = [tabs_g] + tabs_shift
+        w4_planes = [w4s_ord] + w4s_shift
+        gather_words(0, HALVES)
+        gather_words(2, HALVES)
+
+        rack_rows = rack.rearrange("(b p i) m -> b i p m", b=RB, i=PACK)
+        racks = {}
+
+        def load_rack(s):
+            racks[s] = big.tile([P, T2], F32, name=("slot_b", "slot_e", "slot_a")[s % 3], align_bytes=64)
+            nc.sync.dma_start(racks[s][:], rack_rows[s // PACK, s % PACK])
+
+        load_rack(0)
+        w2_raw = big.tile([P, RB, PACK, N], F32, name="slot_a", align_bytes=64)
+        nc.sync.dma_start(w2_raw[:].rearrange("p b i n -> p b (i n)"), w2.rearrange("(b p i) n -> p b (i n)", b=RB, i=PACK))
+        load_rack(1)
+
+        neg_sharp = keep.tile([P, SLOTS], F32, name="neg_sharp")
+        ln_gain = keep.tile([P, SLOTS], F32, name="ln_gain")
+        nc.scalar.activation(ln_gain[:], gain_t[:].rearrange("p b i -> p (b i)"), ACT.Ln)
+        nc.scalar.mul(neg_sharp[:], sharp_t[:].rearrange("p b i -> p (b i)"), -1.0)
+
+        h_tiles = [keep.tile([P, S], F32, name="h%d" % j, align_bytes=64) for j in range(H_BUFS)]
+
+        def h_pass(bank, s, u, a):
+            cols = slice(u * BANK, (u + 1) * BANK)
+            nc.tensor.matmul_mx(
+                out=bank[:],
+                lhsT=w4_ord[a][:, 2 * P * s : 2 * P * (s + 1)].bitcast(FP4X4),
+                lhsT_scale=w4_planes[a][:, P * s : P * (s + 1)],
+                rhs=picked[a][:, cols].bitcast(FP8X4),
+                rhs_scale=tab_planes[a][:, cols],
+                start=(a == 0),
+                stop=(a == KA - 1),
+            )
+
+        def h_out(bank, s, u):
+            nc.scalar.mul(h_tiles[s % H_BUFS][:, u * BANK : (u + 1) * BANK], bank[:], -1.0)
+
+        def h_slot(s):
+            for u in range(HALVES):
+                bank = next_bank()
+                for a in range(KA):
+                    h_pass(bank, s, u, a)
+                h_out(bank, s, u)
+
+        first = [(s, u, next_bank()) for s in range(4) for u in range(HALVES)]
+        for s, u, bank in first:
+            h_pass(bank, s, u, 0)
+        for s, u, bank in first[:4]:
+            h_pass(bank, s, u, 1)
+        h_pass(first[0][2], 0, 0, 2)
+        h_out(first[0][2], 0, 0)
+        for s, u, bank in first[4:]:
+            h_pass(bank, s, u, 1)
+        for s, u, bank in first[1:]:
+            h_pass(bank, s, u, 2)
+            h_out(bank, s, u)
+        for s in range(4, 6):
+            h_slot(s)
+        ring = [banks[3], banks[2], banks[1]]
+
+        w2_bf = keep.tile([P, RB * N * PACK], BF16, name="w2_bf", align_bytes=64)
+        w2_codes = keep.tile([P, RB * N], U32, name="w2_codes", align_bytes=64)
+        w2_scales = keep.tile([P, RB * N], U8, name="w2_scales", align_bytes=64)
+        for b in range(RB):
+            nc.scalar.copy(
+                w2_bf[:, b * N * PACK : (b + 1) * N * PACK].rearrange("p (n i) -> p n i", i=PACK),
+                w2_raw[:, b].rearrange("p i n -> p n i"),
+            )
+        load_rack(2)
+
+        def quantise_w2():
+            for lo, hi in ((0, 512), (512, RB * N)):
+                nc.vector.quantize_mx(out=w2_codes[:, lo:hi].bitcast(FP8X4), scales=w2_scales[:, lo:hi], in_=w2_bf[:, PACK * lo : PACK * hi])
+
+        sq_tiles = [keep.tile([P, BANK], F32, name="sq%d" % j, align_bytes=64) for j in range(SQ_BUFS)]
+        pairs = [keep.tile([P, 2, BANK, 2], BF16, name="pairs%d" % c, align_bytes=64) for c in range(CHUNKS)]
+        z_bf = [keep.tile([P, BANK * PACK], BF16, name="z_bf%d" % c, align_bytes=64) for c in range(CHUNKS)]
+        z_codes = [[keep.tile([P, BANK], U32, name="z_codes%d_%d" % (b, c), align_bytes=64) for c in range(CHUNKS)] for b in range(RB)]
+        z_scales = [[keep.tile([P, BANK], U8, name="z_scales%d_%d" % (b, c), align_bytes=64) for c in range(CHUNKS)] for b in range(RB)]
+
+        def scatter(s, pieces):
+            page = pages[s % PAGES]
+            width = S // pieces
+            for u in range(pieces):
+                cols = slice(u * width, (u + 1) * width)
+                nc.vector.tensor_tensor(
+                    page[:].indirect(offs2_t[:, u * width // 16 : (u + 1) * width // 16]),
+                    h_tiles[s % H_BUFS][:, cols],
+                    wgs_t[:, cols],
+                    ALU.mult,
+                )
+
+        def exp_into_pairs(src, s, c):
+            i = s % PACK
+            nc.scalar.activation(pairs[c][:, i // 2, :, i % 2], src, ACT.Exp, bias=ln_gain[:, s : s + 1], scale=neg_sharp[:, s : s + 1])
+
+        def add_on_vector(s, c):
+            cols = slice(c * BANK, (c + 1) * BANK)
+            nc.vector.tensor_tensor(racks[s][:, cols], racks[s][:, cols], pages[s % PAGES][:, cols], ALU.add)
+
+        def square_from_sbuf(s, c, sq):
+            nc.scalar.activation(sq[:], racks[s][:, c * BANK : (c + 1) * BANK], ACT.Square)
+
+        def add_and_square_turned(s, c, bank, sq):
+            for j in range(BANK // P):
+                cols = slice(c * BANK + j * P, c * BANK + (j + 1) * P)
+                nc.tensor.matmul(bank[:, j * P : (j + 1) * P], racks[s][:, cols], ident[:], start=True, stop=False, is_transpose=True)
+                nc.tensor.matmul(bank[:, j * P : (j + 1) * P], pages[s % PAGES][:, cols], ident[:], start=False, stop=True, is_transpose=True)
+            nc.scalar.activation(sq[:], bank[:], ACT.Square)
+
+        def turn_back_and_exp(s, c, bank, sq):
+            for j in range(BANK // P):
+                nc.tensor.transpose(bank[:, j * P : (j + 1) * P], sq[:, j * P : (j + 1) * P], ident[:])
+            exp_into_pairs(bank[:], s, c)
+
+        def weave(c, on_scalar):
+            dt = U32 if on_scalar else I32
+            dst = z_bf[c][:].bitcast(dt).rearrange("p (m h) -> p m h", h=2)
+            src = pairs[c][:].rearrange("p h m e -> p (h m e)").bitcast(dt).rearrange("p (h m) -> p m h", h=2)
+            if on_scalar:
+                nc.scalar.copy(dst, src)
+            else:
+                nc.vector.tensor_copy(dst, src)
+
+        def quantise_z(b, c):
+            nc.vector.quantize_mx(out=z_codes[b][c][:].bitcast(FP8X4), scales=z_scales[b][c][:], in_=z_bf[c][:])
+
+        def out_pass(bank, b, c, t, opens):
+            cols = slice(b * N + t * P, b * N + (t + 1) * P)
+            nc.tensor.matmul_mx(
+                out=bank[:],
+                lhsT=w2_codes[:, cols].bitcast(FP8X4),
+                lhsT_scale=w2_scales[:, cols],
+                rhs=z_codes[b][c][:].bitcast(FP8X4),
+                rhs_scale=z_scales[b][c][:],
+                start=opens,
+                stop=not opens,
+            )
+
+        for s in range(SLOTS - 1):
+            x, y, z = ring if s % 2 == 0 else ring[::-1]
+            scatter(s, HALVES if s == 0 else 1)
+            add_on_vector(s, 3)
+            if s == 1:
+                quantise_w2()
+            square_from_sbuf(s, 3, sq_tiles[2])
+            exp_into_pairs(sq_tiles[2][:], s, 3)
+            add_and_square_turned(s, 0, x, sq_tiles[0])
+            add_and_square_turned(s, 1, y, sq_tiles[1])
+            turn_back_and_exp(s, 0, z, sq_tiles[0])
+            add_and_square_turned(s, 2, x, sq_tiles[2])
+            turn_back_and_exp(s, 1, y, sq_tiles[1])
+            turn_back_and_exp(s, 2, z, sq_tiles[2])
+            if s + 3 < SLOTS:
+                load_rack(s + 3)
+            if s == PACK - 1:
+                for c in range(CHUNKS):
+                    weave(c, True)
+                    quantise_z(0, c)
+            if s < 2:
+                turn[0] = 4 + 2 * s
+                h_slot(6 + s)
+
+        last = SLOTS - 1
+        scatter(last, 1)
+        for c in range(CHUNKS):
+            add_on_vector(last, c)
+        out_banks = ring + banks[4:8] + [banks[0]]
+        for t in range(NT):
+            out_pass(out_banks[t], 0, 0, t, True)
+        for c in range(CHUNKS):
+            sq = sq_tiles[2 - c % 2]
+            square_from_sbuf(last, c, sq)
+            exp_into_pairs(sq[:], last, c)
+        for c in range(CHUNKS):
+            weave(c, False)
+            quantise_z(1, c)
+        for c in range(CHUNKS):
+            for t in range(NT):
+                bank = out_banks[(c * NT + t) % 8]
+                out_pass(bank, 1, c, t, c > 0)
+                if c > 0:
+                    out_pass(bank, 0, c, t, False)
+            for t in range(NT):
+                bank = out_banks[(c * NT + t) % 8]
+                res = stage.tile([P, BANK], F32, name="res")
+                if (c * NT + t) % 3 == 1:
+                    nc.vector.tensor_copy(res[:], bank[:])
+                else:
+                    nc.scalar.copy(res[:], bank[:])
+                nc.sync.dma_start(out[t * P : (t + 1) * P, c * BANK : (c + 1) * BANK], res[:])

@@ -28,9 +28,11 @@ HALVES = S // BANK
 NT = N // P
 SHIFT_ROWS = 112
 H_BUFS = 8
-PAGES = 3
+PAGES = 2
 SQ_BUFS = 3
 VECTOR_CHUNKS = 1
+H_FIRST = 4
+WEAVE_ON_SCALAR = 3
 
 
 def tile_list_pallet_slot_fit_kernel(tc, tab_words, tab_scales, offs, w4_words, w4_scales, offs2, wgs, rack, sharp, gain, w2, out):
@@ -53,29 +55,25 @@ def tile_list_pallet_slot_fit_kernel(tc, tab_words, tab_scales, offs, w4_words, 
             turn[0] = turn[0] + 1
             return bank
 
-        tabs_win = big.tile([P, T], U8, name="slot_e", align_bytes=64)
-        w4s_raw = keep.tile([P, H], U8, name="picked0", align_bytes=64)
+        tabs_win = keep.tile([P, T], U8, name="picked0", align_bytes=64)
+        w4s_raw = keep.tile([P, H], U8, name="tabs_g", align_bytes=64)
         tabs_shift = [keep.tile([P, S], U8, name="tabs_shift%d" % a, align_bytes=64) for a in range(1, KA)]
         w4s_shift = [keep.tile([P, H], U8, name="w4s_shift%d" % a, align_bytes=64) for a in range(1, KA)]
-        pages = [keep.tile([P, T2], F32, name="page%d" % j, align_bytes=64) for j in range(PAGES - 1)]
+        pages = [keep.tile([P, T2], F32, name="page%d" % j, align_bytes=64) for j in range(PAGES)]
         nc.gpsimd.memset(tabs_win[:].bitcast(I32), 0)
         nc.gpsimd.memset(w4s_raw[:].bitcast(I32), 0)
 
-        w4_first = big.tile([P, 1, 2 * H], U8, name="slot_d", align_bytes=64)
-        w4_rest = big.tile([P, KA - 1, 2 * H], U8, name="slot_c", align_bytes=64)
-        w4_raw = [w4_first[:, 0, :]] + [w4_rest[:, a, :] for a in range(KA - 1)]
+        w4_raw = [big.tile([P, 2 * H], U8, name=slot, align_bytes=64) for slot in ("slot_b", "slot_c", "slot_d")]
         nc.sync.dma_start(offs_t[:], offs)
         nc.sync.dma_start(offs2_t[:], offs2)
         sharp_t = keep.tile([P, RB, PACK], F32, name="sharp_t")
         gain_t = keep.tile([P, RB, PACK], F32, name="gain_t")
-        nc.sync.dma_start(w4_first[:].bitcast(I32), w4_words[0:1].rearrange("a p c -> p a c").bitcast(I32))
-        nc.sync.dma_start(w4_rest[:].bitcast(I32), w4_words[1:KA].rearrange("a p c -> p a c").bitcast(I32))
+        for a in range(KA):
+            nc.sync.dma_start(w4_raw[a][:].bitcast(I32), w4_words[a].bitcast(I32))
         for q in range(4):
             nc.scalar.dma_start(tabs_win[32 * q : 32 * q + 4 * KA, :].bitcast(I32), tab_scales[:, 4 * q : 4 * q + 4, :].bitcast(I32))
         for q in range(4):
             nc.gpsimd.dma_start(w4s_raw[32 * q : 32 * q + 4 * KA, :].bitcast(I32), w4_scales[:, 4 * q : 4 * q + 4, :].bitcast(I32))
-        nc.gpsimd.dma_start(sharp_t[:], sharp.rearrange("(b p i) -> p b i", b=RB, i=PACK))
-        nc.gpsimd.dma_start(gain_t[:], gain.rearrange("(b p i) -> p b i", b=RB, i=PACK))
         tab_win = {}
 
         def load_table(a, slot):
@@ -83,11 +81,11 @@ def tile_list_pallet_slot_fit_kernel(tc, tab_words, tab_scales, offs, w4_words, 
             nc.sync.dma_start(tab_win[a][:], tab_words[a].rearrange("p t i -> p (t i)").bitcast(I32))
 
         load_table(1, "slot_a")
-        load_table(0, "slot_b")
+        nc.sync.dma_start(sharp_t[:], sharp.rearrange("(b p i) -> p b i", b=RB, i=PACK))
+        nc.sync.dma_start(gain_t[:], gain.rearrange("(b p i) -> p b i", b=RB, i=PACK))
         for t in tabs_shift + w4s_shift:
             nc.vector.memset(t[:].bitcast(I32), 0)
-        for page in pages:
-            nc.vector.memset(page[:], 0.0)
+        nc.vector.memset(pages[0][:], 0.0)
         ident = keep.tile([P, P], F32, name="ident", align_bytes=64)
         make_identity(nc, ident[:])
 
@@ -95,13 +93,12 @@ def tile_list_pallet_slot_fit_kernel(tc, tab_words, tab_scales, offs, w4_words, 
         for a in range(KA):
             nc.vector.tensor_copy(
                 w4_ord[a][:].bitcast(U16).rearrange("p (b i m) -> p b i m", b=RB, i=PACK),
-                w4_raw[a].bitcast(U16).rearrange("p (b m i) -> p b i m", b=RB, i=PACK),
+                w4_raw[a][:].bitcast(U16).rearrange("p (b m i) -> p b i m", b=RB, i=PACK),
             )
-        wgs_t = big.tile([P, S], F32, name="slot_d", align_bytes=64)
-        nc.sync.dma_start(wgs_t[:], wgs)
-        last_page = big.tile([P, T2], F32, name="slot_c", align_bytes=64)
-        nc.gpsimd.memset(last_page[:], 0.0)
-        pages.append(last_page)
+        load_table(0, "slot_b")
+        w2_raw = big.tile([P, RB, PACK, N], F32, name="slot_c", align_bytes=64)
+        nc.sync.dma_start(w2_raw[:].rearrange("p b i n -> p b (i n)"), w2.rearrange("(b p i) n -> p b (i n)", b=RB, i=PACK))
+        load_table(2, "slot_d")
 
         picked = {}
 
@@ -114,19 +111,21 @@ def tile_list_pallet_slot_fit_kernel(tc, tab_words, tab_scales, offs, w4_words, 
                     tab_win[a][:].bitcast(U32).indirect(offs_t[:, u * width // 16 : (u + 1) * width // 16]),
                 )
 
+        nc.vector.memset(pages[1][:], 0.0)
         gather_words(1, 1)
-        load_table(2, "slot_a")
-        tabs_g = keep.tile([P, S], U8, name="tabs_g", align_bytes=64)
-        nc.vector.tensor_copy(tabs_g[:], tabs_win[:].indirect(offs_t[:]))
-        for a in range(1, KA):
-            nc.gpsimd.dma_start(tabs_shift[a - 1][0:SHIFT_ROWS, :].bitcast(I32), tabs_g[4 * a : 4 * a + SHIFT_ROWS, :].bitcast(I32))
+        wgs_t = big.tile([P, S], F32, name="slot_a", align_bytes=64)
+        nc.sync.dma_start(wgs_t[:], wgs)
         w4s_ord = keep.tile([P, H], U8, name="w4s_ord", align_bytes=64)
         nc.vector.tensor_copy(
             w4s_ord[:].rearrange("p (b i m) -> p b i m", b=RB, i=PACK),
             w4s_raw[:].rearrange("p (b m i) -> p b i m", b=RB, i=PACK),
         )
         for a in range(1, KA):
-            nc.scalar.dma_start(w4s_shift[a - 1][0:SHIFT_ROWS, :].bitcast(I32), w4s_ord[4 * a : 4 * a + SHIFT_ROWS, :].bitcast(I32))
+            nc.gpsimd.dma_start(w4s_shift[a - 1][0:SHIFT_ROWS, :].bitcast(I32), w4s_ord[4 * a : 4 * a + SHIFT_ROWS, :].bitcast(I32))
+        tabs_g = keep.tile([P, S], U8, name="tabs_g", align_bytes=64)
+        nc.vector.tensor_copy(tabs_g[:], tabs_win[:].indirect(offs_t[:]))
+        for a in range(1, KA):
+            nc.gpsimd.dma_start(tabs_shift[a - 1][0:SHIFT_ROWS, :].bitcast(I32), tabs_g[4 * a : 4 * a + SHIFT_ROWS, :].bitcast(I32))
         tab_planes = [tabs_g] + tabs_shift
         w4_planes = [w4s_ord] + w4s_shift
         gather_words(0, HALVES)
@@ -136,20 +135,20 @@ def tile_list_pallet_slot_fit_kernel(tc, tab_words, tab_scales, offs, w4_words, 
         racks = {}
 
         def load_rack(s):
-            racks[s] = big.tile([P, T2], F32, name=("slot_b", "slot_e", "slot_a")[s % 3], align_bytes=64)
+            racks[s] = big.tile([P, T2], F32, name=("slot_b", "slot_d")[s] if s < 2 else "h%d" % (s - 2), align_bytes=64)
             nc.sync.dma_start(racks[s][:], rack_rows[s // PACK, s % PACK])
 
         load_rack(0)
-        w2_raw = big.tile([P, RB, PACK, N], F32, name="slot_a", align_bytes=64)
-        nc.sync.dma_start(w2_raw[:].rearrange("p b i n -> p b (i n)"), w2.rearrange("(b p i) n -> p b (i n)", b=RB, i=PACK))
         load_rack(1)
 
         neg_sharp = keep.tile([P, SLOTS], F32, name="neg_sharp")
         ln_gain = keep.tile([P, SLOTS], F32, name="ln_gain")
         nc.scalar.activation(ln_gain[:], gain_t[:].rearrange("p b i -> p (b i)"), ACT.Ln)
+        warm = keep.tile([P, 1], F32, name="warm")
+        nc.scalar.activation(warm[:], ln_gain[:, 0:1], ACT.Exp)
         nc.scalar.mul(neg_sharp[:], sharp_t[:].rearrange("p b i -> p (b i)"), -1.0)
 
-        h_tiles = [keep.tile([P, S], F32, name="h%d" % j, align_bytes=64) for j in range(H_BUFS)]
+        h_tiles = [big.tile([P, S], F32, name="h%d" % j, align_bytes=64) for j in range(H_BUFS)]
 
         def h_pass(bank, s, u, a):
             cols = slice(u * BANK, (u + 1) * BANK)
@@ -166,45 +165,40 @@ def tile_list_pallet_slot_fit_kernel(tc, tab_words, tab_scales, offs, w4_words, 
         def h_out(bank, s, u):
             nc.scalar.mul(h_tiles[s % H_BUFS][:, u * BANK : (u + 1) * BANK], bank[:], -1.0)
 
-        def h_slot(s):
+        def h_slot(s, two_banks=None):
             for u in range(HALVES):
-                bank = next_bank()
+                bank = two_banks[u] if two_banks else next_bank()
                 for a in range(KA):
                     h_pass(bank, s, u, a)
                 h_out(bank, s, u)
 
-        first = [(s, u, next_bank()) for s in range(4) for u in range(HALVES)]
+        first = [(s, u, next_bank()) for u in range(HALVES) for s in range(2)]
         for s, u, bank in first:
             h_pass(bank, s, u, 0)
-        for s, u, bank in first[:4]:
+        for s, u, bank in sorted(first, key=lambda item: item[:2]):
             h_pass(bank, s, u, 1)
-        h_pass(first[0][2], 0, 0, 2)
-        h_out(first[0][2], 0, 0)
-        for s, u, bank in first[4:]:
-            h_pass(bank, s, u, 1)
-        for s, u, bank in first[1:]:
             h_pass(bank, s, u, 2)
             h_out(bank, s, u)
-        for s in range(4, 6):
+        for s in range(2, H_FIRST):
             h_slot(s)
-        ring = [banks[3], banks[2], banks[1]]
+        ring = [banks[(2 * H_FIRST - 1 - j) % 8] for j in range(3)]
+        spare = [bank for bank in banks if not any(bank is r for r in ring)]
 
         w2_bf = keep.tile([P, RB * N * PACK], BF16, name="w2_bf", align_bytes=64)
         w2_codes = keep.tile([P, RB * N], U32, name="w2_codes", align_bytes=64)
         w2_scales = keep.tile([P, RB * N], U8, name="w2_scales", align_bytes=64)
         for b in range(RB):
-            nc.scalar.copy(
-                w2_bf[:, b * N * PACK : (b + 1) * N * PACK].rearrange("p (n i) -> p n i", i=PACK),
-                w2_raw[:, b].rearrange("p i n -> p n i"),
-            )
-        load_rack(2)
-
-        def quantise_w2():
-            for lo, hi in ((0, 512), (512, RB * N)):
-                nc.vector.quantize_mx(out=w2_codes[:, lo:hi].bitcast(FP8X4), scales=w2_scales[:, lo:hi], in_=w2_bf[:, PACK * lo : PACK * hi])
+            for t in range(NT):
+                lo = b * N + t * P
+                nc.scalar.copy(
+                    w2_bf[:, lo * PACK : (lo + P) * PACK].rearrange("p (n i) -> p n i", i=PACK),
+                    w2_raw[:, b, :, t * P : (t + 1) * P].rearrange("p i n -> p n i"),
+                )
+        for lo, hi in ((0, 512), (512, RB * N)):
+            nc.vector.quantize_mx(out=w2_codes[:, lo:hi].bitcast(FP8X4), scales=w2_scales[:, lo:hi], in_=w2_bf[:, PACK * lo : PACK * hi])
 
         sq_tiles = [keep.tile([P, BANK], F32, name="sq%d" % j, align_bytes=64) for j in range(SQ_BUFS)]
-        pairs = [keep.tile([P, 2, BANK, 2], BF16, name="pairs%d" % c, align_bytes=64) for c in range(CHUNKS)]
+        pairs = [[keep.tile([P, 2, BANK, 2], BF16, name="pairs%d_%d" % (b, c), align_bytes=64) for c in range(CHUNKS)] for b in range(RB)]
         z_bf = [keep.tile([P, BANK * PACK], BF16, name="z_bf%d" % c, align_bytes=64) for c in range(CHUNKS)]
         z_codes = [[keep.tile([P, BANK], U32, name="z_codes%d_%d" % (b, c), align_bytes=64) for c in range(CHUNKS)] for b in range(RB)]
         z_scales = [[keep.tile([P, BANK], U8, name="z_scales%d_%d" % (b, c), align_bytes=64) for c in range(CHUNKS)] for b in range(RB)]
@@ -223,7 +217,7 @@ def tile_list_pallet_slot_fit_kernel(tc, tab_words, tab_scales, offs, w4_words, 
 
         def exp_into_pairs(src, s, c):
             i = s % PACK
-            nc.scalar.activation(pairs[c][:, i // 2, :, i % 2], src, ACT.Exp, bias=ln_gain[:, s : s + 1], scale=neg_sharp[:, s : s + 1])
+            nc.scalar.activation(pairs[s // PACK][c][:, i // 2, :, i % 2], src, ACT.Exp, bias=ln_gain[:, s : s + 1], scale=neg_sharp[:, s : s + 1])
 
         def add_on_vector(s, c):
             cols = slice(c * BANK, (c + 1) * BANK)
@@ -244,10 +238,10 @@ def tile_list_pallet_slot_fit_kernel(tc, tab_words, tab_scales, offs, w4_words, 
                 nc.tensor.transpose(bank[:, j * P : (j + 1) * P], sq[:, j * P : (j + 1) * P], ident[:])
             exp_into_pairs(bank[:], s, c)
 
-        def weave(c, on_scalar):
+        def weave(b, c, on_scalar):
             dt = U32 if on_scalar else I32
             dst = z_bf[c][:].bitcast(dt).rearrange("p (m h) -> p m h", h=2)
-            src = pairs[c][:].rearrange("p h m e -> p (h m e)").bitcast(dt).rearrange("p (h m) -> p m h", h=2)
+            src = pairs[b][c][:].rearrange("p h m e -> p (h m e)").bitcast(dt).rearrange("p (h m) -> p m h", h=2)
             if on_scalar:
                 nc.scalar.copy(dst, src)
             else:
@@ -269,54 +263,62 @@ def tile_list_pallet_slot_fit_kernel(tc, tab_words, tab_scales, offs, w4_words, 
             )
 
         for s in range(SLOTS - 1):
-            x, y, z = ring if s % 2 == 0 else ring[::-1]
+            x, y, z = (ring[(s + j) % 3] for j in range(3))
             scatter(s, HALVES if s == 0 else 1)
-            add_on_vector(s, 3)
-            if s == 1:
-                quantise_w2()
-            square_from_sbuf(s, 3, sq_tiles[2])
-            exp_into_pairs(sq_tiles[2][:], s, 3)
+            if s + 2 < SLOTS:
+                load_rack(s + 2)
+            if s == 0:
+                add_and_square_turned(s, 3, z, sq_tiles[2])
+                turn_back_and_exp(s, 3, spare[4], sq_tiles[2])
+            else:
+                add_on_vector(s, 3)
+                square_from_sbuf(s, 3, sq_tiles[2])
+                exp_into_pairs(sq_tiles[2][:], s, 3)
             add_and_square_turned(s, 0, x, sq_tiles[0])
             add_and_square_turned(s, 1, y, sq_tiles[1])
-            turn_back_and_exp(s, 0, z, sq_tiles[0])
-            add_and_square_turned(s, 2, x, sq_tiles[2])
-            turn_back_and_exp(s, 1, y, sq_tiles[1])
-            turn_back_and_exp(s, 2, z, sq_tiles[2])
-            if s + 3 < SLOTS:
-                load_rack(s + 3)
-            if s == PACK - 1:
+            later = (z, x, y, z) if s < SLOTS - 2 else (spare[0], z, spare[1], spare[2])
+            turn_back_and_exp(s, 0, later[0], sq_tiles[0])
+            add_and_square_turned(s, 2, later[1], sq_tiles[2])
+            turn_back_and_exp(s, 1, later[2], sq_tiles[1])
+            turn_back_and_exp(s, 2, later[3], sq_tiles[2])
+            if H_FIRST + s < SLOTS:
+                h_slot(H_FIRST + s, spare[2 * (s % 2) : 2 * (s % 2) + 2])
+            if s == PACK:
                 for c in range(CHUNKS):
-                    weave(c, True)
+                    weave(0, c, c < WEAVE_ON_SCALAR)
                     quantise_z(0, c)
-            if s < 2:
-                turn[0] = 4 + 2 * s
-                h_slot(6 + s)
 
         last = SLOTS - 1
         scatter(last, 1)
         for c in range(CHUNKS):
             add_on_vector(last, c)
-        out_banks = ring + banks[4:8] + [banks[0]]
-        for t in range(NT):
-            out_pass(out_banks[t], 0, 0, t, True)
-        for c in range(CHUNKS):
-            sq = sq_tiles[2 - c % 2]
-            square_from_sbuf(last, c, sq)
-            exp_into_pairs(sq[:], last, c)
-        for c in range(CHUNKS):
-            weave(c, False)
+        all_banks = ring + spare
+        early = (0, 1)
+        out_banks = {(c, t): all_banks[(0,1,2,3,4,5,6,7,0,1,2,3)[c * NT + t]] for c in range(CHUNKS) for t in range(NT)}
+        for c in early:
+            for t in range(NT):
+                out_pass(out_banks[c, t], 0, c, t, True)
+
+        def finish_z(c):
+            square_from_sbuf(last, c, sq_tiles[2])
+            exp_into_pairs(sq_tiles[2][:], last, c)
+            weave(1, c, False)
             quantise_z(1, c)
-        for c in range(CHUNKS):
+
+        def finish_out(c):
             for t in range(NT):
-                bank = out_banks[(c * NT + t) % 8]
-                out_pass(bank, 1, c, t, c > 0)
-                if c > 0:
-                    out_pass(bank, 0, c, t, False)
+                out_pass(out_banks[c, t], 1, c, t, c not in early)
+                if c not in early:
+                    out_pass(out_banks[c, t], 0, c, t, False)
             for t in range(NT):
-                bank = out_banks[(c * NT + t) % 8]
                 res = stage.tile([P, BANK], F32, name="res")
-                if (c * NT + t) % 3 == 1:
-                    nc.vector.tensor_copy(res[:], bank[:])
+                if c * NT + t in (5,7,9,11):
+                    nc.vector.tensor_copy(res[:], out_banks[c, t][:])
                 else:
-                    nc.scalar.copy(res[:], bank[:])
+                    nc.scalar.copy(res[:], out_banks[c, t][:])
                 nc.sync.dma_start(out[t * P : (t + 1) * P, c * BANK : (c + 1) * BANK], res[:])
+
+        for c in range(CHUNKS):
+            finish_z(c)
+        for c in range(CHUNKS):
+            finish_out(c)

@@ -1,7 +1,6 @@
 from contextlib import ExitStack
 
 import concourse.mybir as mybir
-from concourse.masks import make_identity
 
 K, T, S, H, T2, N = 1536, 2048, 1024, 1024, 2048, 384
 FLOPS = 2 * K * H * S + 2 * H * N * T2
@@ -29,10 +28,12 @@ NT = N // P
 SHIFT_ROWS = 112
 H_BUFS = 8
 PAGES = 2
-SQ_BUFS = 3
+SQ_BUFS = 4
 VECTOR_CHUNKS = 1
-H_FIRST = 4
-WEAVE_ON_SCALAR = 3
+H_FIRST = 8
+WEIGH_FIRST = 4
+POOL_SQUARES = ()
+WEAVE_ON_SCALAR = 4
 
 
 def tile_list_pallet_slot_fit_kernel(tc, tab_words, tab_scales, offs, w4_words, w4_scales, offs2, wgs, rack, sharp, gain, w2, out):
@@ -86,8 +87,6 @@ def tile_list_pallet_slot_fit_kernel(tc, tab_words, tab_scales, offs, w4_words, 
         for t in tabs_shift + w4s_shift:
             nc.vector.memset(t[:].bitcast(I32), 0)
         nc.vector.memset(pages[0][:], 0.0)
-        ident = keep.tile([P, P], F32, name="ident", align_bytes=64)
-        make_identity(nc, ident[:])
 
         w4_ord = [keep.tile([P, 2 * H], U8, name="w4_ord%d" % a, align_bytes=64) for a in range(KA)]
         for a in range(KA):
@@ -99,6 +98,13 @@ def tile_list_pallet_slot_fit_kernel(tc, tab_words, tab_scales, offs, w4_words, 
         w2_raw = big.tile([P, RB, PACK, N], F32, name="slot_c", align_bytes=64)
         nc.sync.dma_start(w2_raw[:].rearrange("p b i n -> p b (i n)"), w2.rearrange("(b p i) n -> p b (i n)", b=RB, i=PACK))
         load_table(2, "slot_d")
+
+        neg_sharp = keep.tile([P, SLOTS], F32, name="neg_sharp")
+        ln_gain = keep.tile([P, SLOTS], F32, name="ln_gain")
+        nc.scalar.activation(ln_gain[:], gain_t[:].rearrange("p b i -> p (b i)"), ACT.Ln)
+        warm = keep.tile([P, 1], F32, name="warm")
+        nc.scalar.activation(warm[:], ln_gain[:, 0:1], ACT.Exp)
+        nc.scalar.mul(neg_sharp[:], sharp_t[:].rearrange("p b i -> p (b i)"), -1.0)
 
         picked = {}
 
@@ -125,7 +131,7 @@ def tile_list_pallet_slot_fit_kernel(tc, tab_words, tab_scales, offs, w4_words, 
         tabs_g = keep.tile([P, S], U8, name="tabs_g", align_bytes=64)
         nc.vector.tensor_copy(tabs_g[:], tabs_win[:].indirect(offs_t[:]))
         for a in range(1, KA):
-            nc.gpsimd.dma_start(tabs_shift[a - 1][0:SHIFT_ROWS, :].bitcast(I32), tabs_g[4 * a : 4 * a + SHIFT_ROWS, :].bitcast(I32))
+            (nc.gpsimd if a == 1 else nc.scalar).dma_start(tabs_shift[a - 1][0:SHIFT_ROWS, :].bitcast(I32), tabs_g[4 * a : 4 * a + SHIFT_ROWS, :].bitcast(I32))
         tab_planes = [tabs_g] + tabs_shift
         w4_planes = [w4s_ord] + w4s_shift
         gather_words(0, HALVES)
@@ -136,21 +142,17 @@ def tile_list_pallet_slot_fit_kernel(tc, tab_words, tab_scales, offs, w4_words, 
 
         def load_rack(s):
             racks[s] = big.tile([P, T2], F32, name=("slot_b", "slot_d")[s] if s < 2 else "h%d" % (s - 2), align_bytes=64)
-            nc.sync.dma_start(racks[s][:], rack_rows[s // PACK, s % PACK])
+            for cols in (slice(0, S), slice(S, T2)) if s == 0 else (slice(0, T2),):
+                (nc.scalar if s < 2 else nc.sync).dma_start(racks[s][:, cols], rack_rows[s // PACK, s % PACK][:, cols])
 
-        load_rack(0)
-        load_rack(1)
-
-        neg_sharp = keep.tile([P, SLOTS], F32, name="neg_sharp")
-        ln_gain = keep.tile([P, SLOTS], F32, name="ln_gain")
-        nc.scalar.activation(ln_gain[:], gain_t[:].rearrange("p b i -> p (b i)"), ACT.Ln)
-        warm = keep.tile([P, 1], F32, name="warm")
-        nc.scalar.activation(warm[:], ln_gain[:, 0:1], ACT.Exp)
-        nc.scalar.mul(neg_sharp[:], sharp_t[:].rearrange("p b i -> p (b i)"), -1.0)
 
         h_tiles = [big.tile([P, S], F32, name="h%d" % j, align_bytes=64) for j in range(H_BUFS)]
 
-        def h_pass(bank, s, u, a):
+        h_raw = list(h_tiles)
+        for s in (1, 2):
+            h_raw[s] = big.tile([P, S], F32, name=("slot_b", "slot_d")[s - 1], align_bytes=64)
+
+        def h_pass(bank, s, u, a, order=(0, 1, 2)):
             cols = slice(u * BANK, (u + 1) * BANK)
             nc.tensor.matmul_mx(
                 out=bank[:],
@@ -158,18 +160,25 @@ def tile_list_pallet_slot_fit_kernel(tc, tab_words, tab_scales, offs, w4_words, 
                 lhsT_scale=w4_planes[a][:, P * s : P * (s + 1)],
                 rhs=picked[a][:, cols].bitcast(FP8X4),
                 rhs_scale=tab_planes[a][:, cols],
-                start=(a == 0),
-                stop=(a == KA - 1),
+                start=(a == order[0]),
+                stop=(a == order[-1]),
             )
 
         def h_out(bank, s, u):
-            nc.scalar.mul(h_tiles[s % H_BUFS][:, u * BANK : (u + 1) * BANK], bank[:], -1.0)
+            cols = slice(u * BANK, (u + 1) * BANK)
+            if s == 0:
+                nc.vector.tensor_tensor(h_tiles[s][:, cols], bank[:], wgs_t[:, cols], ALU.mult)
+            else:
+                nc.scalar.copy(h_raw[s][:, cols], bank[:])
+
+        def weigh(s):
+            nc.gpsimd.tensor_tensor(h_tiles[s][:], h_raw[s][:], wgs_t[:], ALU.mult)
 
         def h_slot(s, two_banks=None):
             for u in range(HALVES):
                 bank = two_banks[u] if two_banks else next_bank()
-                for a in range(KA):
-                    h_pass(bank, s, u, a)
+                for a in (1, 2, 0):
+                    h_pass(bank, s, u, a, (1, 2, 0))
                 h_out(bank, s, u)
 
         first = [(s, u, next_bank()) for u in range(HALVES) for s in range(2)]
@@ -197,23 +206,18 @@ def tile_list_pallet_slot_fit_kernel(tc, tab_words, tab_scales, offs, w4_words, 
         for lo, hi in ((0, 512), (512, RB * N)):
             nc.vector.quantize_mx(out=w2_codes[:, lo:hi].bitcast(FP8X4), scales=w2_scales[:, lo:hi], in_=w2_bf[:, PACK * lo : PACK * hi])
 
-        sq_tiles = [keep.tile([P, BANK], F32, name="sq%d" % j, align_bytes=64) for j in range(SQ_BUFS)]
+        sq_wide = keep.tile([P, 2 * BANK], F32, name="sq_wide", align_bytes=64)
         pairs = [[keep.tile([P, 2, BANK, 2], BF16, name="pairs%d_%d" % (b, c), align_bytes=64) for c in range(CHUNKS)] for b in range(RB)]
         z_bf = [keep.tile([P, BANK * PACK], BF16, name="z_bf%d" % c, align_bytes=64) for c in range(CHUNKS)]
-        z_codes = [[keep.tile([P, BANK], U32, name="z_codes%d_%d" % (b, c), align_bytes=64) for c in range(CHUNKS)] for b in range(RB)]
-        z_scales = [[keep.tile([P, BANK], U8, name="z_scales%d_%d" % (b, c), align_bytes=64) for c in range(CHUNKS)] for b in range(RB)]
+        z_codes = {(1, c): keep.tile([P, BANK], U32, name="z_codes%d" % c, align_bytes=64)[:] for c in range(CHUNKS)}
+        z_scales = {(1, c): keep.tile([P, BANK], U8, name="z_scales%d" % c, align_bytes=64)[:] for c in range(CHUNKS)}
 
         def scatter(s, pieces):
             page = pages[s % PAGES]
             width = S // pieces
             for u in range(pieces):
                 cols = slice(u * width, (u + 1) * width)
-                nc.vector.tensor_tensor(
-                    page[:].indirect(offs2_t[:, u * width // 16 : (u + 1) * width // 16]),
-                    h_tiles[s % H_BUFS][:, cols],
-                    wgs_t[:, cols],
-                    ALU.mult,
-                )
+                nc.vector.tensor_copy(page[:].indirect(offs2_t[:, u * width // 16 : (u + 1) * width // 16]), h_tiles[s][:, cols])
 
         def exp_into_pairs(src, s, c):
             i = s % PACK
@@ -221,26 +225,14 @@ def tile_list_pallet_slot_fit_kernel(tc, tab_words, tab_scales, offs, w4_words, 
 
         def add_on_vector(s, c):
             cols = slice(c * BANK, (c + 1) * BANK)
-            nc.vector.tensor_tensor(racks[s][:, cols], racks[s][:, cols], pages[s % PAGES][:, cols], ALU.add)
+            nc.vector.tensor_tensor(racks[s][:, cols], racks[s][:, cols], pages[s % PAGES][:, cols], ALU.subtract)
 
         def square_from_sbuf(s, c, sq):
-            nc.scalar.activation(sq[:], racks[s][:, c * BANK : (c + 1) * BANK], ACT.Square)
+            nc.scalar.activation(sq, racks[s][:, c * BANK : (c + 1) * BANK], ACT.Square)
 
-        def add_and_square_turned(s, c, bank, sq):
-            for j in range(BANK // P):
-                cols = slice(c * BANK + j * P, c * BANK + (j + 1) * P)
-                nc.tensor.matmul(bank[:, j * P : (j + 1) * P], racks[s][:, cols], ident[:], start=True, stop=False, is_transpose=True)
-                nc.tensor.matmul(bank[:, j * P : (j + 1) * P], pages[s % PAGES][:, cols], ident[:], start=False, stop=True, is_transpose=True)
-            nc.scalar.activation(sq[:], bank[:], ACT.Square)
-
-        def turn_back_and_exp(s, c, bank, sq):
-            for j in range(BANK // P):
-                nc.tensor.transpose(bank[:, j * P : (j + 1) * P], sq[:, j * P : (j + 1) * P], ident[:])
-            exp_into_pairs(bank[:], s, c)
-
-        def weave(b, c, on_scalar):
+        def weave(b, c, target, on_scalar):
             dt = U32 if on_scalar else I32
-            dst = z_bf[c][:].bitcast(dt).rearrange("p (m h) -> p m h", h=2)
+            dst = target.bitcast(dt).rearrange("p (m h) -> p m h", h=2)
             src = pairs[b][c][:].rearrange("p h m e -> p (h m e)").bitcast(dt).rearrange("p (h m) -> p m h", h=2)
             if on_scalar:
                 nc.scalar.copy(dst, src)
@@ -248,7 +240,7 @@ def tile_list_pallet_slot_fit_kernel(tc, tab_words, tab_scales, offs, w4_words, 
                 nc.vector.tensor_copy(dst, src)
 
         def quantise_z(b, c):
-            nc.vector.quantize_mx(out=z_codes[b][c][:].bitcast(FP8X4), scales=z_scales[b][c][:], in_=z_bf[c][:])
+            nc.vector.quantize_mx(out=z_codes[b, c].bitcast(FP8X4), scales=z_scales[b, c], in_=z_bf[c][:])
 
         def out_pass(bank, b, c, t, opens):
             cols = slice(b * N + t * P, b * N + (t + 1) * P)
@@ -256,37 +248,42 @@ def tile_list_pallet_slot_fit_kernel(tc, tab_words, tab_scales, offs, w4_words, 
                 out=bank[:],
                 lhsT=w2_codes[:, cols].bitcast(FP8X4),
                 lhsT_scale=w2_scales[:, cols],
-                rhs=z_codes[b][c][:].bitcast(FP8X4),
-                rhs_scale=z_scales[b][c][:],
+                rhs=z_codes[b, c].bitcast(FP8X4),
+                rhs_scale=z_scales[b, c],
                 start=opens,
                 stop=not opens,
             )
 
+        for s in range(1, WEIGH_FIRST):
+            weigh(s)
+            if s < 3:
+                load_rack(s - 1)
         for s in range(SLOTS - 1):
-            x, y, z = (ring[(s + j) % 3] for j in range(3))
             scatter(s, HALVES if s == 0 else 1)
             if s + 2 < SLOTS:
                 load_rack(s + 2)
-            if s == 0:
-                add_and_square_turned(s, 3, z, sq_tiles[2])
-                turn_back_and_exp(s, 3, spare[4], sq_tiles[2])
-            else:
-                add_on_vector(s, 3)
-                square_from_sbuf(s, 3, sq_tiles[2])
-                exp_into_pairs(sq_tiles[2][:], s, 3)
-            add_and_square_turned(s, 0, x, sq_tiles[0])
-            add_and_square_turned(s, 1, y, sq_tiles[1])
-            later = (z, x, y, z) if s < SLOTS - 2 else (spare[0], z, spare[1], spare[2])
-            turn_back_and_exp(s, 0, later[0], sq_tiles[0])
-            add_and_square_turned(s, 2, later[1], sq_tiles[2])
-            turn_back_and_exp(s, 1, later[2], sq_tiles[1])
-            turn_back_and_exp(s, 2, later[3], sq_tiles[2])
-            if H_FIRST + s < SLOTS:
-                h_slot(H_FIRST + s, spare[2 * (s % 2) : 2 * (s % 2) + 2])
-            if s == PACK:
-                for c in range(CHUNKS):
-                    weave(0, c, c < WEAVE_ON_SCALAR)
-                    quantise_z(0, c)
+            for half in range(2):
+                cols = slice(half * S, (half + 1) * S)
+                nc.gpsimd.tensor_tensor(racks[s][:, cols], racks[s][:, cols], pages[s % PAGES][:, cols], ALU.subtract)
+                sq = sq_wide[:] if (s, half) == (SLOTS - 2, 1) else racks[s][:, cols]
+                if (s, half) in POOL_SQUARES:
+                    nc.gpsimd.tensor_tensor(sq, racks[s][:, cols], racks[s][:, cols], ALU.mult)
+                else:
+                    nc.scalar.activation(sq, racks[s][:, cols], ACT.Square)
+                for j in range(2):
+                    exp_into_pairs(sq[:, j * BANK : (j + 1) * BANK], s, 2 * half + j)
+            if s + WEIGH_FIRST < SLOTS:
+                weigh(s + WEIGH_FIRST)
+            if s in (PACK - 1, PACK):
+                half = s - PACK + 1
+                wide_bf = big.tile([P, 2 * BANK * PACK], BF16, name=("slot_b", "slot_d")[half], align_bytes=64)
+                wide_codes = big.tile([P, 2 * BANK], U32, name="h%d" % (s - 2), align_bytes=64)
+                wide_scales = keep.tile([P, 2 * BANK], U8, name="wide_scales%d" % half, align_bytes=64)
+                for j in range(2):
+                    weave(0, 2 * half + j, wide_bf[:, j * BANK * PACK : (j + 1) * BANK * PACK], True)
+                    z_codes[0, 2 * half + j] = wide_codes[:, j * BANK : (j + 1) * BANK]
+                    z_scales[0, 2 * half + j] = wide_scales[:, j * BANK : (j + 1) * BANK]
+                nc.vector.quantize_mx(out=wide_codes[:].bitcast(FP8X4), scales=wide_scales[:], in_=wide_bf[:])
 
         last = SLOTS - 1
         scatter(last, 1)
@@ -300,9 +297,10 @@ def tile_list_pallet_slot_fit_kernel(tc, tab_words, tab_scales, offs, w4_words, 
                 out_pass(out_banks[c, t], 0, c, t, True)
 
         def finish_z(c):
-            square_from_sbuf(last, c, sq_tiles[2])
-            exp_into_pairs(sq_tiles[2][:], last, c)
-            weave(1, c, False)
+            sq = sq_wide[:, (c % 2) * BANK : (c % 2 + 1) * BANK]
+            square_from_sbuf(last, c, sq)
+            exp_into_pairs(sq, last, c)
+            weave(1, c, z_bf[c][:], False)
             quantise_z(1, c)
 
         def finish_out(c):

@@ -31,7 +31,8 @@ PAGES = 2
 SQ_BUFS = 4
 VECTOR_CHUNKS = 1
 H_FIRST = 8
-WEIGH_FIRST = 4
+AHEAD = 3
+WEIGH_FIRST = AHEAD
 POOL_SQUARES = ()
 WEAVE_ON_SCALAR = 4
 
@@ -52,7 +53,7 @@ def tile_list_pallet_slot_fit_kernel(tc, tab_words, tab_scales, offs, w4_words, 
         turn = [0]
 
         def next_bank():
-            bank = banks[turn[0] % 8]
+            bank = banks[turn[0] % 4]
             turn[0] = turn[0] + 1
             return bank
 
@@ -67,7 +68,7 @@ def tile_list_pallet_slot_fit_kernel(tc, tab_words, tab_scales, offs, w4_words, 
         w4_raw = [big.tile([P, 2 * H], U8, name=slot, align_bytes=64) for slot in ("slot_b", "slot_c", "slot_d")]
         nc.sync.dma_start(offs_t[:], offs)
         nc.sync.dma_start(offs2_t[:], offs2)
-        sharp_t = keep.tile([P, RB, PACK], F32, name="sharp_t")
+        sharp_t = keep.tile([P, RB, PACK], F32, name="wgs", align_bytes=64)
         gain_t = keep.tile([P, RB, PACK], F32, name="gain_t")
         for a in range(KA):
             nc.sync.dma_start(w4_raw[a][:].bitcast(I32), w4_words[a].bitcast(I32))
@@ -106,6 +107,8 @@ def tile_list_pallet_slot_fit_kernel(tc, tab_words, tab_scales, offs, w4_words, 
         nc.scalar.activation(warm[:], ln_gain[:, 0:1], ACT.Exp)
         nc.scalar.mul(neg_sharp[:], sharp_t[:].rearrange("p b i -> p (b i)"), -1.0)
 
+        wgs_t = keep.tile([P, S], F32, name="wgs", align_bytes=64)
+        nc.sync.dma_start(wgs_t[:], wgs)
         picked = {}
 
         def gather_words(a, pieces):
@@ -119,8 +122,6 @@ def tile_list_pallet_slot_fit_kernel(tc, tab_words, tab_scales, offs, w4_words, 
 
         nc.vector.memset(pages[1][:], 0.0)
         gather_words(1, 1)
-        wgs_t = big.tile([P, S], F32, name="slot_a", align_bytes=64)
-        nc.sync.dma_start(wgs_t[:], wgs)
         w4s_ord = keep.tile([P, H], U8, name="w4s_ord", align_bytes=64)
         nc.vector.tensor_copy(
             w4s_ord[:].rearrange("p (b i m) -> p b i m", b=RB, i=PACK),
@@ -131,7 +132,7 @@ def tile_list_pallet_slot_fit_kernel(tc, tab_words, tab_scales, offs, w4_words, 
         tabs_g = keep.tile([P, S], U8, name="tabs_g", align_bytes=64)
         nc.vector.tensor_copy(tabs_g[:], tabs_win[:].indirect(offs_t[:]))
         for a in range(1, KA):
-            (nc.gpsimd if a == 1 else nc.scalar).dma_start(tabs_shift[a - 1][0:SHIFT_ROWS, :].bitcast(I32), tabs_g[4 * a : 4 * a + SHIFT_ROWS, :].bitcast(I32))
+            nc.gpsimd.dma_start(tabs_shift[a - 1][0:SHIFT_ROWS, :].bitcast(I32), tabs_g[4 * a : 4 * a + SHIFT_ROWS, :].bitcast(I32))
         tab_planes = [tabs_g] + tabs_shift
         w4_planes = [w4s_ord] + w4s_shift
         gather_words(0, HALVES)
@@ -141,16 +142,17 @@ def tile_list_pallet_slot_fit_kernel(tc, tab_words, tab_scales, offs, w4_words, 
         racks = {}
 
         def load_rack(s):
-            racks[s] = big.tile([P, T2], F32, name=("slot_b", "slot_d")[s] if s < 2 else "h%d" % (s - 2), align_bytes=64)
-            for cols in (slice(0, S), slice(S, T2)) if s == 0 else (slice(0, T2),):
-                (nc.scalar if s < 2 else nc.sync).dma_start(racks[s][:, cols], rack_rows[s // PACK, s % PACK][:, cols])
+            slot = ("slot_b", "slot_c", "raw1", "weighted1", "weighted2")[s % 5]
+            racks[s] = big.tile([P, T2], F32, name=slot, align_bytes=64)
+            nc.sync.dma_start(racks[s][:], rack_rows[s // PACK, s % PACK])
 
+        load_rack(0)
 
-        h_tiles = [big.tile([P, S], F32, name="h%d" % j, align_bytes=64) for j in range(H_BUFS)]
-
-        h_raw = list(h_tiles)
-        for s in (1, 2):
-            h_raw[s] = big.tile([P, S], F32, name=("slot_b", "slot_d")[s - 1], align_bytes=64)
+        raw1 = big.tile([P, S], F32, name="raw1", align_bytes=64)
+        spare_half = {(s, u): big.tile([P, S], F32, name="raw%d_%d" % (s, u), align_bytes=64) for s in range(2, SLOTS) for u in range(HALVES)}
+        h_raw = {(1, u): raw1[:, u * BANK : (u + 1) * BANK] for u in range(HALVES)}
+        h_raw.update({key: tile[:, 0:BANK] for key, tile in spare_half.items()})
+        h_tiles = {s: big.tile([P, S], F32, name="weighted%d" % s, align_bytes=64)[:] for s in range(AHEAD)}
 
         def h_pass(bank, s, u, a, order=(0, 1, 2)):
             cols = slice(u * BANK, (u + 1) * BANK)
@@ -169,10 +171,14 @@ def tile_list_pallet_slot_fit_kernel(tc, tab_words, tab_scales, offs, w4_words, 
             if s == 0:
                 nc.vector.tensor_tensor(h_tiles[s][:, cols], bank[:], wgs_t[:, cols], ALU.mult)
             else:
-                nc.scalar.copy(h_raw[s][:, cols], bank[:])
+                nc.scalar.copy(h_raw[s, u], bank[:])
 
         def weigh(s):
-            nc.gpsimd.tensor_tensor(h_tiles[s][:], h_raw[s][:], wgs_t[:], ALU.mult)
+            if s >= AHEAD:
+                h_tiles[s] = racks[s - AHEAD][:, S:T2]
+            for u in range(HALVES):
+                cols = slice(u * BANK, (u + 1) * BANK)
+                nc.gpsimd.tensor_tensor(h_tiles[s][:, cols], h_raw[s, u], wgs_t[:, cols], ALU.mult)
 
         def h_slot(s, two_banks=None):
             for u in range(HALVES):
@@ -194,7 +200,7 @@ def tile_list_pallet_slot_fit_kernel(tc, tab_words, tab_scales, offs, w4_words, 
         spare = [bank for bank in banks if not any(bank is r for r in ring)]
 
         w2_bf = keep.tile([P, RB * N * PACK], BF16, name="w2_bf", align_bytes=64)
-        w2_codes = keep.tile([P, RB * N], U32, name="w2_codes", align_bytes=64)
+        w2_codes = big.tile([P, RB * N], U32, name="slot_d", align_bytes=64)
         w2_scales = keep.tile([P, RB * N], U8, name="w2_scales", align_bytes=64)
         for b in range(RB):
             for t in range(NT):
@@ -206,9 +212,8 @@ def tile_list_pallet_slot_fit_kernel(tc, tab_words, tab_scales, offs, w4_words, 
         for lo, hi in ((0, 512), (512, RB * N)):
             nc.vector.quantize_mx(out=w2_codes[:, lo:hi].bitcast(FP8X4), scales=w2_scales[:, lo:hi], in_=w2_bf[:, PACK * lo : PACK * hi])
 
-        sq_wide = keep.tile([P, 2 * BANK], F32, name="sq_wide", align_bytes=64)
+        sq_first = [keep.tile([P, 2 * BANK], F32, name=name, align_bytes=64) for name in ("picked2", "picked0")]
         pairs = [[keep.tile([P, 2, BANK, 2], BF16, name="pairs%d_%d" % (b, c), align_bytes=64) for c in range(CHUNKS)] for b in range(RB)]
-        z_bf = [keep.tile([P, BANK * PACK], BF16, name="z_bf%d" % c, align_bytes=64) for c in range(CHUNKS)]
         z_codes = {(1, c): keep.tile([P, BANK], U32, name="z_codes%d" % c, align_bytes=64)[:] for c in range(CHUNKS)}
         z_scales = {(1, c): keep.tile([P, BANK], U8, name="z_scales%d" % c, align_bytes=64)[:] for c in range(CHUNKS)}
 
@@ -254,30 +259,35 @@ def tile_list_pallet_slot_fit_kernel(tc, tab_words, tab_scales, offs, w4_words, 
                 stop=not opens,
             )
 
+        load_rack(1)
         for s in range(1, WEIGH_FIRST):
             weigh(s)
-            if s < 3:
-                load_rack(s - 1)
+        load_rack(2)
         for s in range(SLOTS - 1):
             scatter(s, HALVES if s == 0 else 1)
-            if s + 2 < SLOTS:
+            if 1 <= s <= SLOTS - 3:
                 load_rack(s + 2)
-            for half in range(2):
+            if s == SLOTS - 2:
+                for c in range(CHUNKS):
+                    cols = slice(c * BANK, (c + 1) * BANK)
+                    nc.gpsimd.tensor_tensor(racks[s][:, cols], racks[s][:, cols], pages[s % PAGES][:, cols], ALU.subtract)
+                    sq = sq_first[c % 2][:, 0:BANK]
+                    square_from_sbuf(s, c, sq)
+                    exp_into_pairs(sq, s, c)
+            for half in range(2) if s < SLOTS - 2 else ():
                 cols = slice(half * S, (half + 1) * S)
-                nc.gpsimd.tensor_tensor(racks[s][:, cols], racks[s][:, cols], pages[s % PAGES][:, cols], ALU.subtract)
-                sq = sq_wide[:] if (s, half) == (SLOTS - 2, 1) else racks[s][:, cols]
-                if (s, half) in POOL_SQUARES:
-                    nc.gpsimd.tensor_tensor(sq, racks[s][:, cols], racks[s][:, cols], ALU.mult)
-                else:
-                    nc.scalar.activation(sq, racks[s][:, cols], ACT.Square)
+                diff = spare_half[s + AHEAD - 1, half][:]
+                nc.gpsimd.tensor_tensor(diff, racks[s][:, cols], pages[s % PAGES][:, cols], ALU.subtract)
+                sq = sq_first[half][:]
+                nc.scalar.activation(sq, diff, ACT.Square)
                 for j in range(2):
                     exp_into_pairs(sq[:, j * BANK : (j + 1) * BANK], s, 2 * half + j)
             if s + WEIGH_FIRST < SLOTS:
                 weigh(s + WEIGH_FIRST)
             if s in (PACK - 1, PACK):
                 half = s - PACK + 1
-                wide_bf = big.tile([P, 2 * BANK * PACK], BF16, name=("slot_b", "slot_d")[half], align_bytes=64)
-                wide_codes = big.tile([P, 2 * BANK], U32, name="h%d" % (s - 2), align_bytes=64)
+                wide_bf = big.tile([P, 2 * BANK * PACK], BF16, name=("weighted0", "slot_a")[half], align_bytes=64)
+                wide_codes = keep.tile([P, 2 * BANK], U32, name="wide_codes%d" % half, align_bytes=64)
                 wide_scales = keep.tile([P, 2 * BANK], U8, name="wide_scales%d" % half, align_bytes=64)
                 for j in range(2):
                     weave(0, 2 * half + j, wide_bf[:, j * BANK * PACK : (j + 1) * BANK * PACK], True)
@@ -286,18 +296,17 @@ def tile_list_pallet_slot_fit_kernel(tc, tab_words, tab_scales, offs, w4_words, 
                 nc.vector.quantize_mx(out=wide_codes[:].bitcast(FP8X4), scales=wide_scales[:], in_=wide_bf[:])
 
         last = SLOTS - 1
+        z_bf = [big.tile([P, BANK * PACK], BF16, name="raw%d_%d" % (2 + c // 2, c % 2), align_bytes=64) for c in range(CHUNKS)]
         scatter(last, 1)
         for c in range(CHUNKS):
             add_on_vector(last, c)
-        all_banks = ring + spare
-        early = (0, 1)
-        out_banks = {(c, t): all_banks[(0,1,2,3,4,5,6,7,0,1,2,3)[c * NT + t]] for c in range(CHUNKS) for t in range(NT)}
-        for c in early:
-            for t in range(NT):
-                out_pass(out_banks[c, t], 0, c, t, True)
+        out_banks = {(c, t): banks[(c * NT + t) % 8] for c in range(CHUNKS) for t in range(NT)}
+        early = [(c, t) for c in range(CHUNKS) for t in range(NT)][:8]
+        for c, t in early:
+            out_pass(out_banks[c, t], 0, c, t, True)
 
         def finish_z(c):
-            sq = sq_wide[:, (c % 2) * BANK : (c % 2 + 1) * BANK]
+            sq = sq_first[c % 2][:, 0:BANK]
             square_from_sbuf(last, c, sq)
             exp_into_pairs(sq, last, c)
             weave(1, c, z_bf[c][:], False)
@@ -305,9 +314,9 @@ def tile_list_pallet_slot_fit_kernel(tc, tab_words, tab_scales, offs, w4_words, 
 
         def finish_out(c):
             for t in range(NT):
-                out_pass(out_banks[c, t], 1, c, t, c not in early)
-                if c not in early:
-                    out_pass(out_banks[c, t], 0, c, t, False)
+                if (c, t) not in early:
+                    out_pass(out_banks[c, t], 0, c, t, True)
+                out_pass(out_banks[c, t], 1, c, t, False)
             for t in range(NT):
                 res = stage.tile([P, BANK], F32, name="res")
                 if c * NT + t in (5,7,9,11):

@@ -18,23 +18,21 @@ ALU = mybir.AluOpType
 
 P = 128
 PACK = 4
+QUADRANTS = 4
 KA = K // (P * PACK)
 RB = H // (P * PACK)
 SLOTS = RB * PACK
 BANK = 512
+BANKS = 8
+H_BANKS = 4
 CHUNKS = T2 // BANK
 HALVES = S // BANK
 NT = N // P
 SHIFT_ROWS = 112
-H_BUFS = 8
 PAGES = 2
-SQ_BUFS = 4
-VECTOR_CHUNKS = 1
-H_FIRST = 8
 AHEAD = 3
-WEIGH_FIRST = AHEAD
-POOL_SQUARES = ()
-WEAVE_ON_SCALAR = 4
+STAGE_BUFS = 6
+VECTOR_COPIES = (7, 9, 11)
 
 
 def tile_list_pallet_slot_fit_kernel(tc, tab_words, tab_scales, offs, w4_words, w4_scales, offs2, wgs, rack, sharp, gain, w2, out):
@@ -43,50 +41,46 @@ def tile_list_pallet_slot_fit_kernel(tc, tab_words, tab_scales, offs, w4_words, 
         lists = ctx.enter_context(tc.tile_pool(name="lists", bufs=1))
         keep = ctx.enter_context(tc.tile_pool(name="keep", bufs=1))
         big = ctx.enter_context(tc.tile_pool(name="big", bufs=1))
-        stage = ctx.enter_context(tc.tile_pool(name="stage", bufs=6))
+        stage = ctx.enter_context(tc.tile_pool(name="stage", bufs=STAGE_BUFS))
         psum = ctx.enter_context(tc.psum_pool(name="psum", bufs=1))
 
         offs_t = lists.tile([P, S // 16], U16, name="offs_t")
         offs2_t = lists.tile([P, S // 16], U16, name="offs2_t")
+        banks = [psum.tile([P, BANK], F32, name="bank%d" % j) for j in range(BANKS)]
 
-        banks = [psum.tile([P, BANK], F32, name="bank%d" % j) for j in range(8)]
-        turn = [0]
+        def cols_of(j, width):
+            return slice(j * width, (j + 1) * width)
 
-        def next_bank():
-            bank = banks[turn[0] % 4]
-            turn[0] = turn[0] + 1
-            return bank
-
-        tabs_win = keep.tile([P, T], U8, name="picked0", align_bytes=64)
-        w4s_raw = keep.tile([P, H], U8, name="tabs_g", align_bytes=64)
-        tabs_shift = [keep.tile([P, S], U8, name="tabs_shift%d" % a, align_bytes=64) for a in range(1, KA)]
-        w4s_shift = [keep.tile([P, H], U8, name="w4s_shift%d" % a, align_bytes=64) for a in range(1, KA)]
+        tab_scales_raw = keep.tile([P, T], U8, name="picked0", align_bytes=64)
+        w4_scales_raw = keep.tile([P, H], U8, name="tab_plane0", align_bytes=64)
+        tab_shifted = [keep.tile([P, S], U8, name="tab_plane%d" % a, align_bytes=64) for a in range(1, KA)]
+        w4_shifted = [keep.tile([P, H], U8, name="w4_plane%d" % a, align_bytes=64) for a in range(1, KA)]
         pages = [keep.tile([P, T2], F32, name="page%d" % j, align_bytes=64) for j in range(PAGES)]
-        nc.gpsimd.memset(tabs_win[:].bitcast(I32), 0)
-        nc.gpsimd.memset(w4s_raw[:].bitcast(I32), 0)
+        nc.gpsimd.memset(tab_scales_raw[:].bitcast(I32), 0)
+        nc.gpsimd.memset(w4_scales_raw[:].bitcast(I32), 0)
 
-        w4_raw = [big.tile([P, 2 * H], U8, name=slot, align_bytes=64) for slot in ("slot_b", "slot_c", "slot_d")]
+        w4_raw = [big.tile([P, 2 * H], U8, name=area, align_bytes=64) for area in ("area_b", "area_c", "area_d")]
         nc.sync.dma_start(offs_t[:], offs)
         nc.sync.dma_start(offs2_t[:], offs2)
         sharp_t = keep.tile([P, RB, PACK], F32, name="wgs", align_bytes=64)
         gain_t = keep.tile([P, RB, PACK], F32, name="gain_t")
         for a in range(KA):
             nc.sync.dma_start(w4_raw[a][:].bitcast(I32), w4_words[a].bitcast(I32))
-        for q in range(4):
-            nc.scalar.dma_start(tabs_win[32 * q : 32 * q + 4 * KA, :].bitcast(I32), tab_scales[:, 4 * q : 4 * q + 4, :].bitcast(I32))
-        for q in range(4):
-            nc.gpsimd.dma_start(w4s_raw[32 * q : 32 * q + 4 * KA, :].bitcast(I32), w4_scales[:, 4 * q : 4 * q + 4, :].bitcast(I32))
+        for q in range(QUADRANTS):
+            nc.scalar.dma_start(tab_scales_raw[32 * q : 32 * q + 4 * KA, :].bitcast(I32), tab_scales[:, 4 * q : 4 * q + 4, :].bitcast(I32))
+        for q in range(QUADRANTS):
+            nc.gpsimd.dma_start(w4_scales_raw[32 * q : 32 * q + 4 * KA, :].bitcast(I32), w4_scales[:, 4 * q : 4 * q + 4, :].bitcast(I32))
         tab_win = {}
 
-        def load_table(a, slot):
-            tab_win[a] = big.tile([P, T], I32, name=slot, align_bytes=64)
+        def load_table(a, area):
+            tab_win[a] = big.tile([P, T], I32, name=area, align_bytes=64)
             nc.sync.dma_start(tab_win[a][:], tab_words[a].rearrange("p t i -> p (t i)").bitcast(I32))
 
-        load_table(1, "slot_a")
+        load_table(1, "area_a")
         nc.sync.dma_start(sharp_t[:], sharp.rearrange("(b p i) -> p b i", b=RB, i=PACK))
         nc.sync.dma_start(gain_t[:], gain.rearrange("(b p i) -> p b i", b=RB, i=PACK))
-        for t in tabs_shift + w4s_shift:
-            nc.vector.memset(t[:].bitcast(I32), 0)
+        for plane in tab_shifted + w4_shifted:
+            nc.vector.memset(plane[:].bitcast(I32), 0)
         nc.vector.memset(pages[0][:], 0.0)
 
         w4_ord = [keep.tile([P, 2 * H], U8, name="w4_ord%d" % a, align_bytes=64) for a in range(KA)]
@@ -95,16 +89,14 @@ def tile_list_pallet_slot_fit_kernel(tc, tab_words, tab_scales, offs, w4_words, 
                 w4_ord[a][:].bitcast(U16).rearrange("p (b i m) -> p b i m", b=RB, i=PACK),
                 w4_raw[a][:].bitcast(U16).rearrange("p (b m i) -> p b i m", b=RB, i=PACK),
             )
-        load_table(0, "slot_b")
-        w2_raw = big.tile([P, RB, PACK, N], F32, name="slot_c", align_bytes=64)
+        load_table(0, "area_b")
+        w2_raw = big.tile([P, RB, PACK, N], F32, name="area_c", align_bytes=64)
         nc.sync.dma_start(w2_raw[:].rearrange("p b i n -> p b (i n)"), w2.rearrange("(b p i) n -> p b (i n)", b=RB, i=PACK))
-        load_table(2, "slot_d")
+        load_table(2, "area_d")
 
         neg_sharp = keep.tile([P, SLOTS], F32, name="neg_sharp")
         ln_gain = keep.tile([P, SLOTS], F32, name="ln_gain")
         nc.scalar.activation(ln_gain[:], gain_t[:].rearrange("p b i -> p (b i)"), ACT.Ln)
-        warm = keep.tile([P, 1], F32, name="warm")
-        nc.scalar.activation(warm[:], ln_gain[:, 0:1], ACT.Exp)
         nc.scalar.mul(neg_sharp[:], sharp_t[:].rearrange("p b i -> p (b i)"), -1.0)
 
         wgs_t = keep.tile([P, S], F32, name="wgs", align_bytes=64)
@@ -115,217 +107,193 @@ def tile_list_pallet_slot_fit_kernel(tc, tab_words, tab_scales, offs, w4_words, 
             picked[a] = keep.tile([P, S], U32, name="picked%d" % a, align_bytes=64)
             width = S // pieces
             for u in range(pieces):
-                nc.vector.tensor_copy(
-                    picked[a][:, u * width : (u + 1) * width],
-                    tab_win[a][:].bitcast(U32).indirect(offs_t[:, u * width // 16 : (u + 1) * width // 16]),
-                )
+                nc.vector.tensor_copy(picked[a][:, cols_of(u, width)], tab_win[a][:].bitcast(U32).indirect(offs_t[:, cols_of(u, width // 16)]))
+
+        def shift_scale_rows(planes, source):
+            for a in range(1, KA):
+                nc.gpsimd.dma_start(planes[a - 1][0:SHIFT_ROWS, :].bitcast(I32), source[4 * a : 4 * a + SHIFT_ROWS, :].bitcast(I32))
 
         nc.vector.memset(pages[1][:], 0.0)
         gather_words(1, 1)
-        w4s_ord = keep.tile([P, H], U8, name="w4s_ord", align_bytes=64)
+        w4_plane0 = keep.tile([P, H], U8, name="w4_plane0", align_bytes=64)
         nc.vector.tensor_copy(
-            w4s_ord[:].rearrange("p (b i m) -> p b i m", b=RB, i=PACK),
-            w4s_raw[:].rearrange("p (b m i) -> p b i m", b=RB, i=PACK),
+            w4_plane0[:].rearrange("p (b i m) -> p b i m", b=RB, i=PACK),
+            w4_scales_raw[:].rearrange("p (b m i) -> p b i m", b=RB, i=PACK),
         )
-        for a in range(1, KA):
-            nc.gpsimd.dma_start(w4s_shift[a - 1][0:SHIFT_ROWS, :].bitcast(I32), w4s_ord[4 * a : 4 * a + SHIFT_ROWS, :].bitcast(I32))
-        tabs_g = keep.tile([P, S], U8, name="tabs_g", align_bytes=64)
-        nc.vector.tensor_copy(tabs_g[:], tabs_win[:].indirect(offs_t[:]))
-        for a in range(1, KA):
-            nc.gpsimd.dma_start(tabs_shift[a - 1][0:SHIFT_ROWS, :].bitcast(I32), tabs_g[4 * a : 4 * a + SHIFT_ROWS, :].bitcast(I32))
-        tab_planes = [tabs_g] + tabs_shift
-        w4_planes = [w4s_ord] + w4s_shift
+        shift_scale_rows(w4_shifted, w4_plane0)
+        tab_plane0 = keep.tile([P, S], U8, name="tab_plane0", align_bytes=64)
+        nc.vector.tensor_copy(tab_plane0[:], tab_scales_raw[:].indirect(offs_t[:]))
+        shift_scale_rows(tab_shifted, tab_plane0)
+        tab_planes = [tab_plane0] + tab_shifted
+        w4_planes = [w4_plane0] + w4_shifted
         gather_words(0, HALVES)
         gather_words(2, HALVES)
 
         rack_rows = rack.rearrange("(b p i) m -> b i p m", b=RB, i=PACK)
+        rack_areas = ("area_b", "area_c", "h1", "weighted1", "weighted2")
         racks = {}
 
         def load_rack(s):
-            slot = ("slot_b", "slot_c", "raw1", "weighted1", "weighted2")[s % 5]
-            racks[s] = big.tile([P, T2], F32, name=slot, align_bytes=64)
+            racks[s] = big.tile([P, T2], F32, name=rack_areas[s % len(rack_areas)], align_bytes=64)
             nc.sync.dma_start(racks[s][:], rack_rows[s // PACK, s % PACK])
 
         load_rack(0)
 
-        raw1 = big.tile([P, S], F32, name="raw1", align_bytes=64)
-        spare_half = {(s, u): big.tile([P, S], F32, name="raw%d_%d" % (s, u), align_bytes=64) for s in range(2, SLOTS) for u in range(HALVES)}
-        h_raw = {(1, u): raw1[:, u * BANK : (u + 1) * BANK] for u in range(HALVES)}
-        h_raw.update({key: tile[:, 0:BANK] for key, tile in spare_half.items()})
-        h_tiles = {s: big.tile([P, S], F32, name="weighted%d" % s, align_bytes=64)[:] for s in range(AHEAD)}
+        h1 = big.tile([P, S], F32, name="h1", align_bytes=64)
+        half_tiles = {(s, u): big.tile([P, S], F32, name="h%d_%d" % (s, u), align_bytes=64) for s in range(2, SLOTS) for u in range(HALVES)}
+        h_raw = {(1, u): h1[:, cols_of(u, BANK)] for u in range(HALVES)}
+        h_raw.update({key: tile[:, 0:BANK] for key, tile in half_tiles.items()})
+        weighted = {s: big.tile([P, S], F32, name="weighted%d" % s, align_bytes=64)[:] for s in range(AHEAD)}
 
-        def h_pass(bank, s, u, a, order=(0, 1, 2)):
-            cols = slice(u * BANK, (u + 1) * BANK)
+        def h_pass(bank, s, u, a, order):
             nc.tensor.matmul_mx(
                 out=bank[:],
-                lhsT=w4_ord[a][:, 2 * P * s : 2 * P * (s + 1)].bitcast(FP4X4),
-                lhsT_scale=w4_planes[a][:, P * s : P * (s + 1)],
-                rhs=picked[a][:, cols].bitcast(FP8X4),
-                rhs_scale=tab_planes[a][:, cols],
+                lhsT=w4_ord[a][:, cols_of(s, 2 * P)].bitcast(FP4X4),
+                lhsT_scale=w4_planes[a][:, cols_of(s, P)],
+                rhs=picked[a][:, cols_of(u, BANK)].bitcast(FP8X4),
+                rhs_scale=tab_planes[a][:, cols_of(u, BANK)],
                 start=(a == order[0]),
                 stop=(a == order[-1]),
             )
 
         def h_out(bank, s, u):
-            cols = slice(u * BANK, (u + 1) * BANK)
             if s == 0:
-                nc.vector.tensor_tensor(h_tiles[s][:, cols], bank[:], wgs_t[:, cols], ALU.mult)
+                nc.vector.tensor_tensor(weighted[s][:, cols_of(u, BANK)], bank[:], wgs_t[:, cols_of(u, BANK)], ALU.mult)
             else:
                 nc.scalar.copy(h_raw[s, u], bank[:])
 
-        def weigh(s):
-            if s >= AHEAD:
-                h_tiles[s] = racks[s - AHEAD][:, S:T2]
+        opening = H_BANKS // HALVES
+        for u in range(HALVES):
+            for s in range(opening):
+                h_pass(banks[opening * u + s], s, u, 0, (0, 1, 2))
+        for s in range(opening):
             for u in range(HALVES):
-                cols = slice(u * BANK, (u + 1) * BANK)
-                nc.gpsimd.tensor_tensor(h_tiles[s][:, cols], h_raw[s, u], wgs_t[:, cols], ALU.mult)
-
-        def h_slot(s, two_banks=None):
+                h_pass(banks[opening * u + s], s, u, 1, (0, 1, 2))
+                h_pass(banks[opening * u + s], s, u, 2, (0, 1, 2))
+                h_out(banks[opening * u + s], s, u)
+        for s in range(opening, SLOTS):
             for u in range(HALVES):
-                bank = two_banks[u] if two_banks else next_bank()
+                bank = banks[(HALVES * s + u) % H_BANKS]
                 for a in (1, 2, 0):
                     h_pass(bank, s, u, a, (1, 2, 0))
                 h_out(bank, s, u)
 
-        first = [(s, u, next_bank()) for u in range(HALVES) for s in range(2)]
-        for s, u, bank in first:
-            h_pass(bank, s, u, 0)
-        for s, u, bank in sorted(first, key=lambda item: item[:2]):
-            h_pass(bank, s, u, 1)
-            h_pass(bank, s, u, 2)
-            h_out(bank, s, u)
-        for s in range(2, H_FIRST):
-            h_slot(s)
-        ring = [banks[(2 * H_FIRST - 1 - j) % 8] for j in range(3)]
-        spare = [bank for bank in banks if not any(bank is r for r in ring)]
-
         w2_bf = keep.tile([P, RB * N * PACK], BF16, name="w2_bf", align_bytes=64)
-        w2_codes = big.tile([P, RB * N], U32, name="slot_d", align_bytes=64)
+        w2_codes = big.tile([P, RB * N], U32, name="area_d", align_bytes=64)
         w2_scales = keep.tile([P, RB * N], U8, name="w2_scales", align_bytes=64)
         for b in range(RB):
             for t in range(NT):
-                lo = b * N + t * P
                 nc.scalar.copy(
-                    w2_bf[:, lo * PACK : (lo + P) * PACK].rearrange("p (n i) -> p n i", i=PACK),
-                    w2_raw[:, b, :, t * P : (t + 1) * P].rearrange("p i n -> p n i"),
+                    w2_bf[:, cols_of(b * NT + t, P * PACK)].rearrange("p (n i) -> p n i", i=PACK),
+                    w2_raw[:, b, :, cols_of(t, P)].rearrange("p i n -> p n i"),
                 )
         for lo, hi in ((0, 512), (512, RB * N)):
             nc.vector.quantize_mx(out=w2_codes[:, lo:hi].bitcast(FP8X4), scales=w2_scales[:, lo:hi], in_=w2_bf[:, PACK * lo : PACK * hi])
 
-        sq_first = [keep.tile([P, 2 * BANK], F32, name=name, align_bytes=64) for name in ("picked2", "picked0")]
-        pairs = [[keep.tile([P, 2, BANK, 2], BF16, name="pairs%d_%d" % (b, c), align_bytes=64) for c in range(CHUNKS)] for b in range(RB)]
+        squares = [keep.tile([P, S], F32, name=name, align_bytes=64) for name in ("picked2", "picked0")]
+        z_pairs = [keep.tile([P, 2, BANK, 2], BF16, name="z_pairs%d" % c, align_bytes=64) for c in range(CHUNKS)]
+        z_slots = [keep.tile([P, PACK, BANK], BF16, name="z_slots%d" % c, align_bytes=64) for c in range(CHUNKS)]
         z_codes = {(1, c): keep.tile([P, BANK], U32, name="z_codes%d" % c, align_bytes=64)[:] for c in range(CHUNKS)}
         z_scales = {(1, c): keep.tile([P, BANK], U8, name="z_scales%d" % c, align_bytes=64)[:] for c in range(CHUNKS)}
 
+        def weigh(s):
+            if s >= AHEAD:
+                weighted[s] = racks[s - AHEAD][:, S:T2]
+            for u in range(HALVES):
+                nc.gpsimd.tensor_tensor(weighted[s][:, cols_of(u, BANK)], h_raw[s, u], wgs_t[:, cols_of(u, BANK)], ALU.mult)
+
         def scatter(s, pieces):
-            page = pages[s % PAGES]
             width = S // pieces
             for u in range(pieces):
-                cols = slice(u * width, (u + 1) * width)
-                nc.vector.tensor_copy(page[:].indirect(offs2_t[:, u * width // 16 : (u + 1) * width // 16]), h_tiles[s][:, cols])
+                nc.vector.tensor_copy(pages[s % PAGES][:].indirect(offs2_t[:, cols_of(u, width // 16)]), weighted[s][:, cols_of(u, width)])
 
-        def exp_into_pairs(src, s, c):
+        def subtract(engine, diff, s, cols):
+            engine.tensor_tensor(diff, racks[s][:, cols], pages[s % PAGES][:, cols], ALU.subtract)
+
+        def exp_to_z(square, s, c):
             i = s % PACK
-            nc.scalar.activation(pairs[s // PACK][c][:, i // 2, :, i % 2], src, ACT.Exp, bias=ln_gain[:, s : s + 1], scale=neg_sharp[:, s : s + 1])
+            target = z_pairs[c][:, i // 2, :, i % 2] if s < PACK else z_slots[c][:, i, :]
+            nc.scalar.activation(target, square, ACT.Exp, bias=ln_gain[:, s : s + 1], scale=neg_sharp[:, s : s + 1])
 
-        def add_on_vector(s, c):
-            cols = slice(c * BANK, (c + 1) * BANK)
-            nc.vector.tensor_tensor(racks[s][:, cols], racks[s][:, cols], pages[s % PAGES][:, cols], ALU.subtract)
+        def square_and_exp_chunk(s, c):
+            square = squares[c % 2][:, 0:BANK]
+            nc.scalar.activation(square, racks[s][:, cols_of(c, BANK)], ACT.Square)
+            exp_to_z(square, s, c)
 
-        def square_from_sbuf(s, c, sq):
-            nc.scalar.activation(sq, racks[s][:, c * BANK : (c + 1) * BANK], ACT.Square)
+        def slot_by_halves(s):
+            for half in range(HALVES):
+                diff = half_tiles[s + AHEAD - 1, half][:]
+                subtract(nc.gpsimd, diff, s, cols_of(half, S))
+                nc.scalar.activation(squares[half][:], diff, ACT.Square)
+                for j in range(2):
+                    exp_to_z(squares[half][:, cols_of(j, BANK)], s, 2 * half + j)
 
-        def weave(b, c, target, on_scalar):
-            dt = U32 if on_scalar else I32
-            dst = target.bitcast(dt).rearrange("p (m h) -> p m h", h=2)
-            src = pairs[b][c][:].rearrange("p h m e -> p (h m e)").bitcast(dt).rearrange("p (h m) -> p m h", h=2)
-            if on_scalar:
-                nc.scalar.copy(dst, src)
-            else:
-                nc.vector.tensor_copy(dst, src)
-
-        def quantise_z(b, c):
-            nc.vector.quantize_mx(out=z_codes[b, c].bitcast(FP8X4), scales=z_scales[b, c], in_=z_bf[c][:])
-
-        def out_pass(bank, b, c, t, opens):
-            cols = slice(b * N + t * P, b * N + (t + 1) * P)
-            nc.tensor.matmul_mx(
-                out=bank[:],
-                lhsT=w2_codes[:, cols].bitcast(FP8X4),
-                lhsT_scale=w2_scales[:, cols],
-                rhs=z_codes[b, c].bitcast(FP8X4),
-                rhs_scale=z_scales[b, c],
-                start=opens,
-                stop=not opens,
-            )
+        def quantise_pass0(half):
+            z_bf = big.tile([P, S * PACK], BF16, name=("weighted0", "area_a")[half], align_bytes=64)
+            codes = keep.tile([P, S], U32, name="z0_codes%d" % half, align_bytes=64)
+            scales = keep.tile([P, S], U8, name="z0_scales%d" % half, align_bytes=64)
+            for j in range(2):
+                c = 2 * half + j
+                nc.scalar.copy(
+                    z_bf[:, cols_of(j, BANK * PACK)].bitcast(U32).rearrange("p (m h) -> p m h", h=2),
+                    z_pairs[c][:].rearrange("p h m e -> p (h m e)").bitcast(U32).rearrange("p (h m) -> p m h", h=2),
+                )
+                z_codes[0, c] = codes[:, cols_of(j, BANK)]
+                z_scales[0, c] = scales[:, cols_of(j, BANK)]
+            nc.vector.quantize_mx(out=codes[:].bitcast(FP8X4), scales=scales[:], in_=z_bf[:])
 
         load_rack(1)
-        for s in range(1, WEIGH_FIRST):
+        for s in range(1, AHEAD):
             weigh(s)
         load_rack(2)
-        for s in range(SLOTS - 1):
-            scatter(s, HALVES if s == 0 else 1)
-            if 1 <= s <= SLOTS - 3:
-                load_rack(s + 2)
-            if s == SLOTS - 2:
-                for c in range(CHUNKS):
-                    cols = slice(c * BANK, (c + 1) * BANK)
-                    nc.gpsimd.tensor_tensor(racks[s][:, cols], racks[s][:, cols], pages[s % PAGES][:, cols], ALU.subtract)
-                    sq = sq_first[c % 2][:, 0:BANK]
-                    square_from_sbuf(s, c, sq)
-                    exp_into_pairs(sq, s, c)
-            for half in range(2) if s < SLOTS - 2 else ():
-                cols = slice(half * S, (half + 1) * S)
-                diff = spare_half[s + AHEAD - 1, half][:]
-                nc.gpsimd.tensor_tensor(diff, racks[s][:, cols], pages[s % PAGES][:, cols], ALU.subtract)
-                sq = sq_first[half][:]
-                nc.scalar.activation(sq, diff, ACT.Square)
-                for j in range(2):
-                    exp_into_pairs(sq[:, j * BANK : (j + 1) * BANK], s, 2 * half + j)
-            if s + WEIGH_FIRST < SLOTS:
-                weigh(s + WEIGH_FIRST)
-            if s in (PACK - 1, PACK):
-                half = s - PACK + 1
-                wide_bf = big.tile([P, 2 * BANK * PACK], BF16, name=("weighted0", "slot_a")[half], align_bytes=64)
-                wide_codes = keep.tile([P, 2 * BANK], U32, name="wide_codes%d" % half, align_bytes=64)
-                wide_scales = keep.tile([P, 2 * BANK], U8, name="wide_scales%d" % half, align_bytes=64)
-                for j in range(2):
-                    weave(0, 2 * half + j, wide_bf[:, j * BANK * PACK : (j + 1) * BANK * PACK], True)
-                    z_codes[0, 2 * half + j] = wide_codes[:, j * BANK : (j + 1) * BANK]
-                    z_scales[0, 2 * half + j] = wide_scales[:, j * BANK : (j + 1) * BANK]
-                nc.vector.quantize_mx(out=wide_codes[:].bitcast(FP8X4), scales=wide_scales[:], in_=wide_bf[:])
-
         last = SLOTS - 1
-        z_bf = [big.tile([P, BANK * PACK], BF16, name="raw%d_%d" % (2 + c // 2, c % 2), align_bytes=64) for c in range(CHUNKS)]
+        for s in range(last):
+            scatter(s, HALVES if s == 0 else 1)
+            if 1 <= s <= last - 2:
+                load_rack(s + 2)
+            if s == last - 1:
+                for c in range(CHUNKS):
+                    subtract(nc.gpsimd, racks[s][:, cols_of(c, BANK)], s, cols_of(c, BANK))
+                    square_and_exp_chunk(s, c)
+            else:
+                slot_by_halves(s)
+            if s + AHEAD < SLOTS:
+                weigh(s + AHEAD)
+            if s in (PACK - 1, PACK):
+                quantise_pass0(s - PACK + 1)
+
+        z1_bf = [big.tile([P, BANK * PACK], BF16, name="h%d_%d" % (2 + c // 2, c % 2), align_bytes=64) for c in range(CHUNKS)]
         scatter(last, 1)
         for c in range(CHUNKS):
-            add_on_vector(last, c)
-        out_banks = {(c, t): banks[(c * NT + t) % 8] for c in range(CHUNKS) for t in range(NT)}
-        early = [(c, t) for c in range(CHUNKS) for t in range(NT)][:8]
-        for c, t in early:
-            out_pass(out_banks[c, t], 0, c, t, True)
+            subtract(nc.vector, racks[last][:, cols_of(c, BANK)], last, cols_of(c, BANK))
 
-        def finish_z(c):
-            sq = sq_first[c % 2][:, 0:BANK]
-            square_from_sbuf(last, c, sq)
-            exp_into_pairs(sq, last, c)
-            weave(1, c, z_bf[c][:], False)
-            quantise_z(1, c)
+        def out_pass(b, c, t):
+            nc.tensor.matmul_mx(
+                out=banks[(c * NT + t) % BANKS][:],
+                lhsT=w2_codes[:, cols_of(b * NT + t, P)].bitcast(FP8X4),
+                lhsT_scale=w2_scales[:, cols_of(b * NT + t, P)],
+                rhs=z_codes[b, c].bitcast(FP8X4),
+                rhs_scale=z_scales[b, c],
+                start=(b == 0),
+                stop=(b == RB - 1),
+            )
 
-        def finish_out(c):
+        for j in range(BANKS):
+            out_pass(0, j // NT, j % NT)
+        for c in range(CHUNKS):
+            square_and_exp_chunk(last, c)
+            nc.vector.tensor_copy(z1_bf[c][:].rearrange("p (m i) -> p m i", i=PACK), z_slots[c][:].rearrange("p i m -> p m i"))
+            nc.vector.quantize_mx(out=z_codes[1, c].bitcast(FP8X4), scales=z_scales[1, c], in_=z1_bf[c][:])
+        for c in range(CHUNKS):
             for t in range(NT):
-                if (c, t) not in early:
-                    out_pass(out_banks[c, t], 0, c, t, True)
-                out_pass(out_banks[c, t], 1, c, t, False)
+                if c * NT + t >= BANKS:
+                    out_pass(0, c, t)
+                out_pass(1, c, t)
             for t in range(NT):
+                bank = banks[(c * NT + t) % BANKS]
                 res = stage.tile([P, BANK], F32, name="res")
-                if c * NT + t in (5,7,9,11):
-                    nc.vector.tensor_copy(res[:], out_banks[c, t][:])
+                if c * NT + t in VECTOR_COPIES:
+                    nc.vector.tensor_copy(res[:], bank[:])
                 else:
-                    nc.scalar.copy(res[:], out_banks[c, t][:])
-                nc.sync.dma_start(out[t * P : (t + 1) * P, c * BANK : (c + 1) * BANK], res[:])
-
-        for c in range(CHUNKS):
-            finish_z(c)
-        for c in range(CHUNKS):
-            finish_out(c)
+                    nc.scalar.copy(res[:], bank[:])
+                nc.sync.dma_start(out[cols_of(t, P), cols_of(c, BANK)], res[:])

@@ -24,15 +24,40 @@ RB = H // (P * PACK)
 SLOTS = RB * PACK
 BANK = 512
 BANKS = 8
-H_BANKS = 4
 CHUNKS = T2 // BANK
 HALVES = S // BANK
 NT = N // P
 SHIFT_ROWS = 112
-PAGES = 2
+PAGES = 3
 AHEAD = 3
 STAGE_BUFS = 6
 VECTOR_COPIES = (7, 9, 11)
+KB = 1024
+
+W4_SCALES_AT = 7 * KB + 512
+PICKED_AT = (16 * KB, 8 * KB, 74 * KB)
+TAB_SCALES_AT = 157 * KB
+W4_PLANE_AT = TAB_SCALES_AT
+WGS_AT = 158 * KB
+TAB_AT = (56 * KB, 28 * KB, 58 * KB)
+PAGE_AT = (49 * KB, 0, TAB_AT[1])
+TAB_PLANE_AT = 57 * KB
+W4_RAW_REST_AT = TAB_AT[1]
+W2_RAW_AT = 36 * KB
+W4_RAW_FIRST_AT = W2_RAW_AT
+W4_ORD_AT = 66 * KB
+SQUARE_AT = (PICKED_AT[2], PICKED_AT[1])
+H0_AT = 78 * KB
+H1_AT = 80 * KB
+DIFF_AT = 86 * KB
+WEIGHTED_AT = 134 * KB
+PAIRS_AT = 162 * KB
+JOINED0_AT = DIFF_AT
+Z1_CODES_AT = DIFF_AT + 16 * KB
+Z1_SCALES_AT = DIFF_AT + 24 * KB
+W2_BF_AT = 146 * KB
+RACK_AT = (TAB_AT[2], H0_AT, PICKED_AT[0], W4_ORD_AT, W2_RAW_AT, WEIGHTED_AT, TAB_AT[2], H0_AT)
+HALVED = (0,)
 
 
 def tile_list_pallet_slot_fit_kernel(tc, tab_words, tab_scales, offs, w4_words, w4_scales, offs2, wgs, rack, sharp, gain, w2, out):
@@ -40,7 +65,7 @@ def tile_list_pallet_slot_fit_kernel(tc, tab_words, tab_scales, offs, w4_words, 
     with ExitStack() as ctx:
         lists = ctx.enter_context(tc.tile_pool(name="lists", bufs=1))
         keep = ctx.enter_context(tc.tile_pool(name="keep", bufs=1))
-        big = ctx.enter_context(tc.tile_pool(name="big", bufs=1))
+        laid = ctx.enter_context(tc.tile_pool(name="laid", bufs=1))
         stage = ctx.enter_context(tc.tile_pool(name="stage", bufs=STAGE_BUFS))
         psum = ctx.enter_context(tc.psum_pool(name="psum", bufs=1))
 
@@ -51,156 +76,154 @@ def tile_list_pallet_slot_fit_kernel(tc, tab_words, tab_scales, offs, w4_words, 
         def cols_of(j, width):
             return slice(j * width, (j + 1) * width)
 
-        tab_scales_raw = keep.tile([P, T], U8, name="picked0", align_bytes=64)
-        w4_scales_raw = keep.tile([P, H], U8, name="tab_plane0", align_bytes=64)
-        tab_shifted = [keep.tile([P, S], U8, name="tab_plane%d" % a, align_bytes=64) for a in range(1, KA)]
-        w4_shifted = [keep.tile([P, H], U8, name="w4_plane%d" % a, align_bytes=64) for a in range(1, KA)]
-        pages = [keep.tile([P, T2], F32, name="page%d" % j, align_bytes=64) for j in range(PAGES)]
-        nc.gpsimd.memset(tab_scales_raw[:].bitcast(I32), 0)
-        nc.gpsimd.memset(w4_scales_raw[:].bitcast(I32), 0)
+        def place(name, shape, dtype, at):
+            return laid.tile(shape, dtype, name=name, offset=at, align_bytes=64)
 
-        w4_raw = [big.tile([P, 2 * H], U8, name=area, align_bytes=64) for area in ("area_b", "area_c", "area_d")]
+        tab_scales_raw = place("tab_scales_raw", [P, T], U8, TAB_SCALES_AT)
+        w4_scales_raw = place("w4_scales_raw", [P, H], U8, W4_SCALES_AT)
+        nc.gpsimd.memset(tab_scales_raw[:].bitcast(I32), 0)
+        nc.vector.memset(w4_scales_raw[:].bitcast(I32), 0)
+        w4_first = place("w4_first", [P, 2 * H], U8, W4_RAW_FIRST_AT)
+        w4_rest = place("w4_rest", [P, KA - 1, 2 * H], U8, W4_RAW_REST_AT)
+        w4_raw = [w4_first[:]] + [w4_rest[:, a, :] for a in range(KA - 1)]
+        tab_win = {}
+
+        def load_table(a):
+            tab_win[a] = place("tab_win%d" % a, [P, T], I32, TAB_AT[a])
+            nc.sync.dma_start(tab_win[a][:], tab_words[a].rearrange("p t i -> p (t i)").bitcast(I32))
+
+        nc.sync.dma_start(w4_first[:].bitcast(I32), w4_words[0].bitcast(I32))
+        nc.sync.dma_start(w4_rest[:].bitcast(I32), w4_words[1:KA].rearrange("a p n -> p a n").bitcast(I32))
         nc.sync.dma_start(offs_t[:], offs)
+        load_table(0)
         nc.sync.dma_start(offs2_t[:], offs2)
-        sharp_t = keep.tile([P, RB, PACK], F32, name="wgs", align_bytes=64)
         gain_t = keep.tile([P, RB, PACK], F32, name="gain_t")
-        for a in range(KA):
-            nc.sync.dma_start(w4_raw[a][:].bitcast(I32), w4_words[a].bitcast(I32))
+        sharp_t = keep.tile([P, RB, PACK], F32, name="sharp_t")
         for q in range(QUADRANTS):
             nc.scalar.dma_start(tab_scales_raw[32 * q : 32 * q + 4 * KA, :].bitcast(I32), tab_scales[:, 4 * q : 4 * q + 4, :].bitcast(I32))
         for q in range(QUADRANTS):
             nc.gpsimd.dma_start(w4_scales_raw[32 * q : 32 * q + 4 * KA, :].bitcast(I32), w4_scales[:, 4 * q : 4 * q + 4, :].bitcast(I32))
-        tab_win = {}
+        nc.gpsimd.dma_start(gain_t[:], gain.rearrange("(b p i) -> p b i", b=RB, i=PACK))
+        nc.gpsimd.dma_start(sharp_t[:], sharp.rearrange("(b p i) -> p b i", b=RB, i=PACK))
+        w4_shifted = keep.tile([P, KA - 1, H], U8, name="w4_shifted", align_bytes=64)
+        tab_shifted = keep.tile([P, KA - 1, S], U8, name="tab_shifted", align_bytes=64)
+        nc.gpsimd.memset(w4_shifted[:].rearrange("p a n -> p (a n)").bitcast(I32), 0)
+        nc.gpsimd.memset(tab_shifted[:].rearrange("p a n -> p (a n)").bitcast(I32), 0)
 
-        def load_table(a, area):
-            tab_win[a] = big.tile([P, T], I32, name=area, align_bytes=64)
-            nc.sync.dma_start(tab_win[a][:], tab_words[a].rearrange("p t i -> p (t i)").bitcast(I32))
-
-        load_table(1, "area_a")
-        nc.sync.dma_start(sharp_t[:], sharp.rearrange("(b p i) -> p b i", b=RB, i=PACK))
-        nc.sync.dma_start(gain_t[:], gain.rearrange("(b p i) -> p b i", b=RB, i=PACK))
-        for plane in tab_shifted + w4_shifted:
-            nc.vector.memset(plane[:].bitcast(I32), 0)
-        nc.vector.memset(pages[0][:], 0.0)
-
-        w4_ord = [keep.tile([P, 2 * H], U8, name="w4_ord%d" % a, align_bytes=64) for a in range(KA)]
+        w4_ord = [place("w4_ord%d" % a, [P, 2 * H], U8, W4_ORD_AT + 2 * KB * a) for a in range(KA)]
         for a in range(KA):
             nc.vector.tensor_copy(
                 w4_ord[a][:].bitcast(U16).rearrange("p (b i m) -> p b i m", b=RB, i=PACK),
-                w4_raw[a][:].bitcast(U16).rearrange("p (b m i) -> p b i m", b=RB, i=PACK),
+                w4_raw[a].bitcast(U16).rearrange("p (b m i) -> p b i m", b=RB, i=PACK),
             )
-        load_table(0, "area_b")
-        w2_raw = big.tile([P, RB, PACK, N], F32, name="area_c", align_bytes=64)
+        w2_raw = place("w2_raw", [P, RB, PACK, N], F32, W2_RAW_AT)
         nc.sync.dma_start(w2_raw[:].rearrange("p b i n -> p b (i n)"), w2.rearrange("(b p i) n -> p b (i n)", b=RB, i=PACK))
-        load_table(2, "area_d")
+        load_table(1)
+        picked = {}
+
+        def gather_words(a, pieces):
+            picked[a] = place("picked%d" % a, [P, S], U32, PICKED_AT[a])
+            width = S // pieces
+            for u in range(pieces):
+                nc.vector.tensor_copy(picked[a][:, cols_of(u, width)], tab_win[a][:].bitcast(U32).indirect(offs_t[:, cols_of(u, width // 16)]))
+
+        def shift_scale_rows(shifted, source):
+            for a in range(1, KA):
+                nc.sync.dma_start(shifted[0:SHIFT_ROWS, a - 1, :].bitcast(I32), source[4 * a : 4 * a + SHIFT_ROWS, :].bitcast(I32))
+            return [source[:]] + [shifted[:, a, :] for a in range(KA - 1)]
+
+        gather_words(0, 1)
+        load_table(2)
+        tab_plane0 = place("tab_plane0", [P, S], U8, TAB_PLANE_AT)
+        nc.vector.tensor_copy(tab_plane0[:], tab_scales_raw[:].indirect(offs_t[:]))
+        tab_planes = shift_scale_rows(tab_shifted, tab_plane0)
+        w4_plane0 = place("w4_plane0", [P, H], U8, W4_PLANE_AT)
+        nc.vector.tensor_copy(
+            w4_plane0[:].rearrange("p (b i m) -> p b i m", b=RB, i=PACK),
+            w4_scales_raw[:].rearrange("p (b m i) -> p b i m", b=RB, i=PACK),
+        )
+        w4_planes = shift_scale_rows(w4_shifted, w4_plane0)
+        wgs_t = place("wgs_t", [P, S], F32, WGS_AT)
+        nc.sync.dma_start(wgs_t[:], wgs)
+        gather_words(1, 1)
+        gather_words(2, HALVES)
+
+        pages = [place("page%d" % j, [P, T2], F32, PAGE_AT[j]) for j in range(PAGES)]
+        for page in pages:
+            nc.gpsimd.memset(page[:], 0.0)
 
         neg_sharp = keep.tile([P, SLOTS], F32, name="neg_sharp")
         ln_gain = keep.tile([P, SLOTS], F32, name="ln_gain")
         nc.scalar.activation(ln_gain[:], gain_t[:].rearrange("p b i -> p (b i)"), ACT.Ln)
         nc.scalar.mul(neg_sharp[:], sharp_t[:].rearrange("p b i -> p (b i)"), -1.0)
 
-        wgs_t = keep.tile([P, S], F32, name="wgs", align_bytes=64)
-        nc.sync.dma_start(wgs_t[:], wgs)
-        picked = {}
-
-        def gather_words(a, pieces):
-            picked[a] = keep.tile([P, S], U32, name="picked%d" % a, align_bytes=64)
-            width = S // pieces
-            for u in range(pieces):
-                nc.vector.tensor_copy(picked[a][:, cols_of(u, width)], tab_win[a][:].bitcast(U32).indirect(offs_t[:, cols_of(u, width // 16)]))
-
-        def shift_scale_rows(planes, source):
-            for a in range(1, KA):
-                nc.gpsimd.dma_start(planes[a - 1][0:SHIFT_ROWS, :].bitcast(I32), source[4 * a : 4 * a + SHIFT_ROWS, :].bitcast(I32))
-
-        nc.vector.memset(pages[1][:], 0.0)
-        gather_words(1, 1)
-        w4_plane0 = keep.tile([P, H], U8, name="w4_plane0", align_bytes=64)
-        nc.vector.tensor_copy(
-            w4_plane0[:].rearrange("p (b i m) -> p b i m", b=RB, i=PACK),
-            w4_scales_raw[:].rearrange("p (b m i) -> p b i m", b=RB, i=PACK),
-        )
-        shift_scale_rows(w4_shifted, w4_plane0)
-        tab_plane0 = keep.tile([P, S], U8, name="tab_plane0", align_bytes=64)
-        nc.vector.tensor_copy(tab_plane0[:], tab_scales_raw[:].indirect(offs_t[:]))
-        shift_scale_rows(tab_shifted, tab_plane0)
-        tab_planes = [tab_plane0] + tab_shifted
-        w4_planes = [w4_plane0] + w4_shifted
-        gather_words(0, HALVES)
-        gather_words(2, HALVES)
-
-        rack_rows = rack.rearrange("(b p i) m -> b i p m", b=RB, i=PACK)
-        rack_areas = ("area_b", "area_c", "h1", "weighted1", "weighted2")
-        racks = {}
-
-        def load_rack(s):
-            racks[s] = big.tile([P, T2], F32, name=rack_areas[s % len(rack_areas)], align_bytes=64)
-            nc.sync.dma_start(racks[s][:], rack_rows[s // PACK, s % PACK])
-
-        load_rack(0)
-
-        h1 = big.tile([P, S], F32, name="h1", align_bytes=64)
-        half_tiles = {(s, u): big.tile([P, S], F32, name="h%d_%d" % (s, u), align_bytes=64) for s in range(2, SLOTS) for u in range(HALVES)}
-        h_raw = {(1, u): h1[:, cols_of(u, BANK)] for u in range(HALVES)}
-        h_raw.update({key: tile[:, 0:BANK] for key, tile in half_tiles.items()})
-        weighted = {s: big.tile([P, S], F32, name="weighted%d" % s, align_bytes=64)[:] for s in range(AHEAD)}
-
-        def h_pass(bank, s, u, a, order):
-            nc.tensor.matmul_mx(
-                out=bank[:],
-                lhsT=w4_ord[a][:, cols_of(s, 2 * P)].bitcast(FP4X4),
-                lhsT_scale=w4_planes[a][:, cols_of(s, P)],
-                rhs=picked[a][:, cols_of(u, BANK)].bitcast(FP8X4),
-                rhs_scale=tab_planes[a][:, cols_of(u, BANK)],
-                start=(a == order[0]),
-                stop=(a == order[-1]),
-            )
-
-        def h_out(bank, s, u):
-            if s == 0:
-                nc.vector.tensor_tensor(weighted[s][:, cols_of(u, BANK)], bank[:], wgs_t[:, cols_of(u, BANK)], ALU.mult)
-            else:
-                nc.scalar.copy(h_raw[s, u], bank[:])
-
-        opening = H_BANKS // HALVES
-        for u in range(HALVES):
-            for s in range(opening):
-                h_pass(banks[opening * u + s], s, u, 0, (0, 1, 2))
-        for s in range(opening):
-            for u in range(HALVES):
-                h_pass(banks[opening * u + s], s, u, 1, (0, 1, 2))
-                h_pass(banks[opening * u + s], s, u, 2, (0, 1, 2))
-                h_out(banks[opening * u + s], s, u)
-        for s in range(opening, SLOTS):
-            for u in range(HALVES):
-                bank = banks[(HALVES * s + u) % H_BANKS]
-                for a in (1, 2, 0):
-                    h_pass(bank, s, u, a, (1, 2, 0))
-                h_out(bank, s, u)
-
-        w2_bf = keep.tile([P, RB * N * PACK], BF16, name="w2_bf", align_bytes=64)
-        w2_codes = big.tile([P, RB * N], U32, name="area_d", align_bytes=64)
-        w2_scales = keep.tile([P, RB * N], U8, name="w2_scales", align_bytes=64)
+        w2_bf = place("w2_bf", [P, RB * N * PACK], BF16, W2_BF_AT)
         for b in range(RB):
             for t in range(NT):
                 nc.scalar.copy(
                     w2_bf[:, cols_of(b * NT + t, P * PACK)].rearrange("p (n i) -> p n i", i=PACK),
                     w2_raw[:, b, :, cols_of(t, P)].rearrange("p i n -> p n i"),
                 )
-        for lo, hi in ((0, 512), (512, RB * N)):
-            nc.vector.quantize_mx(out=w2_codes[:, lo:hi].bitcast(FP8X4), scales=w2_scales[:, lo:hi], in_=w2_bf[:, PACK * lo : PACK * hi])
 
-        squares = [keep.tile([P, S], F32, name=name, align_bytes=64) for name in ("picked2", "picked0")]
-        z_pairs = [keep.tile([P, 2, BANK, 2], BF16, name="z_pairs%d" % c, align_bytes=64) for c in range(CHUNKS)]
-        z_slots = [keep.tile([P, PACK, BANK], BF16, name="z_slots%d" % c, align_bytes=64) for c in range(CHUNKS)]
-        z_codes = {(1, c): keep.tile([P, BANK], U32, name="z_codes%d" % c, align_bytes=64)[:] for c in range(CHUNKS)}
-        z_scales = {(1, c): keep.tile([P, BANK], U8, name="z_scales%d" % c, align_bytes=64)[:] for c in range(CHUNKS)}
+        rack_rows = rack.rearrange("(b p i) m -> b i p m", b=RB, i=PACK)
+        racks = {}
+
+        def load_rack(s):
+            racks[s] = place("rack%d" % s, [P, T2], F32, RACK_AT[s])
+            nc.sync.dma_start(racks[s][:], rack_rows[s // PACK, s % PACK])
+
+        load_rack(0)
+
+        diffs = [place("diff%d" % s, [P, T2], F32, DIFF_AT + 8 * KB * s) for s in range(SLOTS - AHEAD + 1)]
+        h = {s + AHEAD - 1: diff[:, BANK : BANK + S] for s, diff in enumerate(diffs)}
+        h[1] = place("h1", [P, S], F32, H1_AT)[:]
+        h0_late = place("h0_late", [P, BANK], F32, H0_AT)
+        weighted = {s: place("weighted%d" % s, [P, S], F32, WEIGHTED_AT + 4 * KB * s)[:] for s in range(AHEAD)}
+
+        def h_half(s, u):
+            return h0_late[:] if s == 0 else h[s][:, cols_of(u, BANK)]
+
+        def h_pass(s, u, a):
+            nc.tensor.matmul_mx(
+                out=banks[(HALVES * s + u) % BANKS][:],
+                lhsT=w4_ord[a][:, cols_of(s, 2 * P)].bitcast(FP4X4),
+                lhsT_scale=w4_planes[a][:, cols_of(s, P)],
+                rhs=picked[a][:, cols_of(u, BANK)].bitcast(FP8X4),
+                rhs_scale=tab_planes[a][:, cols_of(u, BANK)],
+                start=(a == 0),
+                stop=(a == KA - 1),
+            )
+
+        def h_out(s, u):
+            bank = banks[(HALVES * s + u) % BANKS]
+            if (s, u) == (0, 0):
+                nc.vector.tensor_tensor(weighted[0][:, 0:BANK], bank[:], wgs_t[:, 0:BANK], ALU.mult)
+            else:
+                nc.scalar.copy(h_half(s, u), bank[:])
 
         def weigh(s):
-            if s >= AHEAD:
-                weighted[s] = racks[s - AHEAD][:, S:T2]
+            nc.gpsimd.tensor_tensor(weighted[s], h[s], wgs_t[:], ALU.mult)
+
+        opening = BANKS // HALVES
+        for s in range(opening):
             for u in range(HALVES):
-                nc.gpsimd.tensor_tensor(weighted[s][:, cols_of(u, BANK)], h_raw[s, u], wgs_t[:, cols_of(u, BANK)], ALU.mult)
+                h_pass(s, u, 0)
+        for s in range(opening):
+            for u in range(HALVES):
+                for a in range(1, KA):
+                    h_pass(s, u, a)
+                h_out(s, u)
+        for s in range(opening, SLOTS):
+            for u in range(HALVES):
+                for a in range(KA):
+                    h_pass(s, u, a)
+                h_out(s, u)
+
+        squares = [place("square%d" % j, [P, S], F32, SQUARE_AT[j]) for j in range(HALVES)]
+        pairs = {(b, c): place("pairs%d_%d" % (b, c), [P, 2, BANK, 2], BF16, PAIRS_AT + 4 * KB * (CHUNKS * b + c)) for b in range(RB) for c in range(CHUNKS)}
+        joined = {}
+        z_codes = {}
+        z_scales = {}
 
         def scatter(s, pieces):
             width = S // pieces
@@ -210,59 +233,73 @@ def tile_list_pallet_slot_fit_kernel(tc, tab_words, tab_scales, offs, w4_words, 
         def subtract(engine, diff, s, cols):
             engine.tensor_tensor(diff, racks[s][:, cols], pages[s % PAGES][:, cols], ALU.subtract)
 
-        def exp_to_z(square, s, c):
+        def exp_to_pairs(s, c):
             i = s % PACK
-            target = z_pairs[c][:, i // 2, :, i % 2] if s < PACK else z_slots[c][:, i, :]
-            nc.scalar.activation(target, square, ACT.Exp, bias=ln_gain[:, s : s + 1], scale=neg_sharp[:, s : s + 1])
+            nc.scalar.activation(
+                pairs[s // PACK, c][:, i // 2, :, i % 2],
+                squares[c // 2][:, cols_of(c % 2, BANK)],
+                ACT.Exp,
+                bias=ln_gain[:, s : s + 1],
+                scale=neg_sharp[:, s : s + 1],
+            )
 
-        def square_and_exp_chunk(s, c):
-            square = squares[c % 2][:, 0:BANK]
-            nc.scalar.activation(square, racks[s][:, cols_of(c, BANK)], ACT.Square)
-            exp_to_z(square, s, c)
-
-        def slot_by_halves(s):
+        def slot_on_gpsimd(s):
+            pieces = HALVES if s in HALVED else 1
+            for u in range(pieces):
+                subtract(nc.gpsimd, diffs[s][:, cols_of(u, T2 // pieces)], s, cols_of(u, T2 // pieces))
             for half in range(HALVES):
-                diff = half_tiles[s + AHEAD - 1, half][:]
-                subtract(nc.gpsimd, diff, s, cols_of(half, S))
-                nc.scalar.activation(squares[half][:], diff, ACT.Square)
+                nc.scalar.activation(squares[half][:], diffs[s][:, cols_of(half, S)], ACT.Square)
                 for j in range(2):
-                    exp_to_z(squares[half][:, cols_of(j, BANK)], s, 2 * half + j)
+                    exp_to_pairs(s, 2 * half + j)
 
-        def quantise_pass0(half):
-            z_bf = big.tile([P, S * PACK], BF16, name=("weighted0", "area_a")[half], align_bytes=64)
-            codes = keep.tile([P, S], U32, name="z0_codes%d" % half, align_bytes=64)
-            scales = keep.tile([P, S], U8, name="z0_scales%d" % half, align_bytes=64)
-            for j in range(2):
-                c = 2 * half + j
-                nc.scalar.copy(
-                    z_bf[:, cols_of(j, BANK * PACK)].bitcast(U32).rearrange("p (m h) -> p m h", h=2),
-                    z_pairs[c][:].rearrange("p h m e -> p (h m e)").bitcast(U32).rearrange("p (h m) -> p m h", h=2),
-                )
-                z_codes[0, c] = codes[:, cols_of(j, BANK)]
-                z_scales[0, c] = scales[:, cols_of(j, BANK)]
-            nc.vector.quantize_mx(out=codes[:].bitcast(FP8X4), scales=scales[:], in_=z_bf[:])
+        def square_and_exp_chunk(s, c, diff):
+            nc.scalar.activation(squares[c // 2][:, cols_of(c % 2, BANK)], diff, ACT.Square)
+            exp_to_pairs(s, c)
 
-        load_rack(1)
+        def join(copy, dtype, b, c, at):
+            joined[b, c] = place("joined%d_%d" % (b, c), [P, BANK * PACK], BF16, at)
+            copy(
+                joined[b, c][:].bitcast(dtype).rearrange("p (m h) -> p m h", h=2),
+                pairs[b, c][:].rearrange("p h m e -> p (h m e)").bitcast(dtype).rearrange("p (h m) -> p m h", h=2),
+            )
+
+        def quantise(b, c, codes_at, scales_at):
+            z_codes[b, c] = place("z_codes%d_%d" % (b, c), [P, BANK], U32, codes_at)
+            z_scales[b, c] = place("z_scales%d_%d" % (b, c), [P, BANK], U8, scales_at)
+            nc.vector.quantize_mx(out=z_codes[b, c][:].bitcast(FP8X4), scales=z_scales[b, c][:], in_=joined[b, c][:])
+
+        nc.gpsimd.tensor_tensor(weighted[0][:, BANK:S], h0_late[:], wgs_t[:, BANK:S], ALU.mult)
         for s in range(1, AHEAD):
             weigh(s)
-        load_rack(2)
+        for s in range(1, 5):
+            load_rack(s)
         last = SLOTS - 1
         for s in range(last):
             scatter(s, HALVES if s == 0 else 1)
-            if 1 <= s <= last - 2:
-                load_rack(s + 2)
+            if s == 1:
+                load_rack(5)
+            if s + AHEAD >= 6 and s + AHEAD < SLOTS:
+                load_rack(s + AHEAD)
             if s == last - 1:
                 for c in range(CHUNKS):
-                    subtract(nc.gpsimd, racks[s][:, cols_of(c, BANK)], s, cols_of(c, BANK))
-                    square_and_exp_chunk(s, c)
+                    subtract(nc.gpsimd, racks[s - 1][:, cols_of(c, BANK)], s, cols_of(c, BANK))
+                    square_and_exp_chunk(s, c, racks[s - 1][:, cols_of(c, BANK)])
             else:
-                slot_by_halves(s)
+                slot_on_gpsimd(s)
             if s + AHEAD < SLOTS:
+                weighted[s + AHEAD] = racks[s][:, S:T2]
                 weigh(s + AHEAD)
-            if s in (PACK - 1, PACK):
-                quantise_pass0(s - PACK + 1)
+            if s == PACK - 1:
+                for c in range(CHUNKS):
+                    join(nc.scalar.copy, U32, 0, c, JOINED0_AT + 4 * KB * c)
 
-        z1_bf = [big.tile([P, BANK * PACK], BF16, name="h%d_%d" % (2 + c // 2, c % 2), align_bytes=64) for c in range(CHUNKS)]
+        early = RACK_AT[last - 1 - AHEAD]
+        w2_codes = place("w2_codes", [P, RB * N], U32, early)
+        w2_scales = place("w2_scales", [P, RB * N], U8, early + 3 * KB)
+        for lo, hi in ((0, 512), (512, RB * N)):
+            nc.vector.quantize_mx(out=w2_codes[:, lo:hi].bitcast(FP8X4), scales=w2_scales[:, lo:hi], in_=w2_bf[:, PACK * lo : PACK * hi])
+        quantise(0, 0, early + 4 * KB, early + 6 * KB)
+
         scatter(last, 1)
         for c in range(CHUNKS):
             subtract(nc.vector, racks[last][:, cols_of(c, BANK)], last, cols_of(c, BANK))
@@ -272,23 +309,13 @@ def tile_list_pallet_slot_fit_kernel(tc, tab_words, tab_scales, offs, w4_words, 
                 out=banks[(c * NT + t) % BANKS][:],
                 lhsT=w2_codes[:, cols_of(b * NT + t, P)].bitcast(FP8X4),
                 lhsT_scale=w2_scales[:, cols_of(b * NT + t, P)],
-                rhs=z_codes[b, c].bitcast(FP8X4),
-                rhs_scale=z_scales[b, c],
+                rhs=z_codes[b, c][:].bitcast(FP8X4),
+                rhs_scale=z_scales[b, c][:],
                 start=(b == 0),
                 stop=(b == RB - 1),
             )
 
-        for j in range(BANKS):
-            out_pass(0, j // NT, j % NT)
-        for c in range(CHUNKS):
-            square_and_exp_chunk(last, c)
-            nc.vector.tensor_copy(z1_bf[c][:].rearrange("p (m i) -> p m i", i=PACK), z_slots[c][:].rearrange("p i m -> p m i"))
-            nc.vector.quantize_mx(out=z_codes[1, c].bitcast(FP8X4), scales=z_scales[1, c], in_=z1_bf[c][:])
-        for c in range(CHUNKS):
-            for t in range(NT):
-                if c * NT + t >= BANKS:
-                    out_pass(0, c, t)
-                out_pass(1, c, t)
+        def store_chunk(c):
             for t in range(NT):
                 bank = banks[(c * NT + t) % BANKS]
                 res = stage.tile([P, BANK], F32, name="res")
@@ -297,3 +324,16 @@ def tile_list_pallet_slot_fit_kernel(tc, tab_words, tab_scales, offs, w4_words, 
                 else:
                     nc.scalar.copy(res[:], bank[:])
                 nc.sync.dma_start(out[cols_of(t, P), cols_of(c, BANK)], res[:])
+
+        for c in range(CHUNKS):
+            square_and_exp_chunk(last, c, racks[last][:, cols_of(c, BANK)])
+            if c > 0:
+                quantise(0, c, PAIRS_AT + 4 * KB * (c - 1), PAIRS_AT + 4 * KB * (c - 1) + 2 * KB)
+            join(nc.vector.tensor_copy, I32, 1, c, PAIRS_AT + 4 * KB * c)
+            quantise(1, c, Z1_CODES_AT + 2 * KB * c, Z1_SCALES_AT + BANK * c)
+            for b in range(RB):
+                for t in range(NT):
+                    out_pass(b, c, t)
+            if c > 0:
+                store_chunk(c - 1)
+        store_chunk(CHUNKS - 1)

@@ -1,6 +1,7 @@
 from contextlib import ExitStack
 
 import concourse.mybir as mybir
+from concourse.masks import make_identity
 
 K, T, S, H, T2, N = 1536, 2048, 1024, 1024, 2048, 384
 FLOPS = 2 * K * H * S + 2 * H * N * T2
@@ -31,33 +32,35 @@ SHIFT_ROWS = 112
 PAGES = 3
 AHEAD = 3
 STAGE_BUFS = 6
-VECTOR_COPIES = (7, 9, 11)
+VECTOR_COPIES = (5, 7, 9, 11)
 KB = 1024
 
 W4_SCALES_AT = 7 * KB + 512
-PICKED_AT = (16 * KB, 8 * KB, 74 * KB)
-TAB_SCALES_AT = 157 * KB
-W4_PLANE_AT = TAB_SCALES_AT
-WGS_AT = 158 * KB
-TAB_AT = (56 * KB, 28 * KB, 58 * KB)
-PAGE_AT = (49 * KB, 0, TAB_AT[1])
-TAB_PLANE_AT = 57 * KB
+PICKED_AT = (16 * KB, 8 * KB, 12 * KB)
+TAB_AT = (48 * KB, 28 * KB, 49 * KB)
+PAGE_AT = (0, 24 * KB, TAB_AT[2])
+TAB_PLANE_AT = TAB_AT[0]
 W4_RAW_REST_AT = TAB_AT[1]
 W2_RAW_AT = 36 * KB
 W4_RAW_FIRST_AT = W2_RAW_AT
-W4_ORD_AT = 66 * KB
-SQUARE_AT = (PICKED_AT[2], PICKED_AT[1])
-H0_AT = 78 * KB
-H1_AT = 80 * KB
-DIFF_AT = 86 * KB
-WEIGHTED_AT = 134 * KB
-PAIRS_AT = 162 * KB
-JOINED0_AT = DIFF_AT
-Z1_CODES_AT = DIFF_AT + 16 * KB
-Z1_SCALES_AT = DIFF_AT + 24 * KB
-W2_BF_AT = 146 * KB
-RACK_AT = (TAB_AT[2], H0_AT, PICKED_AT[0], W4_ORD_AT, W2_RAW_AT, WEIGHTED_AT, TAB_AT[2], H0_AT)
-HALVED = (0,)
+W4_ORD_AT = 57 * KB
+SQUARE_AT = (PICKED_AT[1], PICKED_AT[2])
+H0_AT = 180 * KB
+H_AT = {s: (63 + 4 * s) * KB for s in range(2, SLOTS)}
+H1_AT = 188 * KB
+WEIGHTED_AT = 95 * KB
+W2_BF_AT = 111 * KB
+TAB_SCALES_AT = 117 * KB
+W4_PLANE_AT = TAB_SCALES_AT
+WGS_AT = 118 * KB
+SLOTWISE_AT = 122 * KB
+PAIRS_AT = 138 * KB
+JOINED1_AT = 154 * KB
+Z1_CODES_AT = 170 * KB
+Z1_SCALES_AT = 178 * KB
+RACK_AT = (32 * KB, H0_AT, H1_AT, W4_ORD_AT, 40 * KB, WEIGHTED_AT, WEIGHTED_AT + 8 * KB, 32 * KB)
+TURNED = (2, 3)
+INTERLEAVE_ORDER = (2, 3, 0, 1)
 
 
 def tile_list_pallet_slot_fit_kernel(tc, tab_words, tab_scales, offs, w4_words, w4_scales, offs2, wgs, rack, sharp, gain, w2, out):
@@ -152,6 +155,8 @@ def tile_list_pallet_slot_fit_kernel(tc, tab_words, tab_scales, offs, w4_words, 
         for page in pages:
             nc.gpsimd.memset(page[:], 0.0)
 
+        identity = keep.tile([P, P], F32, name="identity", align_bytes=64)
+        make_identity(nc, identity[:])
         neg_sharp = keep.tile([P, SLOTS], F32, name="neg_sharp")
         ln_gain = keep.tile([P, SLOTS], F32, name="ln_gain")
         nc.scalar.activation(ln_gain[:], gain_t[:].rearrange("p b i -> p (b i)"), ACT.Ln)
@@ -174,9 +179,7 @@ def tile_list_pallet_slot_fit_kernel(tc, tab_words, tab_scales, offs, w4_words, 
 
         load_rack(0)
 
-        diffs = [place("diff%d" % s, [P, T2], F32, DIFF_AT + 8 * KB * s) for s in range(SLOTS - AHEAD + 1)]
-        h = {s + AHEAD - 1: diff[:, BANK : BANK + S] for s, diff in enumerate(diffs)}
-        h[1] = place("h1", [P, S], F32, H1_AT)[:]
+        h = {s: place("h%d" % s, [P, S], F32, H_AT.get(s, H1_AT))[:] for s in range(1, SLOTS)}
         h0_late = place("h0_late", [P, BANK], F32, H0_AT)
         weighted = {s: place("weighted%d" % s, [P, S], F32, WEIGHTED_AT + 4 * KB * s)[:] for s in range(AHEAD)}
 
@@ -197,9 +200,9 @@ def tile_list_pallet_slot_fit_kernel(tc, tab_words, tab_scales, offs, w4_words, 
         def h_out(s, u):
             bank = banks[(HALVES * s + u) % BANKS]
             if (s, u) == (0, 0):
-                nc.vector.tensor_tensor(weighted[0][:, 0:BANK], bank[:], wgs_t[:, 0:BANK], ALU.mult)
+                nc.vector.scalar_tensor_tensor(weighted[0][:, 0:BANK], bank[:], -1.0, wgs_t[:, 0:BANK], ALU.mult, ALU.mult)
             else:
-                nc.scalar.copy(h_half(s, u), bank[:])
+                nc.scalar.mul(h_half(s, u), bank[:], -1.0)
 
         def weigh(s):
             nc.gpsimd.tensor_tensor(weighted[s], h[s], wgs_t[:], ALU.mult)
@@ -220,47 +223,70 @@ def tile_list_pallet_slot_fit_kernel(tc, tab_words, tab_scales, offs, w4_words, 
                 h_out(s, u)
 
         squares = [place("square%d" % j, [P, S], F32, SQUARE_AT[j]) for j in range(HALVES)]
-        pairs = {(b, c): place("pairs%d_%d" % (b, c), [P, 2, BANK, 2], BF16, PAIRS_AT + 4 * KB * (CHUNKS * b + c)) for b in range(RB) for c in range(CHUNKS)}
+        pairs = [place("pairs%d" % c, [P, 2, BANK, 2], BF16, PAIRS_AT + 4 * KB * c) for c in range(CHUNKS)]
+        slotwise = [place("slotwise%d" % c, [P, PACK, BANK], BF16, SLOTWISE_AT + 4 * KB * c) for c in range(CHUNKS)]
         joined = {}
         z_codes = {}
         z_scales = {}
+        turn_banks = {0: ((banks[2], banks[3]), (banks[4], banks[5]))}
+        for s in range(1, SLOTS):
+            sums, backs = turn_banks[s - 1]
+            turn_banks[s] = (backs, sums)
 
         def scatter(s, pieces):
             width = S // pieces
             for u in range(pieces):
                 nc.vector.tensor_copy(pages[s % PAGES][:].indirect(offs2_t[:, cols_of(u, width // 16)]), weighted[s][:, cols_of(u, width)])
 
-        def subtract(engine, diff, s, cols):
-            engine.tensor_tensor(diff, racks[s][:, cols], pages[s % PAGES][:, cols], ALU.subtract)
+        def difference(engine, diff, s, cols):
+            engine.tensor_tensor(diff, racks[s][:, cols], pages[s % PAGES][:, cols], ALU.add)
 
-        def exp_to_pairs(s, c):
-            i = s % PACK
-            nc.scalar.activation(
-                pairs[s // PACK, c][:, i // 2, :, i % 2],
-                squares[c // 2][:, cols_of(c % 2, BANK)],
-                ACT.Exp,
-                bias=ln_gain[:, s : s + 1],
-                scale=neg_sharp[:, s : s + 1],
+        def square_of(c):
+            return squares[c // 2][:, cols_of(c % 2, BANK)]
+
+        def exp_to_z(s, c, square):
+            b, i = divmod(s, PACK)
+            target = slotwise[c][:, i, :] if b == 0 else pairs[c][:, i // 2, :, i % 2]
+            nc.scalar.activation(target, square, ACT.Exp, bias=ln_gain[:, s : s + 1], scale=neg_sharp[:, s : s + 1])
+
+        def turned_chunks(s):
+            sums, backs = turn_banks[s]
+            blocks = BANK // P
+            for c, bank in zip(TURNED, sums):
+                for k, source in enumerate((racks[s], pages[s % PAGES])):
+                    for j in range(blocks):
+                        nc.tensor.matmul(
+                            bank[:, cols_of(j, P)], source[:, cols_of(c * blocks + j, P)], identity[:],
+                            start=(k == 0 and j == 0), stop=(k == 1 and j == blocks - 1), is_transpose=True,
+                        )
+            for c, bank, back in zip(TURNED, sums, backs):
+                nc.scalar.activation(square_of(c), bank[:], ACT.Square)
+                for j in range(blocks):
+                    nc.tensor.transpose(back[:, cols_of(j, P)], square_of(c)[:, cols_of(j, P)], identity[:])
+            for c, back in zip(TURNED, backs):
+                exp_to_z(s, c, back[:])
+
+        def first_half_on_gpsimd(s, at):
+            diff = place("diff%d" % s, [P, S], F32, at)
+            pieces = HALVES if s == SLOTS - 2 else 1
+            for u in range(pieces):
+                cols = cols_of(u, S // pieces)
+                difference(nc.gpsimd, diff[:, cols], s, cols)
+                nc.scalar.activation(squares[0][:, cols], diff[:, cols], ACT.Square)
+            for c in range(2):
+                exp_to_z(s, c, square_of(c))
+
+        def join(c):
+            joined[1, c] = place("joined1_%d" % c, [P, BANK * PACK], BF16, JOINED1_AT + 4 * KB * c)
+            nc.vector.tensor_copy(
+                joined[1, c][:].bitcast(I32).rearrange("p (m h) -> p m h", h=2),
+                pairs[c][:].rearrange("p h m e -> p (h m e)").bitcast(I32).rearrange("p (h m) -> p m h", h=2),
             )
 
-        def slot_on_gpsimd(s):
-            pieces = HALVES if s in HALVED else 1
-            for u in range(pieces):
-                subtract(nc.gpsimd, diffs[s][:, cols_of(u, T2 // pieces)], s, cols_of(u, T2 // pieces))
-            for half in range(HALVES):
-                nc.scalar.activation(squares[half][:], diffs[s][:, cols_of(half, S)], ACT.Square)
-                for j in range(2):
-                    exp_to_pairs(s, 2 * half + j)
-
-        def square_and_exp_chunk(s, c, diff):
-            nc.scalar.activation(squares[c // 2][:, cols_of(c % 2, BANK)], diff, ACT.Square)
-            exp_to_pairs(s, c)
-
-        def join(copy, dtype, b, c, at):
-            joined[b, c] = place("joined%d_%d" % (b, c), [P, BANK * PACK], BF16, at)
-            copy(
-                joined[b, c][:].bitcast(dtype).rearrange("p (m h) -> p m h", h=2),
-                pairs[b, c][:].rearrange("p h m e -> p (h m e)").bitcast(dtype).rearrange("p (h m) -> p m h", h=2),
+        def interleave(c, at):
+            joined[0, c] = place("joined0_%d" % c, [P, BANK * PACK], BF16, at)
+            nc.gpsimd.tensor_scalar(
+                joined[0, c][:].rearrange("p (m i) -> p m i", i=PACK), slotwise[c][:].rearrange("p i m -> p m i"), 1.0, 0.0, ALU.mult, ALU.add
             )
 
         def quantise(b, c, codes_at, scales_at):
@@ -276,37 +302,40 @@ def tile_list_pallet_slot_fit_kernel(tc, tab_words, tab_scales, offs, w4_words, 
         last = SLOTS - 1
         for s in range(last):
             scatter(s, HALVES if s == 0 else 1)
-            if s == 1:
-                load_rack(5)
-            if s + AHEAD >= 6 and s + AHEAD < SLOTS:
-                load_rack(s + AHEAD)
-            if s == last - 1:
-                for c in range(CHUNKS):
-                    subtract(nc.gpsimd, racks[s - 1][:, cols_of(c, BANK)], s, cols_of(c, BANK))
-                    square_and_exp_chunk(s, c, racks[s - 1][:, cols_of(c, BANK)])
+            if 1 <= s <= 3:
+                load_rack(s + 4)
+            turned_chunks(s)
+            if s < PACK:
+                first_half_on_gpsimd(s, H_AT[AHEAD - 1] if s == 0 else H_AT[s + AHEAD])
+                nxt = AHEAD if s == 0 else s + AHEAD + 1
+                weighted[nxt] = racks[s][:, 0:S]
+                weigh(nxt)
+                if s == 0:
+                    weighted[nxt + 1] = place("weighted%d" % (nxt + 1), [P, S], F32, H_AT[nxt])[:]
+                    weigh(nxt + 1)
             else:
-                slot_on_gpsimd(s)
-            if s + AHEAD < SLOTS:
-                weighted[s + AHEAD] = racks[s][:, S:T2]
-                weigh(s + AHEAD)
-            if s == PACK - 1:
-                for c in range(CHUNKS):
-                    join(nc.scalar.copy, U32, 0, c, JOINED0_AT + 4 * KB * c)
-
-        early = RACK_AT[last - 1 - AHEAD]
-        w2_codes = place("w2_codes", [P, RB * N], U32, early)
-        w2_scales = place("w2_scales", [P, RB * N], U8, early + 3 * KB)
-        for lo, hi in ((0, 512), (512, RB * N)):
-            nc.vector.quantize_mx(out=w2_codes[:, lo:hi].bitcast(FP8X4), scales=w2_scales[:, lo:hi], in_=w2_bf[:, PACK * lo : PACK * hi])
-        quantise(0, 0, early + 4 * KB, early + 6 * KB)
+                first_half_on_gpsimd(s, SLOTWISE_AT + 4 * KB * INTERLEAVE_ORDER[s - PACK])
+            if s >= PACK - 1:
+                interleave(INTERLEAVE_ORDER[s - PACK + 1], H_AT[last] if s == PACK - 1 else RACK_AT[s])
 
         scatter(last, 1)
-        for c in range(CHUNKS):
-            subtract(nc.vector, racks[last][:, cols_of(c, BANK)], last, cols_of(c, BANK))
+        for c in range(2):
+            diff = racks[last][:, cols_of(c, BANK)]
+            difference(nc.vector, diff, last, cols_of(c, BANK))
+            nc.scalar.activation(square_of(c), diff, ACT.Square)
+            exp_to_z(last, c, square_of(c))
+        turned_chunks(last)
+        w2_codes = place("w2_codes", [P, RB * N], U32, RACK_AT[3])
+        w2_scales = place("w2_scales", [P, RB * N], U8, RACK_AT[3] + 3 * KB)
+        for lo, hi in ((0, 512), (512, RB * N)):
+            nc.vector.quantize_mx(out=w2_codes[:, lo:hi].bitcast(FP8X4), scales=w2_scales[:, lo:hi], in_=w2_bf[:, PACK * lo : PACK * hi])
+        sums, backs = turn_banks[last]
+        others = [banks[j] for j in (0, 1, 6, 7)]
+        out_banks = others + list(sums) + list(backs) + others
 
         def out_pass(b, c, t):
             nc.tensor.matmul_mx(
-                out=banks[(c * NT + t) % BANKS][:],
+                out=out_banks[c * NT + t][:],
                 lhsT=w2_codes[:, cols_of(b * NT + t, P)].bitcast(FP8X4),
                 lhsT_scale=w2_scales[:, cols_of(b * NT + t, P)],
                 rhs=z_codes[b, c][:].bitcast(FP8X4),
@@ -317,7 +346,7 @@ def tile_list_pallet_slot_fit_kernel(tc, tab_words, tab_scales, offs, w4_words, 
 
         def store_chunk(c):
             for t in range(NT):
-                bank = banks[(c * NT + t) % BANKS]
+                bank = out_banks[c * NT + t]
                 res = stage.tile([P, BANK], F32, name="res")
                 if c * NT + t in VECTOR_COPIES:
                     nc.vector.tensor_copy(res[:], bank[:])
@@ -326,10 +355,9 @@ def tile_list_pallet_slot_fit_kernel(tc, tab_words, tab_scales, offs, w4_words, 
                 nc.sync.dma_start(out[cols_of(t, P), cols_of(c, BANK)], res[:])
 
         for c in range(CHUNKS):
-            square_and_exp_chunk(last, c, racks[last][:, cols_of(c, BANK)])
-            if c > 0:
-                quantise(0, c, PAIRS_AT + 4 * KB * (c - 1), PAIRS_AT + 4 * KB * (c - 1) + 2 * KB)
-            join(nc.vector.tensor_copy, I32, 1, c, PAIRS_AT + 4 * KB * c)
+            at = PAGE_AT[last % PAGES] if c == 0 else JOINED1_AT + 4 * KB * (c - 1)
+            quantise(0, c, at, at + 2 * KB)
+            join(c)
             quantise(1, c, Z1_CODES_AT + 2 * KB * c, Z1_SCALES_AT + BANK * c)
             for b in range(RB):
                 for t in range(NT):

@@ -37,28 +37,31 @@ KB = 1024
 
 W4_SCALES_AT = 7 * KB + 512
 PICKED_AT = (16 * KB, 8 * KB, 12 * KB)
-TAB_AT = (48 * KB, 28 * KB, 49 * KB)
-PAGE_AT = (0, 24 * KB, TAB_AT[2])
+TAB_AT = (200 * KB, 27 * KB + 512, 201 * KB)
+W2_CODES_AT = TAB_AT[2]
+PAGE_AT = (0, TAB_AT[1], TAB_AT[2] + 4 * KB)
 TAB_PLANE_AT = TAB_AT[0]
-W4_RAW_REST_AT = TAB_AT[1]
 W2_RAW_AT = 36 * KB
-W4_RAW_FIRST_AT = W2_RAW_AT
+W4_RAW_REST_AT = W2_RAW_AT - 512
+W4_RAW_FIRST_AT = TAB_AT[1]
 W4_ORD_AT = 57 * KB
-SQUARE_AT = (PICKED_AT[1], PICKED_AT[2])
+SQUARE_AT = (PICKED_AT[1], 196 * KB)
 H0_AT = 180 * KB
 H_AT = {s: (63 + 4 * s) * KB for s in range(2, SLOTS)}
 H1_AT = 188 * KB
 WEIGHTED_AT = 95 * KB
-W2_BF_AT = 111 * KB
-TAB_SCALES_AT = 117 * KB
+W2_BF_AT = 20 * KB
+TAB_SCALES_AT = 112 * KB
 W4_PLANE_AT = TAB_SCALES_AT
-WGS_AT = 118 * KB
+GAIN_AT = W4_RAW_REST_AT
+SHARP_AT = GAIN_AT + 64
+WGS_AT = TAB_SCALES_AT + KB
 SLOTWISE_AT = 122 * KB
 PAIRS_AT = 138 * KB
 JOINED1_AT = 154 * KB
 Z1_CODES_AT = 170 * KB
 Z1_SCALES_AT = 178 * KB
-RACK_AT = (32 * KB, H0_AT, H1_AT, W4_ORD_AT, 40 * KB, WEIGHTED_AT, WEIGHTED_AT + 8 * KB, 32 * KB)
+RACK_AT = (W2_RAW_AT, H0_AT, H1_AT, W2_RAW_AT + 8 * KB, W4_ORD_AT, WEIGHTED_AT, WEIGHTED_AT + 8 * KB, W2_RAW_AT)
 TURNED = (2, 3)
 INTERLEAVE_ORDER = (2, 3, 0, 1)
 
@@ -100,14 +103,10 @@ def tile_list_pallet_slot_fit_kernel(tc, tab_words, tab_scales, offs, w4_words, 
         nc.sync.dma_start(offs_t[:], offs)
         load_table(0)
         nc.sync.dma_start(offs2_t[:], offs2)
-        gain_t = keep.tile([P, RB, PACK], F32, name="gain_t")
-        sharp_t = keep.tile([P, RB, PACK], F32, name="sharp_t")
         for q in range(QUADRANTS):
             nc.scalar.dma_start(tab_scales_raw[32 * q : 32 * q + 4 * KA, :].bitcast(I32), tab_scales[:, 4 * q : 4 * q + 4, :].bitcast(I32))
         for q in range(QUADRANTS):
             nc.gpsimd.dma_start(w4_scales_raw[32 * q : 32 * q + 4 * KA, :].bitcast(I32), w4_scales[:, 4 * q : 4 * q + 4, :].bitcast(I32))
-        nc.gpsimd.dma_start(gain_t[:], gain.rearrange("(b p i) -> p b i", b=RB, i=PACK))
-        nc.gpsimd.dma_start(sharp_t[:], sharp.rearrange("(b p i) -> p b i", b=RB, i=PACK))
         w4_shifted = keep.tile([P, KA - 1, H], U8, name="w4_shifted", align_bytes=64)
         tab_shifted = keep.tile([P, KA - 1, S], U8, name="tab_shifted", align_bytes=64)
         nc.gpsimd.memset(w4_shifted[:].rearrange("p a n -> p (a n)").bitcast(I32), 0)
@@ -119,9 +118,13 @@ def tile_list_pallet_slot_fit_kernel(tc, tab_words, tab_scales, offs, w4_words, 
                 w4_ord[a][:].bitcast(U16).rearrange("p (b i m) -> p b i m", b=RB, i=PACK),
                 w4_raw[a].bitcast(U16).rearrange("p (b m i) -> p b i m", b=RB, i=PACK),
             )
+        load_table(1)
+        gain_t = place("gain_t", [P, RB, PACK], F32, GAIN_AT)
+        sharp_t = place("sharp_t", [P, RB, PACK], F32, SHARP_AT)
+        nc.sync.dma_start(gain_t[:], gain.rearrange("(b p i) -> p b i", b=RB, i=PACK))
+        nc.sync.dma_start(sharp_t[:], sharp.rearrange("(b p i) -> p b i", b=RB, i=PACK))
         w2_raw = place("w2_raw", [P, RB, PACK, N], F32, W2_RAW_AT)
         nc.sync.dma_start(w2_raw[:].rearrange("p b i n -> p b (i n)"), w2.rearrange("(b p i) n -> p b (i n)", b=RB, i=PACK))
-        load_table(1)
         picked = {}
 
         def gather_words(a, pieces):
@@ -151,17 +154,17 @@ def tile_list_pallet_slot_fit_kernel(tc, tab_words, tab_scales, offs, w4_words, 
         gather_words(1, 1)
         gather_words(2, HALVES)
 
+        neg_sharp = keep.tile([P, SLOTS], F32, name="neg_sharp")
+        ln_gain = keep.tile([P, SLOTS], F32, name="ln_gain")
+        nc.scalar.activation(ln_gain[:], gain_t[:].rearrange("p b i -> p (b i)"), ACT.Ln)
+        nc.scalar.mul(neg_sharp[:], sharp_t[:].rearrange("p b i -> p (b i)"), -1.0)
+
         pages = [place("page%d" % j, [P, T2], F32, PAGE_AT[j]) for j in range(PAGES)]
         for page in pages:
             nc.gpsimd.memset(page[:], 0.0)
 
         identity = keep.tile([P, P], F32, name="identity", align_bytes=64)
         make_identity(nc, identity[:])
-        neg_sharp = keep.tile([P, SLOTS], F32, name="neg_sharp")
-        ln_gain = keep.tile([P, SLOTS], F32, name="ln_gain")
-        nc.scalar.activation(ln_gain[:], gain_t[:].rearrange("p b i -> p (b i)"), ACT.Ln)
-        nc.scalar.mul(neg_sharp[:], sharp_t[:].rearrange("p b i -> p (b i)"), -1.0)
-
         w2_bf = place("w2_bf", [P, RB * N * PACK], BF16, W2_BF_AT)
         for b in range(RB):
             for t in range(NT):
@@ -169,6 +172,11 @@ def tile_list_pallet_slot_fit_kernel(tc, tab_words, tab_scales, offs, w4_words, 
                     w2_bf[:, cols_of(b * NT + t, P * PACK)].rearrange("p (n i) -> p n i", i=PACK),
                     w2_raw[:, b, :, cols_of(t, P)].rearrange("p i n -> p n i"),
                 )
+
+        w2_codes = place("w2_codes", [P, RB * N], U32, W2_CODES_AT)
+        w2_scales = place("w2_scales", [P, RB * N], U8, W2_CODES_AT + 3 * KB)
+        for lo, hi in ((0, 512), (512, RB * N)):
+            nc.vector.quantize_mx(out=w2_codes[:, lo:hi].bitcast(FP8X4), scales=w2_scales[:, lo:hi], in_=w2_bf[:, PACK * lo : PACK * hi])
 
         rack_rows = rack.rearrange("(b p i) m -> b i p m", b=RB, i=PACK)
         racks = {}
@@ -186,9 +194,12 @@ def tile_list_pallet_slot_fit_kernel(tc, tab_words, tab_scales, offs, w4_words, 
         def h_half(s, u):
             return h0_late[:] if s == 0 else h[s][:, cols_of(u, BANK)]
 
+        def h_bank(s, u):
+            return banks[u if s == SLOTS - 1 else (HALVES * s + u) % BANKS]
+
         def h_pass(s, u, a):
             nc.tensor.matmul_mx(
-                out=banks[(HALVES * s + u) % BANKS][:],
+                out=h_bank(s, u)[:],
                 lhsT=w4_ord[a][:, cols_of(s, 2 * P)].bitcast(FP4X4),
                 lhsT_scale=w4_planes[a][:, cols_of(s, P)],
                 rhs=picked[a][:, cols_of(u, BANK)].bitcast(FP8X4),
@@ -198,7 +209,7 @@ def tile_list_pallet_slot_fit_kernel(tc, tab_words, tab_scales, offs, w4_words, 
             )
 
         def h_out(s, u):
-            bank = banks[(HALVES * s + u) % BANKS]
+            bank = h_bank(s, u)
             if (s, u) == (0, 0):
                 nc.vector.scalar_tensor_tensor(weighted[0][:, 0:BANK], bank[:], -1.0, wgs_t[:, 0:BANK], ALU.mult, ALU.mult)
             else:
@@ -216,11 +227,15 @@ def tile_list_pallet_slot_fit_kernel(tc, tab_words, tab_scales, offs, w4_words, 
                 for a in range(1, KA):
                     h_pass(s, u, a)
                 h_out(s, u)
-        for s in range(opening, SLOTS):
+
+        def h_slot(s):
             for u in range(HALVES):
                 for a in range(KA):
                     h_pass(s, u, a)
                 h_out(s, u)
+
+        for s in range(opening, SLOTS - 1):
+            h_slot(s)
 
         squares = [place("square%d" % j, [P, S], F32, SQUARE_AT[j]) for j in range(HALVES)]
         pairs = [place("pairs%d" % c, [P, 2, BANK, 2], BF16, PAIRS_AT + 4 * KB * c) for c in range(CHUNKS)]
@@ -228,8 +243,8 @@ def tile_list_pallet_slot_fit_kernel(tc, tab_words, tab_scales, offs, w4_words, 
         joined = {}
         z_codes = {}
         z_scales = {}
-        turn_banks = {0: ((banks[2], banks[3]), (banks[4], banks[5]))}
-        for s in range(1, SLOTS):
+        turn_banks = {0: ((banks[0], banks[1]), (banks[2], banks[3])), 1: ((banks[2], banks[3]), (banks[6], banks[7]))}
+        for s in range(2, SLOTS):
             sums, backs = turn_banks[s - 1]
             turn_banks[s] = (backs, sums)
 
@@ -241,7 +256,7 @@ def tile_list_pallet_slot_fit_kernel(tc, tab_words, tab_scales, offs, w4_words, 
         def difference(engine, diff, s, cols):
             engine.tensor_tensor(diff, racks[s][:, cols], pages[s % PAGES][:, cols], ALU.add)
 
-        def square_of(c):
+        def square_of(s, c):
             return squares[c // 2][:, cols_of(c % 2, BANK)]
 
         def exp_to_z(s, c, square):
@@ -250,6 +265,14 @@ def tile_list_pallet_slot_fit_kernel(tc, tab_words, tab_scales, offs, w4_words, 
             nc.scalar.activation(target, square, ACT.Exp, bias=ln_gain[:, s : s + 1], scale=neg_sharp[:, s : s + 1])
 
         def turned_chunks(s):
+            turned_squares(s)
+            turned_exps(s)
+
+        def turned_exps(s):
+            for c, back in zip(TURNED, turn_banks[s][1]):
+                exp_to_z(s, c, back[:])
+
+        def turned_squares(s):
             sums, backs = turn_banks[s]
             blocks = BANK // P
             for c, bank in zip(TURNED, sums):
@@ -260,11 +283,9 @@ def tile_list_pallet_slot_fit_kernel(tc, tab_words, tab_scales, offs, w4_words, 
                             start=(k == 0 and j == 0), stop=(k == 1 and j == blocks - 1), is_transpose=True,
                         )
             for c, bank, back in zip(TURNED, sums, backs):
-                nc.scalar.activation(square_of(c), bank[:], ACT.Square)
+                nc.scalar.activation(square_of(s, c), bank[:], ACT.Square)
                 for j in range(blocks):
-                    nc.tensor.transpose(back[:, cols_of(j, P)], square_of(c)[:, cols_of(j, P)], identity[:])
-            for c, back in zip(TURNED, backs):
-                exp_to_z(s, c, back[:])
+                    nc.tensor.transpose(back[:, cols_of(j, P)], square_of(s, c)[:, cols_of(j, P)], identity[:])
 
         def first_half_on_gpsimd(s, at):
             diff = place("diff%d" % s, [P, S], F32, at)
@@ -274,7 +295,7 @@ def tile_list_pallet_slot_fit_kernel(tc, tab_words, tab_scales, offs, w4_words, 
                 difference(nc.gpsimd, diff[:, cols], s, cols)
                 nc.scalar.activation(squares[0][:, cols], diff[:, cols], ACT.Square)
             for c in range(2):
-                exp_to_z(s, c, square_of(c))
+                exp_to_z(s, c, square_of(s, c))
 
         def join(c):
             joined[1, c] = place("joined1_%d" % c, [P, BANK * PACK], BF16, JOINED1_AT + 4 * KB * c)
@@ -283,11 +304,12 @@ def tile_list_pallet_slot_fit_kernel(tc, tab_words, tab_scales, offs, w4_words, 
                 pairs[c][:].rearrange("p h m e -> p (h m e)").bitcast(I32).rearrange("p (h m) -> p m h", h=2),
             )
 
-        def interleave(c, at):
+        def interleave(target, source):
+            nc.gpsimd.tensor_scalar(target.rearrange("p (m i) -> p m i", i=PACK), source.rearrange("p i m -> p m i"), 1.0, 0.0, ALU.mult, ALU.add)
+
+        def interleave_chunk(c, at):
             joined[0, c] = place("joined0_%d" % c, [P, BANK * PACK], BF16, at)
-            nc.gpsimd.tensor_scalar(
-                joined[0, c][:].rearrange("p (m i) -> p m i", i=PACK), slotwise[c][:].rearrange("p i m -> p m i"), 1.0, 0.0, ALU.mult, ALU.add
-            )
+            interleave(joined[0, c][:], slotwise[c][:])
 
         def quantise(b, c, codes_at, scales_at):
             z_codes[b, c] = place("z_codes%d_%d" % (b, c), [P, BANK], U32, codes_at)
@@ -297,7 +319,7 @@ def tile_list_pallet_slot_fit_kernel(tc, tab_words, tab_scales, offs, w4_words, 
         nc.gpsimd.tensor_tensor(weighted[0][:, BANK:S], h0_late[:], wgs_t[:, BANK:S], ALU.mult)
         for s in range(1, AHEAD):
             weigh(s)
-        for s in range(1, 5):
+        for s in (1, 2, 3):
             load_rack(s)
         last = SLOTS - 1
         for s in range(last):
@@ -305,6 +327,9 @@ def tile_list_pallet_slot_fit_kernel(tc, tab_words, tab_scales, offs, w4_words, 
             if 1 <= s <= 3:
                 load_rack(s + 4)
             turned_chunks(s)
+            if s == 0:
+                h_slot(last)
+                load_rack(4)
             if s < PACK:
                 first_half_on_gpsimd(s, H_AT[AHEAD - 1] if s == 0 else H_AT[s + AHEAD])
                 nxt = AHEAD if s == 0 else s + AHEAD + 1
@@ -313,25 +338,25 @@ def tile_list_pallet_slot_fit_kernel(tc, tab_words, tab_scales, offs, w4_words, 
                 if s == 0:
                     weighted[nxt + 1] = place("weighted%d" % (nxt + 1), [P, S], F32, H_AT[nxt])[:]
                     weigh(nxt + 1)
+            elif s == PACK:
+                first_half_on_gpsimd(s, H_AT[last])
+                interleave_chunk(2, RACK_AT[s])
+                interleave_chunk(3, RACK_AT[s] + 4 * KB)
             else:
-                first_half_on_gpsimd(s, SLOTWISE_AT + 4 * KB * INTERLEAVE_ORDER[s - PACK])
-            if s >= PACK - 1:
-                interleave(INTERLEAVE_ORDER[s - PACK + 1], H_AT[last] if s == PACK - 1 else RACK_AT[s])
+                first_half_on_gpsimd(s, SLOTWISE_AT + 4 * KB * (3, 0)[s - PACK - 1])
+                interleave_chunk(s - PACK - 1, RACK_AT[s])
 
         scatter(last, 1)
+        last_diff = place("last_diff", [P, S], F32, H_AT[2])
         for c in range(2):
-            diff = racks[last][:, cols_of(c, BANK)]
+            diff = last_diff[:, cols_of(c, BANK)]
             difference(nc.vector, diff, last, cols_of(c, BANK))
-            nc.scalar.activation(square_of(c), diff, ACT.Square)
-            exp_to_z(last, c, square_of(c))
-        turned_chunks(last)
-        w2_codes = place("w2_codes", [P, RB * N], U32, RACK_AT[3])
-        w2_scales = place("w2_scales", [P, RB * N], U8, RACK_AT[3] + 3 * KB)
-        for lo, hi in ((0, 512), (512, RB * N)):
-            nc.vector.quantize_mx(out=w2_codes[:, lo:hi].bitcast(FP8X4), scales=w2_scales[:, lo:hi], in_=w2_bf[:, PACK * lo : PACK * hi])
+            nc.scalar.activation(square_of(last, c), diff, ACT.Square)
+            exp_to_z(last, c, square_of(last, c))
+        turned_squares(last)
         sums, backs = turn_banks[last]
-        others = [banks[j] for j in (0, 1, 6, 7)]
-        out_banks = others + list(sums) + list(backs) + others
+        others = [banks[j] for j in (0, 1, 4, 5)]
+        out_banks = others + list(sums) + [backs[0], others[0], others[1], backs[1], others[2], others[3]]
 
         def out_pass(b, c, t):
             nc.tensor.matmul_mx(
@@ -355,8 +380,10 @@ def tile_list_pallet_slot_fit_kernel(tc, tab_words, tab_scales, offs, w4_words, 
                 nc.sync.dma_start(out[cols_of(t, P), cols_of(c, BANK)], res[:])
 
         for c in range(CHUNKS):
-            at = PAGE_AT[last % PAGES] if c == 0 else JOINED1_AT + 4 * KB * (c - 1)
-            quantise(0, c, at, at + 2 * KB)
+            if c < 2:
+                quantise(0, c, RACK_AT[last] + 4 * KB * c, RACK_AT[last] + 4 * KB * c + 2 * KB)
+            else:
+                quantise(0, c, PAIRS_AT + 4 * KB * (c - 2), PAIRS_AT + 4 * KB * (c - 2) + 2 * KB)
             join(c)
             quantise(1, c, Z1_CODES_AT + 2 * KB * c, Z1_SCALES_AT + BANK * c)
             for b in range(RB):
@@ -364,4 +391,6 @@ def tile_list_pallet_slot_fit_kernel(tc, tab_words, tab_scales, offs, w4_words, 
                     out_pass(b, c, t)
             if c > 0:
                 store_chunk(c - 1)
+            if c < 2:
+                exp_to_z(last, TURNED[c], backs[c][:])
         store_chunk(CHUNKS - 1)

@@ -31,8 +31,7 @@ NT = N // P
 SHIFT_ROWS = 112
 PAGES = 3
 AHEAD = 3
-STAGE_BUFS = 6
-VECTOR_COPIES = (5, 7, 9, 11)
+VECTOR_COPIES = (8, 9, 11)
 KB = 1024
 
 W4_SCALES_AT = 7 * KB + 512
@@ -46,6 +45,7 @@ W4_RAW_REST_AT = W2_RAW_AT - 512
 W4_RAW_FIRST_AT = TAB_AT[1]
 W4_ORD_AT = 57 * KB
 SQUARE_AT = (PICKED_AT[1], 196 * KB)
+RESULT_AT = 71 * KB
 H0_AT = 180 * KB
 H_AT = {s: (63 + 4 * s) * KB for s in range(2, SLOTS)}
 H1_AT = 188 * KB
@@ -62,8 +62,8 @@ JOINED1_AT = 154 * KB
 Z1_CODES_AT = 170 * KB
 Z1_SCALES_AT = 178 * KB
 RACK_AT = (W2_RAW_AT, H0_AT, H1_AT, W2_RAW_AT + 8 * KB, W4_ORD_AT, WEIGHTED_AT, WEIGHTED_AT + 8 * KB, W2_RAW_AT)
+FINE_FROM = 5
 TURNED = (2, 3)
-INTERLEAVE_ORDER = (2, 3, 0, 1)
 
 
 def tile_list_pallet_slot_fit_kernel(tc, tab_words, tab_scales, offs, w4_words, w4_scales, offs2, wgs, rack, sharp, gain, w2, out):
@@ -72,7 +72,6 @@ def tile_list_pallet_slot_fit_kernel(tc, tab_words, tab_scales, offs, w4_words, 
         lists = ctx.enter_context(tc.tile_pool(name="lists", bufs=1))
         keep = ctx.enter_context(tc.tile_pool(name="keep", bufs=1))
         laid = ctx.enter_context(tc.tile_pool(name="laid", bufs=1))
-        stage = ctx.enter_context(tc.tile_pool(name="stage", bufs=STAGE_BUFS))
         psum = ctx.enter_context(tc.psum_pool(name="psum", bufs=1))
 
         offs_t = lists.tile([P, S // 16], U16, name="offs_t")
@@ -238,8 +237,13 @@ def tile_list_pallet_slot_fit_kernel(tc, tab_words, tab_scales, offs, w4_words, 
             h_slot(s)
 
         squares = [place("square%d" % j, [P, S], F32, SQUARE_AT[j]) for j in range(HALVES)]
-        pairs = [place("pairs%d" % c, [P, 2, BANK, 2], BF16, PAIRS_AT + 4 * KB * c) for c in range(CHUNKS)]
-        slotwise = [place("slotwise%d" % c, [P, PACK, BANK], BF16, SLOTWISE_AT + 4 * KB * c) for c in range(CHUNKS)]
+        pairs = {(1, c): place("pairs1_%d" % c, [P, 2, BANK, 2], BF16, PAIRS_AT + 4 * KB * c) for c in range(CHUNKS)}
+        slotwise = {}
+        for c in range(CHUNKS):
+            if c in TURNED:
+                slotwise[c] = place("slotwise%d" % c, [P, PACK, BANK], BF16, SLOTWISE_AT + 4 * KB * c)
+            else:
+                pairs[0, c] = place("pairs0_%d" % c, [P, 2, BANK, 2], BF16, SLOTWISE_AT + 4 * KB * c)
         joined = {}
         z_codes = {}
         z_scales = {}
@@ -261,47 +265,70 @@ def tile_list_pallet_slot_fit_kernel(tc, tab_words, tab_scales, offs, w4_words, 
 
         def exp_to_z(s, c, square):
             b, i = divmod(s, PACK)
-            target = slotwise[c][:, i, :] if b == 0 else pairs[c][:, i // 2, :, i % 2]
+            target = pairs[b, c][:, i // 2, :, i % 2] if (b, c) in pairs else slotwise[c][:, i, :]
             nc.scalar.activation(target, square, ACT.Exp, bias=ln_gain[:, s : s + 1], scale=neg_sharp[:, s : s + 1])
 
-        def turned_chunks(s):
-            turned_squares(s)
-            turned_exps(s)
-
-        def turned_exps(s):
-            for c, back in zip(TURNED, turn_banks[s][1]):
-                exp_to_z(s, c, back[:])
-
-        def turned_squares(s):
-            sums, backs = turn_banks[s]
+        def turned_sums(s):
             blocks = BANK // P
-            for c, bank in zip(TURNED, sums):
+            for c, bank in zip(TURNED, turn_banks[s][0]):
                 for k, source in enumerate((racks[s], pages[s % PAGES])):
                     for j in range(blocks):
                         nc.tensor.matmul(
                             bank[:, cols_of(j, P)], source[:, cols_of(c * blocks + j, P)], identity[:],
                             start=(k == 0 and j == 0), stop=(k == 1 and j == blocks - 1), is_transpose=True,
                         )
-            for c, bank, back in zip(TURNED, sums, backs):
-                nc.scalar.activation(square_of(s, c), bank[:], ACT.Square)
-                for j in range(blocks):
-                    nc.tensor.transpose(back[:, cols_of(j, P)], square_of(s, c)[:, cols_of(j, P)], identity[:])
 
-        def first_half_on_gpsimd(s, at):
+        def square_turned(s, j):
+            c = TURNED[j]
+            nc.scalar.activation(square_of(s, c), turn_banks[s][0][j][:], ACT.Square)
+            for block in range(BANK // P):
+                nc.tensor.transpose(turn_banks[s][1][j][:, cols_of(block, P)], square_of(s, c)[:, cols_of(block, P)], identity[:])
+
+        def exp_turned(s, j):
+            exp_to_z(s, TURNED[j], turn_banks[s][1][j][:])
+
+        def slot_coarse(s, at):
+            turned_sums(s)
+            for j in range(2):
+                square_turned(s, j)
+            for j in range(2):
+                exp_turned(s, j)
+            if s == 0:
+                h_slot(SLOTS - 1)
+                load_rack(4)
             diff = place("diff%d" % s, [P, S], F32, at)
-            pieces = HALVES if s == SLOTS - 2 else 1
-            for u in range(pieces):
-                cols = cols_of(u, S // pieces)
-                difference(nc.gpsimd, diff[:, cols], s, cols)
-                nc.scalar.activation(squares[0][:, cols], diff[:, cols], ACT.Square)
+            difference(nc.gpsimd, diff[:], s, slice(0, S))
+            nc.scalar.activation(squares[0][:], diff[:], ACT.Square)
             for c in range(2):
                 exp_to_z(s, c, square_of(s, c))
 
-        def join(c):
-            joined[1, c] = place("joined1_%d" % c, [P, BANK * PACK], BF16, JOINED1_AT + 4 * KB * c)
-            nc.vector.tensor_copy(
-                joined[1, c][:].bitcast(I32).rearrange("p (m h) -> p m h", h=2),
-                pairs[c][:].rearrange("p h m e -> p (h m e)").bitcast(I32).rearrange("p (h m) -> p m h", h=2),
+        def slot_fine(engine, s, at):
+            diff = place("diff%d" % s, [P, S], F32, at)
+            for c in range(2):
+                difference(engine, diff[:, cols_of(c, BANK)], s, cols_of(c, BANK))
+            turned_sums(s)
+            nc.scalar.activation(square_of(s, 0), diff[:, 0:BANK], ACT.Square)
+            square_turned(s, 0)
+            exp_to_z(s, 0, square_of(s, 0))
+            nc.scalar.activation(square_of(s, 1), diff[:, BANK:S], ACT.Square)
+            square_turned(s, 1)
+            if s < SLOTS - 1:
+                exp_turned(s, 0)
+            exp_to_z(s, 1, square_of(s, 1))
+            if s < SLOTS - 1:
+                exp_turned(s, 1)
+
+        def slot_to_z(s, at):
+            if s < FINE_FROM:
+                slot_coarse(s, at)
+            else:
+                slot_fine(nc.gpsimd, s, at)
+
+        def join(copy, dtype, b, c, at):
+            joined[b, c] = place("joined%d_%d" % (b, c), [P, BANK * PACK], BF16, at)
+            copy(
+                joined[b, c][:].bitcast(dtype).rearrange("p (m h) -> p m h", h=2),
+                pairs[b, c][:].rearrange("p h m e -> p (h m e)").bitcast(dtype).rearrange("p (h m) -> p m h", h=2),
             )
 
         def interleave(target, source):
@@ -326,12 +353,8 @@ def tile_list_pallet_slot_fit_kernel(tc, tab_words, tab_scales, offs, w4_words, 
             scatter(s, HALVES if s == 0 else 1)
             if 1 <= s <= 3:
                 load_rack(s + 4)
-            turned_chunks(s)
-            if s == 0:
-                h_slot(last)
-                load_rack(4)
             if s < PACK:
-                first_half_on_gpsimd(s, H_AT[AHEAD - 1] if s == 0 else H_AT[s + AHEAD])
+                slot_to_z(s, H_AT[AHEAD - 1] if s == 0 else H_AT[s + AHEAD])
                 nxt = AHEAD if s == 0 else s + AHEAD + 1
                 weighted[nxt] = racks[s][:, 0:S]
                 weigh(nxt)
@@ -339,21 +362,17 @@ def tile_list_pallet_slot_fit_kernel(tc, tab_words, tab_scales, offs, w4_words, 
                     weighted[nxt + 1] = place("weighted%d" % (nxt + 1), [P, S], F32, H_AT[nxt])[:]
                     weigh(nxt + 1)
             elif s == PACK:
-                first_half_on_gpsimd(s, H_AT[last])
-                interleave_chunk(2, RACK_AT[s])
-                interleave_chunk(3, RACK_AT[s] + 4 * KB)
+                slot_to_z(s, H_AT[last])
             else:
-                first_half_on_gpsimd(s, SLOTWISE_AT + 4 * KB * (3, 0)[s - PACK - 1])
-                interleave_chunk(s - PACK - 1, RACK_AT[s])
+                slot_to_z(s, SLOTWISE_AT + 4 * KB * TURNED[s - PACK - 1])
+            if s == last - 1:
+                for c in range(2):
+                    join(nc.gpsimd.tensor_copy, U32, 0, c, RACK_AT[s] + 4 * KB * c)
+            if s in (PACK, PACK + 1):
+                interleave_chunk(TURNED[s - PACK], RACK_AT[s])
 
         scatter(last, 1)
-        last_diff = place("last_diff", [P, S], F32, H_AT[2])
-        for c in range(2):
-            diff = last_diff[:, cols_of(c, BANK)]
-            difference(nc.vector, diff, last, cols_of(c, BANK))
-            nc.scalar.activation(square_of(last, c), diff, ACT.Square)
-            exp_to_z(last, c, square_of(last, c))
-        turned_squares(last)
+        slot_fine(nc.vector, last, 213 * KB)
         sums, backs = turn_banks[last]
         others = [banks[j] for j in (0, 1, 4, 5)]
         out_banks = others + list(sums) + [backs[0], others[0], others[1], backs[1], others[2], others[3]]
@@ -372,7 +391,7 @@ def tile_list_pallet_slot_fit_kernel(tc, tab_words, tab_scales, offs, w4_words, 
         def store_chunk(c):
             for t in range(NT):
                 bank = out_banks[c * NT + t]
-                res = stage.tile([P, BANK], F32, name="res")
+                res = place("res%d" % (c * NT + t), [P, BANK], F32, RESULT_AT + 2 * KB * (c * NT + t))
                 if c * NT + t in VECTOR_COPIES:
                     nc.vector.tensor_copy(res[:], bank[:])
                 else:
@@ -380,11 +399,11 @@ def tile_list_pallet_slot_fit_kernel(tc, tab_words, tab_scales, offs, w4_words, 
                 nc.sync.dma_start(out[cols_of(t, P), cols_of(c, BANK)], res[:])
 
         for c in range(CHUNKS):
-            if c < 2:
+            if c < 1:
                 quantise(0, c, RACK_AT[last] + 4 * KB * c, RACK_AT[last] + 4 * KB * c + 2 * KB)
             else:
-                quantise(0, c, PAIRS_AT + 4 * KB * (c - 2), PAIRS_AT + 4 * KB * (c - 2) + 2 * KB)
-            join(c)
+                quantise(0, c, PAIRS_AT + 4 * KB * (c - 1), PAIRS_AT + 4 * KB * (c - 1) + 2 * KB)
+            join(nc.vector.tensor_copy, I32, 1, c, JOINED1_AT + 4 * KB * c)
             quantise(1, c, Z1_CODES_AT + 2 * KB * c, Z1_SCALES_AT + BANK * c)
             for b in range(RB):
                 for t in range(NT):
@@ -392,5 +411,5 @@ def tile_list_pallet_slot_fit_kernel(tc, tab_words, tab_scales, offs, w4_words, 
             if c > 0:
                 store_chunk(c - 1)
             if c < 2:
-                exp_to_z(last, TURNED[c], backs[c][:])
+                exp_turned(last, c)
         store_chunk(CHUNKS - 1)

@@ -365,9 +365,9 @@ def tile_list_pallet_slot_fit_kernel(tc, tab_words, tab_scales, offs, w4_words, 
                 slot_to_z(s, H_AT[last])
             else:
                 slot_to_z(s, SLOTWISE_AT + 4 * KB * TURNED[s - PACK - 1])
-            if s == last - 1:
+            if s == PACK - 1:
                 for c in range(2):
-                    join(nc.gpsimd.tensor_copy, U32, 0, c, RACK_AT[s] + 4 * KB * c)
+                    join(nc.scalar.copy, U32, 0, c, PICKED_AT[2] + 4 * KB * c)
             if s in (PACK, PACK + 1):
                 interleave_chunk(TURNED[s - PACK], RACK_AT[s])
 

@@ -37,12 +37,11 @@ KB = 1024
 W4_SCALES_AT = 7 * KB + 512
 PICKED_AT = (16 * KB, 8 * KB, 12 * KB)
 TAB_AT = (200 * KB, 27 * KB + 512, 201 * KB)
-W2_CODES_AT = TAB_AT[2]
 PAGE_AT = (0, TAB_AT[1], TAB_AT[2] + 4 * KB)
 TAB_PLANE_AT = TAB_AT[0]
 W2_RAW_AT = 36 * KB
-W4_RAW_REST_AT = W2_RAW_AT - 512
-W4_RAW_FIRST_AT = TAB_AT[1]
+W4_RAW_REST_AT = TAB_AT[1]
+W4_RAW_FIRST_AT = W2_RAW_AT
 W4_ORD_AT = 57 * KB
 SQUARE_AT = (PICKED_AT[1], 196 * KB)
 RESULT_AT = 71 * KB
@@ -53,8 +52,6 @@ WEIGHTED_AT = 95 * KB
 W2_BF_AT = 20 * KB
 TAB_SCALES_AT = 112 * KB
 W4_PLANE_AT = TAB_SCALES_AT
-GAIN_AT = W4_RAW_REST_AT
-SHARP_AT = GAIN_AT + 64
 WGS_AT = TAB_SCALES_AT + KB
 SLOTWISE_AT = 122 * KB
 PAIRS_AT = 138 * KB
@@ -62,6 +59,7 @@ JOINED1_AT = 154 * KB
 Z1_CODES_AT = 170 * KB
 Z1_SCALES_AT = 178 * KB
 RACK_AT = (W2_RAW_AT, H0_AT, H1_AT, W2_RAW_AT + 8 * KB, W4_ORD_AT, WEIGHTED_AT, WEIGHTED_AT + 8 * KB, W2_RAW_AT)
+W2_CODES_AT = RACK_AT[3]
 FINE_FROM = 5
 TURNED = (2, 3)
 
@@ -106,6 +104,10 @@ def tile_list_pallet_slot_fit_kernel(tc, tab_words, tab_scales, offs, w4_words, 
             nc.scalar.dma_start(tab_scales_raw[32 * q : 32 * q + 4 * KA, :].bitcast(I32), tab_scales[:, 4 * q : 4 * q + 4, :].bitcast(I32))
         for q in range(QUADRANTS):
             nc.gpsimd.dma_start(w4_scales_raw[32 * q : 32 * q + 4 * KA, :].bitcast(I32), w4_scales[:, 4 * q : 4 * q + 4, :].bitcast(I32))
+        gain_t = keep.tile([P, RB, PACK], F32, name="gain_t")
+        sharp_t = keep.tile([P, RB, PACK], F32, name="sharp_t")
+        nc.gpsimd.dma_start(gain_t[:], gain.rearrange("(b p i) -> p b i", b=RB, i=PACK))
+        nc.gpsimd.dma_start(sharp_t[:], sharp.rearrange("(b p i) -> p b i", b=RB, i=PACK))
         w4_shifted = keep.tile([P, KA - 1, H], U8, name="w4_shifted", align_bytes=64)
         tab_shifted = keep.tile([P, KA - 1, S], U8, name="tab_shifted", align_bytes=64)
         nc.gpsimd.memset(w4_shifted[:].rearrange("p a n -> p (a n)").bitcast(I32), 0)
@@ -117,13 +119,9 @@ def tile_list_pallet_slot_fit_kernel(tc, tab_words, tab_scales, offs, w4_words, 
                 w4_ord[a][:].bitcast(U16).rearrange("p (b i m) -> p b i m", b=RB, i=PACK),
                 w4_raw[a].bitcast(U16).rearrange("p (b m i) -> p b i m", b=RB, i=PACK),
             )
-        load_table(1)
-        gain_t = place("gain_t", [P, RB, PACK], F32, GAIN_AT)
-        sharp_t = place("sharp_t", [P, RB, PACK], F32, SHARP_AT)
-        nc.sync.dma_start(gain_t[:], gain.rearrange("(b p i) -> p b i", b=RB, i=PACK))
-        nc.sync.dma_start(sharp_t[:], sharp.rearrange("(b p i) -> p b i", b=RB, i=PACK))
         w2_raw = place("w2_raw", [P, RB, PACK, N], F32, W2_RAW_AT)
         nc.sync.dma_start(w2_raw[:].rearrange("p b i n -> p b (i n)"), w2.rearrange("(b p i) n -> p b (i n)", b=RB, i=PACK))
+        load_table(1)
         picked = {}
 
         def gather_words(a, pieces):
@@ -171,11 +169,6 @@ def tile_list_pallet_slot_fit_kernel(tc, tab_words, tab_scales, offs, w4_words, 
                     w2_bf[:, cols_of(b * NT + t, P * PACK)].rearrange("p (n i) -> p n i", i=PACK),
                     w2_raw[:, b, :, cols_of(t, P)].rearrange("p i n -> p n i"),
                 )
-
-        w2_codes = place("w2_codes", [P, RB * N], U32, W2_CODES_AT)
-        w2_scales = place("w2_scales", [P, RB * N], U8, W2_CODES_AT + 3 * KB)
-        for lo, hi in ((0, 512), (512, RB * N)):
-            nc.vector.quantize_mx(out=w2_codes[:, lo:hi].bitcast(FP8X4), scales=w2_scales[:, lo:hi], in_=w2_bf[:, PACK * lo : PACK * hi])
 
         rack_rows = rack.rearrange("(b p i) m -> b i p m", b=RB, i=PACK)
         racks = {}
@@ -373,6 +366,11 @@ def tile_list_pallet_slot_fit_kernel(tc, tab_words, tab_scales, offs, w4_words, 
 
         scatter(last, 1)
         slot_fine(nc.vector, last, 213 * KB)
+        w2_codes = place("w2_codes", [P, RB * N], U32, W2_CODES_AT)
+        w2_scales = place("w2_scales", [P, RB * N], U8, W2_CODES_AT + 3 * KB)
+        for lo, hi in ((0, 512), (512, RB * N)):
+            nc.vector.quantize_mx(out=w2_codes[:, lo:hi].bitcast(FP8X4), scales=w2_scales[:, lo:hi], in_=w2_bf[:, PACK * lo : PACK * hi])
+
         sums, backs = turn_banks[last]
         others = [banks[j] for j in (0, 1, 4, 5)]
         out_banks = others + list(sums) + [backs[0], others[0], others[1], backs[1], others[2], others[3]]

@@ -32,6 +32,7 @@ SHIFT_ROWS = 112
 PAGES = 3
 AHEAD = 3
 VECTOR_COPIES = (8, 9, 11)
+LINE = 4
 KB = 1024
 
 W4_SCALES_AT = 7 * KB + 512
@@ -166,8 +167,8 @@ def tile_list_pallet_slot_fit_kernel(tc, tab_words, tab_scales, offs, w4_words, 
         for b in range(RB):
             for t in range(NT):
                 nc.scalar.copy(
-                    w2_bf[:, cols_of(b * NT + t, P * PACK)].rearrange("p (n i) -> p n i", i=PACK),
-                    w2_raw[:, b, :, cols_of(t, P)].rearrange("p i n -> p n i"),
+                    w2_bf[:, cols_of(b * NT + t, P * PACK)].rearrange("p (n e i) -> p n i e", e=LINE, i=PACK),
+                    w2_raw[:, b, :, cols_of(t, P)].rearrange("p i (n e) -> p n i e", e=LINE),
                 )
 
         rack_rows = rack.rearrange("(b p i) m -> b i p m", b=RB, i=PACK)
@@ -320,8 +321,8 @@ def tile_list_pallet_slot_fit_kernel(tc, tab_words, tab_scales, offs, w4_words, 
         def join(copy, dtype, b, c, at):
             joined[b, c] = place("joined%d_%d" % (b, c), [P, BANK * PACK], BF16, at)
             copy(
-                joined[b, c][:].bitcast(dtype).rearrange("p (m h) -> p m h", h=2),
-                pairs[b, c][:].rearrange("p h m e -> p (h m e)").bitcast(dtype).rearrange("p (h m) -> p m h", h=2),
+                joined[b, c][:].bitcast(dtype).rearrange("p (m e h) -> p m h e", e=LINE, h=2),
+                pairs[b, c][:].rearrange("p h m e -> p (h m e)").bitcast(dtype).rearrange("p (h m e) -> p m h e", e=LINE, h=2),
             )
 
         def interleave(target, source):

@@ -36,30 +36,33 @@ LINE = 4
 KB = 1024
 
 W4_SCALES_AT = 7 * KB + 512
-PICKED_AT = (16 * KB, 8 * KB, 12 * KB)
-TAB_AT = (200 * KB, 27 * KB + 512, 201 * KB)
-PAGE_AT = (0, TAB_AT[1], TAB_AT[2] + 4 * KB)
-TAB_PLANE_AT = TAB_AT[0]
-W2_RAW_AT = 36 * KB
+PICKED_AT = (12 * KB, 113 * KB, 16 * KB)
+TAB_AT = (200 * KB, 28 * KB, 201 * KB + 512)
+PAGE_AT = (0, TAB_AT[1] - 4 * KB, TAB_AT[1] + 4 * KB)
+WGS_AT = TAB_AT[0] - 3 * KB - 512
+TAB_PLANE_AT = TAB_AT[0] + 512
+W2_RAW_AT = (40 * KB, TAB_AT[2])
+JOINED0_AT = W2_RAW_AT[0]
 W4_RAW_REST_AT = TAB_AT[1]
-W4_RAW_FIRST_AT = W2_RAW_AT
+W4_RAW_FIRST_AT = W2_RAW_AT[0]
+LN_GAIN_AT = 8 * KB
 W4_ORD_AT = 57 * KB
-SQUARE_AT = (PICKED_AT[1], 196 * KB)
+SQUARE_AT = (PICKED_AT[1], 48 * KB)
 RESULT_AT = 71 * KB
 H0_AT = 180 * KB
 H_AT = {s: (63 + 4 * s) * KB for s in range(2, SLOTS)}
 H1_AT = 188 * KB
-WEIGHTED_AT = 95 * KB
-W2_BF_AT = 20 * KB
+WEIGHTED_AT = (222 * KB, 95 * KB, 99 * KB)
+W2_BF_AT = 216 * KB
 TAB_SCALES_AT = 112 * KB
-W4_PLANE_AT = TAB_SCALES_AT
-WGS_AT = TAB_SCALES_AT + KB
+W4_PLANE_AT = 52 * KB
+LAST_DIFF_AT = 117 * KB
 SLOTWISE_AT = 122 * KB
 PAIRS_AT = 138 * KB
 JOINED1_AT = 154 * KB
 Z1_CODES_AT = 170 * KB
 Z1_SCALES_AT = 178 * KB
-RACK_AT = (W2_RAW_AT, H0_AT, H1_AT, W2_RAW_AT + 8 * KB, W4_ORD_AT, WEIGHTED_AT, WEIGHTED_AT + 8 * KB, W2_RAW_AT)
+RACK_AT = (TAB_AT[2] + 6 * KB, H0_AT, H1_AT, WEIGHTED_AT[0], PICKED_AT[0], WEIGHTED_AT[1], W4_ORD_AT, H0_AT)
 W2_CODES_AT = RACK_AT[3]
 FINE_FROM = 5
 TURNED = (2, 3)
@@ -120,8 +123,14 @@ def tile_list_pallet_slot_fit_kernel(tc, tab_words, tab_scales, offs, w4_words, 
                 w4_ord[a][:].bitcast(U16).rearrange("p (b i m) -> p b i m", b=RB, i=PACK),
                 w4_raw[a].bitcast(U16).rearrange("p (b m i) -> p b i m", b=RB, i=PACK),
             )
-        w2_raw = place("w2_raw", [P, RB, PACK, N], F32, W2_RAW_AT)
-        nc.sync.dma_start(w2_raw[:].rearrange("p b i n -> p b (i n)"), w2.rearrange("(b p i) n -> p b (i n)", b=RB, i=PACK))
+        w2_rows = w2.rearrange("(b p i) n -> b p (i n)", b=RB, i=PACK)
+        w2_raw = {}
+
+        def load_w2(b):
+            w2_raw[b] = place("w2_raw%d" % b, [P, PACK, N], F32, W2_RAW_AT[b])
+            nc.sync.dma_start(w2_raw[b][:].rearrange("p i n -> p (i n)"), w2_rows[b])
+
+        load_w2(0)
         load_table(1)
         picked = {}
 
@@ -131,29 +140,29 @@ def tile_list_pallet_slot_fit_kernel(tc, tab_words, tab_scales, offs, w4_words, 
             for u in range(pieces):
                 nc.vector.tensor_copy(picked[a][:, cols_of(u, width)], tab_win[a][:].bitcast(U32).indirect(offs_t[:, cols_of(u, width // 16)]))
 
-        def shift_scale_rows(shifted, source):
+        def shift_scale_rows(queue, shifted, source):
             for a in range(1, KA):
-                nc.sync.dma_start(shifted[0:SHIFT_ROWS, a - 1, :].bitcast(I32), source[4 * a : 4 * a + SHIFT_ROWS, :].bitcast(I32))
+                queue.dma_start(shifted[0:SHIFT_ROWS, a - 1, :].bitcast(I32), source[4 * a : 4 * a + SHIFT_ROWS, :].bitcast(I32))
             return [source[:]] + [shifted[:, a, :] for a in range(KA - 1)]
 
-        gather_words(0, 1)
-        load_table(2)
-        tab_plane0 = place("tab_plane0", [P, S], U8, TAB_PLANE_AT)
-        nc.vector.tensor_copy(tab_plane0[:], tab_scales_raw[:].indirect(offs_t[:]))
-        tab_planes = shift_scale_rows(tab_shifted, tab_plane0)
         w4_plane0 = place("w4_plane0", [P, H], U8, W4_PLANE_AT)
-        nc.vector.tensor_copy(
+        nc.gpsimd.tensor_copy(
             w4_plane0[:].rearrange("p (b i m) -> p b i m", b=RB, i=PACK),
             w4_scales_raw[:].rearrange("p (b m i) -> p b i m", b=RB, i=PACK),
         )
-        w4_planes = shift_scale_rows(w4_shifted, w4_plane0)
+        w4_planes = shift_scale_rows(nc.scalar, w4_shifted, w4_plane0)
+        gather_words(0, 1)
+        load_table(2)
         wgs_t = place("wgs_t", [P, S], F32, WGS_AT)
         nc.sync.dma_start(wgs_t[:], wgs)
+        tab_plane0 = place("tab_plane0", [P, S], U8, TAB_PLANE_AT)
+        nc.vector.tensor_copy(tab_plane0[:], tab_scales_raw[:].indirect(offs_t[:]))
+        tab_planes = shift_scale_rows(nc.sync, tab_shifted, tab_plane0)
         gather_words(1, 1)
         gather_words(2, HALVES)
 
-        neg_sharp = keep.tile([P, SLOTS], F32, name="neg_sharp")
-        ln_gain = keep.tile([P, SLOTS], F32, name="ln_gain")
+        neg_sharp = place("neg_sharp", [P, SLOTS], F32, LN_GAIN_AT + 64)
+        ln_gain = place("ln_gain", [P, SLOTS], F32, LN_GAIN_AT)
         nc.scalar.activation(ln_gain[:], gain_t[:].rearrange("p b i -> p (b i)"), ACT.Ln)
         nc.scalar.mul(neg_sharp[:], sharp_t[:].rearrange("p b i -> p (b i)"), -1.0)
 
@@ -163,13 +172,17 @@ def tile_list_pallet_slot_fit_kernel(tc, tab_words, tab_scales, offs, w4_words, 
 
         identity = keep.tile([P, P], F32, name="identity", align_bytes=64)
         make_identity(nc, identity[:])
-        w2_bf = place("w2_bf", [P, RB * N * PACK], BF16, W2_BF_AT)
-        for b in range(RB):
+        w2_bf = {}
+
+        def round_w2(copy, b, at):
+            w2_bf[b] = place("w2_bf%d" % b, [P, N * PACK], BF16, at)
             for t in range(NT):
-                nc.scalar.copy(
-                    w2_bf[:, cols_of(b * NT + t, P * PACK)].rearrange("p (n e i) -> p n i e", e=LINE, i=PACK),
-                    w2_raw[:, b, :, cols_of(t, P)].rearrange("p i (n e) -> p n i e", e=LINE),
+                copy(
+                    w2_bf[b][:, cols_of(t, P * PACK)].rearrange("p (n i) -> p n i", i=PACK),
+                    w2_raw[b][:, :, cols_of(t, P)].rearrange("p i n -> p n i"),
                 )
+
+        round_w2(nc.scalar.copy, 0, W2_BF_AT)
 
         rack_rows = rack.rearrange("(b p i) m -> b i p m", b=RB, i=PACK)
         racks = {}
@@ -179,10 +192,11 @@ def tile_list_pallet_slot_fit_kernel(tc, tab_words, tab_scales, offs, w4_words, 
             nc.sync.dma_start(racks[s][:], rack_rows[s // PACK, s % PACK])
 
         load_rack(0)
+        load_w2(1)
 
         h = {s: place("h%d" % s, [P, S], F32, H_AT.get(s, H1_AT))[:] for s in range(1, SLOTS)}
         h0_late = place("h0_late", [P, BANK], F32, H0_AT)
-        weighted = {s: place("weighted%d" % s, [P, S], F32, WEIGHTED_AT + 4 * KB * s)[:] for s in range(AHEAD)}
+        weighted = {s: place("weighted%d" % s, [P, S], F32, WEIGHTED_AT[s])[:] for s in range(AHEAD)}
 
         def h_half(s, u):
             return h0_late[:] if s == 0 else h[s][:, cols_of(u, BANK)]
@@ -290,6 +304,7 @@ def tile_list_pallet_slot_fit_kernel(tc, tab_words, tab_scales, offs, w4_words, 
             if s == 0:
                 h_slot(SLOTS - 1)
                 load_rack(4)
+                load_rack(6)
             diff = place("diff%d" % s, [P, S], F32, at)
             difference(nc.gpsimd, diff[:], s, slice(0, S))
             nc.scalar.activation(squares[0][:], diff[:], ACT.Square)
@@ -340,13 +355,13 @@ def tile_list_pallet_slot_fit_kernel(tc, tab_words, tab_scales, offs, w4_words, 
         nc.gpsimd.tensor_tensor(weighted[0][:, BANK:S], h0_late[:], wgs_t[:, BANK:S], ALU.mult)
         for s in range(1, AHEAD):
             weigh(s)
-        for s in (1, 2, 3):
+        for s in (1, 2):
             load_rack(s)
         last = SLOTS - 1
         for s in range(last):
             scatter(s, HALVES if s == 0 else 1)
-            if 1 <= s <= 3:
-                load_rack(s + 4)
+            if s in (0, 2, 5):
+                load_rack({0: 3, 2: 5, 5: 7}[s])
             if s < PACK:
                 slot_to_z(s, H_AT[AHEAD - 1] if s == 0 else H_AT[s + AHEAD])
                 nxt = AHEAD if s == 0 else s + AHEAD + 1
@@ -361,16 +376,17 @@ def tile_list_pallet_slot_fit_kernel(tc, tab_words, tab_scales, offs, w4_words, 
                 slot_to_z(s, SLOTWISE_AT + 4 * KB * TURNED[s - PACK - 1])
             if s == PACK - 1:
                 for c in range(2):
-                    join(nc.scalar.copy, U32, 0, c, PICKED_AT[2] + 4 * KB * c)
+                    join(nc.scalar.copy, U32, 0, c, JOINED0_AT + 4 * KB * c)
             if s in (PACK, PACK + 1):
                 interleave_chunk(TURNED[s - PACK], RACK_AT[s])
 
+        round_w2(nc.gpsimd.tensor_copy, 1, RACK_AT[last - 1])
         scatter(last, 1)
-        slot_fine(nc.vector, last, 213 * KB)
+        slot_fine(nc.vector, last, LAST_DIFF_AT)
         w2_codes = place("w2_codes", [P, RB * N], U32, W2_CODES_AT)
         w2_scales = place("w2_scales", [P, RB * N], U8, W2_CODES_AT + 3 * KB)
-        for lo, hi in ((0, 512), (512, RB * N)):
-            nc.vector.quantize_mx(out=w2_codes[:, lo:hi].bitcast(FP8X4), scales=w2_scales[:, lo:hi], in_=w2_bf[:, PACK * lo : PACK * hi])
+        for b in range(RB):
+            nc.vector.quantize_mx(out=w2_codes[:, cols_of(b, N)].bitcast(FP8X4), scales=w2_scales[:, cols_of(b, N)], in_=w2_bf[b][:])
 
         sums, backs = turn_banks[last]
         others = [banks[j] for j in (0, 1, 4, 5)]

@@ -37,15 +37,14 @@ KB = 1024
 
 W4_SCALES_AT = 7 * KB + 512
 PICKED_AT = (12 * KB, 113 * KB, 16 * KB)
-TAB_AT = (200 * KB, 28 * KB, 201 * KB + 512)
+TAB_AT = (200 * KB, 28 * KB, 208 * KB)
 PAGE_AT = (0, TAB_AT[1] - 4 * KB, TAB_AT[1] + 4 * KB)
 WGS_AT = TAB_AT[0] - 3 * KB - 512
 TAB_PLANE_AT = TAB_AT[0] + 512
-W2_RAW_AT = (40 * KB, TAB_AT[2])
-JOINED0_AT = W2_RAW_AT[0]
-W4_RAW_REST_AT = TAB_AT[1]
-W4_RAW_FIRST_AT = W2_RAW_AT[0]
-LN_GAIN_AT = 8 * KB
+W2_RAW_AT = (106 * KB + 512, TAB_AT[2])
+JOINED0_AT = 40 * KB
+W4_RAW_REST_AT = TAB_AT[2]
+W4_RAW_FIRST_AT = TAB_AT[1]
 W4_ORD_AT = 57 * KB
 SQUARE_AT = (PICKED_AT[1], 48 * KB)
 RESULT_AT = 71 * KB
@@ -53,7 +52,7 @@ H0_AT = 180 * KB
 H_AT = {s: (63 + 4 * s) * KB for s in range(2, SLOTS)}
 H1_AT = 188 * KB
 WEIGHTED_AT = (222 * KB, 95 * KB, 99 * KB)
-W2_BF_AT = 216 * KB
+W2_BF_AT = TAB_AT[0] + 2 * KB
 TAB_SCALES_AT = 112 * KB
 W4_PLANE_AT = 52 * KB
 LAST_DIFF_AT = 117 * KB
@@ -89,7 +88,7 @@ def tile_list_pallet_slot_fit_kernel(tc, tab_words, tab_scales, offs, w4_words, 
         tab_scales_raw = place("tab_scales_raw", [P, T], U8, TAB_SCALES_AT)
         w4_scales_raw = place("w4_scales_raw", [P, H], U8, W4_SCALES_AT)
         nc.gpsimd.memset(tab_scales_raw[:].bitcast(I32), 0)
-        nc.vector.memset(w4_scales_raw[:].bitcast(I32), 0)
+        nc.gpsimd.memset(w4_scales_raw[:].bitcast(I32), 0)
         w4_first = place("w4_first", [P, 2 * H], U8, W4_RAW_FIRST_AT)
         w4_rest = place("w4_rest", [P, KA - 1, 2 * H], U8, W4_RAW_REST_AT)
         w4_raw = [w4_first[:]] + [w4_rest[:, a, :] for a in range(KA - 1)]
@@ -103,15 +102,17 @@ def tile_list_pallet_slot_fit_kernel(tc, tab_words, tab_scales, offs, w4_words, 
         nc.sync.dma_start(w4_rest[:].bitcast(I32), w4_words[1:KA].rearrange("a p n -> p a n").bitcast(I32))
         nc.sync.dma_start(offs_t[:], offs)
         load_table(0)
-        nc.sync.dma_start(offs2_t[:], offs2)
         for q in range(QUADRANTS):
             nc.scalar.dma_start(tab_scales_raw[32 * q : 32 * q + 4 * KA, :].bitcast(I32), tab_scales[:, 4 * q : 4 * q + 4, :].bitcast(I32))
         for q in range(QUADRANTS):
-            nc.gpsimd.dma_start(w4_scales_raw[32 * q : 32 * q + 4 * KA, :].bitcast(I32), w4_scales[:, 4 * q : 4 * q + 4, :].bitcast(I32))
+            queue = nc.gpsimd if q < QUADRANTS // 2 else nc.scalar
+            queue.dma_start(w4_scales_raw[32 * q : 32 * q + 4 * KA, :].bitcast(I32), w4_scales[:, 4 * q : 4 * q + 4, :].bitcast(I32))
         gain_t = keep.tile([P, RB, PACK], F32, name="gain_t")
         sharp_t = keep.tile([P, RB, PACK], F32, name="sharp_t")
         nc.gpsimd.dma_start(gain_t[:], gain.rearrange("(b p i) -> p b i", b=RB, i=PACK))
         nc.gpsimd.dma_start(sharp_t[:], sharp.rearrange("(b p i) -> p b i", b=RB, i=PACK))
+        identity = keep.tile([P, P], F32, name="identity", align_bytes=64)
+        make_identity(nc, identity[:])
         w4_shifted = keep.tile([P, KA - 1, H], U8, name="w4_shifted", align_bytes=64)
         tab_shifted = keep.tile([P, KA - 1, S], U8, name="tab_shifted", align_bytes=64)
         nc.gpsimd.memset(w4_shifted[:].rearrange("p a n -> p (a n)").bitcast(I32), 0)
@@ -130,8 +131,8 @@ def tile_list_pallet_slot_fit_kernel(tc, tab_words, tab_scales, offs, w4_words, 
             w2_raw[b] = place("w2_raw%d" % b, [P, PACK, N], F32, W2_RAW_AT[b])
             nc.sync.dma_start(w2_raw[b][:].rearrange("p i n -> p (i n)"), w2_rows[b])
 
-        load_w2(0)
         load_table(1)
+        load_table(2)
         picked = {}
 
         def gather_words(a, pieces):
@@ -152,17 +153,18 @@ def tile_list_pallet_slot_fit_kernel(tc, tab_words, tab_scales, offs, w4_words, 
         )
         w4_planes = shift_scale_rows(nc.scalar, w4_shifted, w4_plane0)
         gather_words(0, 1)
-        load_table(2)
         wgs_t = place("wgs_t", [P, S], F32, WGS_AT)
         nc.sync.dma_start(wgs_t[:], wgs)
+        nc.sync.dma_start(offs2_t[:], offs2)
         tab_plane0 = place("tab_plane0", [P, S], U8, TAB_PLANE_AT)
         nc.vector.tensor_copy(tab_plane0[:], tab_scales_raw[:].indirect(offs_t[:]))
         tab_planes = shift_scale_rows(nc.sync, tab_shifted, tab_plane0)
+        load_w2(0)
         gather_words(1, 1)
         gather_words(2, HALVES)
 
-        neg_sharp = place("neg_sharp", [P, SLOTS], F32, LN_GAIN_AT + 64)
-        ln_gain = place("ln_gain", [P, SLOTS], F32, LN_GAIN_AT)
+        neg_sharp = keep.tile([P, SLOTS], F32, name="neg_sharp")
+        ln_gain = keep.tile([P, SLOTS], F32, name="ln_gain")
         nc.scalar.activation(ln_gain[:], gain_t[:].rearrange("p b i -> p (b i)"), ACT.Ln)
         nc.scalar.mul(neg_sharp[:], sharp_t[:].rearrange("p b i -> p (b i)"), -1.0)
 
@@ -170,8 +172,6 @@ def tile_list_pallet_slot_fit_kernel(tc, tab_words, tab_scales, offs, w4_words, 
         for page in pages:
             nc.gpsimd.memset(page[:], 0.0)
 
-        identity = keep.tile([P, P], F32, name="identity", align_bytes=64)
-        make_identity(nc, identity[:])
         w2_bf = {}
 
         def round_w2(copy, b, at):

@@ -36,23 +36,22 @@ LINE = 4
 KB = 1024
 
 W4_SCALES_AT = 7 * KB + 512
-PICKED_AT = (12 * KB, 113 * KB, 16 * KB)
+PICKED_AT = (20 * KB, 113 * KB, 16 * KB)
 TAB_AT = (200 * KB, 28 * KB, 208 * KB)
-PAGE_AT = (0, TAB_AT[1] - 4 * KB, TAB_AT[1] + 4 * KB)
+PAGE_AT = (0, 8 * KB, TAB_AT[1])
 WGS_AT = TAB_AT[0] - 3 * KB - 512
 TAB_PLANE_AT = TAB_AT[0] + 512
-W2_RAW_AT = (106 * KB + 512, TAB_AT[2])
-JOINED0_AT = 40 * KB
+W2_RAW_AT = TAB_AT[2] + 2 * KB
+JOINED0_AT = TAB_AT[2] + 14 * KB
 W4_RAW_REST_AT = TAB_AT[2]
 W4_RAW_FIRST_AT = TAB_AT[1]
 W4_ORD_AT = 57 * KB
 SQUARE_AT = (PICKED_AT[1], 48 * KB)
 RESULT_AT = 71 * KB
 H0_AT = 180 * KB
-H_AT = {s: (63 + 4 * s) * KB for s in range(2, SLOTS)}
+H_AT = {2: 71 * KB, 3: 75 * KB, 4: 79 * KB, 5: 83 * KB, 6: 88 * KB, 7: 93 * KB}
 H1_AT = 188 * KB
-WEIGHTED_AT = (222 * KB, 95 * KB, 99 * KB)
-W2_BF_AT = TAB_AT[0] + 2 * KB
+WEIGHTED_AT = (40 * KB, 98 * KB, 102 * KB)
 TAB_SCALES_AT = 112 * KB
 W4_PLANE_AT = 52 * KB
 LAST_DIFF_AT = 117 * KB
@@ -61,8 +60,8 @@ PAIRS_AT = 138 * KB
 JOINED1_AT = 154 * KB
 Z1_CODES_AT = 170 * KB
 Z1_SCALES_AT = 178 * KB
-RACK_AT = (TAB_AT[2] + 6 * KB, H0_AT, H1_AT, WEIGHTED_AT[0], PICKED_AT[0], WEIGHTED_AT[1], W4_ORD_AT, H0_AT)
-W2_CODES_AT = RACK_AT[3]
+RACK_AT = (TAB_AT[2] - 6 * KB, H0_AT, H1_AT, WEIGHTED_AT[0], PICKED_AT[2], WEIGHTED_AT[1], W4_ORD_AT, H0_AT)
+W2_CODES_AT = SLOTWISE_AT + 4 * KB * 3
 FINE_FROM = 5
 TURNED = (2, 3)
 
@@ -102,6 +101,7 @@ def tile_list_pallet_slot_fit_kernel(tc, tab_words, tab_scales, offs, w4_words, 
         nc.sync.dma_start(w4_rest[:].bitcast(I32), w4_words[1:KA].rearrange("a p n -> p a n").bitcast(I32))
         nc.sync.dma_start(offs_t[:], offs)
         load_table(0)
+        nc.sync.dma_start(offs2_t[:], offs2)
         for q in range(QUADRANTS):
             nc.scalar.dma_start(tab_scales_raw[32 * q : 32 * q + 4 * KA, :].bitcast(I32), tab_scales[:, 4 * q : 4 * q + 4, :].bitcast(I32))
         for q in range(QUADRANTS):
@@ -124,13 +124,6 @@ def tile_list_pallet_slot_fit_kernel(tc, tab_words, tab_scales, offs, w4_words, 
                 w4_ord[a][:].bitcast(U16).rearrange("p (b i m) -> p b i m", b=RB, i=PACK),
                 w4_raw[a].bitcast(U16).rearrange("p (b m i) -> p b i m", b=RB, i=PACK),
             )
-        w2_rows = w2.rearrange("(b p i) n -> b p (i n)", b=RB, i=PACK)
-        w2_raw = {}
-
-        def load_w2(b):
-            w2_raw[b] = place("w2_raw%d" % b, [P, PACK, N], F32, W2_RAW_AT[b])
-            nc.sync.dma_start(w2_raw[b][:].rearrange("p i n -> p (i n)"), w2_rows[b])
-
         load_table(1)
         load_table(2)
         picked = {}
@@ -141,8 +134,8 @@ def tile_list_pallet_slot_fit_kernel(tc, tab_words, tab_scales, offs, w4_words, 
             for u in range(pieces):
                 nc.vector.tensor_copy(picked[a][:, cols_of(u, width)], tab_win[a][:].bitcast(U32).indirect(offs_t[:, cols_of(u, width // 16)]))
 
-        def shift_scale_rows(queue, shifted, source):
-            for a in range(1, KA):
+        def shift_scale_rows(queues, shifted, source):
+            for a, queue in zip(range(1, KA), queues):
                 queue.dma_start(shifted[0:SHIFT_ROWS, a - 1, :].bitcast(I32), source[4 * a : 4 * a + SHIFT_ROWS, :].bitcast(I32))
             return [source[:]] + [shifted[:, a, :] for a in range(KA - 1)]
 
@@ -151,15 +144,13 @@ def tile_list_pallet_slot_fit_kernel(tc, tab_words, tab_scales, offs, w4_words, 
             w4_plane0[:].rearrange("p (b i m) -> p b i m", b=RB, i=PACK),
             w4_scales_raw[:].rearrange("p (b m i) -> p b i m", b=RB, i=PACK),
         )
-        w4_planes = shift_scale_rows(nc.scalar, w4_shifted, w4_plane0)
+        w4_planes = shift_scale_rows((nc.scalar, nc.scalar), w4_shifted, w4_plane0)
         gather_words(0, 1)
         wgs_t = place("wgs_t", [P, S], F32, WGS_AT)
         nc.sync.dma_start(wgs_t[:], wgs)
-        nc.sync.dma_start(offs2_t[:], offs2)
         tab_plane0 = place("tab_plane0", [P, S], U8, TAB_PLANE_AT)
         nc.vector.tensor_copy(tab_plane0[:], tab_scales_raw[:].indirect(offs_t[:]))
-        tab_planes = shift_scale_rows(nc.sync, tab_shifted, tab_plane0)
-        load_w2(0)
+        tab_planes = shift_scale_rows((nc.sync, nc.scalar), tab_shifted, tab_plane0)
         gather_words(1, 1)
         gather_words(2, HALVES)
 
@@ -174,15 +165,9 @@ def tile_list_pallet_slot_fit_kernel(tc, tab_words, tab_scales, offs, w4_words, 
 
         w2_bf = {}
 
-        def round_w2(copy, b, at):
-            w2_bf[b] = place("w2_bf%d" % b, [P, N * PACK], BF16, at)
-            for t in range(NT):
-                copy(
-                    w2_bf[b][:, cols_of(t, P * PACK)].rearrange("p (n i) -> p n i", i=PACK),
-                    w2_raw[b][:, :, cols_of(t, P)].rearrange("p i n -> p n i"),
-                )
-
-        round_w2(nc.scalar.copy, 0, W2_BF_AT)
+        def round_w2(b, t, at):
+            w2_bf[b, t] = place("w2_bf%d_%d" % (b, t), [P, P * PACK], BF16, at)
+            nc.gpsimd.tensor_copy(w2_bf[b, t][:].rearrange("p (n i) -> p n i", i=PACK), w2_raw[:, b, :, cols_of(t, P)].rearrange("p i n -> p n i"))
 
         rack_rows = rack.rearrange("(b p i) m -> b i p m", b=RB, i=PACK)
         racks = {}
@@ -192,9 +177,10 @@ def tile_list_pallet_slot_fit_kernel(tc, tab_words, tab_scales, offs, w4_words, 
             nc.sync.dma_start(racks[s][:], rack_rows[s // PACK, s % PACK])
 
         load_rack(0)
-        load_w2(1)
+        w2_raw = place("w2_raw", [P, RB, PACK, N], F32, W2_RAW_AT)
+        nc.sync.dma_start(w2_raw[:].rearrange("p b i n -> p b (i n)"), w2.rearrange("(b p i) n -> p b (i n)", b=RB, i=PACK))
 
-        h = {s: place("h%d" % s, [P, S], F32, H_AT.get(s, H1_AT))[:] for s in range(1, SLOTS)}
+        h = {s: place("h%d" % s, [P, S + (KB // 4 if s >= SLOTS - NT else 0)], F32, H_AT.get(s, H1_AT))[:, 0:S] for s in range(1, SLOTS)}
         h0_late = place("h0_late", [P, BANK], F32, H0_AT)
         weighted = {s: place("weighted%d" % s, [P, S], F32, WEIGHTED_AT[s])[:] for s in range(AHEAD)}
 
@@ -295,21 +281,32 @@ def tile_list_pallet_slot_fit_kernel(tc, tab_words, tab_scales, offs, w4_words, 
         def exp_turned(s, j):
             exp_to_z(s, TURNED[j], turn_banks[s][1][j][:])
 
-        def slot_coarse(s, at):
-            turned_sums(s)
+        def slot_first(at):
+            turned_sums(0)
             for j in range(2):
-                square_turned(s, j)
+                square_turned(0, j)
             for j in range(2):
-                exp_turned(s, j)
-            if s == 0:
-                h_slot(SLOTS - 1)
-                load_rack(4)
-                load_rack(6)
-            diff = place("diff%d" % s, [P, S], F32, at)
-            difference(nc.gpsimd, diff[:], s, slice(0, S))
+                exp_turned(0, j)
+            h_slot(SLOTS - 1)
+            load_rack(4)
+            load_rack(6)
+            diff = place("diff0", [P, S], F32, at)
+            difference(nc.gpsimd, diff[:], 0, slice(0, S))
             nc.scalar.activation(squares[0][:], diff[:], ACT.Square)
             for c in range(2):
+                exp_to_z(0, c, square_of(0, c))
+
+        def slot_coarse(s, at):
+            diff = place("diff%d" % s, [P, S], F32, at)
+            difference(nc.gpsimd, diff[:], s, slice(0, S))
+            turned_sums(s)
+            square_turned(s, 0)
+            nc.scalar.activation(squares[0][:], diff[:], ACT.Square)
+            square_turned(s, 1)
+            exp_turned(s, 0)
+            for c in range(2):
                 exp_to_z(s, c, square_of(s, c))
+            exp_turned(s, 1)
 
         def slot_fine(engine, s, at):
             diff = place("diff%d" % s, [P, S], F32, at)
@@ -328,7 +325,9 @@ def tile_list_pallet_slot_fit_kernel(tc, tab_words, tab_scales, offs, w4_words, 
                 exp_turned(s, 1)
 
         def slot_to_z(s, at):
-            if s < FINE_FROM:
+            if s == 0:
+                slot_first(at)
+            elif s < FINE_FROM:
                 slot_coarse(s, at)
             else:
                 slot_fine(nc.gpsimd, s, at)
@@ -367,6 +366,8 @@ def tile_list_pallet_slot_fit_kernel(tc, tab_words, tab_scales, offs, w4_words, 
                 nxt = AHEAD if s == 0 else s + AHEAD + 1
                 weighted[nxt] = racks[s][:, 0:S]
                 weigh(nxt)
+                if s > 0:
+                    round_w2(0, s - 1, H_AT[nxt] + 4 * KB)
                 if s == 0:
                     weighted[nxt + 1] = place("weighted%d" % (nxt + 1), [P, S], F32, H_AT[nxt])[:]
                     weigh(nxt + 1)
@@ -380,13 +381,15 @@ def tile_list_pallet_slot_fit_kernel(tc, tab_words, tab_scales, offs, w4_words, 
             if s in (PACK, PACK + 1):
                 interleave_chunk(TURNED[s - PACK], RACK_AT[s])
 
-        round_w2(nc.gpsimd.tensor_copy, 1, RACK_AT[last - 1])
+        for t in range(NT):
+            round_w2(1, t, RACK_AT[last - 1] + KB * t)
         scatter(last, 1)
         slot_fine(nc.vector, last, LAST_DIFF_AT)
         w2_codes = place("w2_codes", [P, RB * N], U32, W2_CODES_AT)
         w2_scales = place("w2_scales", [P, RB * N], U8, W2_CODES_AT + 3 * KB)
-        for b in range(RB):
-            nc.vector.quantize_mx(out=w2_codes[:, cols_of(b, N)].bitcast(FP8X4), scales=w2_scales[:, cols_of(b, N)], in_=w2_bf[b][:])
+        for (b, t), rounded in w2_bf.items():
+            cols = cols_of(b * NT + t, P)
+            nc.vector.quantize_mx(out=w2_codes[:, cols].bitcast(FP8X4), scales=w2_scales[:, cols], in_=rounded[:])
 
         sums, backs = turn_banks[last]
         others = [banks[j] for j in (0, 1, 4, 5)]

@@ -26,44 +26,46 @@ SLOTS = RB * PACK
 BANK = 512
 BANKS = 8
 CHUNKS = T2 // BANK
-HALVES = S // BANK
 NT = N // P
+QUARTER = S // 4
+HALF = P // 2
 SHIFT_ROWS = 112
-PAGES = 3
-AHEAD = 3
-VECTOR_COPIES = (8, 9, 11)
+PAGES = 2
+AHEAD = 4
 LINE = 4
 KB = 1024
-
-W4_SCALES_AT = 7 * KB + 512
-PICKED_AT = (20 * KB, 113 * KB, 16 * KB)
-TAB_AT = (200 * KB, 28 * KB, 208 * KB)
-PAGE_AT = (0, 8 * KB, TAB_AT[1])
-WGS_AT = TAB_AT[0] - 3 * KB - 512
-TAB_PLANE_AT = TAB_AT[0] + 512
-W2_RAW_AT = TAB_AT[2] + 2 * KB
-JOINED0_AT = TAB_AT[2] + 14 * KB
-W4_RAW_REST_AT = TAB_AT[2]
-W4_RAW_FIRST_AT = TAB_AT[1]
-W4_ORD_AT = 57 * KB
-SQUARE_AT = (PICKED_AT[1], 48 * KB)
-RESULT_AT = 71 * KB
-H0_AT = 180 * KB
-H_AT = {2: 71 * KB, 3: 75 * KB, 4: 79 * KB, 5: 83 * KB, 6: 88 * KB, 7: 93 * KB}
-H1_AT = 188 * KB
-WEIGHTED_AT = (40 * KB, 98 * KB, 102 * KB)
-TAB_SCALES_AT = 112 * KB
-W4_PLANE_AT = 52 * KB
-LAST_DIFF_AT = 117 * KB
-SLOTWISE_AT = 122 * KB
-PAIRS_AT = 138 * KB
-JOINED1_AT = 154 * KB
-Z1_CODES_AT = 170 * KB
-Z1_SCALES_AT = 178 * KB
-RACK_AT = (TAB_AT[2] - 6 * KB, H0_AT, H1_AT, WEIGHTED_AT[0], PICKED_AT[2], WEIGHTED_AT[1], W4_ORD_AT, H0_AT)
-W2_CODES_AT = SLOTWISE_AT + 4 * KB * 3
-FINE_FROM = 5
+DIRECT = (0, 1)
 TURNED = (2, 3)
+VECTOR_COPIES = (9, 10, 11)
+
+PAGE_AT = (0, 8 * KB)
+W4_SCALES_AT = PAGE_AT[1]
+TAB_AT = (16 * KB, 208 * KB, 23 * KB)
+TAB_PLANE_AT = TAB_AT[0]
+WGS_AT = 36 * KB
+W4_RAW_AT = 202 * KB
+W4_ORD_AT = 46 * KB
+W4_PLANES_AT = 42 * KB
+SHIFTED_AT = 52 * KB
+PICKED_AT = (57 * KB, 32 * KB, TAB_AT[1])
+TAB_SCALES_AT = PICKED_AT[1] + 3 * KB
+H_AT = (76 * KB, 90 * KB, 98 * KB, 106 * KB, 114 * KB, 118 * KB, 122 * KB, 126 * KB)
+RACK_AT = (TAB_AT[1] + 4 * KB, TAB_AT[2], H_AT[0] - 6 * KB, H_AT[1] - 6 * KB, H_AT[2], H_AT[3], TAB_AT[1] + 4 * KB, TAB_AT[2])
+W2_RAW_AT = (H_AT[0] + 2 * KB, H_AT[1] + 2 * KB)
+W2_BF_AT = (H_AT[5], H_AT[6])
+SQUARE_AT = 130 * KB
+PAIRS_AT = (138 * KB, W4_ORD_AT)
+DIFF_AT = (W4_ORD_AT + KA * 2 * P * (SLOTS - 1) - 4 * KB, H_AT[4], W2_RAW_AT[0], W2_RAW_AT[1], H_AT[7], PAIRS_AT[0], PAIRS_AT[0] + 12 * KB, 220 * KB)
+LAST_SQUARE_AT = PAIRS_AT[0] + 10 * KB
+JOINED_AT = ((RACK_AT[4] + 4 * KB, RACK_AT[6], RACK_AT[4], RACK_AT[5]), (PAIRS_AT[0], PAIRS_AT[0] + 4 * KB, 154 * KB, 158 * KB))
+Z_CODES_AT = ((PAIRS_AT[0] + 14 * KB, PAIRS_AT[1], PAIRS_AT[1] + 4 * KB, PAIRS_AT[1] + 8 * KB), tuple(164 * KB + 2 * KB * c for c in range(CHUNKS)))
+Z_SCALES_AT = (RACK_AT[3], 172 * KB)
+W2_CODES_AT = 174 * KB
+W2_SCALES_AT = RACK_AT[3] + 2 * KB
+RESULT_AT = 178 * KB
+TURN_BANKS = {2: 4, 3: 5}
+LATE_H_BANKS = {3: (0, 1), 4: (2, 3), 5: (6, 7), 6: (4, 5), 7: (0, 1)}
+OUT_BANKS = (0, 1, 2, 3, 6, 7, 4, 0, 1, 5, 2, 3)
 
 
 def tile_list_pallet_slot_fit_kernel(tc, tab_words, tab_scales, offs, w4_words, w4_scales, offs2, wgs, rack, sharp, gain, w2, out):
@@ -81,93 +83,107 @@ def tile_list_pallet_slot_fit_kernel(tc, tab_words, tab_scales, offs, w4_words, 
         def cols_of(j, width):
             return slice(j * width, (j + 1) * width)
 
+        def listed(cols):
+            return slice(cols.start // 16, cols.stop // 16)
+
         def place(name, shape, dtype, at):
             return laid.tile(shape, dtype, name=name, offset=at, align_bytes=64)
 
         tab_scales_raw = place("tab_scales_raw", [P, T], U8, TAB_SCALES_AT)
         w4_scales_raw = place("w4_scales_raw", [P, H], U8, W4_SCALES_AT)
-        nc.gpsimd.memset(tab_scales_raw[:].bitcast(I32), 0)
-        nc.gpsimd.memset(w4_scales_raw[:].bitcast(I32), 0)
-        w4_first = place("w4_first", [P, 2 * H], U8, W4_RAW_FIRST_AT)
-        w4_rest = place("w4_rest", [P, KA - 1, 2 * H], U8, W4_RAW_REST_AT)
-        w4_raw = [w4_first[:]] + [w4_rest[:, a, :] for a in range(KA - 1)]
+        tab_shifted = place("tab_shifted", [P, (KA - 1) * S], U8, SHIFTED_AT)
+        pages = [place("page%d" % j, [P, T2], F32, PAGE_AT[j]) for j in range(PAGES)]
+        for zeroed in (tab_scales_raw, w4_scales_raw):
+            nc.vector.memset(zeroed[:].bitcast(I32), 0)
+        for cols in (slice(0, T2 - 1), slice(T2 - 1, T2)):
+            nc.vector.memset(pages[0][:, cols], 0.0)
+
+        gain_t = keep.tile([P, RB, PACK], F32, name="gain_t")
+        sharp_t = place("sharp_t", [P, RB, PACK], F32, TAB_AT[1])
+        neg_sharp = keep.tile([P, SLOTS], F32, name="neg_sharp")
+        ln_gain = keep.tile([P, SLOTS], F32, name="ln_gain")
+        nc.scalar.dma_start(sharp_t[:], sharp.rearrange("(b p i) -> p b i", b=RB, i=PACK))
+        nc.scalar.dma_start(gain_t[:], gain.rearrange("(b p i) -> p b i", b=RB, i=PACK))
+        nc.vector.tensor_scalar(neg_sharp[:], sharp_t[:].rearrange("p b i -> p (b i)"), -1.0, None, ALU.mult)
+
         tab_win = {}
+        w4_raw = place("w4_raw", [P, KA, 2 * H], U8, W4_RAW_AT)
 
         def load_table(a):
             tab_win[a] = place("tab_win%d" % a, [P, T], I32, TAB_AT[a])
             nc.sync.dma_start(tab_win[a][:], tab_words[a].rearrange("p t i -> p (t i)").bitcast(I32))
 
-        nc.sync.dma_start(w4_first[:].bitcast(I32), w4_words[0].bitcast(I32))
-        nc.sync.dma_start(w4_rest[:].bitcast(I32), w4_words[1:KA].rearrange("a p n -> p a n").bitcast(I32))
+        def load_table_scales(first_row, passes, q):
+            rows = slice(first_row, first_row + 4 * (passes.stop - passes.start))
+            nc.scalar.dma_start(tab_scales_raw[rows, :].bitcast(I32), tab_scales[passes, 4 * q : 4 * q + 4, :].bitcast(I32))
+
         nc.sync.dma_start(offs_t[:], offs)
-        load_table(0)
         nc.sync.dma_start(offs2_t[:], offs2)
+        load_table(0)
+        nc.sync.dma_start(w4_raw[:].bitcast(I32), w4_words.rearrange("a p n -> p a n").bitcast(I32))
+        load_table(1)
+        for q in (2, 3):
+            load_table_scales(32 * q - 8, slice(1, KA), q)
+            load_table_scales(32 * q, slice(0, 1), q)
+        for q in (0, 1):
+            load_table_scales(32 * q, slice(0, KA), q)
+        nc.scalar.activation(ln_gain[:], gain_t[:].rearrange("p b i -> p (b i)"), ACT.Ln)
         for q in range(QUADRANTS):
-            nc.scalar.dma_start(tab_scales_raw[32 * q : 32 * q + 4 * KA, :].bitcast(I32), tab_scales[:, 4 * q : 4 * q + 4, :].bitcast(I32))
-        for q in range(QUADRANTS):
-            queue = nc.gpsimd if q < QUADRANTS // 2 else nc.scalar
-            queue.dma_start(w4_scales_raw[32 * q : 32 * q + 4 * KA, :].bitcast(I32), w4_scales[:, 4 * q : 4 * q + 4, :].bitcast(I32))
-        gain_t = keep.tile([P, RB, PACK], F32, name="gain_t")
-        sharp_t = keep.tile([P, RB, PACK], F32, name="sharp_t")
-        nc.gpsimd.dma_start(gain_t[:], gain.rearrange("(b p i) -> p b i", b=RB, i=PACK))
-        nc.gpsimd.dma_start(sharp_t[:], sharp.rearrange("(b p i) -> p b i", b=RB, i=PACK))
+            nc.gpsimd.dma_start(w4_scales_raw[32 * q : 32 * q + 4 * KA, :].bitcast(I32), w4_scales[:, 4 * q : 4 * q + 4, :].bitcast(I32))
+
+        ord_slots = (range(0, PACK), range(PACK, SLOTS - 1), range(SLOTS - 1, SLOTS))
+        w4_ord = [place("w4_ord%d" % j, [P, KA * len(slots) * 2 * P], U8, W4_ORD_AT + KA * 2 * P * slots[0]) for j, slots in enumerate(ord_slots)]
+        w4_plane0 = place("w4_plane0", [P, H], U8, W4_PLANES_AT)
+        w4_shifted = place("w4_shifted", [P, (KA - 1) * H], U8, W4_PLANES_AT + H)
+
+        def order_w4_words(a, j):
+            b, i = divmod(ord_slots[j][0], PACK)
+            count = len(ord_slots[j])
+            nc.scalar.copy(
+                w4_ord[j][:].bitcast(U16)[:, cols_of(a, count * P)].rearrange("p (i m) -> p i m", i=count),
+                w4_raw[:, a, :].bitcast(U16)[:, cols_of(b, BANK)].rearrange("p (m i) -> p i m", i=PACK)[:, i : i + count, :],
+            )
+
+        def w4_codes(s, a):
+            j = [s in slots for slots in ord_slots].index(True)
+            return w4_ord[j][:, cols_of(a * len(ord_slots[j]) + s - ord_slots[j][0], 2 * P)]
+
         identity = keep.tile([P, P], F32, name="identity", align_bytes=64)
         make_identity(nc, identity[:])
-        w4_shifted = keep.tile([P, KA - 1, H], U8, name="w4_shifted", align_bytes=64)
-        tab_shifted = keep.tile([P, KA - 1, S], U8, name="tab_shifted", align_bytes=64)
-        nc.gpsimd.memset(w4_shifted[:].rearrange("p a n -> p (a n)").bitcast(I32), 0)
-        nc.gpsimd.memset(tab_shifted[:].rearrange("p a n -> p (a n)").bitcast(I32), 0)
-
-        w4_ord = [place("w4_ord%d" % a, [P, 2 * H], U8, W4_ORD_AT + 2 * KB * a) for a in range(KA)]
-        for a in range(KA):
-            nc.vector.tensor_copy(
-                w4_ord[a][:].bitcast(U16).rearrange("p (b i m) -> p b i m", b=RB, i=PACK),
-                w4_raw[a].bitcast(U16).rearrange("p (b m i) -> p b i m", b=RB, i=PACK),
-            )
-        load_table(1)
-        load_table(2)
-        picked = {}
-
-        def gather_words(a, pieces):
-            picked[a] = place("picked%d" % a, [P, S], U32, PICKED_AT[a])
-            width = S // pieces
-            for u in range(pieces):
-                nc.vector.tensor_copy(picked[a][:, cols_of(u, width)], tab_win[a][:].bitcast(U32).indirect(offs_t[:, cols_of(u, width // 16)]))
-
-        def shift_scale_rows(queues, shifted, source):
-            for a, queue in zip(range(1, KA), queues):
-                queue.dma_start(shifted[0:SHIFT_ROWS, a - 1, :].bitcast(I32), source[4 * a : 4 * a + SHIFT_ROWS, :].bitcast(I32))
-            return [source[:]] + [shifted[:, a, :] for a in range(KA - 1)]
-
-        w4_plane0 = place("w4_plane0", [P, H], U8, W4_PLANE_AT)
+        nc.gpsimd.memset(w4_shifted[:].bitcast(I32), 0)
         nc.gpsimd.tensor_copy(
             w4_plane0[:].rearrange("p (b i m) -> p b i m", b=RB, i=PACK),
             w4_scales_raw[:].rearrange("p (b m i) -> p b i m", b=RB, i=PACK),
         )
-        w4_planes = shift_scale_rows((nc.scalar, nc.scalar), w4_shifted, w4_plane0)
-        gather_words(0, 1)
-        wgs_t = place("wgs_t", [P, S], F32, WGS_AT)
-        nc.sync.dma_start(wgs_t[:], wgs)
+        for a in range(1, KA):
+            nc.gpsimd.dma_start(w4_shifted[0:SHIFT_ROWS, cols_of(a - 1, H)].bitcast(I32), w4_plane0[4 * a : 4 * a + SHIFT_ROWS, :].bitcast(I32))
+        w4_planes = [w4_plane0[:]] + [w4_shifted[:, cols_of(a, H)] for a in range(KA - 1)]
+        nc.gpsimd.memset(pages[1][:], 0.0)
+        for j in range(len(ord_slots)):
+            for a in range(KA):
+                order_w4_words(a, j)
+
+        picked = [place("picked%d" % a, [P, S], U32, PICKED_AT[a]) for a in range(KA)]
+        first, second, upper = slice(0, QUARTER), slice(QUARTER, BANK), slice(BANK, S)
+        lower, rest, whole = slice(0, BANK), slice(QUARTER, S), slice(0, S)
+
+        def gather_words(a, cols):
+            nc.vector.tensor_copy(picked[a][:, cols], tab_win[a][:].bitcast(U32).indirect(offs_t[:, listed(cols)]))
+
+        gather_words(0, whole)
         tab_plane0 = place("tab_plane0", [P, S], U8, TAB_PLANE_AT)
         nc.vector.tensor_copy(tab_plane0[:], tab_scales_raw[:].indirect(offs_t[:]))
-        tab_planes = shift_scale_rows((nc.sync, nc.scalar), tab_shifted, tab_plane0)
-        gather_words(1, 1)
-        gather_words(2, HALVES)
+        load_table(2)
+        for a in range(1, KA):
+            for half, source in enumerate((4 * a, HALF - 12 + 4 * a)):
+                nc.sync.dma_start(tab_shifted[cols_of(half, HALF), cols_of(a - 1, S)].bitcast(I32), tab_plane0[source : source + HALF, :].bitcast(I32))
+        wgs_t = place("wgs_t", [P, S], F32, WGS_AT)
+        nc.sync.dma_start(wgs_t[:], wgs)
+        tab_planes = [tab_plane0[:]] + [tab_shifted[:, cols_of(a, S)] for a in range(KA - 1)]
+        gather_words(1, whole)
+        for cols in (first, second, upper):
+            gather_words(2, cols)
 
-        neg_sharp = keep.tile([P, SLOTS], F32, name="neg_sharp")
-        ln_gain = keep.tile([P, SLOTS], F32, name="ln_gain")
-        nc.scalar.activation(ln_gain[:], gain_t[:].rearrange("p b i -> p (b i)"), ACT.Ln)
-        nc.scalar.mul(neg_sharp[:], sharp_t[:].rearrange("p b i -> p (b i)"), -1.0)
-
-        pages = [place("page%d" % j, [P, T2], F32, PAGE_AT[j]) for j in range(PAGES)]
-        for page in pages:
-            nc.gpsimd.memset(page[:], 0.0)
-
-        w2_bf = {}
-
-        def round_w2(b, t, at):
-            w2_bf[b, t] = place("w2_bf%d_%d" % (b, t), [P, P * PACK], BF16, at)
-            nc.gpsimd.tensor_copy(w2_bf[b, t][:].rearrange("p (n i) -> p n i", i=PACK), w2_raw[:, b, :, cols_of(t, P)].rearrange("p i n -> p n i"))
 
         rack_rows = rack.rearrange("(b p i) m -> b i p m", b=RB, i=PACK)
         racks = {}
@@ -177,257 +193,229 @@ def tile_list_pallet_slot_fit_kernel(tc, tab_words, tab_scales, offs, w4_words, 
             nc.sync.dma_start(racks[s][:], rack_rows[s // PACK, s % PACK])
 
         load_rack(0)
-        w2_raw = place("w2_raw", [P, RB, PACK, N], F32, W2_RAW_AT)
-        nc.sync.dma_start(w2_raw[:].rearrange("p b i n -> p b (i n)"), w2.rearrange("(b p i) n -> p b (i n)", b=RB, i=PACK))
+        load_rack(1)
 
-        h = {s: place("h%d" % s, [P, S + (KB // 4 if s >= SLOTS - NT else 0)], F32, H_AT.get(s, H1_AT))[:, 0:S] for s in range(1, SLOTS)}
-        h0_late = place("h0_late", [P, BANK], F32, H0_AT)
-        weighted = {s: place("weighted%d" % s, [P, S], F32, WEIGHTED_AT[s])[:] for s in range(AHEAD)}
+        h = [place("h%d" % s, [P, S], F32, H_AT[s]) for s in range(SLOTS)]
+        weighted = {s: h[s][:] for s in range(AHEAD)}
 
-        def h_half(s, u):
-            return h0_late[:] if s == 0 else h[s][:, cols_of(u, BANK)]
-
-        def h_bank(s, u):
-            return banks[u if s == SLOTS - 1 else (HALVES * s + u) % BANKS]
-
-        def h_pass(s, u, a):
+        def h_pass(s, cols, bank, a, order=tuple(range(KA))):
             nc.tensor.matmul_mx(
-                out=h_bank(s, u)[:],
-                lhsT=w4_ord[a][:, cols_of(s, 2 * P)].bitcast(FP4X4),
+                out=banks[bank][:, 0 : cols.stop - cols.start],
+                lhsT=w4_codes(s, a).bitcast(FP4X4),
                 lhsT_scale=w4_planes[a][:, cols_of(s, P)],
-                rhs=picked[a][:, cols_of(u, BANK)].bitcast(FP8X4),
-                rhs_scale=tab_planes[a][:, cols_of(u, BANK)],
-                start=(a == 0),
-                stop=(a == KA - 1),
+                rhs=picked[a][:, cols].bitcast(FP8X4),
+                rhs_scale=tab_planes[a][:, cols],
+                start=(a == order[0]),
+                stop=(a == order[-1]),
             )
 
-        def h_out(s, u):
-            bank = h_bank(s, u)
-            if (s, u) == (0, 0):
-                nc.vector.scalar_tensor_tensor(weighted[0][:, 0:BANK], bank[:], -1.0, wgs_t[:, 0:BANK], ALU.mult, ALU.mult)
-            else:
-                nc.scalar.mul(h_half(s, u), bank[:], -1.0)
-
-        def weigh(s):
-            nc.gpsimd.tensor_tensor(weighted[s], h[s], wgs_t[:], ALU.mult)
-
-        opening = BANKS // HALVES
-        for s in range(opening):
-            for u in range(HALVES):
-                h_pass(s, u, 0)
-        for s in range(opening):
-            for u in range(HALVES):
-                for a in range(1, KA):
-                    h_pass(s, u, a)
-                h_out(s, u)
+        def h_out(s, cols, bank):
+            nc.scalar.mul(h[s][:, cols], banks[bank][:, 0 : cols.stop - cols.start], -1.0)
 
         def h_slot(s):
-            for u in range(HALVES):
+            for cols, bank in zip((lower, upper), LATE_H_BANKS[s]):
                 for a in range(KA):
-                    h_pass(s, u, a)
-                h_out(s, u)
+                    h_pass(s, cols, bank, a)
+                h_out(s, cols, bank)
 
-        for s in range(opening, SLOTS - 1):
+        def weigh(s, cols):
+            nc.gpsimd.tensor_tensor(weighted[s][:, cols], h[s][:, cols], wgs_t[:, cols], ALU.mult)
+
+        def scatter(s, cols):
+            nc.vector.tensor_copy(pages[s % PAGES][:].indirect(offs2_t[:, listed(cols)]), weighted[s][:, cols])
+
+        opening = [(0, first), (1, first), (0, second), (1, second), (0, upper), (1, upper), (2, lower), (2, upper)]
+        for bank, (s, cols) in enumerate(opening):
+            h_pass(s, cols, bank, 0)
+        for bank in (0, 1, 2, 4, 3, 5, 6, 7):
+            s, cols = opening[bank]
+            order = (0, 1, 2) if s < 2 else (0, 2, 1)
+            for a in order[1:]:
+                h_pass(s, cols, bank, a, order)
+            h_out(s, cols, bank)
+        for cols in (first, rest):
+            for s in range(2):
+                weigh(s, cols)
+        weigh(2, whole)
+        for s in range(3, SLOTS - 1):
             h_slot(s)
+        weigh(3, whole)
 
-        squares = [place("square%d" % j, [P, S], F32, SQUARE_AT[j]) for j in range(HALVES)]
-        pairs = {(1, c): place("pairs1_%d" % c, [P, 2, BANK, 2], BF16, PAIRS_AT + 4 * KB * c) for c in range(CHUNKS)}
+        pairs = {}
         slotwise = {}
-        for c in range(CHUNKS):
-            if c in TURNED:
-                slotwise[c] = place("slotwise%d" % c, [P, PACK, BANK], BF16, SLOTWISE_AT + 4 * KB * c)
-            else:
-                pairs[0, c] = place("pairs0_%d" % c, [P, 2, BANK, 2], BF16, SLOTWISE_AT + 4 * KB * c)
         joined = {}
         z_codes = {}
         z_scales = {}
-        turn_banks = {0: ((banks[0], banks[1]), (banks[2], banks[3])), 1: ((banks[2], banks[3]), (banks[6], banks[7]))}
-        for s in range(2, SLOTS):
-            sums, backs = turn_banks[s - 1]
-            turn_banks[s] = (backs, sums)
+        diffs = {}
+        squares = {}
 
-        def scatter(s, pieces):
-            width = S // pieces
-            for u in range(pieces):
-                nc.vector.tensor_copy(pages[s % PAGES][:].indirect(offs2_t[:, cols_of(u, width // 16)]), weighted[s][:, cols_of(u, width)])
+        def open_pairs(b):
+            for c in range(CHUNKS):
+                if b == 0 and c in TURNED:
+                    slotwise[c] = place("slotwise%d" % c, [P, PACK, BANK], BF16, PAIRS_AT[b] + 4 * KB * c)
+                else:
+                    pairs[b, c] = place("pairs%d_%d" % (b, c), [P, 2, BANK, 2], BF16, PAIRS_AT[b] + 4 * KB * c)
 
-        def difference(engine, diff, s, cols):
-            engine.tensor_tensor(diff, racks[s][:, cols], pages[s % PAGES][:, cols], ALU.add)
+        def difference(engine, s, cols):
+            engine.tensor_tensor(diffs[s][:, cols], racks[s][:, cols], pages[s % PAGES][:, cols], ALU.add)
 
-        def square_of(s, c):
-            return squares[c // 2][:, cols_of(c % 2, BANK)]
+        def square_direct(s, cols):
+            nc.scalar.activation(diffs[s][:, cols], diffs[s][:, cols], ACT.Square)
 
         def exp_to_z(s, c, square):
             b, i = divmod(s, PACK)
             target = pairs[b, c][:, i // 2, :, i % 2] if (b, c) in pairs else slotwise[c][:, i, :]
             nc.scalar.activation(target, square, ACT.Exp, bias=ln_gain[:, s : s + 1], scale=neg_sharp[:, s : s + 1])
 
+        def exp_direct(s, c):
+            exp_to_z(s, c, diffs[s][:, cols_of(c, BANK)])
+
         def turned_sums(s):
             blocks = BANK // P
-            for c, bank in zip(TURNED, turn_banks[s][0]):
-                for k, source in enumerate((racks[s], pages[s % PAGES])):
+            for k, source in enumerate((racks[s], pages[s % PAGES])):
+                for c, bank in TURN_BANKS.items():
                     for j in range(blocks):
                         nc.tensor.matmul(
-                            bank[:, cols_of(j, P)], source[:, cols_of(c * blocks + j, P)], identity[:],
+                            banks[bank][:, cols_of(j, P)], source[:, cols_of(c * blocks + j, P)], identity[:],
                             start=(k == 0 and j == 0), stop=(k == 1 and j == blocks - 1), is_transpose=True,
                         )
 
-        def square_turned(s, j):
-            c = TURNED[j]
-            nc.scalar.activation(square_of(s, c), turn_banks[s][0][j][:], ACT.Square)
+        def square_turned(s, c, bank):
+            at = SQUARE_AT + 2 * KB * TURNED.index(c)
+            squares[s, c] = place("square%d_%d" % (s, c), [P, BANK], F32, at)
+            nc.scalar.activation(squares[s, c][:], banks[bank][:], ACT.Square)
             for block in range(BANK // P):
-                nc.tensor.transpose(turn_banks[s][1][j][:, cols_of(block, P)], square_of(s, c)[:, cols_of(block, P)], identity[:])
+                nc.tensor.transpose(banks[bank][:, cols_of(block, P)], squares[s, c][:, cols_of(block, P)], identity[:])
 
-        def exp_turned(s, j):
-            exp_to_z(s, TURNED[j], turn_banks[s][1][j][:])
+        def exp_turned(s, c, bank):
+            exp_to_z(s, c, banks[bank][:])
 
-        def slot_first(at):
-            turned_sums(0)
-            for j in range(2):
-                square_turned(0, j)
-            for j in range(2):
-                exp_turned(0, j)
-            h_slot(SLOTS - 1)
-            load_rack(4)
-            load_rack(6)
-            diff = place("diff0", [P, S], F32, at)
-            difference(nc.gpsimd, diff[:], 0, slice(0, S))
-            nc.scalar.activation(squares[0][:], diff[:], ACT.Square)
-            for c in range(2):
-                exp_to_z(0, c, square_of(0, c))
+        def open_slot(s):
+            diffs[s] = place("diff%d" % s, [P, S], F32, DIFF_AT[s])
 
-        def slot_coarse(s, at):
-            diff = place("diff%d" % s, [P, S], F32, at)
-            difference(nc.gpsimd, diff[:], s, slice(0, S))
+        def slot_to_z(s):
+            open_slot(s)
+            for c in DIRECT:
+                difference(nc.gpsimd, s, cols_of(c, BANK))
             turned_sums(s)
-            square_turned(s, 0)
-            nc.scalar.activation(squares[0][:], diff[:], ACT.Square)
-            square_turned(s, 1)
-            exp_turned(s, 0)
-            for c in range(2):
-                exp_to_z(s, c, square_of(s, c))
-            exp_turned(s, 1)
+            for c, bank in TURN_BANKS.items():
+                square_turned(s, c, bank)
+            for c, (turned, bank) in zip(DIRECT, TURN_BANKS.items()):
+                square_direct(s, cols_of(c, BANK))
+                exp_turned(s, turned, bank)
+            for c in DIRECT:
+                exp_direct(s, c)
 
-        def slot_fine(engine, s, at):
-            diff = place("diff%d" % s, [P, S], F32, at)
-            for c in range(2):
-                difference(engine, diff[:, cols_of(c, BANK)], s, cols_of(c, BANK))
-            turned_sums(s)
-            nc.scalar.activation(square_of(s, 0), diff[:, 0:BANK], ACT.Square)
-            square_turned(s, 0)
-            exp_to_z(s, 0, square_of(s, 0))
-            nc.scalar.activation(square_of(s, 1), diff[:, BANK:S], ACT.Square)
-            square_turned(s, 1)
-            if s < SLOTS - 1:
-                exp_turned(s, 0)
-            exp_to_z(s, 1, square_of(s, 1))
-            if s < SLOTS - 1:
-                exp_turned(s, 1)
-
-        def slot_to_z(s, at):
-            if s == 0:
-                slot_first(at)
-            elif s < FINE_FROM:
-                slot_coarse(s, at)
-            else:
-                slot_fine(nc.gpsimd, s, at)
-
-        def join(copy, dtype, b, c, at):
-            joined[b, c] = place("joined%d_%d" % (b, c), [P, BANK * PACK], BF16, at)
+        def join(copy, dtype, b, c):
+            joined[b, c] = place("joined%d_%d" % (b, c), [P, BANK * PACK], BF16, JOINED_AT[b][c])
             copy(
                 joined[b, c][:].bitcast(dtype).rearrange("p (m e h) -> p m h e", e=LINE, h=2),
                 pairs[b, c][:].rearrange("p h m e -> p (h m e)").bitcast(dtype).rearrange("p (h m e) -> p m h e", e=LINE, h=2),
             )
 
-        def interleave(target, source):
-            nc.gpsimd.tensor_scalar(target.rearrange("p (m i) -> p m i", i=PACK), source.rearrange("p i m -> p m i"), 1.0, 0.0, ALU.mult, ALU.add)
+        def interleave(c):
+            joined[0, c] = place("joined0_%d" % c, [P, BANK * PACK], BF16, JOINED_AT[0][c])
+            nc.gpsimd.tensor_scalar(joined[0, c][:].rearrange("p (m i) -> p m i", i=PACK), slotwise[c][:].rearrange("p i m -> p m i"), 1.0, 0.0, ALU.mult, ALU.add)
 
-        def interleave_chunk(c, at):
-            joined[0, c] = place("joined0_%d" % c, [P, BANK * PACK], BF16, at)
-            interleave(joined[0, c][:], slotwise[c][:])
-
-        def quantise(b, c, codes_at, scales_at):
-            z_codes[b, c] = place("z_codes%d_%d" % (b, c), [P, BANK], U32, codes_at)
-            z_scales[b, c] = place("z_scales%d_%d" % (b, c), [P, BANK], U8, scales_at)
+        def quantise(b, c):
+            z_codes[b, c] = place("z_codes%d_%d" % (b, c), [P, BANK], U32, Z_CODES_AT[b][c])
+            z_scales[b, c] = place("z_scales%d_%d" % (b, c), [P, BANK], U8, Z_SCALES_AT[b] + BANK * c)
             nc.vector.quantize_mx(out=z_codes[b, c][:].bitcast(FP8X4), scales=z_scales[b, c][:], in_=joined[b, c][:])
 
-        nc.gpsimd.tensor_tensor(weighted[0][:, BANK:S], h0_late[:], wgs_t[:, BANK:S], ALU.mult)
-        for s in range(1, AHEAD):
-            weigh(s)
-        for s in (1, 2):
-            load_rack(s)
+        w2_bf = {}
+
+        w2_raw = {}
+
+        def load_w2(b):
+            w2_raw[b] = place("w2_raw%d" % b, [P, PACK, N], F32, W2_RAW_AT[b])
+            nc.sync.dma_start(w2_raw[b][:].rearrange("p i n -> p (i n)"), w2.rearrange("(b p i) n -> b p (i n)", b=RB, i=PACK)[b])
+
+        def round_w2(b):
+            w2_bf[b] = place("w2_bf%d" % b, [P, N * PACK], BF16, W2_BF_AT[b])
+            nc.gpsimd.tensor_scalar(w2_bf[b][:].rearrange("p (n i) -> p n i", i=PACK), w2_raw[b][:].rearrange("p i n -> p n i"), 1.0, 0.0, ALU.mult, ALU.add)
+
+        for cols in (first, rest):
+            for s in range(2):
+                scatter(s, cols)
+        for b in range(RB):
+            load_rack(2 + b)
+            load_w2(b)
+        open_pairs(0)
         last = SLOTS - 1
         for s in range(last):
-            scatter(s, HALVES if s == 0 else 1)
-            if s in (0, 2, 5):
-                load_rack({0: 3, 2: 5, 5: 7}[s])
-            if s < PACK:
-                slot_to_z(s, H_AT[AHEAD - 1] if s == 0 else H_AT[s + AHEAD])
-                nxt = AHEAD if s == 0 else s + AHEAD + 1
-                weighted[nxt] = racks[s][:, 0:S]
-                weigh(nxt)
-                if s > 0:
-                    round_w2(0, s - 1, H_AT[nxt] + 4 * KB)
-                if s == 0:
-                    weighted[nxt + 1] = place("weighted%d" % (nxt + 1), [P, S], F32, H_AT[nxt])[:]
-                    weigh(nxt + 1)
-            elif s == PACK:
-                slot_to_z(s, H_AT[last])
-            else:
-                slot_to_z(s, SLOTWISE_AT + 4 * KB * TURNED[s - PACK - 1])
-            if s == PACK - 1:
-                for c in range(2):
-                    join(nc.scalar.copy, U32, 0, c, JOINED0_AT + 4 * KB * c)
-            if s in (PACK, PACK + 1):
-                interleave_chunk(TURNED[s - PACK], RACK_AT[s])
+            if s == PACK:
+                open_pairs(1)
+            slot_to_z(s)
+            if s == 0:
+                h_slot(last)
+            nxt = s + AHEAD
+            if nxt < SLOTS:
+                weighted[nxt] = racks[s][:, whole]
+                weigh(nxt, whole)
+            if s + 2 < SLOTS:
+                scatter(s + 2, whole)
+            if s + 4 < SLOTS:
+                load_rack(s + 4)
+            if s in (1, 2):
+                round_w2(s - 1)
+            if s in (4, 5):
+                interleave(TURNED[s - 4])
+            if s in (4, 6):
+                join(nc.gpsimd.tensor_copy, U32, 0, DIRECT[(s - 4) // 2])
 
-        for t in range(NT):
-            round_w2(1, t, RACK_AT[last - 1] + KB * t)
-        scatter(last, 1)
-        slot_fine(nc.vector, last, LAST_DIFF_AT)
+        open_slot(last)
+        for c in DIRECT:
+            difference(nc.vector, last, cols_of(c, BANK))
+        turned_sums(last)
+        last_diff, diffs[last] = diffs[last], place("last_square", [P, S], F32, LAST_SQUARE_AT)
+        for c in DIRECT:
+            nc.scalar.activation(diffs[last][:, cols_of(c, BANK)], last_diff[:, cols_of(c, BANK)], ACT.Square)
+        for c, (turned, bank) in zip(DIRECT, TURN_BANKS.items()):
+            exp_direct(last, c)
+            square_turned(last, turned, bank)
         w2_codes = place("w2_codes", [P, RB * N], U32, W2_CODES_AT)
-        w2_scales = place("w2_scales", [P, RB * N], U8, W2_CODES_AT + 3 * KB)
-        for (b, t), rounded in w2_bf.items():
-            cols = cols_of(b * NT + t, P)
+        w2_scales = place("w2_scales", [P, RB * N], U8, W2_SCALES_AT)
+        for k, rounded in w2_bf.items():
+            cols = cols_of(k, N)
             nc.vector.quantize_mx(out=w2_codes[:, cols].bitcast(FP8X4), scales=w2_scales[:, cols], in_=rounded[:])
 
-        sums, backs = turn_banks[last]
-        others = [banks[j] for j in (0, 1, 4, 5)]
-        out_banks = others + list(sums) + [backs[0], others[0], others[1], backs[1], others[2], others[3]]
-
-        def out_pass(b, c, t):
-            nc.tensor.matmul_mx(
-                out=out_banks[c * NT + t][:],
-                lhsT=w2_codes[:, cols_of(b * NT + t, P)].bitcast(FP8X4),
-                lhsT_scale=w2_scales[:, cols_of(b * NT + t, P)],
-                rhs=z_codes[b, c][:].bitcast(FP8X4),
-                rhs_scale=z_scales[b, c][:],
-                start=(b == 0),
-                stop=(b == RB - 1),
-            )
-
-        def store_chunk(c):
+        def out_pass(b, c):
             for t in range(NT):
-                bank = out_banks[c * NT + t]
-                res = place("res%d" % (c * NT + t), [P, BANK], F32, RESULT_AT + 2 * KB * (c * NT + t))
-                if c * NT + t in VECTOR_COPIES:
-                    nc.vector.tensor_copy(res[:], bank[:])
-                else:
-                    nc.scalar.copy(res[:], bank[:])
-                nc.sync.dma_start(out[cols_of(t, P), cols_of(c, BANK)], res[:])
+                nc.tensor.matmul_mx(
+                    out=banks[OUT_BANKS[c * NT + t]][:],
+                    lhsT=w2_codes[:, cols_of(b * NT + t, P)].bitcast(FP8X4),
+                    lhsT_scale=w2_scales[:, cols_of(b * NT + t, P)],
+                    rhs=z_codes[b, c][:].bitcast(FP8X4),
+                    rhs_scale=z_scales[b, c][:],
+                    start=(b == 0),
+                    stop=(b == RB - 1),
+                )
 
-        for c in range(CHUNKS):
-            if c < 1:
-                quantise(0, c, RACK_AT[last] + 4 * KB * c, RACK_AT[last] + 4 * KB * c + 2 * KB)
-            else:
-                quantise(0, c, PAIRS_AT + 4 * KB * (c - 1), PAIRS_AT + 4 * KB * (c - 1) + 2 * KB)
-            join(nc.vector.tensor_copy, I32, 1, c, JOINED1_AT + 4 * KB * c)
-            quantise(1, c, Z1_CODES_AT + 2 * KB * c, Z1_SCALES_AT + BANK * c)
-            for b in range(RB):
-                for t in range(NT):
-                    out_pass(b, c, t)
+        def store(k):
+            c, t = divmod(k, NT)
+            res = place("res%d" % k, [P, BANK], F32, RESULT_AT + 2 * KB * k)
+            copy = nc.vector.tensor_copy if k in VECTOR_COPIES else nc.scalar.copy
+            copy(res[:], banks[OUT_BANKS[k]][:])
+            nc.sync.dma_start(out[cols_of(t, P), cols_of(c, BANK)], res[:])
+
+        def chunk_product(c):
+            join(nc.vector.tensor_copy, I32, 1, c)
             if c > 0:
-                store_chunk(c - 1)
-            if c < 2:
-                exp_turned(last, c)
-        store_chunk(CHUNKS - 1)
+                quantise(0, c)
+            quantise(1, c)
+            for b in range(RB):
+                out_pass(b, c)
+
+        quantise(0, 0)
+        for c in DIRECT:
+            chunk_product(c)
+        for j, (c, bank) in enumerate(TURN_BANKS.items()):
+            store(j)
+            exp_turned(last, c, bank)
+        store(2)
+        chunk_product(2)
+        for k in range(NT, 2 * NT):
+            store(k)
+        chunk_product(3)
+        for k in range(2 * NT, CHUNKS * NT):
+            store(k)

@@ -29,7 +29,6 @@ CHUNKS = T2 // BANK
 NT = N // P
 QUARTER = S // 4
 HALF = P // 2
-SHIFT_ROWS = 112
 PAGES = 2
 AHEAD = 4
 LINE = 4
@@ -39,23 +38,23 @@ TURNED = (2, 3)
 VECTOR_COPIES = (9, 10, 11)
 
 PAGE_AT = (0, 8 * KB)
-W4_SCALES_AT = PAGE_AT[1]
+W4_SCALES_AT = 224 * KB
 TAB_AT = (16 * KB, 208 * KB, 23 * KB)
 TAB_PLANE_AT = TAB_AT[0]
 WGS_AT = 36 * KB
-W4_RAW_AT = 202 * KB
+W4_RAW_AT = (TAB_AT[1] - 4 * KB, TAB_AT[1] + 4 * KB)
 W4_ORD_AT = 46 * KB
 W4_PLANES_AT = 42 * KB
 SHIFTED_AT = 52 * KB
 PICKED_AT = (57 * KB, 32 * KB, TAB_AT[1])
 TAB_SCALES_AT = PICKED_AT[1] + 3 * KB
 H_AT = (76 * KB, 90 * KB, 98 * KB, 106 * KB, 114 * KB, 118 * KB, 122 * KB, 126 * KB)
-RACK_AT = (TAB_AT[1] + 4 * KB, TAB_AT[2], H_AT[0] - 6 * KB, H_AT[1] - 6 * KB, H_AT[2], H_AT[3], TAB_AT[1] + 4 * KB, TAB_AT[2])
+RACK_AT = (TAB_AT[1] + 7 * KB, TAB_AT[2], H_AT[0] - 6 * KB, H_AT[1] - 6 * KB, H_AT[2], H_AT[3], TAB_AT[1] + 7 * KB, TAB_AT[2])
 W2_RAW_AT = (H_AT[0] + 2 * KB, H_AT[1] + 2 * KB)
 W2_BF_AT = (H_AT[5], H_AT[6])
 SQUARE_AT = 130 * KB
 PAIRS_AT = (138 * KB, W4_ORD_AT)
-DIFF_AT = (W4_ORD_AT + KA * 2 * P * (SLOTS - 1) - 4 * KB, H_AT[4], W2_RAW_AT[0], W2_RAW_AT[1], H_AT[7], PAIRS_AT[0], PAIRS_AT[0] + 12 * KB, 220 * KB)
+DIFF_AT = (W4_ORD_AT + KA * 2 * P * (SLOTS - 1) - 4 * KB, H_AT[4], W2_RAW_AT[0], W2_RAW_AT[1], H_AT[7], PAIRS_AT[0], PAIRS_AT[0] + 12 * KB, 227 * KB)
 LAST_SQUARE_AT = PAIRS_AT[0] + 10 * KB
 JOINED_AT = ((RACK_AT[4] + 4 * KB, RACK_AT[6], RACK_AT[4], RACK_AT[5]), (PAIRS_AT[0], PAIRS_AT[0] + 4 * KB, 154 * KB, 158 * KB))
 Z_CODES_AT = ((PAIRS_AT[0] + 14 * KB, PAIRS_AT[1], PAIRS_AT[1] + 4 * KB, PAIRS_AT[1] + 8 * KB), tuple(164 * KB + 2 * KB * c for c in range(CHUNKS)))
@@ -90,78 +89,83 @@ def tile_list_pallet_slot_fit_kernel(tc, tab_words, tab_scales, offs, w4_words, 
             return laid.tile(shape, dtype, name=name, offset=at, align_bytes=64)
 
         tab_scales_raw = place("tab_scales_raw", [P, T], U8, TAB_SCALES_AT)
-        w4_scales_raw = place("w4_scales_raw", [P, H], U8, W4_SCALES_AT)
+        w4_scales_raw = place("w4_scales_raw", [P, KA * H], U8, W4_SCALES_AT)
         tab_shifted = place("tab_shifted", [P, (KA - 1) * S], U8, SHIFTED_AT)
         pages = [place("page%d" % j, [P, T2], F32, PAGE_AT[j]) for j in range(PAGES)]
-        for zeroed in (tab_scales_raw, w4_scales_raw):
-            nc.vector.memset(zeroed[:].bitcast(I32), 0)
-        for cols in (slice(0, T2 - 1), slice(T2 - 1, T2)):
-            nc.vector.memset(pages[0][:, cols], 0.0)
+        nc.gpsimd.memset(w4_scales_raw[:].bitcast(I32), 0)
+        for zeroed in (tab_scales_raw[:].bitcast(I32), pages[0][:]):
+            words = zeroed.shape[1]
+            for cols in (slice(0, words - 1), slice(words - 1, words)):
+                nc.vector.memset(zeroed[:, cols], 0)
+        nc.vector.memset(pages[1][:], 0.0)
 
         gain_t = keep.tile([P, RB, PACK], F32, name="gain_t")
-        sharp_t = place("sharp_t", [P, RB, PACK], F32, TAB_AT[1])
+        sharp_t = keep.tile([P, SLOTS], F32, name="sharp_t")
         neg_sharp = keep.tile([P, SLOTS], F32, name="neg_sharp")
         ln_gain = keep.tile([P, SLOTS], F32, name="ln_gain")
-        nc.scalar.dma_start(sharp_t[:], sharp.rearrange("(b p i) -> p b i", b=RB, i=PACK))
         nc.scalar.dma_start(gain_t[:], gain.rearrange("(b p i) -> p b i", b=RB, i=PACK))
-        nc.vector.tensor_scalar(neg_sharp[:], sharp_t[:].rearrange("p b i -> p (b i)"), -1.0, None, ALU.mult)
+        nc.scalar.dma_start(sharp_t[:].rearrange("p (b i) -> p b i", b=RB), sharp.rearrange("(b p i) -> p b i", b=RB, i=PACK))
 
         tab_win = {}
-        w4_raw = place("w4_raw", [P, KA, 2 * H], U8, W4_RAW_AT)
 
         def load_table(a):
             tab_win[a] = place("tab_win%d" % a, [P, T], I32, TAB_AT[a])
             nc.sync.dma_start(tab_win[a][:], tab_words[a].rearrange("p t i -> p (t i)").bitcast(I32))
 
+        nc.sync.dma_start(offs_t[:], offs)
+        nc.sync.dma_start(offs2_t[:], offs2)
+        load_table(0)
+        w4_raw = {}
+
+        def load_w4(b):
+            w4_raw[b] = place("w4_raw%d" % b, [P, KA, H], U8, W4_RAW_AT[b])
+            nc.sync.dma_start(w4_raw[b][:].bitcast(I32), w4_words[:, :, cols_of(b, H)].rearrange("a p n -> p a n").bitcast(I32))
+
+        load_w4(0)
+        load_table(1)
+
         def load_table_scales(first_row, passes, q):
             rows = slice(first_row, first_row + 4 * (passes.stop - passes.start))
             nc.scalar.dma_start(tab_scales_raw[rows, :].bitcast(I32), tab_scales[passes, 4 * q : 4 * q + 4, :].bitcast(I32))
 
-        nc.sync.dma_start(offs_t[:], offs)
-        nc.sync.dma_start(offs2_t[:], offs2)
-        load_table(0)
-        nc.sync.dma_start(w4_raw[:].bitcast(I32), w4_words.rearrange("a p n -> p a n").bitcast(I32))
-        load_table(1)
+        for q in (0, 1):
+            load_table_scales(32 * q, slice(0, KA), q)
         for q in (2, 3):
             load_table_scales(32 * q - 8, slice(1, KA), q)
             load_table_scales(32 * q, slice(0, 1), q)
-        for q in (0, 1):
-            load_table_scales(32 * q, slice(0, KA), q)
-        nc.scalar.activation(ln_gain[:], gain_t[:].rearrange("p b i -> p (b i)"), ACT.Ln)
         for q in range(QUADRANTS):
-            nc.gpsimd.dma_start(w4_scales_raw[32 * q : 32 * q + 4 * KA, :].bitcast(I32), w4_scales[:, 4 * q : 4 * q + 4, :].bitcast(I32))
+            nc.gpsimd.dma_start(
+                w4_scales_raw[32 * q : 32 * q + 4, :].bitcast(I32).rearrange("p (a n) -> p a n", a=KA),
+                w4_scales[:, 4 * q : 4 * q + 4, :].bitcast(I32).rearrange("a r n -> r a n"),
+            )
+        identity = keep.tile([P, P], F32, name="identity", align_bytes=64)
+        make_identity(nc, identity[:])
+        nc.scalar.activation(ln_gain[:], gain_t[:].rearrange("p b i -> p (b i)"), ACT.Ln)
+        nc.scalar.mul(neg_sharp[:], sharp_t[:], -1.0)
 
         ord_slots = (range(0, PACK), range(PACK, SLOTS - 1), range(SLOTS - 1, SLOTS))
         w4_ord = [place("w4_ord%d" % j, [P, KA * len(slots) * 2 * P], U8, W4_ORD_AT + KA * 2 * P * slots[0]) for j, slots in enumerate(ord_slots)]
-        w4_plane0 = place("w4_plane0", [P, H], U8, W4_PLANES_AT)
-        w4_shifted = place("w4_shifted", [P, (KA - 1) * H], U8, W4_PLANES_AT + H)
+        w4_planes = [place("w4_planes%d" % b, [P, KA * BANK], U8, W4_PLANES_AT + KA * BANK * b) for b in range(RB)]
 
         def order_w4_words(a, j):
             b, i = divmod(ord_slots[j][0], PACK)
             count = len(ord_slots[j])
             nc.scalar.copy(
                 w4_ord[j][:].bitcast(U16)[:, cols_of(a, count * P)].rearrange("p (i m) -> p i m", i=count),
-                w4_raw[:, a, :].bitcast(U16)[:, cols_of(b, BANK)].rearrange("p (m i) -> p i m", i=PACK)[:, i : i + count, :],
+                w4_raw[b][:, a, :].bitcast(U16).rearrange("p (m i) -> p i m", i=PACK)[:, i : i + count, :],
             )
 
         def w4_codes(s, a):
             j = [s in slots for slots in ord_slots].index(True)
             return w4_ord[j][:, cols_of(a * len(ord_slots[j]) + s - ord_slots[j][0], 2 * P)]
 
-        identity = keep.tile([P, P], F32, name="identity", align_bytes=64)
-        make_identity(nc, identity[:])
-        nc.gpsimd.memset(w4_shifted[:].bitcast(I32), 0)
-        nc.gpsimd.tensor_copy(
-            w4_plane0[:].rearrange("p (b i m) -> p b i m", b=RB, i=PACK),
-            w4_scales_raw[:].rearrange("p (b m i) -> p b i m", b=RB, i=PACK),
-        )
-        for a in range(1, KA):
-            nc.gpsimd.dma_start(w4_shifted[0:SHIFT_ROWS, cols_of(a - 1, H)].bitcast(I32), w4_plane0[4 * a : 4 * a + SHIFT_ROWS, :].bitcast(I32))
-        w4_planes = [w4_plane0[:]] + [w4_shifted[:, cols_of(a, H)] for a in range(KA - 1)]
-        nc.gpsimd.memset(pages[1][:], 0.0)
-        for j in range(len(ord_slots)):
-            for a in range(KA):
-                order_w4_words(a, j)
+        for b in range(RB):
+            nc.gpsimd.tensor_copy(
+                w4_planes[b][:].rearrange("p (a i m) -> p a i m", a=KA, i=PACK),
+                w4_scales_raw[:].rearrange("p (a b m i) -> p b a i m", a=KA, b=RB, i=PACK)[:, b],
+            )
+        for a in range(KA):
+            order_w4_words(a, 0)
 
         picked = [place("picked%d" % a, [P, S], U32, PICKED_AT[a]) for a in range(KA)]
         first, second, upper = slice(0, QUARTER), slice(QUARTER, BANK), slice(BANK, S)
@@ -174,6 +178,8 @@ def tile_list_pallet_slot_fit_kernel(tc, tab_words, tab_scales, offs, w4_words, 
         tab_plane0 = place("tab_plane0", [P, S], U8, TAB_PLANE_AT)
         nc.vector.tensor_copy(tab_plane0[:], tab_scales_raw[:].indirect(offs_t[:]))
         load_table(2)
+        wgs_first = place("wgs_first", [P, QUARTER], F32, TAB_PLANE_AT + KB)
+        nc.sync.dma_start(wgs_first[:], wgs[:, first])
         for a in range(1, KA):
             for half, source in enumerate((4 * a, HALF - 12 + 4 * a)):
                 nc.sync.dma_start(tab_shifted[cols_of(half, HALF), cols_of(a - 1, S)].bitcast(I32), tab_plane0[source : source + HALF, :].bitcast(I32))
@@ -181,9 +187,9 @@ def tile_list_pallet_slot_fit_kernel(tc, tab_words, tab_scales, offs, w4_words, 
         nc.sync.dma_start(wgs_t[:], wgs)
         tab_planes = [tab_plane0[:]] + [tab_shifted[:, cols_of(a, S)] for a in range(KA - 1)]
         gather_words(1, whole)
+        load_w4(1)
         for cols in (first, second, upper):
             gather_words(2, cols)
-
 
         rack_rows = rack.rearrange("(b p i) m -> b i p m", b=RB, i=PACK)
         racks = {}
@@ -202,7 +208,7 @@ def tile_list_pallet_slot_fit_kernel(tc, tab_words, tab_scales, offs, w4_words, 
             nc.tensor.matmul_mx(
                 out=banks[bank][:, 0 : cols.stop - cols.start],
                 lhsT=w4_codes(s, a).bitcast(FP4X4),
-                lhsT_scale=w4_planes[a][:, cols_of(s, P)],
+                lhsT_scale=w4_planes[s // PACK][:, cols_of(a * PACK + s % PACK, P)],
                 rhs=picked[a][:, cols].bitcast(FP8X4),
                 rhs_scale=tab_planes[a][:, cols],
                 start=(a == order[0]),
@@ -219,7 +225,7 @@ def tile_list_pallet_slot_fit_kernel(tc, tab_words, tab_scales, offs, w4_words, 
                 h_out(s, cols, bank)
 
         def weigh(s, cols):
-            nc.gpsimd.tensor_tensor(weighted[s][:, cols], h[s][:, cols], wgs_t[:, cols], ALU.mult)
+            nc.gpsimd.tensor_tensor(weighted[s][:, cols], h[s][:, cols], wgs_first[:] if cols == first else wgs_t[:, cols], ALU.mult)
 
         def scatter(s, cols):
             nc.vector.tensor_copy(pages[s % PAGES][:].indirect(offs2_t[:, listed(cols)]), weighted[s][:, cols])
@@ -237,6 +243,9 @@ def tile_list_pallet_slot_fit_kernel(tc, tab_words, tab_scales, offs, w4_words, 
             for s in range(2):
                 weigh(s, cols)
         weigh(2, whole)
+        for j in range(1, len(ord_slots)):
+            for a in range(KA):
+                order_w4_words(a, j)
         for s in range(3, SLOTS - 1):
             h_slot(s)
         weigh(3, whole)

@@ -28,6 +28,7 @@ BANKS = 8
 CHUNKS = T2 // BANK
 NT = N // P
 QUARTER = S // 4
+SHIFT_ROWS = 112
 HALF = P // 2
 PAGES = 2
 AHEAD = 4
@@ -35,28 +36,33 @@ LINE = 4
 KB = 1024
 DIRECT = (0, 1)
 TURNED = (2, 3)
-VECTOR_COPIES = (9, 10, 11)
+INTERLEAVED = (2, 3, 1)
+VECTOR_COPIES = (0, 10, 11)
 
-PAGE_AT = (0, 8 * KB)
-W4_SCALES_AT = 224 * KB
-TAB_AT = (16 * KB, 208 * KB, 23 * KB)
-TAB_PLANE_AT = TAB_AT[0]
-WGS_AT = 36 * KB
+PAGE_AT = (227 * KB, 8 * KB)
+W4_SCALES_AT = 15 * KB + 512
+TAB_AT = (21 * KB, 208 * KB, 28 * KB)
+W4_PLANE0_AT = 40 * KB
+TAB_PLANE_AT = TAB_AT[0] + 6 * KB
+LAST_ORD_AT = TAB_AT[0] + 4 * KB
+WGS_FIRST_AT = LAST_ORD_AT - 512
+WGS_AT = 16 * KB
 W4_RAW_AT = (TAB_AT[1] - 4 * KB, TAB_AT[1] + 4 * KB)
 W4_ORD_AT = 46 * KB
+ORD_AT = (W4_ORD_AT, LAST_ORD_AT - KA * 2 * P * (PACK - 1), LAST_ORD_AT)
 W4_PLANES_AT = 42 * KB
 SHIFTED_AT = 52 * KB
-PICKED_AT = (57 * KB, 32 * KB, TAB_AT[1])
-TAB_SCALES_AT = PICKED_AT[1] + 3 * KB
+PICKED_AT = (57 * KB, 36 * KB, 66 * KB)
+TAB_SCALES_AT = 40 * KB
 H_AT = (76 * KB, 90 * KB, 98 * KB, 106 * KB, 114 * KB, 118 * KB, 122 * KB, 126 * KB)
 RACK_AT = (TAB_AT[1] + 7 * KB, TAB_AT[2], H_AT[0] - 6 * KB, H_AT[1] - 6 * KB, H_AT[2], H_AT[3], TAB_AT[1] + 7 * KB, TAB_AT[2])
 W2_RAW_AT = (H_AT[0] + 2 * KB, H_AT[1] + 2 * KB)
-W2_BF_AT = (H_AT[5], H_AT[6])
+W2_BF_AT = (H_AT[6], H_AT[7])
 SQUARE_AT = 130 * KB
 PAIRS_AT = (138 * KB, W4_ORD_AT)
-DIFF_AT = (W4_ORD_AT + KA * 2 * P * (SLOTS - 1) - 4 * KB, H_AT[4], W2_RAW_AT[0], W2_RAW_AT[1], H_AT[7], PAIRS_AT[0], PAIRS_AT[0] + 12 * KB, 227 * KB)
+DIFF_AT = (LAST_ORD_AT - 4 * KB, H_AT[4], H_AT[5], W2_RAW_AT[0], W2_RAW_AT[1], PAIRS_AT[0] + 8 * KB, PAIRS_AT[0] + 12 * KB, 0)
 LAST_SQUARE_AT = PAIRS_AT[0] + 10 * KB
-JOINED_AT = ((RACK_AT[4] + 4 * KB, RACK_AT[6], RACK_AT[4], RACK_AT[5]), (PAIRS_AT[0], PAIRS_AT[0] + 4 * KB, 154 * KB, 158 * KB))
+JOINED_AT = ((62 * KB, RACK_AT[6], RACK_AT[4], RACK_AT[5]), (PAIRS_AT[0], PAIRS_AT[0] + 4 * KB, 154 * KB, 158 * KB))
 Z_CODES_AT = ((PAIRS_AT[0] + 14 * KB, PAIRS_AT[1], PAIRS_AT[1] + 4 * KB, PAIRS_AT[1] + 8 * KB), tuple(164 * KB + 2 * KB * c for c in range(CHUNKS)))
 Z_SCALES_AT = (RACK_AT[3], 172 * KB)
 W2_CODES_AT = 174 * KB
@@ -89,23 +95,23 @@ def tile_list_pallet_slot_fit_kernel(tc, tab_words, tab_scales, offs, w4_words, 
             return laid.tile(shape, dtype, name=name, offset=at, align_bytes=64)
 
         tab_scales_raw = place("tab_scales_raw", [P, T], U8, TAB_SCALES_AT)
-        w4_scales_raw = place("w4_scales_raw", [P, KA * H], U8, W4_SCALES_AT)
+        w4_scales_raw = place("w4_scales_raw", [P, H], U8, W4_SCALES_AT)
         tab_shifted = place("tab_shifted", [P, (KA - 1) * S], U8, SHIFTED_AT)
         pages = [place("page%d" % j, [P, T2], F32, PAGE_AT[j]) for j in range(PAGES)]
+        w4_shifted = place("w4_shifted", [P, (KA - 1) * H], U8, W4_PLANES_AT + H)
         nc.gpsimd.memset(w4_scales_raw[:].bitcast(I32), 0)
-        for zeroed in (tab_scales_raw[:].bitcast(I32), pages[0][:]):
+        for zeroed in (tab_scales_raw[:].bitcast(I32), w4_shifted[:].bitcast(I32), pages[0][:]):
             words = zeroed.shape[1]
             for cols in (slice(0, words - 1), slice(words - 1, words)):
                 nc.vector.memset(zeroed[:, cols], 0)
-        nc.vector.memset(pages[1][:], 0.0)
 
         gain_t = keep.tile([P, RB, PACK], F32, name="gain_t")
         sharp_t = keep.tile([P, SLOTS], F32, name="sharp_t")
         neg_sharp = keep.tile([P, SLOTS], F32, name="neg_sharp")
         ln_gain = keep.tile([P, SLOTS], F32, name="ln_gain")
+
         nc.scalar.dma_start(gain_t[:], gain.rearrange("(b p i) -> p b i", b=RB, i=PACK))
         nc.scalar.dma_start(sharp_t[:].rearrange("p (b i) -> p b i", b=RB), sharp.rearrange("(b p i) -> p b i", b=RB, i=PACK))
-
         tab_win = {}
 
         def load_table(a):
@@ -134,18 +140,14 @@ def tile_list_pallet_slot_fit_kernel(tc, tab_words, tab_scales, offs, w4_words, 
             load_table_scales(32 * q - 8, slice(1, KA), q)
             load_table_scales(32 * q, slice(0, 1), q)
         for q in range(QUADRANTS):
-            nc.gpsimd.dma_start(
-                w4_scales_raw[32 * q : 32 * q + 4, :].bitcast(I32).rearrange("p (a n) -> p a n", a=KA),
-                w4_scales[:, 4 * q : 4 * q + 4, :].bitcast(I32).rearrange("a r n -> r a n"),
-            )
+            nc.gpsimd.dma_start(w4_scales_raw[32 * q : 32 * q + 4 * KA, :].bitcast(I32), w4_scales[:, 4 * q : 4 * q + 4, :].bitcast(I32))
         identity = keep.tile([P, P], F32, name="identity", align_bytes=64)
         make_identity(nc, identity[:])
         nc.scalar.activation(ln_gain[:], gain_t[:].rearrange("p b i -> p (b i)"), ACT.Ln)
         nc.scalar.mul(neg_sharp[:], sharp_t[:], -1.0)
 
         ord_slots = (range(0, PACK), range(PACK, SLOTS - 1), range(SLOTS - 1, SLOTS))
-        w4_ord = [place("w4_ord%d" % j, [P, KA * len(slots) * 2 * P], U8, W4_ORD_AT + KA * 2 * P * slots[0]) for j, slots in enumerate(ord_slots)]
-        w4_planes = [place("w4_planes%d" % b, [P, KA * BANK], U8, W4_PLANES_AT + KA * BANK * b) for b in range(RB)]
+        w4_ord = [place("w4_ord%d" % j, [P, KA * len(slots) * 2 * P], U8, ORD_AT[j]) for j, slots in enumerate(ord_slots)]
 
         def order_w4_words(a, j):
             b, i = divmod(ord_slots[j][0], PACK)
@@ -159,11 +161,6 @@ def tile_list_pallet_slot_fit_kernel(tc, tab_words, tab_scales, offs, w4_words, 
             j = [s in slots for slots in ord_slots].index(True)
             return w4_ord[j][:, cols_of(a * len(ord_slots[j]) + s - ord_slots[j][0], 2 * P)]
 
-        for b in range(RB):
-            nc.gpsimd.tensor_copy(
-                w4_planes[b][:].rearrange("p (a i m) -> p a i m", a=KA, i=PACK),
-                w4_scales_raw[:].rearrange("p (a b m i) -> p b a i m", a=KA, b=RB, i=PACK)[:, b],
-            )
         for a in range(KA):
             order_w4_words(a, 0)
 
@@ -174,18 +171,30 @@ def tile_list_pallet_slot_fit_kernel(tc, tab_words, tab_scales, offs, w4_words, 
         def gather_words(a, cols):
             nc.vector.tensor_copy(picked[a][:, cols], tab_win[a][:].bitcast(U32).indirect(offs_t[:, listed(cols)]))
 
+        def shift_scale_rows(queues, shifted, source, width):
+            for a, queue in zip(range(1, KA), queues):
+                queue.dma_start(shifted[0:SHIFT_ROWS, cols_of(a - 1, width)].bitcast(I32), source[4 * a : 4 * a + SHIFT_ROWS, :].bitcast(I32))
+            return [source[:]] + [shifted[:, cols_of(a, width)] for a in range(KA - 1)]
+
         gather_words(0, whole)
         tab_plane0 = place("tab_plane0", [P, S], U8, TAB_PLANE_AT)
         nc.vector.tensor_copy(tab_plane0[:], tab_scales_raw[:].indirect(offs_t[:]))
+        w4_plane0 = place("w4_plane0", [P, H], U8, W4_PLANE0_AT)
+        nc.vector.tensor_copy(
+            w4_plane0[:].rearrange("p (b i m) -> p b i m", b=RB, i=PACK),
+            w4_scales_raw[:].rearrange("p (b m i) -> p b i m", b=RB, i=PACK),
+        )
         load_table(2)
-        wgs_first = place("wgs_first", [P, QUARTER], F32, TAB_PLANE_AT + KB)
+        wgs_first = place("wgs_first", [P, QUARTER], F32, WGS_FIRST_AT)
         nc.sync.dma_start(wgs_first[:], wgs[:, first])
         for a in range(1, KA):
             for half, source in enumerate((4 * a, HALF - 12 + 4 * a)):
                 nc.sync.dma_start(tab_shifted[cols_of(half, HALF), cols_of(a - 1, S)].bitcast(I32), tab_plane0[source : source + HALF, :].bitcast(I32))
+        tab_planes = [tab_plane0[:]] + [tab_shifted[:, cols_of(a, S)] for a in range(KA - 1)]
+        w4_planes = shift_scale_rows((nc.scalar, nc.sync), w4_shifted, w4_plane0, H)
+        nc.gpsimd.memset(pages[1][:], 0.0)
         wgs_t = place("wgs_t", [P, S], F32, WGS_AT)
         nc.sync.dma_start(wgs_t[:], wgs)
-        tab_planes = [tab_plane0[:]] + [tab_shifted[:, cols_of(a, S)] for a in range(KA - 1)]
         gather_words(1, whole)
         load_w4(1)
         for cols in (first, second, upper):
@@ -208,7 +217,7 @@ def tile_list_pallet_slot_fit_kernel(tc, tab_words, tab_scales, offs, w4_words, 
             nc.tensor.matmul_mx(
                 out=banks[bank][:, 0 : cols.stop - cols.start],
                 lhsT=w4_codes(s, a).bitcast(FP4X4),
-                lhsT_scale=w4_planes[s // PACK][:, cols_of(a * PACK + s % PACK, P)],
+                lhsT_scale=w4_planes[a][:, cols_of(s, P)],
                 rhs=picked[a][:, cols].bitcast(FP8X4),
                 rhs_scale=tab_planes[a][:, cols],
                 start=(a == order[0]),
@@ -235,7 +244,7 @@ def tile_list_pallet_slot_fit_kernel(tc, tab_words, tab_scales, offs, w4_words, 
             h_pass(s, cols, bank, 0)
         for bank in (0, 1, 2, 4, 3, 5, 6, 7):
             s, cols = opening[bank]
-            order = (0, 1, 2) if s < 2 else (0, 2, 1)
+            order = (0, 1, 2) if cols == first else (0, 2, 1)
             for a in order[1:]:
                 h_pass(s, cols, bank, a, order)
             h_out(s, cols, bank)
@@ -260,7 +269,7 @@ def tile_list_pallet_slot_fit_kernel(tc, tab_words, tab_scales, offs, w4_words, 
 
         def open_pairs(b):
             for c in range(CHUNKS):
-                if b == 0 and c in TURNED:
+                if b == 0 and c in INTERLEAVED:
                     slotwise[c] = place("slotwise%d" % c, [P, PACK, BANK], BF16, PAIRS_AT[b] + 4 * KB * c)
                 else:
                     pairs[b, c] = place("pairs%d_%d" % (b, c), [P, 2, BANK, 2], BF16, PAIRS_AT[b] + 4 * KB * c)
@@ -365,12 +374,12 @@ def tile_list_pallet_slot_fit_kernel(tc, tab_words, tab_scales, offs, w4_words, 
                 scatter(s + 2, whole)
             if s + 4 < SLOTS:
                 load_rack(s + 4)
-            if s in (1, 2):
-                round_w2(s - 1)
-            if s in (4, 5):
-                interleave(TURNED[s - 4])
-            if s in (4, 6):
-                join(nc.gpsimd.tensor_copy, U32, 0, DIRECT[(s - 4) // 2])
+            if s in (2, 3):
+                round_w2(s - 2)
+            if s == PACK - 1:
+                join(nc.scalar.copy, U32, 0, 0)
+            if s >= PACK:
+                interleave(INTERLEAVED[s - PACK])
 
         open_slot(last)
         for c in DIRECT:
@@ -418,10 +427,10 @@ def tile_list_pallet_slot_fit_kernel(tc, tab_words, tab_scales, offs, w4_words, 
         quantise(0, 0)
         for c in DIRECT:
             chunk_product(c)
-        for j, (c, bank) in enumerate(TURN_BANKS.items()):
-            store(j)
+        for c, bank in TURN_BANKS.items():
             exp_turned(last, c, bank)
-        store(2)
+        for k in range(NT):
+            store(k)
         chunk_product(2)
         for k in range(NT, 2 * NT):
             store(k)

@@ -145,6 +145,8 @@ def tile_list_pallet_slot_fit_kernel(tc, tab_words, tab_scales, offs, w4_words, 
         make_identity(nc, identity[:])
         nc.scalar.activation(ln_gain[:], gain_t[:].rearrange("p b i -> p (b i)"), ACT.Ln)
         nc.scalar.mul(neg_sharp[:], sharp_t[:], -1.0)
+        warm = keep.tile([P, 1], F32, name="warm")
+        nc.scalar.activation(warm[:], neg_sharp[:, 0:1], ACT.Exp)
 
         ord_slots = (range(0, PACK), range(PACK, SLOTS - 1), range(SLOTS - 1, SLOTS))
         w4_ord = [place("w4_ord%d" % j, [P, KA * len(slots) * 2 * P], U8, ORD_AT[j]) for j, slots in enumerate(ord_slots)]

@@ -37,7 +37,7 @@ KB = 1024
 DIRECT = (0, 1)
 TURNED = (2, 3)
 INTERLEAVED = (2, 3, 1)
-VECTOR_COPIES = (0, 10, 11)
+VECTOR_COPIES = (9, 11)
 
 PAGE_AT = (227 * KB, 8 * KB)
 W4_SCALES_AT = 15 * KB + 512
@@ -61,12 +61,13 @@ W2_BF_AT = (H_AT[6], H_AT[7])
 SQUARE_AT = 130 * KB
 PAIRS_AT = (138 * KB, W4_ORD_AT)
 DIFF_AT = (LAST_ORD_AT - 4 * KB, H_AT[4], H_AT[5], W2_RAW_AT[0], W2_RAW_AT[1], PAIRS_AT[0] + 8 * KB, PAIRS_AT[0] + 12 * KB, 0)
-LAST_SQUARE_AT = PAIRS_AT[0] + 10 * KB
-JOINED_AT = ((62 * KB, RACK_AT[6], RACK_AT[4], RACK_AT[5]), (PAIRS_AT[0], PAIRS_AT[0] + 4 * KB, 154 * KB, 158 * KB))
-Z_CODES_AT = ((PAIRS_AT[0] + 14 * KB, PAIRS_AT[1], PAIRS_AT[1] + 4 * KB, PAIRS_AT[1] + 8 * KB), tuple(164 * KB + 2 * KB * c for c in range(CHUNKS)))
-Z_SCALES_AT = (RACK_AT[3], 172 * KB)
+LAST_SQUARE_AT = PAIRS_AT[0] + 8 * KB + 512
+LAST_TURNED_SQUARES_AT = (PAIRS_AT[0] + 13 * KB, PAIRS_AT[0] + 15 * KB)
+JOINED_AT = ((62 * KB, RACK_AT[6], RACK_AT[4], RACK_AT[5]), (PAIRS_AT[0], PAIRS_AT[0] + 4 * KB, 155 * KB, 159 * KB))
+Z_CODES_AT = ((RACK_AT[3] + 2 * KB, PAIRS_AT[1], PAIRS_AT[1] + 4 * KB, PAIRS_AT[1] + 8 * KB), tuple(164 * KB + 2 * KB * c for c in range(CHUNKS)))
+Z_SCALES_AT = ((LAST_SQUARE_AT + 4 * KB, RACK_AT[3], RACK_AT[3] + BANK, RACK_AT[3] + 2 * BANK), tuple(172 * KB + BANK * c for c in range(CHUNKS)))
 W2_CODES_AT = 174 * KB
-W2_SCALES_AT = RACK_AT[3] + 2 * KB
+W2_SCALES_AT = RACK_AT[7]
 RESULT_AT = 178 * KB
 TURN_BANKS = {2: 4, 3: 5}
 LATE_H_BANKS = {3: (0, 1), 4: (2, 3), 5: (6, 7), 6: (4, 5), 7: (0, 1)}
@@ -301,7 +302,7 @@ def tile_list_pallet_slot_fit_kernel(tc, tab_words, tab_scales, offs, w4_words, 
                         )
 
         def square_turned(s, c, bank):
-            at = SQUARE_AT + 2 * KB * TURNED.index(c)
+            at = LAST_TURNED_SQUARES_AT[TURNED.index(c)] if s == SLOTS - 1 else SQUARE_AT + 2 * KB * TURNED.index(c)
             squares[s, c] = place("square%d_%d" % (s, c), [P, BANK], F32, at)
             nc.scalar.activation(squares[s, c][:], banks[bank][:], ACT.Square)
             for block in range(BANK // P):
@@ -318,11 +319,13 @@ def tile_list_pallet_slot_fit_kernel(tc, tab_words, tab_scales, offs, w4_words, 
             for c in DIRECT:
                 difference(nc.gpsimd, s, cols_of(c, BANK))
             turned_sums(s)
-            for c, bank in TURN_BANKS.items():
-                square_turned(s, c, bank)
-            for c, (turned, bank) in zip(DIRECT, TURN_BANKS.items()):
-                square_direct(s, cols_of(c, BANK))
-                exp_turned(s, turned, bank)
+            (c2, bank2), (c3, bank3) = TURN_BANKS.items()
+            square_turned(s, c2, bank2)
+            square_direct(s, lower)
+            square_turned(s, c3, bank3)
+            exp_turned(s, c2, bank2)
+            square_direct(s, upper)
+            exp_turned(s, c3, bank3)
             for c in DIRECT:
                 exp_direct(s, c)
 
@@ -339,7 +342,7 @@ def tile_list_pallet_slot_fit_kernel(tc, tab_words, tab_scales, offs, w4_words, 
 
         def quantise(b, c):
             z_codes[b, c] = place("z_codes%d_%d" % (b, c), [P, BANK], U32, Z_CODES_AT[b][c])
-            z_scales[b, c] = place("z_scales%d_%d" % (b, c), [P, BANK], U8, Z_SCALES_AT[b] + BANK * c)
+            z_scales[b, c] = place("z_scales%d_%d" % (b, c), [P, BANK], U8, Z_SCALES_AT[b][c])
             nc.vector.quantize_mx(out=z_codes[b, c][:].bitcast(FP8X4), scales=z_scales[b, c][:], in_=joined[b, c][:])
 
         w2_bf = {}
@@ -388,16 +391,16 @@ def tile_list_pallet_slot_fit_kernel(tc, tab_words, tab_scales, offs, w4_words, 
             difference(nc.vector, last, cols_of(c, BANK))
         turned_sums(last)
         last_diff, diffs[last] = diffs[last], place("last_square", [P, S], F32, LAST_SQUARE_AT)
-        for c in DIRECT:
-            nc.scalar.activation(diffs[last][:, cols_of(c, BANK)], last_diff[:, cols_of(c, BANK)], ACT.Square)
         for c, (turned, bank) in zip(DIRECT, TURN_BANKS.items()):
-            exp_direct(last, c)
+            nc.scalar.activation(diffs[last][:, cols_of(c, BANK)], last_diff[:, cols_of(c, BANK)], ACT.Square)
             square_turned(last, turned, bank)
+            exp_direct(last, c)
         w2_codes = place("w2_codes", [P, RB * N], U32, W2_CODES_AT)
         w2_scales = place("w2_scales", [P, RB * N], U8, W2_SCALES_AT)
-        for k, rounded in w2_bf.items():
-            cols = cols_of(k, N)
-            nc.vector.quantize_mx(out=w2_codes[:, cols].bitcast(FP8X4), scales=w2_scales[:, cols], in_=rounded[:])
+
+        def quantise_w2(b):
+            cols = cols_of(b, N)
+            nc.vector.quantize_mx(out=w2_codes[:, cols].bitcast(FP8X4), scales=w2_scales[:, cols], in_=w2_bf[b][:])
 
         def out_pass(b, c):
             for t in range(NT):
@@ -422,20 +425,21 @@ def tile_list_pallet_slot_fit_kernel(tc, tab_words, tab_scales, offs, w4_words, 
             join(nc.vector.tensor_copy, I32, 1, c)
             if c > 0:
                 quantise(0, c)
+                out_pass(0, c)
             quantise(1, c)
-            for b in range(RB):
-                out_pass(b, c)
+            out_pass(1, c)
 
+        quantise_w2(0)
         quantise(0, 0)
-        for c in DIRECT:
-            chunk_product(c)
+        quantise_w2(1)
+        out_pass(0, 0)
+        chunk_product(0)
+        chunk_product(1)
         for c, bank in TURN_BANKS.items():
             exp_turned(last, c, bank)
-        for k in range(NT):
-            store(k)
-        chunk_product(2)
-        for k in range(NT, 2 * NT):
-            store(k)
-        chunk_product(3)
+        for c in TURNED:
+            for k in range(NT * (c - 2), NT * (c - 1)):
+                store(k)
+            chunk_product(c)
         for k in range(2 * NT, CHUNKS * NT):
             store(k)

@@ -28,7 +28,7 @@ BANKS = 8
 CHUNKS = T2 // BANK
 NT = N // P
 QUARTER = S // 4
-SHIFT_ROWS = 112
+PAGE_SPLIT = 1536
 HALF = P // 2
 PAGES = 2
 AHEAD = 4
@@ -40,20 +40,19 @@ INTERLEAVED = (2, 3, 1)
 VECTOR_COPIES = (9, 11)
 
 PAGE_AT = (227 * KB, 8 * KB)
-W4_SCALES_AT = 15 * KB + 512
+W4_SCALES_AT = 16 * KB
 TAB_AT = (21 * KB, 208 * KB, 28 * KB)
-W4_PLANE0_AT = 40 * KB
 TAB_PLANE_AT = TAB_AT[0] + 6 * KB
 LAST_ORD_AT = TAB_AT[0] + 4 * KB
 WGS_FIRST_AT = LAST_ORD_AT - 512
-WGS_AT = 16 * KB
+WGS_AT = 54 * KB
 W4_RAW_AT = (TAB_AT[1] - 4 * KB, TAB_AT[1] + 4 * KB)
 W4_ORD_AT = 46 * KB
 ORD_AT = (W4_ORD_AT, LAST_ORD_AT - KA * 2 * P * (PACK - 1), LAST_ORD_AT)
 W4_PLANES_AT = 42 * KB
 SHIFTED_AT = 52 * KB
-PICKED_AT = (57 * KB, 36 * KB, 66 * KB)
-TAB_SCALES_AT = 40 * KB
+PICKED_AT = (58 * KB, 36 * KB, 66 * KB)
+TAB_SCALES_AT = WGS_AT
 H_AT = (76 * KB, 90 * KB, 98 * KB, 106 * KB, 114 * KB, 118 * KB, 122 * KB, 126 * KB)
 RACK_AT = (TAB_AT[1] + 7 * KB, TAB_AT[2], H_AT[0] - 6 * KB, H_AT[1] - 6 * KB, H_AT[2], H_AT[3], TAB_AT[1] + 7 * KB, TAB_AT[2])
 W2_RAW_AT = (H_AT[0] + 2 * KB, H_AT[1] + 2 * KB)
@@ -96,12 +95,11 @@ def tile_list_pallet_slot_fit_kernel(tc, tab_words, tab_scales, offs, w4_words, 
             return laid.tile(shape, dtype, name=name, offset=at, align_bytes=64)
 
         tab_scales_raw = place("tab_scales_raw", [P, T], U8, TAB_SCALES_AT)
-        w4_scales_raw = place("w4_scales_raw", [P, H], U8, W4_SCALES_AT)
+        w4_scales_raw = place("w4_scales_raw", [P, KA * H], U8, W4_SCALES_AT)
         tab_shifted = place("tab_shifted", [P, (KA - 1) * S], U8, SHIFTED_AT)
         pages = [place("page%d" % j, [P, T2], F32, PAGE_AT[j]) for j in range(PAGES)]
-        w4_shifted = place("w4_shifted", [P, (KA - 1) * H], U8, W4_PLANES_AT + H)
         nc.gpsimd.memset(w4_scales_raw[:].bitcast(I32), 0)
-        for zeroed in (tab_scales_raw[:].bitcast(I32), w4_shifted[:].bitcast(I32), pages[0][:]):
+        for zeroed in (tab_scales_raw[:].bitcast(I32), pages[0][:], pages[1][:, 0:PAGE_SPLIT]):
             words = zeroed.shape[1]
             for cols in (slice(0, words - 1), slice(words - 1, words)):
                 nc.vector.memset(zeroed[:, cols], 0)
@@ -141,9 +139,13 @@ def tile_list_pallet_slot_fit_kernel(tc, tab_words, tab_scales, offs, w4_words, 
             load_table_scales(32 * q - 8, slice(1, KA), q)
             load_table_scales(32 * q, slice(0, 1), q)
         for q in range(QUADRANTS):
-            nc.gpsimd.dma_start(w4_scales_raw[32 * q : 32 * q + 4 * KA, :].bitcast(I32), w4_scales[:, 4 * q : 4 * q + 4, :].bitcast(I32))
+            nc.gpsimd.dma_start(
+                w4_scales_raw[32 * q : 32 * q + 4, :].bitcast(I32).rearrange("p (a n) -> p a n", a=KA),
+                w4_scales[:, 4 * q : 4 * q + 4, :].bitcast(I32).rearrange("a r n -> r a n"),
+            )
         identity = keep.tile([P, P], F32, name="identity", align_bytes=64)
         make_identity(nc, identity[:])
+        nc.gpsimd.memset(pages[1][:, PAGE_SPLIT:T2], 0.0)
         nc.scalar.activation(ln_gain[:], gain_t[:].rearrange("p b i -> p (b i)"), ACT.Ln)
         nc.scalar.mul(neg_sharp[:], sharp_t[:], -1.0)
         warm = keep.tile([P, 1], F32, name="warm")
@@ -167,6 +169,13 @@ def tile_list_pallet_slot_fit_kernel(tc, tab_words, tab_scales, offs, w4_words, 
         for a in range(KA):
             order_w4_words(a, 0)
 
+        w4_planes = [place("w4_planes%d" % b, [P, KA * BANK], U8, W4_PLANES_AT + KA * BANK * b) for b in range(RB)]
+        for b in range(RB):
+            nc.gpsimd.tensor_copy(
+                w4_planes[b][:].rearrange("p (a i m) -> p a i m", a=KA, i=PACK),
+                w4_scales_raw[:].rearrange("p (a b m i) -> p b a i m", a=KA, b=RB, i=PACK)[:, b],
+            )
+
         picked = [place("picked%d" % a, [P, S], U32, PICKED_AT[a]) for a in range(KA)]
         first, second, upper = slice(0, QUARTER), slice(QUARTER, BANK), slice(BANK, S)
         lower, rest, whole = slice(0, BANK), slice(QUARTER, S), slice(0, S)
@@ -174,19 +183,9 @@ def tile_list_pallet_slot_fit_kernel(tc, tab_words, tab_scales, offs, w4_words, 
         def gather_words(a, cols):
             nc.vector.tensor_copy(picked[a][:, cols], tab_win[a][:].bitcast(U32).indirect(offs_t[:, listed(cols)]))
 
-        def shift_scale_rows(queues, shifted, source, width):
-            for a, queue in zip(range(1, KA), queues):
-                queue.dma_start(shifted[0:SHIFT_ROWS, cols_of(a - 1, width)].bitcast(I32), source[4 * a : 4 * a + SHIFT_ROWS, :].bitcast(I32))
-            return [source[:]] + [shifted[:, cols_of(a, width)] for a in range(KA - 1)]
-
         gather_words(0, whole)
         tab_plane0 = place("tab_plane0", [P, S], U8, TAB_PLANE_AT)
         nc.vector.tensor_copy(tab_plane0[:], tab_scales_raw[:].indirect(offs_t[:]))
-        w4_plane0 = place("w4_plane0", [P, H], U8, W4_PLANE0_AT)
-        nc.vector.tensor_copy(
-            w4_plane0[:].rearrange("p (b i m) -> p b i m", b=RB, i=PACK),
-            w4_scales_raw[:].rearrange("p (b m i) -> p b i m", b=RB, i=PACK),
-        )
         load_table(2)
         wgs_first = place("wgs_first", [P, QUARTER], F32, WGS_FIRST_AT)
         nc.sync.dma_start(wgs_first[:], wgs[:, first])
@@ -194,8 +193,6 @@ def tile_list_pallet_slot_fit_kernel(tc, tab_words, tab_scales, offs, w4_words, 
             for half, source in enumerate((4 * a, HALF - 12 + 4 * a)):
                 nc.sync.dma_start(tab_shifted[cols_of(half, HALF), cols_of(a - 1, S)].bitcast(I32), tab_plane0[source : source + HALF, :].bitcast(I32))
         tab_planes = [tab_plane0[:]] + [tab_shifted[:, cols_of(a, S)] for a in range(KA - 1)]
-        w4_planes = shift_scale_rows((nc.scalar, nc.sync), w4_shifted, w4_plane0, H)
-        nc.gpsimd.memset(pages[1][:], 0.0)
         wgs_t = place("wgs_t", [P, S], F32, WGS_AT)
         nc.sync.dma_start(wgs_t[:], wgs)
         gather_words(1, whole)
@@ -220,7 +217,7 @@ def tile_list_pallet_slot_fit_kernel(tc, tab_words, tab_scales, offs, w4_words, 
             nc.tensor.matmul_mx(
                 out=banks[bank][:, 0 : cols.stop - cols.start],
                 lhsT=w4_codes(s, a).bitcast(FP4X4),
-                lhsT_scale=w4_planes[a][:, cols_of(s, P)],
+                lhsT_scale=w4_planes[s // PACK][:, cols_of(a * PACK + s % PACK, P)],
                 rhs=picked[a][:, cols].bitcast(FP8X4),
                 rhs_scale=tab_planes[a][:, cols],
                 start=(a == order[0]),

@@ -31,6 +31,7 @@ QUARTER = S // 4
 PAGE_SPLIT = 1536
 HALF = P // 2
 PAGES = 2
+EARLY_GROUPS = 5
 AHEAD = 4
 LINE = 4
 KB = 1024
@@ -240,12 +241,13 @@ def tile_list_pallet_slot_fit_kernel(tc, tab_words, tab_scales, offs, w4_words, 
             nc.vector.tensor_copy(pages[s % PAGES][:].indirect(offs2_t[:, listed(cols)]), weighted[s][:, cols])
 
         opening = [(0, first), (1, first), (0, second), (1, second), (0, upper), (1, upper), (2, lower), (2, upper)]
-        for bank, (s, cols) in enumerate(opening):
+        early = opening[:EARLY_GROUPS]
+        for bank, (s, cols) in enumerate(early):
             h_pass(s, cols, bank, 0)
         for bank in (0, 1, 2, 4, 3, 5, 6, 7):
             s, cols = opening[bank]
-            order = (0, 1, 2) if cols == first else (0, 2, 1)
-            for a in order[1:]:
+            order = (0, 1, 2) if cols == first else (0, 2, 1) if (s, cols) in early else (2, 0, 1)
+            for a in order[1:] if (s, cols) in early else order:
                 h_pass(s, cols, bank, a, order)
             h_out(s, cols, bank)
         for cols in (first, rest):

@@ -56,11 +56,11 @@ PICKED_AT = (58 * KB, 36 * KB, 66 * KB)
 TAB_SCALES_AT = WGS_AT
 H_AT = (76 * KB, 90 * KB, 98 * KB, 106 * KB, 114 * KB, 118 * KB, 122 * KB, 126 * KB)
 RACK_AT = (TAB_AT[1] + 7 * KB, TAB_AT[2], H_AT[0] - 6 * KB, H_AT[1] - 6 * KB, H_AT[2], H_AT[3], TAB_AT[1] + 7 * KB, TAB_AT[2])
-W2_RAW_AT = (H_AT[0] + 2 * KB, H_AT[1] + 2 * KB)
-W2_BF_AT = (H_AT[6], H_AT[7])
+W2_RAW_AT = (TAB_AT[1] - 2 * KB, H_AT[1] + 2 * KB)
+W2_BF_AT = (H_AT[0] + 4 * KB, H_AT[7])
 SQUARE_AT = 130 * KB
 PAIRS_AT = (138 * KB, W4_ORD_AT)
-DIFF_AT = (LAST_ORD_AT - 4 * KB, H_AT[4], H_AT[5], W2_RAW_AT[0], W2_RAW_AT[1], PAIRS_AT[0] + 8 * KB, PAIRS_AT[0] + 12 * KB, 0)
+DIFF_AT = (LAST_ORD_AT - 4 * KB, H_AT[4], H_AT[5], H_AT[6], W2_RAW_AT[1], PAIRS_AT[0] + 8 * KB, PAIRS_AT[0] + 12 * KB, 0)
 LAST_SQUARE_AT = PAIRS_AT[0] + 8 * KB + 512
 LAST_TURNED_SQUARES_AT = (PAIRS_AT[0] + 13 * KB, PAIRS_AT[0] + 15 * KB)
 JOINED_AT = ((62 * KB, RACK_AT[6], RACK_AT[4], RACK_AT[5]), (PAIRS_AT[0], PAIRS_AT[0] + 4 * KB, 155 * KB, 159 * KB))
@@ -208,6 +208,13 @@ def tile_list_pallet_slot_fit_kernel(tc, tab_words, tab_scales, offs, w4_words, 
             racks[s] = place("rack%d" % s, [P, T2], F32, RACK_AT[s])
             nc.sync.dma_start(racks[s][:], rack_rows[s // PACK, s % PACK])
 
+        w2_raw = {}
+
+        def load_w2(b):
+            w2_raw[b] = place("w2_raw%d" % b, [P, PACK, N], F32, W2_RAW_AT[b])
+            nc.sync.dma_start(w2_raw[b][:].rearrange("p i n -> p (i n)"), w2.rearrange("(b p i) n -> b p (i n)", b=RB, i=PACK)[b])
+
+        load_w2(0)
         load_rack(0)
         load_rack(1)
 
@@ -257,8 +264,11 @@ def tile_list_pallet_slot_fit_kernel(tc, tab_words, tab_scales, offs, w4_words, 
         for j in range(1, len(ord_slots)):
             for a in range(KA):
                 order_w4_words(a, j)
-        for s in range(3, SLOTS - 1):
+        w2_bf = {0: place("w2_bf0", [P, N * PACK], BF16, W2_BF_AT[0])}
+        for t, s in enumerate(range(3, SLOTS - 1)):
             h_slot(s)
+            if t < NT:
+                nc.scalar.copy(w2_bf[0][:, cols_of(t, P * PACK)].rearrange("p (n i) -> p n i", i=PACK), w2_raw[0][:, :, cols_of(t, P)].rearrange("p i n -> p n i"))
         weigh(3, whole)
 
         pairs = {}
@@ -344,13 +354,6 @@ def tile_list_pallet_slot_fit_kernel(tc, tab_words, tab_scales, offs, w4_words, 
             z_scales[b, c] = place("z_scales%d_%d" % (b, c), [P, BANK], U8, Z_SCALES_AT[b][c])
             nc.vector.quantize_mx(out=z_codes[b, c][:].bitcast(FP8X4), scales=z_scales[b, c][:], in_=joined[b, c][:])
 
-        w2_bf = {}
-
-        w2_raw = {}
-
-        def load_w2(b):
-            w2_raw[b] = place("w2_raw%d" % b, [P, PACK, N], F32, W2_RAW_AT[b])
-            nc.sync.dma_start(w2_raw[b][:].rearrange("p i n -> p (i n)"), w2.rearrange("(b p i) n -> b p (i n)", b=RB, i=PACK)[b])
 
         def round_w2(b):
             w2_bf[b] = place("w2_bf%d" % b, [P, N * PACK], BF16, W2_BF_AT[b])
@@ -359,9 +362,9 @@ def tile_list_pallet_slot_fit_kernel(tc, tab_words, tab_scales, offs, w4_words, 
         for cols in (first, rest):
             for s in range(2):
                 scatter(s, cols)
-        for b in range(RB):
-            load_rack(2 + b)
-            load_w2(b)
+        load_rack(2)
+        load_rack(3)
+        load_w2(1)
         open_pairs(0)
         last = SLOTS - 1
         for s in range(last):
@@ -378,8 +381,8 @@ def tile_list_pallet_slot_fit_kernel(tc, tab_words, tab_scales, offs, w4_words, 
                 scatter(s + 2, whole)
             if s + 4 < SLOTS:
                 load_rack(s + 4)
-            if s in (2, 3):
-                round_w2(s - 2)
+            if s == 3:
+                round_w2(1)
             if s == PACK - 1:
                 join(nc.scalar.copy, U32, 0, 0)
             if s >= PACK:

@@ -38,7 +38,7 @@ KB = 1024
 DIRECT = (0, 1)
 TURNED = (2, 3)
 INTERLEAVED = (2, 3, 1)
-VECTOR_COPIES = (9, 11)
+VECTOR_COPIES = (3, 9, 11)
 
 PAGE_AT = (227 * KB, 8 * KB)
 W4_SCALES_AT = 16 * KB
@@ -71,7 +71,7 @@ W2_SCALES_AT = RACK_AT[7]
 RESULT_AT = 178 * KB
 TURN_BANKS = {2: 4, 3: 5}
 LATE_H_BANKS = {3: (0, 1), 4: (2, 3), 5: (6, 7), 6: (4, 5), 7: (0, 1)}
-OUT_BANKS = (0, 1, 2, 3, 6, 7, 4, 0, 1, 5, 2, 3)
+OUT_BANKS = (0, 1, 2, 3, 6, 7, 4, 5, 1, 0, 2, 3)
 
 
 def tile_list_pallet_slot_fit_kernel(tc, tab_words, tab_scales, offs, w4_words, w4_scales, offs2, wgs, rack, sharp, gain, w2, out):
@@ -310,12 +310,16 @@ def tile_list_pallet_slot_fit_kernel(tc, tab_words, tab_scales, offs, w4_words, 
                             start=(k == 0 and j == 0), stop=(k == 1 and j == blocks - 1), is_transpose=True,
                         )
 
-        def square_turned(s, c, bank):
+        def turn_back(s, c, bank):
+            for block in range(BANK // P):
+                nc.tensor.transpose(banks[bank][:, cols_of(block, P)], squares[s, c][:, cols_of(block, P)], identity[:])
+
+        def square_turned(s, c, bank, back=True):
             at = LAST_TURNED_SQUARES_AT[TURNED.index(c)] if s == SLOTS - 1 else SQUARE_AT + 2 * KB * TURNED.index(c)
             squares[s, c] = place("square%d_%d" % (s, c), [P, BANK], F32, at)
             nc.scalar.activation(squares[s, c][:], banks[bank][:], ACT.Square)
-            for block in range(BANK // P):
-                nc.tensor.transpose(banks[bank][:, cols_of(block, P)], squares[s, c][:, cols_of(block, P)], identity[:])
+            if back:
+                turn_back(s, c, bank)
 
         def exp_turned(s, c, bank):
             exp_to_z(s, c, banks[bank][:])
@@ -395,7 +399,7 @@ def tile_list_pallet_slot_fit_kernel(tc, tab_words, tab_scales, offs, w4_words, 
         last_diff, diffs[last] = diffs[last], place("last_square", [P, S], F32, LAST_SQUARE_AT)
         for c, (turned, bank) in zip(DIRECT, TURN_BANKS.items()):
             nc.scalar.activation(diffs[last][:, cols_of(c, BANK)], last_diff[:, cols_of(c, BANK)], ACT.Square)
-            square_turned(last, turned, bank)
+            square_turned(last, turned, bank, back=(c == 0))
             exp_direct(last, c)
         w2_codes = place("w2_codes", [P, RB * N], U32, W2_CODES_AT)
         w2_scales = place("w2_scales", [P, RB * N], U8, W2_SCALES_AT)
@@ -437,11 +441,15 @@ def tile_list_pallet_slot_fit_kernel(tc, tab_words, tab_scales, offs, w4_words, 
         out_pass(0, 0)
         chunk_product(0)
         chunk_product(1)
-        for c, bank in TURN_BANKS.items():
-            exp_turned(last, c, bank)
-        for c in TURNED:
-            for k in range(NT * (c - 2), NT * (c - 1)):
-                store(k)
-            chunk_product(c)
+        exp_turned(last, TURNED[0], TURN_BANKS[TURNED[0]])
+        store(0)
+        turn_back(last, TURNED[1], OUT_BANKS[0])
+        for k in range(1, NT):
+            store(k)
+        exp_turned(last, TURNED[1], OUT_BANKS[0])
+        chunk_product(2)
+        for k in range(NT, 2 * NT):
+            store(k)
+        chunk_product(3)
         for k in range(2 * NT, CHUNKS * NT):
             store(k)

@@ -18,6 +18,7 @@ ACT = mybir.ActivationFunctionType
 ALU = mybir.AluOpType
 
 P = 128
+HALF = P // 2
 PACK = 4
 QUADRANTS = 4
 KA = K // (P * PACK)
@@ -25,53 +26,58 @@ RB = H // (P * PACK)
 SLOTS = RB * PACK
 BANK = 512
 BANKS = 8
-CHUNKS = T2 // BANK
 NT = N // P
-QUARTER = S // 4
-PAGE_SPLIT = 1536
-HALF = P // 2
-PAGES = 2
-EARLY_GROUPS = 5
-AHEAD = 4
 LINE = 4
 KB = 1024
-DIRECT = (0, 1)
-TURNED = (2, 3)
-INTERLEAVED = (2, 3, 1)
-VECTOR_COPIES = (3, 9, 11)
+EDGE = 64
 
-PAGE_AT = (227 * KB, 8 * KB)
-W4_SCALES_AT = 16 * KB
-TAB_AT = (21 * KB, 208 * KB, 28 * KB)
-TAB_PLANE_AT = TAB_AT[0] + 6 * KB
-LAST_ORD_AT = TAB_AT[0] + 4 * KB
-WGS_FIRST_AT = LAST_ORD_AT - 512
-WGS_AT = 54 * KB
-W4_RAW_AT = (TAB_AT[1] - 4 * KB, TAB_AT[1] + 4 * KB)
-W4_ORD_AT = 46 * KB
-ORD_AT = (W4_ORD_AT, LAST_ORD_AT - KA * 2 * P * (PACK - 1), LAST_ORD_AT)
-W4_PLANES_AT = 42 * KB
-SHIFTED_AT = 52 * KB
-PICKED_AT = (58 * KB, 36 * KB, 66 * KB)
-TAB_SCALES_AT = WGS_AT
-H_AT = (76 * KB, 90 * KB, 98 * KB, 106 * KB, 114 * KB, 118 * KB, 122 * KB, 126 * KB)
-RACK_AT = (TAB_AT[1] + 7 * KB, TAB_AT[2], H_AT[0] - 6 * KB, H_AT[1] - 6 * KB, H_AT[2], H_AT[3], TAB_AT[1] + 7 * KB, TAB_AT[2])
-W2_RAW_AT = (TAB_AT[1] - 2 * KB, H_AT[1] + 2 * KB)
-W2_BF_AT = (H_AT[0] + 4 * KB, H_AT[7])
-SQUARE_AT = 130 * KB
-PAIRS_AT = (138 * KB, W4_ORD_AT)
-DIFF_AT = (LAST_ORD_AT - 4 * KB, H_AT[4], H_AT[5], H_AT[6], W2_RAW_AT[1], PAIRS_AT[0] + 8 * KB, PAIRS_AT[0] + 12 * KB, 0)
-LAST_SQUARE_AT = PAIRS_AT[0] + 8 * KB + 512
-LAST_TURNED_SQUARES_AT = (PAIRS_AT[0] + 13 * KB, PAIRS_AT[0] + 15 * KB)
-JOINED_AT = ((62 * KB, RACK_AT[6], RACK_AT[4], RACK_AT[5]), (PAIRS_AT[0], PAIRS_AT[0] + 4 * KB, 155 * KB, 159 * KB))
-Z_CODES_AT = ((RACK_AT[3] + 2 * KB, PAIRS_AT[1], PAIRS_AT[1] + 4 * KB, PAIRS_AT[1] + 8 * KB), tuple(164 * KB + 2 * KB * c for c in range(CHUNKS)))
-Z_SCALES_AT = ((LAST_SQUARE_AT + 4 * KB, RACK_AT[3], RACK_AT[3] + BANK, RACK_AT[3] + 2 * BANK), tuple(172 * KB + BANK * c for c in range(CHUNKS)))
-W2_CODES_AT = 174 * KB
-W2_SCALES_AT = RACK_AT[7]
-RESULT_AT = 178 * KB
-TURN_BANKS = {2: 4, 3: 5}
-LATE_H_BANKS = {3: (0, 1), 4: (2, 3), 5: (6, 7), 6: (4, 5), 7: (0, 1)}
-OUT_BANKS = (0, 1, 2, 3, 6, 7, 4, 5, 1, 0, 2, 3)
+PIECES = (slice(0, 128), slice(128, 512), slice(512, 1024))
+CHUNKS = {"A": slice(0, 256), "E": slice(256, 512), "B": slice(512, 1024), "C": slice(1024, 1536), "D": slice(1536, 2048)}
+SPANS = {"A": CHUNKS["A"], "E": CHUNKS["E"], "B": CHUNKS["B"], "C": CHUNKS["C"], "D": slice(CHUNKS["D"].start, T2)}
+CUTS = (SPANS, CHUNKS)
+SPAN_OF = {"A": "A", "E": "E", "B": "B", "C": "C", "D": "D", "F": "D"}
+TURN_BANKS = {s: {"C": 6, "D": 7} if s else {"C": 4, "D": 5} for s in range(SLOTS)}
+INTERLEAVED = {4: ("B",), 5: ("C",), 6: ("D",)}
+SPLIT_FROM = 4
+SCALE_ROWS = (40, 72)
+H_BANKS = {3: (0, 1), 4: (2, 3), 5: (4, 5), 6: (6, 7), 7: (0, 1)}
+OUT_BANKS = {"B": (0, 1, 2), "A": (3, 6, 7), "C": (4, 5, 3), "D": (6, 7, 0), "E": (1, 2, 4)}
+
+PAGE_AT = (0, 8 * KB)
+SQUARE_AT = 150 * KB
+TAB_PLANES_AT = (16 * KB, 17 * KB, 18 * KB)
+W4_PLANES_AT = 19 * KB
+W4_ORD_AT = (22 * KB, SQUARE_AT + KB + 512)
+W4_SCALES_AT = 98 * KB
+PICKED_SCALES_AT = 33 * KB
+TAB_AT = (50 * KB, 58 * KB, 66 * KB)
+TAB_SCALES_AT = TAB_AT[2] + 6 * KB
+WGS_FIRST_AT = TAB_AT[0] + EDGE - 2 * KB
+W4_RAW_AT = (25 * KB, TAB_AT[1] + 4 * KB + EDGE)
+WGS_AT = TAB_AT[1] + EDGE
+W2_PARTS = ((0, slice(0, N)), (1, slice(0, P)), (1, slice(P, N)))
+W2_RAW_AT = (TAB_AT[1] + EDGE - 6 * KB, PICKED_SCALES_AT + 512, W4_ORD_AT[0] - 512)
+PIECE_AT = ((SQUARE_AT + 2 * KB + 512, 234 * KB + 512, 75 * KB), (85 * KB + 512, 79 * KB, 77 * KB))
+H_AT = {2: 94 * KB, 3: 90 * KB, 4: 102 * KB, 5: 106 * KB, 6: 110 * KB, 7: 114 * KB}
+PICKED_AT = 127 * KB
+RACK_AT = (PICKED_SCALES_AT + 512 - 8 * KB, TAB_AT[2] - KB + EDGE, WGS_FIRST_AT + EDGE - 8 * KB, PICKED_AT - 8 * KB + EDGE, PICKED_AT + EDGE, PICKED_AT + 8 * KB + EDGE, 75 * KB, 86 * KB)
+WEIGHTED_AT = {2: RACK_AT[7], 7: H_AT[6]}
+W2_BF_AT = (236 * KB - 256, H_AT[2], H_AT[5])
+PAIRS_AT = (173 * KB, 189 * KB)
+DIFF_AT = (W2_RAW_AT[1] + KB + 512, H_AT[3], H_AT[4], W2_RAW_AT[2], H_AT[7], PAIRS_AT[0] + 4 * KB, PAIRS_AT[0] + 8 * KB, H_AT[3])
+JOINED0_AT = {"A": 230 * KB + 512, "B": RACK_AT[4], "C": RACK_AT[5], "E": 233 * KB - 512, "D": RACK_AT[6]}
+JOINED1_AT = 205 * KB
+Z_CODES_AT = (16 * KB, 221 * KB)
+Z_SCALES1_AT = 24 * KB
+W2_CODES_AT = WEIGHTED_AT[7]
+RESULT_AT = TAB_AT[0]
+LOW_SQUARE_AT = (SQUARE_AT, SQUARE_AT + 2 * KB - EDGE)
+HIGH_SQUARE_AT = (SQUARE_AT + 4 * KB - 2 * EDGE, SQUARE_AT - 2 * KB + EDGE)
+FIRST_SQUARE_AT = {"C": TAB_PLANES_AT[0], "D": TAB_PLANES_AT[2]}
+LAST_SQUARE_AT = {"A": SQUARE_AT + 3 * KB - EDGE, "B": SQUARE_AT + 4 * KB - EDGE, "C": SQUARE_AT + 6 * KB - EDGE, "D": 166 * KB, "E": 169 * KB}
+W2_SCALES_AT = DIFF_AT[6] + 2 * KB + EDGE
+LAST_DIFF_AT = {"A": H_AT[4], "B": H_AT[4] + KB, "C": W2_SCALES_AT - 2 * KB, "D": LAST_SQUARE_AT["A"] - 2 * KB + EDGE, "E": LAST_SQUARE_AT["C"] + 2 * KB - EDGE}
+Z_SCALES0_AT = {"B": W2_SCALES_AT + KB, "A": W2_SCALES_AT + KB + BANK, "C": LAST_SQUARE_AT["B"], "D": PAIRS_AT[1] + 8 * KB, "E": LAST_SQUARE_AT["D"]}
 
 
 def tile_list_pallet_slot_fit_kernel(tc, tab_words, tab_scales, offs, w4_words, w4_scales, offs2, wgs, rack, sharp, gain, w2, out):
@@ -92,84 +98,76 @@ def tile_list_pallet_slot_fit_kernel(tc, tab_words, tab_scales, offs, w4_words, 
         def listed(cols):
             return slice(cols.start // 16, cols.stop // 16)
 
+        def width(cols):
+            return cols.stop - cols.start
+
         def place(name, shape, dtype, at):
             return laid.tile(shape, dtype, name=name, offset=at, align_bytes=64)
 
+        def zero(engine, words):
+            count = words.shape[1]
+            for cols in (slice(0, count - 1), slice(count - 1, count)):
+                engine.memset(words[:, cols], 0)
+
+        lower, upper, whole = slice(0, BANK), slice(BANK, S), slice(0, S)
+
+        tab_win = [place("tab_win%d" % a, [P, T], I32, TAB_AT[a]) for a in range(KA)]
         tab_scales_raw = place("tab_scales_raw", [P, T], U8, TAB_SCALES_AT)
         w4_scales_raw = place("w4_scales_raw", [P, KA * H], U8, W4_SCALES_AT)
-        tab_shifted = place("tab_shifted", [P, (KA - 1) * S], U8, SHIFTED_AT)
-        pages = [place("page%d" % j, [P, T2], F32, PAGE_AT[j]) for j in range(PAGES)]
-        nc.gpsimd.memset(w4_scales_raw[:].bitcast(I32), 0)
-        for zeroed in (tab_scales_raw[:].bitcast(I32), pages[0][:], pages[1][:, 0:PAGE_SPLIT]):
-            words = zeroed.shape[1]
-            for cols in (slice(0, words - 1), slice(words - 1, words)):
-                nc.vector.memset(zeroed[:, cols], 0)
-
+        pages = [place("page%d" % j, [P, T2], F32, PAGE_AT[j]) for j in range(2)]
         gain_t = keep.tile([P, RB, PACK], F32, name="gain_t")
         sharp_t = keep.tile([P, SLOTS], F32, name="sharp_t")
         neg_sharp = keep.tile([P, SLOTS], F32, name="neg_sharp")
         ln_gain = keep.tile([P, SLOTS], F32, name="ln_gain")
-
-        nc.scalar.dma_start(gain_t[:], gain.rearrange("(b p i) -> p b i", b=RB, i=PACK))
-        nc.scalar.dma_start(sharp_t[:].rearrange("p (b i) -> p b i", b=RB), sharp.rearrange("(b p i) -> p b i", b=RB, i=PACK))
-        tab_win = {}
+        identity = keep.tile([P, P], F32, name="identity", align_bytes=64)
+        w4_raw = {}
 
         def load_table(a):
-            tab_win[a] = place("tab_win%d" % a, [P, T], I32, TAB_AT[a])
             nc.sync.dma_start(tab_win[a][:], tab_words[a].rearrange("p t i -> p (t i)").bitcast(I32))
-
-        nc.sync.dma_start(offs_t[:], offs)
-        nc.sync.dma_start(offs2_t[:], offs2)
-        load_table(0)
-        w4_raw = {}
 
         def load_w4(b):
             w4_raw[b] = place("w4_raw%d" % b, [P, KA, H], U8, W4_RAW_AT[b])
             nc.sync.dma_start(w4_raw[b][:].bitcast(I32), w4_words[:, :, cols_of(b, H)].rearrange("a p n -> p a n").bitcast(I32))
 
+        nc.sync.dma_start(offs_t[:], offs)
+        nc.scalar.dma_start(gain_t[:], gain.rearrange("(b p i) -> p b i", b=RB, i=PACK))
+        nc.scalar.dma_start(sharp_t[:].rearrange("p (b i) -> p b i", b=RB), sharp.rearrange("(b p i) -> p b i", b=RB, i=PACK))
+        scale_rows = tab_scales.bitcast(I32).rearrange("a (h e r) t -> e (a h) r t", h=2, e=2)
+        for e, row in enumerate(SCALE_ROWS):
+            nc.scalar.dma_start(tab_scales_raw[row : row + 8 * KA, :].bitcast(I32), scale_rows[e])
+        load_table(0)
+        nc.sync.dma_start(offs2_t[:], offs2)
         load_w4(0)
         load_table(1)
 
-        def load_table_scales(first_row, passes, q):
-            rows = slice(first_row, first_row + 4 * (passes.stop - passes.start))
-            nc.scalar.dma_start(tab_scales_raw[rows, :].bitcast(I32), tab_scales[passes, 4 * q : 4 * q + 4, :].bitcast(I32))
-
-        for q in (0, 1):
-            load_table_scales(32 * q, slice(0, KA), q)
-        for q in (2, 3):
-            load_table_scales(32 * q - 8, slice(1, KA), q)
-            load_table_scales(32 * q, slice(0, 1), q)
+        for rows in (slice(0, SCALE_ROWS[0]), slice(HALF, SCALE_ROWS[1]), slice(SCALE_ROWS[1] + 8 * KA, P)):
+            zero(nc.vector, tab_scales_raw[rows, :].bitcast(I32))
+        zero(nc.vector, pages[0][:])
+        nc.gpsimd.memset(w4_scales_raw[:].bitcast(I32), 0)
         for q in range(QUADRANTS):
             nc.gpsimd.dma_start(
                 w4_scales_raw[32 * q : 32 * q + 4, :].bitcast(I32).rearrange("p (a n) -> p a n", a=KA),
                 w4_scales[:, 4 * q : 4 * q + 4, :].bitcast(I32).rearrange("a r n -> r a n"),
             )
-        identity = keep.tile([P, P], F32, name="identity", align_bytes=64)
         make_identity(nc, identity[:])
-        nc.gpsimd.memset(pages[1][:, PAGE_SPLIT:T2], 0.0)
+        nc.gpsimd.memset(pages[1][:], 0.0)
         nc.scalar.activation(ln_gain[:], gain_t[:].rearrange("p b i -> p (b i)"), ACT.Ln)
         nc.scalar.mul(neg_sharp[:], sharp_t[:], -1.0)
         warm = keep.tile([P, 1], F32, name="warm")
         nc.scalar.activation(warm[:], neg_sharp[:, 0:1], ACT.Exp)
 
-        ord_slots = (range(0, PACK), range(PACK, SLOTS - 1), range(SLOTS - 1, SLOTS))
-        w4_ord = [place("w4_ord%d" % j, [P, KA * len(slots) * 2 * P], U8, ORD_AT[j]) for j, slots in enumerate(ord_slots)]
+        w4_ord = {}
 
-        def order_w4_words(a, j):
-            b, i = divmod(ord_slots[j][0], PACK)
-            count = len(ord_slots[j])
-            nc.scalar.copy(
-                w4_ord[j][:].bitcast(U16)[:, cols_of(a, count * P)].rearrange("p (i m) -> p i m", i=count),
-                w4_raw[b][:, a, :].bitcast(U16).rearrange("p (m i) -> p i m", i=PACK)[:, i : i + count, :],
-            )
+        def order_w4_words(b):
+            w4_ord[b] = place("w4_ord%d" % b, [P, KA * H], U8, W4_ORD_AT[b])
+            for two in (slice(0, 2), slice(2, PACK)):
+                for a in range(KA):
+                    nc.scalar.copy(
+                        w4_ord[b][:].bitcast(U16)[:, cols_of(a, BANK)].rearrange("p (i m) -> p i m", i=PACK)[:, two, :],
+                        w4_raw[b][:, a, :].bitcast(U16).rearrange("p (m i) -> p i m", i=PACK)[:, two, :],
+                    )
 
-        def w4_codes(s, a):
-            j = [s in slots for slots in ord_slots].index(True)
-            return w4_ord[j][:, cols_of(a * len(ord_slots[j]) + s - ord_slots[j][0], 2 * P)]
-
-        for a in range(KA):
-            order_w4_words(a, 0)
-
+        order_w4_words(0)
         w4_planes = [place("w4_planes%d" % b, [P, KA * BANK], U8, W4_PLANES_AT + KA * BANK * b) for b in range(RB)]
         for b in range(RB):
             nc.gpsimd.tensor_copy(
@@ -177,279 +175,321 @@ def tile_list_pallet_slot_fit_kernel(tc, tab_words, tab_scales, offs, w4_words, 
                 w4_scales_raw[:].rearrange("p (a b m i) -> p b a i m", a=KA, b=RB, i=PACK)[:, b],
             )
 
-        picked = [place("picked%d" % a, [P, S], U32, PICKED_AT[a]) for a in range(KA)]
-        first, second, upper = slice(0, QUARTER), slice(QUARTER, BANK), slice(BANK, S)
-        lower, rest, whole = slice(0, BANK), slice(QUARTER, S), slice(0, S)
+        picked = [place("picked%d" % a, [P, S], U32, PICKED_AT + 4 * KB * a) for a in range(KA)]
 
         def gather_words(a, cols):
             nc.vector.tensor_copy(picked[a][:, cols], tab_win[a][:].bitcast(U32).indirect(offs_t[:, listed(cols)]))
 
+        picked_scales = place("picked_scales", [P, S], U8, PICKED_SCALES_AT)
+        nc.vector.tensor_copy(picked_scales[:], tab_scales_raw[:].indirect(offs_t[:]))
+        tab_planes = [place("tab_plane%d" % a, [P, S], U8, TAB_PLANES_AT[a]) for a in range(KA)]
+        for a in range(KA):
+            if a == 1:
+                load_table(2)
+            for half in range(2):
+                source = SCALE_ROWS[0] + 8 * a + 4 * half
+                nc.sync.dma_start(tab_planes[a][cols_of(half, HALF), :].bitcast(I32), picked_scales[source : source + HALF, :].bitcast(I32))
         gather_words(0, whole)
-        tab_plane0 = place("tab_plane0", [P, S], U8, TAB_PLANE_AT)
-        nc.vector.tensor_copy(tab_plane0[:], tab_scales_raw[:].indirect(offs_t[:]))
-        load_table(2)
-        wgs_first = place("wgs_first", [P, QUARTER], F32, WGS_FIRST_AT)
-        nc.sync.dma_start(wgs_first[:], wgs[:, first])
-        for a in range(1, KA):
-            for half, source in enumerate((4 * a, HALF - 12 + 4 * a)):
-                nc.sync.dma_start(tab_shifted[cols_of(half, HALF), cols_of(a - 1, S)].bitcast(I32), tab_plane0[source : source + HALF, :].bitcast(I32))
-        tab_planes = [tab_plane0[:]] + [tab_shifted[:, cols_of(a, S)] for a in range(KA - 1)]
-        wgs_t = place("wgs_t", [P, S], F32, WGS_AT)
-        nc.sync.dma_start(wgs_t[:], wgs)
+        wgs_first = place("wgs_first", [P, PIECES[1].stop], F32, WGS_FIRST_AT)
+        nc.sync.dma_start(wgs_first[:], wgs[:, 0 : PIECES[1].stop])
         gather_words(1, whole)
-        load_w4(1)
-        for cols in (first, second, upper):
+        for cols in PIECES:
             gather_words(2, cols)
 
         rack_rows = rack.rearrange("(b p i) m -> b i p m", b=RB, i=PACK)
         racks = {}
+        w2_raw = {}
 
         def load_rack(s):
             racks[s] = place("rack%d" % s, [P, T2], F32, RACK_AT[s])
             nc.sync.dma_start(racks[s][:], rack_rows[s // PACK, s % PACK])
 
-        w2_raw = {}
+        def load_w2(part):
+            b, cols = W2_PARTS[part]
+            w2_raw[part] = place("w2_raw%d" % part, [P, PACK, width(cols)], F32, W2_RAW_AT[part])
+            nc.sync.dma_start(w2_raw[part][:], w2.rearrange("(b p i) n -> b p i n", b=RB, i=PACK)[b, :, :, cols])
 
-        def load_w2(b):
-            w2_raw[b] = place("w2_raw%d" % b, [P, PACK, N], F32, W2_RAW_AT[b])
-            nc.sync.dma_start(w2_raw[b][:].rearrange("p i n -> p (i n)"), w2.rearrange("(b p i) n -> b p (i n)", b=RB, i=PACK)[b])
-
+        wgs_t = place("wgs_t", [P, S], F32, WGS_AT)
+        load_w4(1)
+        nc.sync.dma_start(wgs_t[:], wgs)
         load_w2(0)
         load_rack(0)
+        load_w2(1)
         load_rack(1)
 
-        h = [place("h%d" % s, [P, S], F32, H_AT[s]) for s in range(SLOTS)]
-        weighted = {s: h[s][:] for s in range(AHEAD)}
+        def h_pass(s, cols, bank, a, order=(0, 1, 2)):
+            b, i = divmod(s, PACK)
+            runs = [cols] if width(cols) != 3 * P else [slice(cols.start, cols.start + P), slice(cols.start + P, cols.stop)]
+            for run in runs:
+                nc.tensor.matmul_mx(
+                    out=banks[bank][:, run.start - cols.start : run.stop - cols.start],
+                    lhsT=w4_ord[b][:, cols_of(a * PACK + i, 2 * P)].bitcast(FP4X4),
+                    lhsT_scale=w4_planes[b][:, cols_of(a * PACK + i, P)],
+                    rhs=picked[a][:, run].bitcast(FP8X4),
+                    rhs_scale=tab_planes[a][:, run],
+                    start=(a == order[0] and run is runs[0]),
+                    stop=(a == order[-1] and run is runs[-1]),
+                )
 
-        def h_pass(s, cols, bank, a, order=tuple(range(KA))):
-            nc.tensor.matmul_mx(
-                out=banks[bank][:, 0 : cols.stop - cols.start],
-                lhsT=w4_codes(s, a).bitcast(FP4X4),
-                lhsT_scale=w4_planes[s // PACK][:, cols_of(a * PACK + s % PACK, P)],
-                rhs=picked[a][:, cols].bitcast(FP8X4),
-                rhs_scale=tab_planes[a][:, cols],
-                start=(a == order[0]),
-                stop=(a == order[-1]),
-            )
+        def h_group(s, cols, bank, target):
+            for a in range(KA):
+                h_pass(s, cols, bank, a)
+            nc.scalar.mul(target, banks[bank][:, 0 : width(cols)], -1.0)
 
-        def h_out(s, cols, bank):
-            nc.scalar.mul(h[s][:, cols], banks[bank][:, 0 : cols.stop - cols.start], -1.0)
+        def scatter(s, cols, source):
+            nc.vector.tensor_copy(pages[s % 2][:].indirect(offs2_t[:, listed(cols)]), source)
+
+        opening = [(s, cols) for cols in PIECES for s in range(2)] + [(2, lower), (2, upper)]
+        ahead = [2 if cols == PIECES[0] else 1 if s < 2 else 0 for s, cols in opening]
+        for a in range(KA - 1):
+            for bank, (s, cols) in enumerate(opening):
+                if a < ahead[bank]:
+                    h_pass(s, cols, bank, a, (0, 1, 2) if ahead[bank] == 2 else (0, 2, 1))
+        h = {2: place("h2", [P, S], F32, H_AT[2])}
+        for bank, (s, cols) in enumerate(opening):
+            order = ((2, 0, 1), (0, 2, 1), (0, 1, 2))[ahead[bank]]
+            for a in order[ahead[bank] :]:
+                h_pass(s, cols, bank, a, order)
+            k = bank // 2
+            if bank == 2 * (len(PIECES) - 1):
+                order_w4_words(1)
+            piece = h[2][:, cols] if s == 2 else place("piece%d_%d" % (s, k), [P, width(cols)], F32, PIECE_AT[s][k])[:]
+            nc.scalar.mul(piece, banks[bank][:, 0 : width(cols)], -1.0)
+            if s < 2:
+                nc.gpsimd.tensor_tensor(piece, piece, wgs_first[:, cols] if k < 2 else wgs_t[:, cols], ALU.mult)
+                scatter(s, cols, piece)
+        load_rack(2)
+
+        weighted = {}
 
         def h_slot(s):
-            for cols, bank in zip((lower, upper), LATE_H_BANKS[s]):
-                for a in range(KA):
-                    h_pass(s, cols, bank, a)
-                h_out(s, cols, bank)
+            h[s] = place("h%d" % s, [P, S], F32, H_AT[s])
+            for cols, bank in zip((lower, upper), H_BANKS[s]):
+                h_group(s, cols, bank, h[s][:, cols])
 
-        def weigh(s, cols):
-            nc.gpsimd.tensor_tensor(weighted[s][:, cols], h[s][:, cols], wgs_first[:] if cols == first else wgs_t[:, cols], ALU.mult)
-
-        def scatter(s, cols):
-            nc.vector.tensor_copy(pages[s % PAGES][:].indirect(offs2_t[:, listed(cols)]), weighted[s][:, cols])
-
-        opening = [(0, first), (1, first), (0, second), (1, second), (0, upper), (1, upper), (2, lower), (2, upper)]
-        early = opening[:EARLY_GROUPS]
-        for bank, (s, cols) in enumerate(early):
-            h_pass(s, cols, bank, 0)
-        for bank in (0, 1, 2, 4, 3, 5, 6, 7):
-            s, cols = opening[bank]
-            order = (0, 1, 2) if cols == first else (0, 2, 1) if (s, cols) in early else (2, 0, 1)
-            for a in order[1:] if (s, cols) in early else order:
-                h_pass(s, cols, bank, a, order)
-            h_out(s, cols, bank)
-        for cols in (first, rest):
-            for s in range(2):
-                weigh(s, cols)
-        weigh(2, whole)
-        for j in range(1, len(ord_slots)):
-            for a in range(KA):
-                order_w4_words(a, j)
-        w2_bf = {0: place("w2_bf0", [P, N * PACK], BF16, W2_BF_AT[0])}
-        for t, s in enumerate(range(3, SLOTS - 1)):
+        for s in range(3, SLOTS - 1):
             h_slot(s)
-            if t < NT:
-                nc.scalar.copy(w2_bf[0][:, cols_of(t, P * PACK)].rearrange("p (n i) -> p n i", i=PACK), w2_raw[0][:, :, cols_of(t, P)].rearrange("p i n -> p n i"))
-        weigh(3, whole)
+
+        def weigh(s):
+            weighted[s] = place("weighted%d" % s, [P, S], F32, WEIGHTED_AT[s])[:] if s in WEIGHTED_AT else racks[s - 3][:, whole]
+            nc.gpsimd.tensor_tensor(weighted[s], h[s][:], wgs_t[:], ALU.mult)
+
+        w2_bf = {}
+
+        def round_w2(part):
+            w2_bf[part] = place("w2_bf%d" % part, [P, width(W2_PARTS[part][1]) * PACK], BF16, W2_BF_AT[part])
+            nc.gpsimd.tensor_scalar(w2_bf[part][:].rearrange("p (n i) -> p n i", i=PACK), w2_raw[part][:].rearrange("p i n -> p n i"), 1.0, 0.0, ALU.mult, ALU.add)
+
+        weigh(2)
+        round_w2(1)
+        w2_bf[0] = place("w2_bf0", [P, N * PACK], BF16, W2_BF_AT[0])
+        for t in range(2 * NT):
+            nc.scalar.copy(w2_bf[0][:, cols_of(t, HALF * PACK)].rearrange("p (n i) -> p n i", i=PACK), w2_raw[0][:, :, cols_of(t, HALF)].rearrange("p i n -> p n i"))
 
         pairs = {}
         slotwise = {}
         joined = {}
         z_codes = {}
         z_scales = {}
-        diffs = {}
-        squares = {}
 
         def open_pairs(b):
-            for c in range(CHUNKS):
-                if b == 0 and c in INTERLEAVED:
-                    slotwise[c] = place("slotwise%d" % c, [P, PACK, BANK], BF16, PAIRS_AT[b] + 4 * KB * c)
+            for c, cols in CUTS[b].items():
+                at = PAIRS_AT[b] + 2 * PACK * cols.start
+                if b == 0 and c not in "AE":
+                    slotwise[c] = place("slotwise" + c, [P, PACK, width(cols)], BF16, at)
                 else:
-                    pairs[b, c] = place("pairs%d_%d" % (b, c), [P, 2, BANK, 2], BF16, PAIRS_AT[b] + 4 * KB * c)
-
-        def difference(engine, s, cols):
-            engine.tensor_tensor(diffs[s][:, cols], racks[s][:, cols], pages[s % PAGES][:, cols], ALU.add)
-
-        def square_direct(s, cols):
-            nc.scalar.activation(diffs[s][:, cols], diffs[s][:, cols], ACT.Square)
+                    pairs[b, c] = place("pairs%d%s" % (b, c), [P, 2, width(cols), 2], BF16, at)
 
         def exp_to_z(s, c, square):
             b, i = divmod(s, PACK)
             target = pairs[b, c][:, i // 2, :, i % 2] if (b, c) in pairs else slotwise[c][:, i, :]
             nc.scalar.activation(target, square, ACT.Exp, bias=ln_gain[:, s : s + 1], scale=neg_sharp[:, s : s + 1])
 
-        def exp_direct(s, c):
-            exp_to_z(s, c, diffs[s][:, cols_of(c, BANK)])
-
         def turned_sums(s):
-            blocks = BANK // P
-            for k, source in enumerate((racks[s], pages[s % PAGES])):
-                for c, bank in TURN_BANKS.items():
+            for c, bank in TURN_BANKS[s].items():
+                blocks = BANK // P
+                for k, source in enumerate((racks[s], pages[s % 2])):
                     for j in range(blocks):
                         nc.tensor.matmul(
-                            banks[bank][:, cols_of(j, P)], source[:, cols_of(c * blocks + j, P)], identity[:],
+                            banks[bank][:, cols_of(j, P)], source[:, cols_of(CHUNKS[c].start // P + j, P)], identity[:],
                             start=(k == 0 and j == 0), stop=(k == 1 and j == blocks - 1), is_transpose=True,
                         )
 
-        def turn_back(s, c, bank):
-            for block in range(BANK // P):
-                nc.tensor.transpose(banks[bank][:, cols_of(block, P)], squares[s, c][:, cols_of(block, P)], identity[:])
 
-        def square_turned(s, c, bank, back=True):
-            at = LAST_TURNED_SQUARES_AT[TURNED.index(c)] if s == SLOTS - 1 else SQUARE_AT + 2 * KB * TURNED.index(c)
-            squares[s, c] = place("square%d_%d" % (s, c), [P, BANK], F32, at)
-            nc.scalar.activation(squares[s, c][:], banks[bank][:], ACT.Square)
-            if back:
-                turn_back(s, c, bank)
+        def square_turned(s, c, at):
+            square = place("square%d%s" % (s, c), [P, BANK], F32, at)
+            nc.scalar.activation(square[:], banks[TURN_BANKS[s][c]][:], ACT.Square)
+            for j in range(BANK // P):
+                nc.tensor.transpose(banks[TURN_BANKS[s][c]][:, cols_of(j, P)], square[:, cols_of(j, P)], identity[:])
 
-        def exp_turned(s, c, bank):
-            exp_to_z(s, c, banks[bank][:])
-
-        def open_slot(s):
-            diffs[s] = place("diff%d" % s, [P, S], F32, DIFF_AT[s])
+        last = SLOTS - 1
 
         def slot_to_z(s):
-            open_slot(s)
-            for c in DIRECT:
-                difference(nc.gpsimd, s, cols_of(c, BANK))
+            parts = (lower, upper) if s >= SPLIT_FROM else (whole,)
+            diffs = [place("diff%d_%d" % (s, cols.start), [P, width(cols)], F32, DIFF_AT[s] + 4 * cols.start) for cols in parts]
+            for diff, cols in zip(diffs, parts):
+                nc.gpsimd.tensor_tensor(diff[:], racks[s][:, cols], pages[s % 2][:, cols], ALU.add)
             turned_sums(s)
-            (c2, bank2), (c3, bank3) = TURN_BANKS.items()
-            square_turned(s, c2, bank2)
-            square_direct(s, lower)
-            square_turned(s, c3, bank3)
-            exp_turned(s, c2, bank2)
-            square_direct(s, upper)
-            exp_turned(s, c3, bank3)
-            for c in DIRECT:
-                exp_direct(s, c)
+            if s == 0:
+                h_slot(last)
+            turned_at = FIRST_SQUARE_AT if s == 0 else {"C": DIFF_AT[s], "D": DIFF_AT[s] + 2 * KB}
+            low = place("low_square%d" % s, [P, BANK], F32, LOW_SQUARE_AT[s % 2])
+            high = place("high_square%d" % s, [P, BANK], F32, HIGH_SQUARE_AT[s % 2])
+            nc.scalar.activation(low[:], diffs[0][:, lower], ACT.Square)
+            if len(parts) == 2:
+                square_turned(s, "C", turned_at["C"])
+            nc.scalar.activation(high[:], diffs[-1][:, lower if len(parts) == 2 else upper], ACT.Square)
+            if len(parts) == 1:
+                square_turned(s, "C", turned_at["C"])
+            square_turned(s, "D", turned_at["D"])
+            for c in "ACBED":
+                exp_to_z(s, c, banks[TURN_BANKS[s][c]][:] if c in TURN_BANKS[s] else high[:] if c == "B" else low[:, CHUNKS[c]])
 
         def join(copy, dtype, b, c):
-            joined[b, c] = place("joined%d_%d" % (b, c), [P, BANK * PACK], BF16, JOINED_AT[b][c])
+            cols = CHUNKS[c]
+            at = JOINED0_AT[c] if b == 0 else JOINED1_AT + 2 * PACK * cols.start
+            joined[b, c] = place("joined%d%s" % (b, c), [P, width(cols) * PACK], BF16, at)
             copy(
                 joined[b, c][:].bitcast(dtype).rearrange("p (m e h) -> p m h e", e=LINE, h=2),
                 pairs[b, c][:].rearrange("p h m e -> p (h m e)").bitcast(dtype).rearrange("p (h m e) -> p m h e", e=LINE, h=2),
             )
 
         def interleave(c):
-            joined[0, c] = place("joined0_%d" % c, [P, BANK * PACK], BF16, JOINED_AT[0][c])
+            joined[0, c] = place("joined0" + c, [P, BANK * PACK], BF16, JOINED0_AT[c])
             nc.gpsimd.tensor_scalar(joined[0, c][:].rearrange("p (m i) -> p m i", i=PACK), slotwise[c][:].rearrange("p i m -> p m i"), 1.0, 0.0, ALU.mult, ALU.add)
 
-        def quantise(b, c):
-            z_codes[b, c] = place("z_codes%d_%d" % (b, c), [P, BANK], U32, Z_CODES_AT[b][c])
-            z_scales[b, c] = place("z_scales%d_%d" % (b, c), [P, BANK], U8, Z_SCALES_AT[b][c])
-            nc.vector.quantize_mx(out=z_codes[b, c][:].bitcast(FP8X4), scales=z_scales[b, c][:], in_=joined[b, c][:])
-
-
-        def round_w2(b):
-            w2_bf[b] = place("w2_bf%d" % b, [P, N * PACK], BF16, W2_BF_AT[b])
-            nc.gpsimd.tensor_scalar(w2_bf[b][:].rearrange("p (n i) -> p n i", i=PACK), w2_raw[b][:].rearrange("p i n -> p n i"), 1.0, 0.0, ALU.mult, ALU.add)
-
-        for cols in (first, rest):
-            for s in range(2):
-                scatter(s, cols)
-        load_rack(2)
-        load_rack(3)
-        load_w2(1)
         open_pairs(0)
-        last = SLOTS - 1
         for s in range(last):
             if s == PACK:
                 open_pairs(1)
             slot_to_z(s)
-            if s == 0:
-                h_slot(last)
-            nxt = s + AHEAD
-            if nxt < SLOTS:
-                weighted[nxt] = racks[s][:, whole]
-                weigh(nxt, whole)
             if s + 2 < SLOTS:
-                scatter(s + 2, whole)
-            if s + 4 < SLOTS:
-                load_rack(s + 4)
-            if s == 3:
-                round_w2(1)
+                scatter(s + 2, whole, weighted[s + 2])
+            if s == 0:
+                load_w2(2)
+                for later in range(3, last):
+                    load_rack(later)
+            if s == 1:
+                load_rack(last)
+            for nxt in {0: (3,), 1: (4,), 2: (5,), 3: (6, 7)}.get(s, ()):
+                weigh(nxt)
+            if s == 2:
+                round_w2(2)
             if s == PACK - 1:
-                join(nc.scalar.copy, U32, 0, 0)
-            if s >= PACK:
-                interleave(INTERLEAVED[s - PACK])
+                for c in "AE":
+                    join(nc.scalar.copy, U32, 0, c)
+            for c in INTERLEAVED.get(s, ()):
+                interleave(c)
 
-        open_slot(last)
-        for c in DIRECT:
-            difference(nc.vector, last, cols_of(c, BANK))
-        turned_sums(last)
-        last_diff, diffs[last] = diffs[last], place("last_square", [P, S], F32, LAST_SQUARE_AT)
-        for c, (turned, bank) in zip(DIRECT, TURN_BANKS.items()):
-            nc.scalar.activation(diffs[last][:, cols_of(c, BANK)], last_diff[:, cols_of(c, BANK)], ACT.Square)
-            square_turned(last, turned, bank, back=(c == 0))
-            exp_direct(last, c)
         w2_codes = place("w2_codes", [P, RB * N], U32, W2_CODES_AT)
         w2_scales = place("w2_scales", [P, RB * N], U8, W2_SCALES_AT)
+        diffs = {}
+        squares = {}
 
-        def quantise_w2(b):
-            cols = cols_of(b, N)
-            nc.vector.quantize_mx(out=w2_codes[:, cols].bitcast(FP8X4), scales=w2_scales[:, cols], in_=w2_bf[b][:])
+        def last_difference(c):
+            cols = SPANS[c]
+            diffs[c] = place("last_diff" + c, [P, width(cols)], F32, LAST_DIFF_AT[c])
+            nc.vector.tensor_tensor(diffs[c][:], racks[last][:, cols], pages[last % 2][:, cols], ALU.add)
 
-        def out_pass(b, c):
+        def last_square(c):
+            squares[c] = place("last_square" + c, [P, width(CHUNKS[c])], F32, LAST_SQUARE_AT[c])
+            nc.scalar.activation(squares[c][:], diffs[c][:], ACT.Square)
+
+        def last_exp(c):
+            exp_to_z(last, c, squares[c][:])
+
+        def quantise_w2(part):
+            b, cols = W2_PARTS[part]
+            cols = slice(b * N + cols.start, b * N + cols.stop)
+            nc.vector.quantize_mx(out=w2_codes[:, cols].bitcast(FP8X4), scales=w2_scales[:, cols], in_=w2_bf[part][:])
+
+        def product(b, c):
+            cols = CUTS[b][c]
+            codes = place("z_codes%d%s" % (b, c), [P, width(cols)], U32, Z_CODES_AT[b] + 4 * cols.start)
+            scales = place("z_scales%d%s" % (b, c), [P, width(cols)], U8, Z_SCALES0_AT[c] if b == 0 else Z_SCALES1_AT + cols.start)
+            nc.vector.quantize_mx(out=codes[:].bitcast(FP8X4), scales=scales[:], in_=joined[b, c][:])
+            z_codes[b, c], z_scales[b, c] = codes, scales
+
+        opened = set()
+
+        def out_pass(passes, c):
             for t in range(NT):
-                nc.tensor.matmul_mx(
-                    out=banks[OUT_BANKS[c * NT + t]][:],
-                    lhsT=w2_codes[:, cols_of(b * NT + t, P)].bitcast(FP8X4),
-                    lhsT_scale=w2_scales[:, cols_of(b * NT + t, P)],
-                    rhs=z_codes[b, c][:].bitcast(FP8X4),
-                    rhs_scale=z_scales[b, c][:],
-                    start=(b == 0),
-                    stop=(b == RB - 1),
-                )
+                for b in passes:
+                    held = c if b == 1 else SPAN_OF[c]
+                    first = CUTS[b][held].start
+                    cols = slice(CHUNKS[c].start - first, CHUNKS[c].stop - first)
+                    nc.tensor.matmul_mx(
+                        out=banks[OUT_BANKS[c][t]][:, 0 : width(CHUNKS[c])],
+                        lhsT=w2_codes[:, cols_of(b * NT + t, P)].bitcast(FP8X4),
+                        lhsT_scale=w2_scales[:, cols_of(b * NT + t, P)],
+                        rhs=z_codes[b, held][:, cols].bitcast(FP8X4),
+                        rhs_scale=z_scales[b, held][:, cols],
+                        start=(c, t) not in opened,
+                        stop=(c, t) in opened,
+                    )
+                    opened.add((c, t))
 
-        def store(k):
-            c, t = divmod(k, NT)
-            res = place("res%d" % k, [P, BANK], F32, RESULT_AT + 2 * KB * k)
-            copy = nc.vector.tensor_copy if k in VECTOR_COPIES else nc.scalar.copy
-            copy(res[:], banks[OUT_BANKS[k]][:])
-            nc.sync.dma_start(out[cols_of(t, P), cols_of(c, BANK)], res[:])
+        def store(c, t, copy):
+            cols = CHUNKS[c]
+            res = place("res%s%d" % (c, t), [P, width(cols)], F32, RESULT_AT + 4 * (NT * cols.start + t * width(cols)))
+            copy(res[:], banks[OUT_BANKS[c][t]][:, 0 : width(cols)])
+            nc.sync.dma_start(out[cols_of(t, P), cols], res[:])
 
-        def chunk_product(c):
+        def join_last(c):
             join(nc.vector.tensor_copy, I32, 1, c)
-            if c > 0:
-                quantise(0, c)
-                out_pass(0, c)
-            quantise(1, c)
-            out_pass(1, c)
 
+        on_scalar, on_vector = nc.scalar.copy, nc.vector.tensor_copy
+        last_difference("A")
+        last_difference("B")
         quantise_w2(0)
-        quantise(0, 0)
+        product(0, "B")
+        out_pass((0,), "B")
+        last_difference("C")
         quantise_w2(1)
-        out_pass(0, 0)
-        chunk_product(0)
-        chunk_product(1)
-        exp_turned(last, TURNED[0], TURN_BANKS[TURNED[0]])
-        store(0)
-        turn_back(last, TURNED[1], OUT_BANKS[0])
-        for k in range(1, NT):
-            store(k)
-        exp_turned(last, TURNED[1], OUT_BANKS[0])
-        chunk_product(2)
-        for k in range(NT, 2 * NT):
-            store(k)
-        chunk_product(3)
-        for k in range(2 * NT, CHUNKS * NT):
-            store(k)
+        quantise_w2(2)
+        product(0, "A")
+        last_square("A")
+        last_square("B")
+        last_exp("A")
+        last_exp("B")
+        join_last("A")
+        last_difference("D")
+        product(1, "A")
+        out_pass((1, 0,), "A")
+        last_square("C")
+        join_last("B")
+        product(0, "C")
+        product(1, "B")
+        out_pass((1,), "B")
+        last_exp("C")
+        store("A", 0, on_scalar)
+        store("A", 1, on_scalar)
+        store("A", 2, on_scalar)
+        last_square("D")
+        join_last("C")
+        last_difference("E")
+        product(1, "C")
+        out_pass((1, 0,), "C")
+        store("B", 0, on_scalar)
+        last_exp("D")
+        store("B", 1, on_scalar)
+        product(0, "D")
+        store("B", 2, on_scalar)
+        join_last("D")
+        product(0, "E")
+        product(1, "D")
+        last_square("E")
+        store("C", 0, on_scalar)
+        last_exp("E")
+        store("C", 1, on_scalar)
+        out_pass((1, 0,), "D")
+        join_last("E")
+        store("C", 2, on_vector)
+        product(1, "E")
+        store("D", 0, on_scalar)
+        out_pass((1, 0,), "E")
+        store("D", 1, on_vector)
+        store("D", 2, on_scalar)
+        store("E", 0, on_vector)
+        store("E", 1, on_scalar)
+        store("E", 2, on_vector)

@@ -39,7 +39,8 @@ SPAN_OF = {"A": "A", "E": "E", "B": "B", "C": "C", "D": "D", "F": "D"}
 TURN_BANKS = {s: {"C": 6, "D": 7} if s else {"C": 4, "D": 5} for s in range(SLOTS)}
 INTERLEAVED = {4: ("B",), 5: ("C",), 6: ("D",)}
 SPLIT_FROM = 4
-SCALE_ROWS = (40, 72)
+SCALE_ROWS = (64, 80, 112)
+EARLY_SHIFTS = 6
 H_BANKS = {3: (0, 1), 4: (2, 3), 5: (4, 5), 6: (6, 7), 7: (0, 1)}
 OUT_BANKS = {"B": (0, 1, 2), "A": (3, 6, 7), "C": (4, 5, 3), "D": (6, 7, 0), "E": (1, 2, 4)}
 
@@ -132,16 +133,19 @@ def tile_list_pallet_slot_fit_kernel(tc, tab_words, tab_scales, offs, w4_words, 
         nc.sync.dma_start(offs_t[:], offs)
         nc.scalar.dma_start(gain_t[:], gain.rearrange("(b p i) -> p b i", b=RB, i=PACK))
         nc.scalar.dma_start(sharp_t[:].rearrange("p (b i) -> p b i", b=RB), sharp.rearrange("(b p i) -> p b i", b=RB, i=PACK))
-        scale_rows = tab_scales.bitcast(I32).rearrange("a (h e r) t -> e (a h) r t", h=2, e=2)
-        for e, row in enumerate(SCALE_ROWS):
-            nc.scalar.dma_start(tab_scales_raw[row : row + 8 * KA, :].bitcast(I32), scale_rows[e])
+        scale_rows = tab_scales.bitcast(I32).rearrange("a r t -> (a r) t")
+        for row, rows in ((SCALE_ROWS[0], slice(0, 32)), (SCALE_ROWS[2], slice(32, 48))):
+            nc.sync.dma_start(tab_scales_raw[row : row + width(rows), :].bitcast(I32), scale_rows[rows, :])
         load_table(0)
         nc.sync.dma_start(offs2_t[:], offs2)
         load_w4(0)
         load_table(1)
 
-        for rows in (slice(0, SCALE_ROWS[0]), slice(HALF, SCALE_ROWS[1]), slice(SCALE_ROWS[1] + 8 * KA, P)):
+        for rows in (slice(0, HALF), slice(96, SCALE_ROWS[2])):
             zero(nc.vector, tab_scales_raw[rows, :].bitcast(I32))
+        all_planes = place("tab_planes", [P, KA * S], U8, TAB_PLANES_AT[0])
+        tab_planes = [all_planes[:, cols_of(a, S)] for a in range(KA)]
+        zero(nc.vector, all_planes[:].bitcast(I32))
         zero(nc.vector, pages[0][:])
         nc.gpsimd.memset(w4_scales_raw[:].bitcast(I32), 0)
         for q in range(QUADRANTS):
@@ -182,13 +186,12 @@ def tile_list_pallet_slot_fit_kernel(tc, tab_words, tab_scales, offs, w4_words, 
 
         picked_scales = place("picked_scales", [P, S], U8, PICKED_SCALES_AT)
         nc.vector.tensor_copy(picked_scales[:], tab_scales_raw[:].indirect(offs_t[:]))
-        tab_planes = [place("tab_plane%d" % a, [P, S], U8, TAB_PLANES_AT[a]) for a in range(KA)]
-        for a in range(KA):
-            if a == 1:
+        for shift in range(KA * QUADRANTS):
+            if shift == EARLY_SHIFTS:
                 load_table(2)
-            for half in range(2):
-                source = SCALE_ROWS[0] + 8 * a + 4 * half
-                nc.sync.dma_start(tab_planes[a][cols_of(half, HALF), :].bitcast(I32), picked_scales[source : source + HALF, :].bitcast(I32))
+            a, q = divmod(shift, QUADRANTS)
+            source = SCALE_ROWS[a] + 4 * q
+            nc.sync.dma_start(tab_planes[a][32 * q : 32 * q + 4, :].bitcast(I32), picked_scales[source : source + 4, :].bitcast(I32))
         gather_words(0, whole)
         wgs_first = place("wgs_first", [P, PIECES[1].stop], F32, WGS_FIRST_AT)
         nc.sync.dma_start(wgs_first[:], wgs[:, 0 : PIECES[1].stop])

@@ -32,6 +32,7 @@ KB = 1024
 EDGE = 64
 
 PIECES = (slice(0, 128), slice(128, 512), slice(512, 1024))
+CUTS_OF_LIST = (PIECES, (slice(0, 128), slice(128, 256), slice(256, 1024)))
 CHUNKS = {"A": slice(0, 256), "E": slice(256, 512), "B": slice(512, 1024), "C": slice(1024, 1536), "D": slice(1536, 2048)}
 SPANS = {"A": CHUNKS["A"], "E": CHUNKS["E"], "B": CHUNKS["B"], "C": CHUNKS["C"], "D": slice(CHUNKS["D"].start, T2)}
 CUTS = (SPANS, CHUNKS)
@@ -58,7 +59,7 @@ W4_RAW_AT = (25 * KB, TAB_AT[1] + 4 * KB + EDGE)
 WGS_AT = TAB_AT[1] + EDGE
 W2_PARTS = ((0, slice(0, N)), (1, slice(0, P)), (1, slice(P, N)))
 W2_RAW_AT = (TAB_AT[1] + EDGE - 6 * KB, PICKED_SCALES_AT + 512, W4_ORD_AT[0] - 512)
-PIECE_AT = ((SQUARE_AT + 2 * KB + 512, 234 * KB + 512, 75 * KB), (85 * KB + 512, 79 * KB, 77 * KB))
+PIECE_AT = ((SQUARE_AT + 2 * KB + 512, 234 * KB + 512, 75 * KB), (85 * KB + 512, 81 * KB, 77 * KB))
 H_AT = {2: 94 * KB, 3: 90 * KB, 4: 102 * KB, 5: 106 * KB, 6: 110 * KB, 7: 114 * KB}
 PICKED_AT = 127 * KB
 RACK_AT = (PICKED_SCALES_AT + 512 - 8 * KB, TAB_AT[2] - KB + EDGE, WGS_FIRST_AT + EDGE - 8 * KB, PICKED_AT - 8 * KB + EDGE, PICKED_AT + EDGE, PICKED_AT + 8 * KB + EDGE, 75 * KB, 86 * KB)
@@ -73,8 +74,8 @@ Z_SCALES1_AT = 24 * KB
 W2_CODES_AT = WEIGHTED_AT[7]
 RESULT_AT = TAB_AT[0]
 LOW_SQUARE_AT = (SQUARE_AT, SQUARE_AT + 2 * KB - EDGE)
-HIGH_SQUARE_AT = (SQUARE_AT + 4 * KB - 2 * EDGE, SQUARE_AT - 2 * KB + EDGE)
-FIRST_SQUARE_AT = {"C": TAB_PLANES_AT[0], "D": TAB_PLANES_AT[2]}
+HIGH_SQUARE_AT = (SQUARE_AT + 4 * KB - 2 * EDGE, SQUARE_AT - 2 * KB - EDGE)
+FIRST_SQUARES_AT = ({"C": TAB_PLANES_AT[0], "D": TAB_PLANES_AT[2]}, {"C": SQUARE_AT + 6 * KB - EDGE, "D": SQUARE_AT + 4 * KB - EDGE})
 LAST_SQUARE_AT = {"A": SQUARE_AT + 3 * KB - EDGE, "B": SQUARE_AT + 4 * KB - EDGE, "C": SQUARE_AT + 6 * KB - EDGE, "D": 166 * KB, "E": 169 * KB}
 W2_SCALES_AT = DIFF_AT[6] + 2 * KB + EDGE
 LAST_DIFF_AT = {"A": H_AT[4], "B": H_AT[4] + KB, "C": W2_SCALES_AT - 2 * KB, "D": LAST_SQUARE_AT["A"] - 2 * KB + EDGE, "E": LAST_SQUARE_AT["C"] + 2 * KB - EDGE}
@@ -248,19 +249,28 @@ def tile_list_pallet_slot_fit_kernel(tc, tab_words, tab_scales, offs, w4_words, 
             for bank, (s, cols) in enumerate(opening):
                 if a < ahead[bank]:
                     h_pass(s, cols, bank, a, (0, 1, 2) if ahead[bank] == 2 else (0, 2, 1))
+        pieces = {}
         h = {2: place("h2", [P, S], F32, H_AT[2])}
         for bank, (s, cols) in enumerate(opening):
             order = ((2, 0, 1), (0, 2, 1), (0, 1, 2))[ahead[bank]]
             for a in order[ahead[bank] :]:
                 h_pass(s, cols, bank, a, order)
-            k = bank // 2
             if bank == 2 * (len(PIECES) - 1):
                 order_w4_words(1)
-            piece = h[2][:, cols] if s == 2 else place("piece%d_%d" % (s, k), [P, width(cols)], F32, PIECE_AT[s][k])[:]
-            nc.scalar.mul(piece, banks[bank][:, 0 : width(cols)], -1.0)
-            if s < 2:
-                nc.gpsimd.tensor_tensor(piece, piece, wgs_first[:, cols] if k < 2 else wgs_t[:, cols], ALU.mult)
-                scatter(s, cols, piece)
+            if s == 2:
+                nc.scalar.mul(h[2][:, cols], banks[bank][:], -1.0)
+                continue
+            for j, cut in enumerate(CUTS_OF_LIST[s]):
+                both = slice(max(cut.start, cols.start), min(cut.stop, cols.stop))
+                if both.start >= both.stop:
+                    continue
+                if (s, j) not in pieces:
+                    pieces[s, j] = place("piece%d_%d" % (s, j), [P, width(cut)], F32, PIECE_AT[s][j])
+                piece = pieces[s, j]
+                nc.scalar.mul(piece[:, both.start - cut.start : both.stop - cut.start], banks[bank][:, both.start - cols.start : both.stop - cols.start], -1.0)
+                if both.stop == cut.stop:
+                    nc.gpsimd.tensor_tensor(piece[:], piece[:], wgs_first[:, cut] if cut.stop <= BANK else wgs_t[:, cut], ALU.mult)
+                    scatter(s, cut, piece[:])
         load_rack(2)
 
         weighted = {}
@@ -270,7 +280,7 @@ def tile_list_pallet_slot_fit_kernel(tc, tab_words, tab_scales, offs, w4_words, 
             for cols, bank in zip((lower, upper), H_BANKS[s]):
                 h_group(s, cols, bank, h[s][:, cols])
 
-        for s in range(3, SLOTS - 1):
+        for s in range(3, SLOTS - 2):
             h_slot(s)
 
         def weigh(s):
@@ -334,19 +344,22 @@ def tile_list_pallet_slot_fit_kernel(tc, tab_words, tab_scales, offs, w4_words, 
                 nc.gpsimd.tensor_tensor(diff[:], racks[s][:, cols], pages[s % 2][:, cols], ALU.add)
             turned_sums(s)
             if s == 0:
+                h_slot(last - 1)
                 h_slot(last)
-            turned_at = FIRST_SQUARE_AT if s == 0 else {"C": DIFF_AT[s], "D": DIFF_AT[s] + 2 * KB}
+            turned_at = FIRST_SQUARES_AT[s] if s < 2 else {"C": DIFF_AT[s], "D": DIFF_AT[s] + 2 * KB}
+            if s == 1:
+                for c in "CD":
+                    square_turned(s, c, turned_at[c])
             low = place("low_square%d" % s, [P, BANK], F32, LOW_SQUARE_AT[s % 2])
-            high = place("high_square%d" % s, [P, BANK], F32, HIGH_SQUARE_AT[s % 2])
+            high = place("high_square%d" % s, [P, BANK + 2 * EDGE // 4], F32, HIGH_SQUARE_AT[s % 2])[:, lower]
             nc.scalar.activation(low[:], diffs[0][:, lower], ACT.Square)
             if len(parts) == 2:
                 square_turned(s, "C", turned_at["C"])
-            nc.scalar.activation(high[:], diffs[-1][:, lower if len(parts) == 2 else upper], ACT.Square)
-            if len(parts) == 1:
-                square_turned(s, "C", turned_at["C"])
-            square_turned(s, "D", turned_at["D"])
-            for c in "ACBED":
-                exp_to_z(s, c, banks[TURN_BANKS[s][c]][:] if c in TURN_BANKS[s] else high[:] if c == "B" else low[:, CHUNKS[c]])
+            nc.scalar.activation(high, diffs[-1][:, lower if len(parts) == 2 else upper], ACT.Square)
+            for c in "" if s == 1 else "D" if len(parts) == 2 else "CD":
+                square_turned(s, c, turned_at[c])
+            for c in "CDABE" if s == 1 else "ACBED":
+                exp_to_z(s, c, banks[TURN_BANKS[s][c]][:] if c in TURN_BANKS[s] else high if c == "B" else low[:, CHUNKS[c]])
 
         def join(copy, dtype, b, c):
             cols = CHUNKS[c]

@@ -40,8 +40,9 @@ SPAN_OF = {"A": "A", "E": "E", "B": "B", "C": "C", "D": "D", "F": "D"}
 TURN_BANKS = {s: {"C": 6, "D": 7} if s else {"C": 4, "D": 5} for s in range(SLOTS)}
 INTERLEAVED = {4: ("B",), 5: ("C",), 6: ("D",)}
 SPLIT_FROM = 4
-SCALE_ROWS = (64, 80, 112)
+SCALE_ROWS = (96, 112, 80)
 EARLY_SHIFTS = 6
+EARLY_GROUPS = 3
 H_BANKS = {3: (0, 1), 4: (2, 3), 5: (4, 5), 6: (6, 7), 7: (0, 1)}
 OUT_BANKS = {"B": (0, 1, 2), "A": (3, 6, 7), "C": (4, 5, 3), "D": (6, 7, 0), "E": (1, 2, 4)}
 
@@ -142,8 +143,7 @@ def tile_list_pallet_slot_fit_kernel(tc, tab_words, tab_scales, offs, w4_words, 
         load_w4(0)
         load_table(1)
 
-        for rows in (slice(0, HALF), slice(96, SCALE_ROWS[2])):
-            zero(nc.vector, tab_scales_raw[rows, :].bitcast(I32))
+        zero(nc.vector, tab_scales_raw[0 : SCALE_ROWS[2], :].bitcast(I32))
         all_planes = place("tab_planes", [P, KA * S], U8, TAB_PLANES_AT[0])
         tab_planes = [all_planes[:, cols_of(a, S)] for a in range(KA)]
         zero(nc.vector, all_planes[:].bitcast(I32))
@@ -244,7 +244,7 @@ def tile_list_pallet_slot_fit_kernel(tc, tab_words, tab_scales, offs, w4_words, 
             nc.vector.tensor_copy(pages[s % 2][:].indirect(offs2_t[:, listed(cols)]), source)
 
         opening = [(s, cols) for cols in PIECES for s in range(2)] + [(2, lower), (2, upper)]
-        ahead = [2 if cols == PIECES[0] else 1 if s < 2 else 0 for s, cols in opening]
+        ahead = [2 if bank < EARLY_GROUPS else 0 for bank in range(BANKS)]
         for a in range(KA - 1):
             for bank, (s, cols) in enumerate(opening):
                 if a < ahead[bank]:

from contextlib import ExitStack

import concourse.mybir as mybir
from concourse.masks import make_identity

K, T, S, H, T2, N = 1536, 2048, 1024, 1024, 2048, 384
FLOPS = 2 * K * H * S + 2 * H * N * T2

F32 = mybir.dt.float32
BF16 = mybir.dt.bfloat16
I32 = mybir.dt.int32
U32 = mybir.dt.uint32
U16 = mybir.dt.uint16
U8 = mybir.dt.uint8
FP8X4 = mybir.dt.float8_e4m3fn_x4
FP4X4 = mybir.dt.float4_e2m1fn_x4
ACT = mybir.ActivationFunctionType
ALU = mybir.AluOpType

P = 128
HALF = P // 2
PACK = 4
QUADRANTS = 4
KA = K // (P * PACK)
RB = H // (P * PACK)
SLOTS = RB * PACK
BANK = 512
BANKS = 8
NT = N // P
LINE = 4
KB = 1024
EDGE = 64

PIECES = (slice(0, 128), slice(128, 512), slice(512, 1024))
CUTS_OF_LIST = (PIECES, (slice(0, 128), slice(128, 256), slice(256, 1024)))
CHUNKS = {"A": slice(0, 256), "E": slice(256, 512), "B": slice(512, 1024), "C": slice(1024, 1536), "D": slice(1536, 2048)}
SPANS = {"A": CHUNKS["A"], "E": CHUNKS["E"], "B": CHUNKS["B"], "C": CHUNKS["C"], "D": slice(CHUNKS["D"].start, T2)}
CUTS = (SPANS, CHUNKS)
SPAN_OF = {"A": "A", "E": "E", "B": "B", "C": "C", "D": "D", "F": "D"}
TURN_BANKS = {s: {"C": 6, "D": 7} if s else {"C": 4, "D": 5} for s in range(SLOTS)}
INTERLEAVED = {4: ("B",), 5: ("C",), 6: ("D",)}
SPLIT_FROM = 4
SCALE_ROWS = (96, 112, 80)
EARLY_SHIFTS = 6
EARLY_GROUPS = 3
H_BANKS = {3: (0, 1), 4: (2, 3), 5: (4, 5), 6: (6, 7), 7: (0, 1)}
OUT_BANKS = {"B": (0, 1, 2), "A": (3, 6, 7), "C": (4, 5, 3), "D": (6, 7, 0), "E": (1, 2, 4)}

PAGE_AT = (0, 8 * KB)
SQUARE_AT = 150 * KB
TAB_PLANES_AT = (16 * KB, 17 * KB, 18 * KB)
W4_PLANES_AT = 19 * KB
W4_ORD_AT = (22 * KB, SQUARE_AT + KB + 512)
W4_SCALES_AT = 98 * KB
PICKED_SCALES_AT = 33 * KB
TAB_AT = (50 * KB, 58 * KB, 66 * KB)
TAB_SCALES_AT = TAB_AT[2] + 6 * KB
WGS_FIRST_AT = TAB_AT[0] + EDGE - 2 * KB
W4_RAW_AT = (25 * KB, TAB_AT[1] + 4 * KB + EDGE)
WGS_AT = TAB_AT[1] + EDGE
W2_PARTS = ((0, slice(0, N)), (1, slice(0, P)), (1, slice(P, N)))
W2_RAW_AT = (TAB_AT[1] + EDGE - 6 * KB, PICKED_SCALES_AT + 512, W4_ORD_AT[0] - 512)
PIECE_AT = ((SQUARE_AT + 2 * KB + 512, 234 * KB + 512, 75 * KB), (85 * KB + 512, 81 * KB, 77 * KB))
H_AT = {2: 94 * KB, 3: 90 * KB, 4: 102 * KB, 5: 106 * KB, 6: 110 * KB, 7: 114 * KB}
PICKED_AT = 127 * KB
RACK_AT = (PICKED_SCALES_AT + 512 - 8 * KB, TAB_AT[2] - KB + EDGE, WGS_FIRST_AT + EDGE - 8 * KB, PICKED_AT - 8 * KB + EDGE, PICKED_AT + EDGE, PICKED_AT + 8 * KB + EDGE, 75 * KB, 86 * KB)
WEIGHTED_AT = {2: RACK_AT[7], 7: H_AT[6]}
W2_BF_AT = (236 * KB - 256, H_AT[2], H_AT[5])
PAIRS_AT = (173 * KB, 189 * KB)
DIFF_AT = (W2_RAW_AT[1] + KB + 512, H_AT[3], H_AT[4], W2_RAW_AT[2], H_AT[7], PAIRS_AT[0] + 4 * KB, PAIRS_AT[0] + 8 * KB, H_AT[3])
JOINED0_AT = {"A": 230 * KB + 512, "B": RACK_AT[4], "C": RACK_AT[5], "E": 233 * KB - 512, "D": RACK_AT[6]}
JOINED1_AT = 205 * KB
Z_CODES_AT = (16 * KB, 221 * KB)
Z_SCALES1_AT = 24 * KB
W2_CODES_AT = WEIGHTED_AT[7]
RESULT_AT = TAB_AT[0]
LOW_SQUARE_AT = (SQUARE_AT, SQUARE_AT + 2 * KB - EDGE)
HIGH_SQUARE_AT = (SQUARE_AT + 4 * KB - 2 * EDGE, SQUARE_AT - 2 * KB - EDGE)
FIRST_SQUARES_AT = ({"C": TAB_PLANES_AT[0], "D": TAB_PLANES_AT[2]}, {"C": SQUARE_AT + 6 * KB - EDGE, "D": SQUARE_AT + 4 * KB - EDGE})
LAST_SQUARE_AT = {"A": SQUARE_AT + 3 * KB - EDGE, "B": SQUARE_AT + 4 * KB - EDGE, "C": SQUARE_AT + 6 * KB - EDGE, "D": 166 * KB, "E": 169 * KB}
W2_SCALES_AT = DIFF_AT[6] + 2 * KB + EDGE
LAST_DIFF_AT = {"A": H_AT[4], "B": H_AT[4] + KB, "C": W2_SCALES_AT - 2 * KB, "D": LAST_SQUARE_AT["A"] - 2 * KB + EDGE, "E": LAST_SQUARE_AT["C"] + 2 * KB - EDGE}
Z_SCALES0_AT = {"B": W2_SCALES_AT + KB, "A": W2_SCALES_AT + KB + BANK, "C": LAST_SQUARE_AT["B"], "D": PAIRS_AT[1] + 8 * KB, "E": LAST_SQUARE_AT["D"]}


def tile_list_pallet_slot_fit_kernel(tc, tab_words, tab_scales, offs, w4_words, w4_scales, offs2, wgs, rack, sharp, gain, w2, out):
    nc = tc.nc
    with ExitStack() as ctx:
        lists = ctx.enter_context(tc.tile_pool(name="lists", bufs=1))
        keep = ctx.enter_context(tc.tile_pool(name="keep", bufs=1))
        laid = ctx.enter_context(tc.tile_pool(name="laid", bufs=1))
        psum = ctx.enter_context(tc.psum_pool(name="psum", bufs=1))

        offs_t = lists.tile([P, S // 16], U16, name="offs_t")
        offs2_t = lists.tile([P, S // 16], U16, name="offs2_t")
        banks = [psum.tile([P, BANK], F32, name="bank%d" % j) for j in range(BANKS)]

        def cols_of(j, width):
            return slice(j * width, (j + 1) * width)

        def listed(cols):
            return slice(cols.start // 16, cols.stop // 16)

        def width(cols):
            return cols.stop - cols.start

        def place(name, shape, dtype, at):
            return laid.tile(shape, dtype, name=name, offset=at, align_bytes=64)

        def zero(engine, words):
            count = words.shape[1]
            for cols in (slice(0, count - 1), slice(count - 1, count)):
                engine.memset(words[:, cols], 0)

        lower, upper, whole = slice(0, BANK), slice(BANK, S), slice(0, S)

        tab_win = [place("tab_win%d" % a, [P, T], I32, TAB_AT[a]) for a in range(KA)]
        tab_scales_raw = place("tab_scales_raw", [P, T], U8, TAB_SCALES_AT)
        w4_scales_raw = place("w4_scales_raw", [P, KA * H], U8, W4_SCALES_AT)
        pages = [place("page%d" % j, [P, T2], F32, PAGE_AT[j]) for j in range(2)]
        gain_t = keep.tile([P, RB, PACK], F32, name="gain_t")
        sharp_t = keep.tile([P, SLOTS], F32, name="sharp_t")
        neg_sharp = keep.tile([P, SLOTS], F32, name="neg_sharp")
        ln_gain = keep.tile([P, SLOTS], F32, name="ln_gain")
        identity = keep.tile([P, P], F32, name="identity", align_bytes=64)
        w4_raw = {}

        def load_table(a):
            nc.sync.dma_start(tab_win[a][:], tab_words[a].rearrange("p t i -> p (t i)").bitcast(I32))

        def load_w4(b):
            w4_raw[b] = place("w4_raw%d" % b, [P, KA, H], U8, W4_RAW_AT[b])
            nc.sync.dma_start(w4_raw[b][:].bitcast(I32), w4_words[:, :, cols_of(b, H)].rearrange("a p n -> p a n").bitcast(I32))

        nc.sync.dma_start(offs_t[:], offs)
        nc.scalar.dma_start(gain_t[:], gain.rearrange("(b p i) -> p b i", b=RB, i=PACK))
        nc.scalar.dma_start(sharp_t[:].rearrange("p (b i) -> p b i", b=RB), sharp.rearrange("(b p i) -> p b i", b=RB, i=PACK))
        scale_rows = tab_scales.bitcast(I32).rearrange("a r t -> (a r) t")
        for row, rows in ((SCALE_ROWS[0], slice(0, 32)), (SCALE_ROWS[2], slice(32, 48))):
            nc.sync.dma_start(tab_scales_raw[row : row + width(rows), :].bitcast(I32), scale_rows[rows, :])
        load_table(0)
        nc.sync.dma_start(offs2_t[:], offs2)
        load_w4(0)
        load_table(1)

        zero(nc.vector, tab_scales_raw[0 : SCALE_ROWS[2], :].bitcast(I32))
        all_planes = place("tab_planes", [P, KA * S], U8, TAB_PLANES_AT[0])
        tab_planes = [all_planes[:, cols_of(a, S)] for a in range(KA)]
        zero(nc.vector, all_planes[:].bitcast(I32))
        zero(nc.vector, pages[0][:])
        nc.gpsimd.memset(w4_scales_raw[:].bitcast(I32), 0)
        for q in range(QUADRANTS):
            nc.gpsimd.dma_start(
                w4_scales_raw[32 * q : 32 * q + 4, :].bitcast(I32).rearrange("p (a n) -> p a n", a=KA),
                w4_scales[:, 4 * q : 4 * q + 4, :].bitcast(I32).rearrange("a r n -> r a n"),
            )
        make_identity(nc, identity[:])
        nc.gpsimd.memset(pages[1][:], 0.0)
        nc.scalar.activation(ln_gain[:], gain_t[:].rearrange("p b i -> p (b i)"), ACT.Ln)
        nc.scalar.mul(neg_sharp[:], sharp_t[:], -1.0)
        warm = keep.tile([P, 1], F32, name="warm")
        nc.scalar.activation(warm[:], neg_sharp[:, 0:1], ACT.Exp)

        w4_ord = {}

        def order_w4_words(b):
            w4_ord[b] = place("w4_ord%d" % b, [P, KA * H], U8, W4_ORD_AT[b])
            for two in (slice(0, 2), slice(2, PACK)):
                for a in range(KA):
                    nc.scalar.copy(
                        w4_ord[b][:].bitcast(U16)[:, cols_of(a, BANK)].rearrange("p (i m) -> p i m", i=PACK)[:, two, :],
                        w4_raw[b][:, a, :].bitcast(U16).rearrange("p (m i) -> p i m", i=PACK)[:, two, :],
                    )

        order_w4_words(0)
        w4_planes = [place("w4_planes%d" % b, [P, KA * BANK], U8, W4_PLANES_AT + KA * BANK * b) for b in range(RB)]
        for b in range(RB):
            nc.gpsimd.tensor_copy(
                w4_planes[b][:].rearrange("p (a i m) -> p a i m", a=KA, i=PACK),
                w4_scales_raw[:].rearrange("p (a b m i) -> p b a i m", a=KA, b=RB, i=PACK)[:, b],
            )

        picked = [place("picked%d" % a, [P, S], U32, PICKED_AT + 4 * KB * a) for a in range(KA)]

        def gather_words(a, cols):
            nc.vector.tensor_copy(picked[a][:, cols], tab_win[a][:].bitcast(U32).indirect(offs_t[:, listed(cols)]))

        picked_scales = place("picked_scales", [P, S], U8, PICKED_SCALES_AT)
        nc.vector.tensor_copy(picked_scales[:], tab_scales_raw[:].indirect(offs_t[:]))
        for shift in range(KA * QUADRANTS):
            if shift == EARLY_SHIFTS:
                load_table(2)
            a, q = divmod(shift, QUADRANTS)
            source = SCALE_ROWS[a] + 4 * q
            nc.sync.dma_start(tab_planes[a][32 * q : 32 * q + 4, :].bitcast(I32), picked_scales[source : source + 4, :].bitcast(I32))
        gather_words(0, whole)
        wgs_first = place("wgs_first", [P, PIECES[1].stop], F32, WGS_FIRST_AT)
        nc.sync.dma_start(wgs_first[:], wgs[:, 0 : PIECES[1].stop])
        gather_words(1, whole)
        for cols in PIECES:
            gather_words(2, cols)

        rack_rows = rack.rearrange("(b p i) m -> b i p m", b=RB, i=PACK)
        racks = {}
        w2_raw = {}

        def load_rack(s):
            racks[s] = place("rack%d" % s, [P, T2], F32, RACK_AT[s])
            nc.sync.dma_start(racks[s][:], rack_rows[s // PACK, s % PACK])

        def load_w2(part):
            b, cols = W2_PARTS[part]
            w2_raw[part] = place("w2_raw%d" % part, [P, PACK, width(cols)], F32, W2_RAW_AT[part])
            nc.sync.dma_start(w2_raw[part][:], w2.rearrange("(b p i) n -> b p i n", b=RB, i=PACK)[b, :, :, cols])

        wgs_t = place("wgs_t", [P, S], F32, WGS_AT)
        load_w4(1)
        nc.sync.dma_start(wgs_t[:], wgs)
        load_w2(0)
        load_rack(0)
        load_w2(1)
        load_rack(1)

        def h_pass(s, cols, bank, a, order=(0, 1, 2)):
            b, i = divmod(s, PACK)
            runs = [cols] if width(cols) != 3 * P else [slice(cols.start, cols.start + P), slice(cols.start + P, cols.stop)]
            for run in runs:
                nc.tensor.matmul_mx(
                    out=banks[bank][:, run.start - cols.start : run.stop - cols.start],
                    lhsT=w4_ord[b][:, cols_of(a * PACK + i, 2 * P)].bitcast(FP4X4),
                    lhsT_scale=w4_planes[b][:, cols_of(a * PACK + i, P)],
                    rhs=picked[a][:, run].bitcast(FP8X4),
                    rhs_scale=tab_planes[a][:, run],
                    start=(a == order[0] and run is runs[0]),
                    stop=(a == order[-1] and run is runs[-1]),
                )

        def h_group(s, cols, bank, target):
            for a in range(KA):
                h_pass(s, cols, bank, a)
            nc.scalar.mul(target, banks[bank][:, 0 : width(cols)], -1.0)

        def scatter(s, cols, source):
            nc.vector.tensor_copy(pages[s % 2][:].indirect(offs2_t[:, listed(cols)]), source)

        opening = [(s, cols) for cols in PIECES for s in range(2)] + [(2, lower), (2, upper)]
        ahead = [2 if bank < EARLY_GROUPS else 0 for bank in range(BANKS)]
        for a in range(KA - 1):
            for bank, (s, cols) in enumerate(opening):
                if a < ahead[bank]:
                    h_pass(s, cols, bank, a, (0, 1, 2) if ahead[bank] == 2 else (0, 2, 1))
        pieces = {}
        h = {2: place("h2", [P, S], F32, H_AT[2])}
        for bank, (s, cols) in enumerate(opening):
            order = ((2, 0, 1), (0, 2, 1), (0, 1, 2))[ahead[bank]]
            for a in order[ahead[bank] :]:
                h_pass(s, cols, bank, a, order)
            if bank == 2 * (len(PIECES) - 1):
                order_w4_words(1)
            if s == 2:
                nc.scalar.mul(h[2][:, cols], banks[bank][:], -1.0)
                continue
            for j, cut in enumerate(CUTS_OF_LIST[s]):
                both = slice(max(cut.start, cols.start), min(cut.stop, cols.stop))
                if both.start >= both.stop:
                    continue
                if (s, j) not in pieces:
                    pieces[s, j] = place("piece%d_%d" % (s, j), [P, width(cut)], F32, PIECE_AT[s][j])
                piece = pieces[s, j]
                nc.scalar.mul(piece[:, both.start - cut.start : both.stop - cut.start], banks[bank][:, both.start - cols.start : both.stop - cols.start], -1.0)
                if both.stop == cut.stop:
                    nc.gpsimd.tensor_tensor(piece[:], piece[:], wgs_first[:, cut] if cut.stop <= BANK else wgs_t[:, cut], ALU.mult)
                    scatter(s, cut, piece[:])
        load_rack(2)

        weighted = {}

        def h_slot(s):
            h[s] = place("h%d" % s, [P, S], F32, H_AT[s])
            for cols, bank in zip((lower, upper), H_BANKS[s]):
                h_group(s, cols, bank, h[s][:, cols])

        for s in range(3, SLOTS - 2):
            h_slot(s)

        def weigh(s):
            weighted[s] = place("weighted%d" % s, [P, S], F32, WEIGHTED_AT[s])[:] if s in WEIGHTED_AT else racks[s - 3][:, whole]
            nc.gpsimd.tensor_tensor(weighted[s], h[s][:], wgs_t[:], ALU.mult)

        w2_bf = {}

        def round_w2(part):
            w2_bf[part] = place("w2_bf%d" % part, [P, width(W2_PARTS[part][1]) * PACK], BF16, W2_BF_AT[part])
            nc.gpsimd.tensor_scalar(w2_bf[part][:].rearrange("p (n i) -> p n i", i=PACK), w2_raw[part][:].rearrange("p i n -> p n i"), 1.0, 0.0, ALU.mult, ALU.add)

        weigh(2)
        round_w2(1)
        w2_bf[0] = place("w2_bf0", [P, N * PACK], BF16, W2_BF_AT[0])
        for t in range(2 * NT):
            nc.scalar.copy(w2_bf[0][:, cols_of(t, HALF * PACK)].rearrange("p (n i) -> p n i", i=PACK), w2_raw[0][:, :, cols_of(t, HALF)].rearrange("p i n -> p n i"))

        pairs = {}
        slotwise = {}
        joined = {}
        z_codes = {}
        z_scales = {}

        def open_pairs(b):
            for c, cols in CUTS[b].items():
                at = PAIRS_AT[b] + 2 * PACK * cols.start
                if b == 0 and c not in "AE":
                    slotwise[c] = place("slotwise" + c, [P, PACK, width(cols)], BF16, at)
                else:
                    pairs[b, c] = place("pairs%d%s" % (b, c), [P, 2, width(cols), 2], BF16, at)

        def exp_to_z(s, c, square):
            b, i = divmod(s, PACK)
            target = pairs[b, c][:, i // 2, :, i % 2] if (b, c) in pairs else slotwise[c][:, i, :]
            nc.scalar.activation(target, square, ACT.Exp, bias=ln_gain[:, s : s + 1], scale=neg_sharp[:, s : s + 1])

        def turned_sums(s):
            for c, bank in TURN_BANKS[s].items():
                blocks = BANK // P
                for k, source in enumerate((racks[s], pages[s % 2])):
                    for j in range(blocks):
                        nc.tensor.matmul(
                            banks[bank][:, cols_of(j, P)], source[:, cols_of(CHUNKS[c].start // P + j, P)], identity[:],
                            start=(k == 0 and j == 0), stop=(k == 1 and j == blocks - 1), is_transpose=True,
                        )


        def square_turned(s, c, at):
            square = place("square%d%s" % (s, c), [P, BANK], F32, at)
            nc.scalar.activation(square[:], banks[TURN_BANKS[s][c]][:], ACT.Square)
            for j in range(BANK // P):
                nc.tensor.transpose(banks[TURN_BANKS[s][c]][:, cols_of(j, P)], square[:, cols_of(j, P)], identity[:])

        last = SLOTS - 1

        def slot_to_z(s):
            parts = (lower, upper) if s >= SPLIT_FROM else (whole,)
            diffs = [place("diff%d_%d" % (s, cols.start), [P, width(cols)], F32, DIFF_AT[s] + 4 * cols.start) for cols in parts]
            for diff, cols in zip(diffs, parts):
                nc.gpsimd.tensor_tensor(diff[:], racks[s][:, cols], pages[s % 2][:, cols], ALU.add)
            turned_sums(s)
            if s == 0:
                h_slot(last - 1)
                h_slot(last)
            turned_at = FIRST_SQUARES_AT[s] if s < 2 else {"C": DIFF_AT[s], "D": DIFF_AT[s] + 2 * KB}
            if s == 1:
                for c in "CD":
                    square_turned(s, c, turned_at[c])
            low = place("low_square%d" % s, [P, BANK], F32, LOW_SQUARE_AT[s % 2])
            high = place("high_square%d" % s, [P, BANK + 2 * EDGE // 4], F32, HIGH_SQUARE_AT[s % 2])[:, lower]
            nc.scalar.activation(low[:], diffs[0][:, lower], ACT.Square)
            if len(parts) == 2:
                square_turned(s, "C", turned_at["C"])
            nc.scalar.activation(high, diffs[-1][:, lower if len(parts) == 2 else upper], ACT.Square)
            for c in "" if s == 1 else "D" if len(parts) == 2 else "CD":
                square_turned(s, c, turned_at[c])
            for c in "CDABE" if s == 1 else "ACBED":
                exp_to_z(s, c, banks[TURN_BANKS[s][c]][:] if c in TURN_BANKS[s] else high if c == "B" else low[:, CHUNKS[c]])

        def join(copy, dtype, b, c):
            cols = CHUNKS[c]
            at = JOINED0_AT[c] if b == 0 else JOINED1_AT + 2 * PACK * cols.start
            joined[b, c] = place("joined%d%s" % (b, c), [P, width(cols) * PACK], BF16, at)
            copy(
                joined[b, c][:].bitcast(dtype).rearrange("p (m e h) -> p m h e", e=LINE, h=2),
                pairs[b, c][:].rearrange("p h m e -> p (h m e)").bitcast(dtype).rearrange("p (h m e) -> p m h e", e=LINE, h=2),
            )

        def interleave(c):
            joined[0, c] = place("joined0" + c, [P, BANK * PACK], BF16, JOINED0_AT[c])
            nc.gpsimd.tensor_scalar(joined[0, c][:].rearrange("p (m i) -> p m i", i=PACK), slotwise[c][:].rearrange("p i m -> p m i"), 1.0, 0.0, ALU.mult, ALU.add)

        open_pairs(0)
        for s in range(last):
            if s == PACK:
                open_pairs(1)
            slot_to_z(s)
            if s + 2 < SLOTS:
                scatter(s + 2, whole, weighted[s + 2])
            if s == 0:
                load_w2(2)
                for later in range(3, last):
                    load_rack(later)
            if s == 1:
                load_rack(last)
            for nxt in {0: (3,), 1: (4,), 2: (5,), 3: (6, 7)}.get(s, ()):
                weigh(nxt)
            if s == 2:
                round_w2(2)
            if s == PACK - 1:
                for c in "AE":
                    join(nc.scalar.copy, U32, 0, c)
            for c in INTERLEAVED.get(s, ()):
                interleave(c)

        w2_codes = place("w2_codes", [P, RB * N], U32, W2_CODES_AT)
        w2_scales = place("w2_scales", [P, RB * N], U8, W2_SCALES_AT)
        diffs = {}
        squares = {}

        def last_difference(c):
            cols = SPANS[c]
            diffs[c] = place("last_diff" + c, [P, width(cols)], F32, LAST_DIFF_AT[c])
            nc.vector.tensor_tensor(diffs[c][:], racks[last][:, cols], pages[last % 2][:, cols], ALU.add)

        def last_square(c):
            squares[c] = place("last_square" + c, [P, width(CHUNKS[c])], F32, LAST_SQUARE_AT[c])
            nc.scalar.activation(squares[c][:], diffs[c][:], ACT.Square)

        def last_exp(c):
            exp_to_z(last, c, squares[c][:])

        def quantise_w2(part):
            b, cols = W2_PARTS[part]
            cols = slice(b * N + cols.start, b * N + cols.stop)
            nc.vector.quantize_mx(out=w2_codes[:, cols].bitcast(FP8X4), scales=w2_scales[:, cols], in_=w2_bf[part][:])

        def product(b, c):
            cols = CUTS[b][c]
            codes = place("z_codes%d%s" % (b, c), [P, width(cols)], U32, Z_CODES_AT[b] + 4 * cols.start)
            scales = place("z_scales%d%s" % (b, c), [P, width(cols)], U8, Z_SCALES0_AT[c] if b == 0 else Z_SCALES1_AT + cols.start)
            nc.vector.quantize_mx(out=codes[:].bitcast(FP8X4), scales=scales[:], in_=joined[b, c][:])
            z_codes[b, c], z_scales[b, c] = codes, scales

        opened = set()

        def out_pass(passes, c):
            for t in range(NT):
                for b in passes:
                    held = c if b == 1 else SPAN_OF[c]
                    first = CUTS[b][held].start
                    cols = slice(CHUNKS[c].start - first, CHUNKS[c].stop - first)
                    nc.tensor.matmul_mx(
                        out=banks[OUT_BANKS[c][t]][:, 0 : width(CHUNKS[c])],
                        lhsT=w2_codes[:, cols_of(b * NT + t, P)].bitcast(FP8X4),
                        lhsT_scale=w2_scales[:, cols_of(b * NT + t, P)],
                        rhs=z_codes[b, held][:, cols].bitcast(FP8X4),
                        rhs_scale=z_scales[b, held][:, cols],
                        start=(c, t) not in opened,
                        stop=(c, t) in opened,
                    )
                    opened.add((c, t))

        def store(c, t, copy):
            cols = CHUNKS[c]
            res = place("res%s%d" % (c, t), [P, width(cols)], F32, RESULT_AT + 4 * (NT * cols.start + t * width(cols)))
            copy(res[:], banks[OUT_BANKS[c][t]][:, 0 : width(cols)])
            nc.sync.dma_start(out[cols_of(t, P), cols], res[:])

        def join_last(c):
            join(nc.vector.tensor_copy, I32, 1, c)

        on_scalar, on_vector = nc.scalar.copy, nc.vector.tensor_copy
        last_difference("A")
        last_difference("B")
        quantise_w2(0)
        product(0, "B")
        out_pass((0,), "B")
        last_difference("C")
        quantise_w2(1)
        quantise_w2(2)
        product(0, "A")
        last_square("A")
        last_square("B")
        last_exp("A")
        last_exp("B")
        join_last("A")
        last_difference("D")
        product(1, "A")
        out_pass((1, 0,), "A")
        last_square("C")
        join_last("B")
        product(0, "C")
        product(1, "B")
        out_pass((1,), "B")
        last_exp("C")
        store("A", 0, on_scalar)
        store("A", 1, on_scalar)
        store("A", 2, on_scalar)
        last_square("D")
        join_last("C")
        last_difference("E")
        product(1, "C")
        out_pass((1, 0,), "C")
        store("B", 0, on_scalar)
        last_exp("D")
        store("B", 1, on_scalar)
        product(0, "D")
        store("B", 2, on_scalar)
        join_last("D")
        product(0, "E")
        product(1, "D")
        last_square("E")
        store("C", 0, on_scalar)
        last_exp("E")
        store("C", 1, on_scalar)
        out_pass((1, 0,), "D")
        join_last("E")
        store("C", 2, on_vector)
        product(1, "E")
        store("D", 0, on_scalar)
        out_pass((1, 0,), "E")
        store("D", 1, on_vector)
        store("D", 2, on_scalar)
        store("E", 0, on_vector)
        store("E", 1, on_scalar)
        store("E", 2, on_vector)
